import numpy as np, ml_dtypes
CORES = [10,34,74,98]
N = 4
import mx_ref
BF = ml_dtypes.bfloat16
def gentries(a):
    return np.ascontiguousarray(a.reshape(8, 16, -1).transpose(0, 2, 1)).reshape(8, -1)
def gtable(e):
    e = np.asarray(e); return np.ascontiguousarray(e.reshape(8, -1, 16).transpose(0, 2, 1)).reshape(128, -1).astype(np.int32)
def gcols(t, e):
    v = np.concatenate([t.reshape(8, 16, -1, 4), np.zeros((8, 16, 1, 4), BF)], axis=2)
    return np.ascontiguousarray(np.stack([v[g][:, e[g]] for g in range(8)])).reshape(128, -1)
def tile(rs):
    return np.stack(rs, axis=2).reshape(128, -1).astype(BF)
def pick(q, e):
    c = np.concatenate([q[0].reshape(128, -1, 4), np.zeros((128, 1, 4), np.uint8)], axis=1); s = np.concatenate([q[1], np.ones((16, 1), np.uint8)], axis=1)
    return (np.ascontiguousarray(c[:, e].reshape(128, -1)), np.ascontiguousarray(s[:, e]))
def join(*qs):
    return (np.concatenate([q[0] for q in qs], axis=1), np.concatenate([q[1] for q in qs], axis=1))
def put(q, e, v):
    c, s = q[0].reshape(128, -1, 4).copy(), q[1].copy(); c[:, e] = v[0].reshape(128, -1, 4); s[:, e] = v[1]
    return (c.reshape(128, -1), s)
def pk(c, s):
    return (np.ascontiguousarray(c), mx_ref.live(s))
def emit(q):
    return q[0], q[1]
def packed(v, rng):
    q = [mx_ref.quantize(np.ascontiguousarray(v[r])) for r in range(N)]
    return np.stack([a for a, b in q]), np.stack([mx_ref.plane(b, rng) for a, b in q])
def values_of_codes():
    e, c = np.zeros((128, 128, 4), np.float32), np.zeros((128, 2, 4), np.uint8)
    e[np.arange(128), np.arange(128), 0] = 1
    c[:127, :, 0] = np.arange(256).reshape(2, 128).T[:127]
    return mx_ref.matmul(mx_ref.quantize(e.reshape(128, 512).astype(BF)), (c.reshape(128, 8), np.full((16, 2), 127, np.uint8))).T.reshape(-1).astype(np.float64)
CODE_VALUE, SCALE_VALUE = values_of_codes(), 2.0 ** (np.arange(256) - 127.0)
def decode(q):
    return (CODE_VALUE[q[0]].reshape(16, 8, -1, 4) * SCALE_VALUE[q[1]][:, None, :, None] + 0.0).reshape(128, -1).astype(np.float32)
def f(rng, *shape):
    return mx_ref.flush((rng.standard_normal(shape, dtype=np.float32) * np.exp2(rng.integers(-2, 3, shape[:-1] + (1,)))).astype(BF))
def wide(rng, *shape, cols=0):
    v = rng.standard_normal(shape, dtype=np.float32) * np.exp2(rng.integers(-12, 13, shape)).astype(np.float32)
    if cols: v *= np.repeat(np.exp2(rng.integers(-cols, cols + 1, shape[:-2] + (1, shape[-1] // 4))) * (rng.random(shape[:-2] + (1, shape[-1] // 4)) > 0.0625), 4, axis=-1).astype(np.float32)
    return mx_ref.flush(v.astype(BF))
C = 320
STEP = [1, 2, 3]
HOPS = 128
def numbers_of(rng):
    return {"x": np.array(f(rng, N, 128, 4 * C)), "u": np.array(f(rng, N, 128, 512)), "v": np.array(f(rng, N, 128, 512))}
def orders(rng):
    e = np.tile(np.arange(C), (N, 8, 1))
    k, a, t = rng.permuted(e, axis=2), rng.permuted(e, axis=2)[:, :, 16:], e.copy()
    np.put_along_axis(t, a[:, :, 0::2], a[:, :, 1::2], axis=2)
    np.put_along_axis(t, a[:, :, 1::2], a[:, :, 0::2], axis=2)
    return k, t
def stored(k, t):
    return {"nx": np.stack([gtable(k[r]) for r in range(N)]), "mt": np.stack([gtable(t[r]) for r in range(N)])}
def layers(rng, still=[]):
    w = np.array(f(rng, N, 128, 2048)).reshape(N, 8, 16, 4, 8, 16, 4)
    for i in still:
        w[:, :, i] = 0
        w[:, :, :, :, :, i] = 0
    return w
def weights(rng, w):
    c, p = packed(np.ascontiguousarray(w).reshape(N, 128, 2048), rng)
    return {"wc": c, "ws": p}
def setup_inputs(rng):
    return {**numbers_of(rng), **stored(*orders(rng)), **weights(rng, layers(rng))}
def setup_inputs_ties(rng):
    d = numbers_of(rng)
    k, t = orders(rng)
    o = rng.permutation(N) % 4
    n = rng.integers(0, 4, (N, 8, C))
    c = np.ones((N, 8), np.float32)
    for r in range(N):
        c[r] = rng.permutation(8) % 2 * 2.0 - 1.0
        for g in range(8):
            if o[r] < 2:
                e = rng.permutation(C)
                a = np.arange(C) + 1 if c[r, g] < 0 else C - np.arange(C)
                n[r, g, e] = a if o[r] == 0 else (a + 1) // 2
                k[r, g, e] = np.roll(e, -1)
            if o[r] == 3: n[r, g] = rng.integers(0, 2, C) if g % 2 else 1
        if o[r] < 2: t[r, rng.permutation(8)[:4]] = np.arange(C)
    digits = (n[..., None] & (1 << np.arange(12))).reshape(N, 8, C, 3, 4)
    x = d["x"].reshape(N, 8, 16, C, 4)
    x[:, :, 8:] = 0
    x[:, :, 8:11] = digits.transpose(0, 1, 3, 2, 4).astype(np.float32).astype(BF)
    u = d["u"].reshape(N, 128, 128, 4)
    u[:, :, ::16] = 0
    for g in range(8): u[:, 16 * g + 8:16 * g + 11, 16 * g] = c[:, g].astype(BF)[:, None, None]
    w = layers(rng)
    w[:, :, :, :, :, 8:] = 0
    return {"x": x.reshape(N, 128, 4 * C), "u": u.reshape(N, 128, 512), "v": d["v"], **stored(k, t), **weights(rng, w)}
def setup_inputs_near(rng):
    d = numbers_of(rng)
    x = d["x"].astype(np.float32).reshape(N, 8, 16, C, 4)
    x[:, :, :2] = 0
    x[:, :, 8:] = 0
    u = d["u"].reshape(N, 128, 128, 4)
    u[:, :, ::16] = 0
    w = layers(rng, [0, 1, 8, 9, 10, 11, 12, 13, 14, 15])
    o = (np.arange(N) + rng.integers(N)) % 4
    for r in range(N):
        c = rng.choice([-1.0, 1.0], (8, 1))
        s = rng.integers(0, 16, (8, C))
        digits = ((s[:, :, None] >> np.arange(4)) & 1) * np.exp2(np.arange(4) - 23.0)
        if o[r] < 2:
            x[r, :, 0, :, 0] = c
            x[r, :, 8] = digits
            x[r, :, 11, :, 0] = 2.0 ** -10
        else:
            x[r, :, :8] = 0
            x[r, :, 13, :, 0] = 2.0 ** -30
            x[r, :, 1, :, 0] = rng.choice([-1.0, 1.0], (8, C)) * 2.0 ** -30
            w[r] = 0
            for g in range(8): w[r, g, 1, 0, g, 12, 0] = 2.0 ** -8
        if o[r] == 2: x[r, :, 8] = digits * rng.choice([-1.0, 1.0], (8, C, 1))
        if o[r] == 3:
            x[r, :, 8, :, 0] = np.where(s < 8, 1.25, 0.0) * 2.0 ** -30 * c
            x[r, :, 9, :, 0] = np.where(s < 8, 0.0, 1.125) * 2.0 ** -30 * c
            for g in rng.permutation(8)[:4]:
                e = rng.choice([-1.0, 1.0], C) * 2.0 ** -30
                x[r, g, 8, :, 0] = 1.25 * e
                x[r, g, 9, :, 0] = -1.125 * e
        at = [0, C - 1, int(rng.integers(C)), int(rng.integers(C))]
        for g, j in zip(rng.permutation(8)[:4], at): x[r, g, 0, j, 0] = 2.0 ** 29 * rng.choice([-1.0, 1.0])
        k = 1.0 if o[r] == 0 else 2.0 ** -30
        for h in range(0, 128, 16):
            u[r, h, h, 0] = k if o[r] < 2 else 1.0
            if o[r] < 2: u[r, h + 11, h, 0] = k
            if o[r] < 3: u[r, h + 8, h] = k
            else:
                u[r, h + 8, h, 0] = k
                u[r, h + 9, h, 0] = 1.125 * k
                u[r, h + 12, h, 0] = k
    return {"x": x.reshape(N, 128, 4 * C).astype(BF), "u": u.reshape(N, 128, 512), "v": d["v"], **stored(*orders(rng)), **weights(rng, w)}
def setup_inputs_odd(rng):
    d = numbers_of(rng)
    w = layers(rng, [0, 8])
    x = (1.0 + (2 * rng.integers(0, 64, (N, 16, 8, C, 4)) + 1) * 2.0 ** -7) * np.exp2(-rng.integers(0, 7, (N, 16, 8, C, 4)).astype(np.float64)) * rng.choice([-1.0, 1.0], (N, 16, 8, C, 4))
    x[:, 0::2, 0, :, 0] = 1.96875 * 2.0 ** 8 * rng.choice([-1.0, 1.0], (8, 1))
    x[:, 1::2, 0, :, 0] = rng.choice([1.96875 * 2.0 ** 8, 8.0], (N, 8, C)) * rng.choice([-1.0, 1.0], (N, 8, C))
    for g in range(8): w[:, g, 0, 0, g, 0, 0] = -0.5
    u = d["u"].reshape(N, 16, 8, 128, 4)
    u[:, :, 0, ::16] = 0
    for r in rng.permutation(N)[:N // 2]:
        for i, g in enumerate(rng.permutation(8)[:4]):
            x[r, 2 * g, 1, :, 0] = (8 + rng.integers(0, 2, C)) * 2.0 ** (i - 8)
            u[r, :, :, 16 * g] = 0
            u[r, 2 * g, 1, 16 * g, 0] = 1.0
            w[r, :, :, 0, g, 1] = 0
    return {"x": x.astype(np.float32).reshape(N, 128, 4 * C).astype(BF), "u": u.reshape(N, 128, 512), "v": d["v"], **stored(*orders(rng)), **weights(rng, w)}
def setup_inputs_ends(rng):
    d = numbers_of(rng)
    k, t = orders(rng)
    o, e, m = rng.permutation(N) % 4, rng.permutation(N) % 4, rng.permutation(N) % 4
    for r in range(N):
        s = (r - STEP[-1]) % N
        if o[r] == 3 and o[s] == 2:
            a = rng.choice([n for n in range(N) if o[n] < 2 and o[(n + STEP[-1]) % N] != 3])
            o[s] = o[a]
            o[a] = 2
    i = np.arange(C)
    k[e == 0] = i
    k[e == 1] = (i + 1) % C
    k[e == 2] = C - 1 - i
    k[e == 3] = (i - 1) % C
    t[m == 0] = i
    t[m == 1] = C - 1 - i
    t[m == 2] = i ^ 1
    x = np.zeros((N, 8, 16, C, 4))
    u = d["u"].astype(np.float32).reshape(N, 128, 128, 4)
    v = d["v"].astype(np.float32)
    w = np.zeros((N, 128, 4, 128, 4), np.float32)
    j = np.arange(128)
    for r in range(N):
        h = rng.permutation(8)
        c = np.where(h < 2, 0.0, h % 2 * 2.0 - 1.0)[None, :, None]
        low = -(0.7 + 0.1 * rng.random((8, 16, C, 4))) * 2.0 ** 30
        if o[r] == 0: x[r] = low
        if o[r] == 1: x[r] = low * rng.choice([-1.0, 1.0], (C, 1))
        if o[r] == 2: x[r] = -(1.0 + 0.125 * rng.integers(0, 8, (8, 16, C, 4))) * 2.0 ** -30
        if o[r] == 3: x[r] = d["x"][r].astype(np.float32).reshape(8, 16, C, 4)[:, :, :1]
        if o[r] < 2:
            u[r, :, ::16] = c * (0.9 + 0.1 * rng.random((128, 8, 4))) * 2.0 ** 30
            v[r] = rng.choice([-1.0, 1.0], (128, 512)) * (0.9 + 0.1 * rng.random((128, 512))) * 2.0 ** 30
        if o[r] == 2:
            u[r, :, ::16] = c * (1.0 + 0.125 * rng.integers(0, 8, (128, 8, 4))) * 2.0 ** -30
            v[r] = rng.choice([-1.0, 1.0], (128, 512)) * (1.0 + 0.125 * rng.integers(0, 8, (128, 512))) * 2.0 ** -30
        if o[r] == 3: u[r, :, ::16] *= np.abs(c).astype(np.float32)
        a = np.array([2.0, 2.0 ** -8, -0.25])[rng.permutation(8) % 3][j // 16]
        if o[r] == 2: a = np.zeros(128)
        a[120:] = 256.0
        for b in range(4): w[r, j, b, j, b] = a
    x[:, 7, 8:] = -2.0 ** -30
    return {"x": x.astype(np.float32).reshape(N, 128, 4 * C).astype(BF), "u": u.reshape(N, 128, 512).astype(BF), "v": v.astype(BF), **stored(k, t), **weights(rng, w.astype(BF))}
def setup_inputs_spread(rng):
    d = setup_inputs(rng)
    d["x"] = wide(rng, N, 128, 4 * C, cols=6)
    return d
def check_inputs(d):
    b = []
    for k in ("x", "u", "v"):
        a = np.abs(d[k].astype(np.float32))
        if not (np.isfinite(a).all() and ((a == 0) | (a >= 2.0 ** -30) & (a <= 2.0 ** 30)).all()): b.append("a value of " + k)
    none, least, most = [emit(mx_ref.quantize(np.full((128, 16), k, np.float32).astype(BF)))[1][0, 0] for k in (0.0, 2.0 ** -8, 2.0 ** 8)]
    for r in range(N):
        k, t = gentries(d["nx"][r]), gentries(d["mt"][r])
        if not (np.sort(k, axis=1) == np.arange(C)).all(): b.append("nx: not every column once")
        if not (((t >= 0) & (t < C)).all() and (np.take_along_axis(t, np.clip(t, 0, C - 1), axis=1) == np.arange(C)).all()): b.append("mt: not each other's")
        if ((d["wc"][r] == 0x7F) | (d["wc"][r] == 0xFF)).any(): b.append("wc: a code that is no number")
        s = mx_ref.live(d["ws"][r])
        if ((s != none) & ((s < least) | (s > most))).any(): b.append("ws: a scale out of range")
        if (((d["wc"][r].reshape(16, 8, 512, 4) & 0x7F) != 0) & (s == none)[:, None, :, None]).any(): b.append("wc: a code other than zero under the scale of zeros")
    return b
def at(a, e):
    return np.take_along_axis(a, e, axis=1)
def search(s, follow):
    b = np.tile(np.arange(C), (8, 1))
    p, left = b.copy(), np.ones((8, C), bool)
    for hop in range(1, HOPS + 1):
        to = at(follow, p)
        larger = left & (at(s, to) > s)
        b = np.where(larger, to, b)
        left = left & ~larger
        if hop < HOPS: p = np.where(left, to, p)
    return b, p
def layer(w, q):
    return tile([mx_ref.matmul(pick(w, np.arange(128 * k, 128 * k + 128)), q) * np.float32(0.03125) for k in range(4)])
def reference(x, u, v, nx, mt, wc, ws):
    qu = [mx_ref.quantize(u[r]) for r in range(N)]
    lay = [pk(wc[r], ws[r]) for r in range(N)]
    follow, mate = [gentries(nx[r]) for r in range(N)], [gentries(mt[r]) for r in range(N)]
    now = [x[r] for r in range(N)]
    for step in STEP:
        t, z, first = [], [], []
        for r in range(N):
            q = mx_ref.quantize(now[r])
            s = mx_ref.matmul(qu[r], q)[::16] + np.float32(0.0)
            b, p = search(s, follow[r])
            t.append(decode(q))
            c = t[r].astype(BF)
            z.append(mx_ref.quantize(((gcols(c, b).astype(np.float32) + gcols(c, p).astype(np.float32)) * np.float32(0.5)).astype(BF)))
            first.append(b)
            e = at(s, b)
            swap = at(e, np.minimum(mate[r], np.arange(C))) > at(e, np.maximum(mate[r], np.arange(C)))
            follow[r] = np.where(swap, at(follow[r], mate[r]), follow[r])
        now = [(t[r] + gcols(layer(lay[r], z[(r - step) % N]), first[r]).astype(np.float32)).astype(BF) for r in range(N)]
    y, nf = np.zeros((N, 128, C), np.float32), np.zeros((N, 8, C), np.float32)
    oc, osc = np.zeros((N, 128, 4 * C), np.uint8), np.zeros((N, 16, C), np.uint8)
    for r in range(N):
        q = mx_ref.quantize(now[r])
        y[r] = mx_ref.matmul(mx_ref.quantize(v[r]), q)
        nf[r] = follow[r]
        oc[r], osc[r] = emit(q)
    return {"y": y, "nf": nf, "oc": oc, "osc": osc}

@@ -1,0 +1,477 @@
+import numpy as np
+from concourse.mybir import dt, AluOpType, ActivationFunctionType
+A = AluOpType
+AF = ActivationFunctionType
+C = 320
+BANK = 512
+ROUNDS = 3
+BIG = 1e29
+GROUPS = [[6, 5], [4, 3], [2, 1], [0, -1]]
+
+SCRATCH = {
+    "x0": ("sbuf", [128, 4 * C], "bfloat16"), "ut": ("sbuf", [128, 512], "bfloat16"), "vt": ("sbuf", [128, 512], "bfloat16"),
+    "nxi": ("sbuf", [128, 20], "int32"), "mti": ("sbuf", [128, 20], "int32"),
+    "wq": ("sbuf", [128, 512], "float8_e4m3fn_x4"), "wp": ("sbuf", [128, 512], "uint8"),
+    "uq": ("sbuf", [128, 128], "float8_e4m3fn_x4"), "up": ("sbuf", [128, 128], "uint8"),
+    "uqr": ("sbuf", [128, 128], "float8_e4m3fn_x4"), "upr": ("sbuf", [128, 128], "uint8"),
+    "vq": ("sbuf", [128, 128], "float8_e4m3fn_x4"), "vp": ("sbuf", [128, 128], "uint8"),
+    "eq": ("sbuf", [128, 512], "float8_e4m3fn_x4"), "ep": ("sbuf", [128, 512], "uint8"),
+    "one": ("sbuf", [128, 528], "bfloat16"), "big": ("sbuf", [128, 528], "bfloat16"),
+    "ji": ("sbuf", [128, C], "int32"), "dg": ("sbuf", [128, C], "int32"), "t1": ("sbuf", [128, C], "float32"), "t2": ("sbuf", [128, C], "float32"),
+    "rs0": ("sbuf", [128, C], "bfloat16"), "rs": ("sbuf", [128, C], "bfloat16"), "wt": ("sbuf", [128, C], "bfloat16"),
+    "mask": ("sbuf", [128, C], "bfloat16"), "cap": ("sbuf", [128, C], "float32"), "idr": ("sbuf", [128, C], "bfloat16"),
+    "pi": ("sbuf", [128, 20], "int32"), "pa15": ("sbuf", [128, 20], "int32"), "ci": ("sbuf", [128, 20], "int32"),
+    "ui": ("sbuf", [128, 8], "int32"), "uo": ("sbuf", [128, 8], "uint16"),
+    "mt16": ("sbuf", [128, 20], "uint16"), "lo16": ("sbuf", [128, 20], "uint16"), "hi16": ("sbuf", [128, 20], "uint16"),
+    "srow": ("sbuf", [128, C], "float32"), "sm": ("sbuf", [128, C], "float32"),
+    "pr": ("sbuf", [128, C], "bfloat16"), "pws": ("sbuf", [128, C], "float16"),
+    "d0": ("sbuf", [128, C], "float32"), "d1": ("sbuf", [128, C], "float32"),
+    "cb": ("sbuf", [128, C], "bfloat16"), "cs": ("sbuf", [128, C], "bfloat16"),
+    "pb": ("sbuf", [128, C], "bfloat16"), "psn": ("sbuf", [128, C], "float16"),
+    "fb": ("sbuf", [128, C], "bfloat16"), "fr": ("sbuf", [128, C], "bfloat16"), "fsn": ("sbuf", [128, C], "float16"),
+    "fs": ("sbuf", [128, C], "bfloat16"),
+    "o0": ("sbuf", [128, 20], "uint16"), "o1": ("sbuf", [128, 20], "uint16"), "o3": ("sbuf", [128, 20], "uint16"),
+    "er": ("sbuf", [128, C], "float32"), "eh": ("sbuf", [128, C], "float32"), "sw": ("sbuf", [128, C], "bfloat16"),
+    "scn": ("sbuf", [128, C], "float16"), "swn": ("sbuf", [128, C], "float16"), "fmn": ("sbuf", [128, C], "float16"), "fmr": ("sbuf", [128, C], "bfloat16"),
+    "fo": ("sbuf", [128, 4 * C], "bfloat16"), "fh": ("sbuf", [128, 4 * C], "bfloat16"), "gp": ("sbuf", [128, 4 * C], "bfloat16"),
+    "z": ("sbuf", [128, 4 * C], "bfloat16"), "zq": ("sbuf", [128, C], "float8_e4m3fn_x4"), "zp": ("sbuf", [128, C], "uint8"),
+    "h": ("sbuf", [128, 4 * C], "bfloat16"),
+    "pu": ("psum", [128, 2048], "float32"), "pw": ("psum", [128, 2048], "float32"),
+}
+LISTS = ["cw", "cwu", "col", "f0", "f1", "h0", "h1", "pif", "bd", "be", "bf", "swc", "fmv", "fw", "fd", "fe", "fn", "fv"]
+SCRATCH["sml"] = ("sbuf", [128, 20 * len(LISTS)], "float32")
+TABLES, PASSED = {}, {}
+for _i, _l in enumerate(GROUPS):
+    SCRATCH["p%d" % _i] = ("sbuf", [128, C * 2 ** len(_l)], "bfloat16")
+    for _j, _k in enumerate(_l):
+        TABLES[_k] = "m%d" % _k if _k >= 0 else "ml"
+        PASSED[_k] = _l[:_j] if _j else GROUPS[_i - 1] if _i else []
+        SCRATCH[TABLES[_k]] = ("sbuf", [128, C * 2 ** len(PASSED[_k])], "float32")
+LAST = "p%d" % (len(GROUPS) - 1)
+for _k in range(7):
+    SCRATCH["l%d" % _k] = ("sbuf", [128, 20], "uint16")
+for _r in range(ROUNDS + 1):
+    if _r:
+        SCRATCH["x%d" % _r] = ("sbuf", [128, 4 * C], "bfloat16")
+    SCRATCH["xq%d" % _r] = ("sbuf", [128, C], "float8_e4m3fn_x4")
+    SCRATCH["xp%d" % _r] = ("sbuf", [128, C], "uint8")
+for _r in range(ROUNDS):
+    SCRATCH["aq%d" % _r] = ("sbuf", [128, C], "float8_e4m3fn_x4")
+    SCRATCH["ap%d" % _r] = ("sbuf", [128, C], "uint8")
+    for _n in ("lp", "lb", "rp", "rb"):
+        SCRATCH["%s%d" % (_n, _r)] = ("sbuf", [128, 20], "uint16")
+SEMAPHORES = ["ev", "es", "et", "eg", "snd", "st"]
+SEMAPHORES += ["%s%d" % (_n, _r) for _n in ("ax", "arp", "arb") for _r in range(ROUNDS)]
+SEMAPHORES += ["ld_" + _n for _n in ("x", "u", "v", "nx", "mt", "wc", "ws")]
+
+GATHER, SCAN2, SCAN4, ROW, SMALL = 0.58, 0.17, 0.33, 0.34, 0.08
+HOP, SAME = 0.2, 0.1
+SHARED = {}
+
+
+def new_plan():
+    return {"tasks": [], "w": {}, "r": {}}
+
+
+def overlap(a, b):
+    return a[0] < b[1] and b[0] < a[1]
+
+
+def task(P, eng, dur, fn, reads, writes, kind="op", sem=None, inc=1, after=(), behind=()):
+    def reg(x):
+        return (x, 0, 1 << 20) if isinstance(x, str) else x
+    n = len(P["tasks"])
+    deps = {}
+    for a in after:
+        deps[a] = True
+    rd, wr = [reg(x) for x in reads], [reg(x) for x in writes]
+    for b, lo, hi in rd:
+        for (l, h, t) in P["w"].get(b, []):
+            if overlap((lo, hi), (l, h)):
+                deps[t] = True
+        if b in ("pu", "pw"):
+            for (l, h, t) in P["r"].get(b, []):
+                if overlap((lo, hi), (l, h)) and P["tasks"][t]["eng"] != eng:
+                    deps.setdefault(t, False)
+    for b, lo, hi in wr:
+        for (l, h, t) in P["w"].get(b, []):
+            if overlap((lo, hi), (l, h)):
+                deps[t] = True
+        for (l, h, t) in P["r"].get(b, []):
+            if overlap((lo, hi), (l, h)):
+                deps.setdefault(t, False)
+    for b, lo, hi in wr:
+        P["w"][b] = [e for e in P["w"].get(b, []) if not (lo <= e[0] and e[1] <= hi)] + [(lo, hi, n)]
+        P["r"][b] = [e for e in P["r"].get(b, []) if not (lo <= e[0] and e[1] <= hi)]
+    for b, lo, hi in rd:
+        P["r"].setdefault(b, []).append((lo, hi, n))
+    deps.pop(n, None)
+    for a in behind:
+        deps.setdefault(a, False)
+    P["tasks"].append({"eng": eng, "dur": dur, "fn": fn, "deps": deps, "kind": kind, "sem": sem, "inc": inc})
+    return n
+
+
+def schedule(P, tries=5000):
+    ts = P["tasks"]
+    n = len(ts)
+    lags = [[(d, HOP if ts[d]["eng"] != t["eng"] else SAME if t["deps"][d] else 0.0) for d in t["deps"]] for t in ts]
+    succ = [[] for _ in range(n)]
+    for i in range(n):
+        for d, _ in lags[i]:
+            succ[d].append(i)
+    up = [t["dur"] for t in ts]
+    for i in range(n - 1, -1, -1):
+        for d, lag in lags[i]:
+            up[d] = max(up[d], ts[d]["dur"] + lag + up[i])
+
+    def place(rank):
+        left = [len(x) for x in lags]
+        ready = [i for i in range(n) if left[i] == 0]
+        slots = {}
+        start, end = [0.0] * n, [0.0] * n
+        while ready:
+            i = max(ready, key=lambda k: rank[k])
+            ready.remove(i)
+            t = ts[i]
+            at, dur = 0.0, t["dur"]
+            for d, lag in lags[i]:
+                at = max(at, end[d] + lag)
+            if t["eng"] != "net":
+                line = slots.setdefault(t["eng"], [])
+                k = len(line)
+                while k and line[k - 1][1] > at:
+                    k -= 1
+                while True:
+                    s = max(at, line[k - 1][1] if k else 0.0)
+                    if k == len(line) or s + dur <= line[k][0] + 1e-9:
+                        break
+                    k += 1
+                line.insert(k, (s, s + dur, i))
+                at = s
+            start[i], end[i] = at, at + dur
+            for s in succ[i]:
+                left[s] -= 1
+                if left[s] == 0:
+                    ready.append(s)
+        return max(end), {e: [x[2] for x in line] for e, line in slots.items()}, start
+    best, rank = place(up), up
+    rng = np.random.default_rng(7)
+    for _ in range(tries):
+        at, width = rng.random() * max(up), [2, 5, 10][rng.integers(3)]
+        part, step = [0.05, 0.15, 0.4][rng.integers(3)], [0.5, 1.5, 4.0][rng.integers(3)]
+        hit, by = rng.random(n) < part, rng.standard_normal(n) * step
+        trial = [float(rank[i] + by[i]) if hit[i] and abs(up[i] - at) < width else rank[i] for i in range(n)]
+        got = place(trial)
+        if got[0] <= best[0]:
+            best, rank = got, trial
+    return best[1], best[2], best[0]
+
+
+def issue(P, order, start, g, T):
+    ts = P["tasks"]
+    queue = {"v": g.vector, "s": g.scalar, "t": g.tensor, "g": g, "y": g.sync}
+    counter = {"v": "ev", "s": "es", "t": "et", "g": "eg"}
+    mark, count = {}, {}
+    for e, line in order.items():
+        for i in line:
+            t = ts[i]
+            if t["kind"] == "op":
+                count[counter[e]] = count.get(counter[e], 0) + 1
+                mark[i] = (counter[e], count[counter[e]])
+            else:
+                mark[i] = (t["sem"], t["inc"])
+    for i, t in enumerate(ts):
+        if t["kind"] == "land":
+            mark[i] = (t["sem"], t["inc"])
+    seen = {e: {} for e in queue}
+    known = {}
+    pos = {i: k for line in order.values() for k, i in enumerate(line)}
+    for i in sorted(pos, key=lambda i: (start[i], pos[i])):
+        t = ts[i]
+        e = t["eng"]
+        q, have = queue[e], seen[e]
+        need = {}
+        for d, result in t["deps"].items():
+            if ts[d]["kind"] == "send" or (ts[d]["eng"] == e and not result and ts[d]["kind"] == "op"):
+                continue
+            s, v = mark[d]
+            need[s] = max(need.get(s, 0), v)
+        for s, v in sorted(need.items()):
+            if have.get(s, 0) < v:
+                q.wait_ge(T.sem[s], v)
+                have[s] = v
+        for d, result in t["deps"].items():
+            if d in known and not (ts[d]["eng"] == e and not result):
+                for s, v in known[d].items():
+                    have[s] = max(have.get(s, 0), v)
+        k = dict(have)
+        if t["kind"] == "op":
+            t["fn"](q).then_inc(T.sem[mark[i][0]], 1)
+            k[mark[i][0]] = max(k.get(mark[i][0], 0), mark[i][1])
+        elif t["kind"] == "dma":
+            t["fn"](q).then_inc(T.sem[t["sem"]], 16)
+        else:
+            t["fn"](q)
+        if t["kind"] == "op":
+            known[i] = k
+    return count
+
+
+def build(P, g, core, T, topo):
+    rank = T.rank_of(core)
+    n = len(T.cores)
+    lists = {name: T.sml[:, 20 * i:20 * i + 20] for i, name in enumerate(LISTS)}
+    col = T.sml[:, 20 * LISTS.index("col"):20 * LISTS.index("col") + 1]
+
+    def L(name):
+        return lists[name]
+
+    def V(dur, fn, reads, writes, behind=()):
+        return task(P, "v", dur, fn, reads, writes, behind=behind)
+
+    def S(dur, fn, reads, writes):
+        return task(P, "s", dur, fn, reads, writes)
+
+    def E(dur, fn, reads, writes):
+        return task(P, "t", dur, fn, reads, writes)
+
+    def K(dur, fn, reads, writes):
+        return task(P, "g", dur, fn, reads, writes)
+
+    def every16(b):
+        return T[b][:, 15:C:16]
+
+    def at(b, a):
+        return T[b][:, C * a:C * a + C]
+
+    def copy(q, out, in_, **kw):
+        return q.activation(out, in_, AF.Copy, **kw)
+
+    def load(q, name, fn, writes):
+        k = task(P, q, 0.07, fn, [], [], "dma", "ld_" + name, 16)
+        task(P, "net", 2.0, None, [], writes, "land", "ld_" + name, 16, after=[k])
+
+    load("y", "x", lambda q: q.dma_start(T.x0[:], T.x[:]), ["x0"])
+    load("s", "nx", lambda q: q.dma_start(T.nxi[:], T.nx[:]), ["nxi"])
+    load("y", "u", lambda q: q.dma_start(T.ut[:], T.u[:]), ["ut"])
+    load("s", "mt", lambda q: q.dma_start(T.mti[:], T.mt[:]), ["mti"])
+    load("y", "wc", lambda q: q.dma_start(T.wq[:].bitcast(dt.uint8), T.wc[:]), ["wq"])
+    load("y", "ws", lambda q: q.dma_start(T.wp[:], T.ws[:]), ["wp"])
+    load("y", "v", lambda q: q.dma_start(T.vt[:], T.v[:]), ["vt"])
+
+    K(0.67, lambda q: q.iota(T.ji[:], [[1, C]], 0, -1), [], ["ji"])
+    K(0.67, lambda q: q.iota(T.idr[:], [[1, C]], -160, 0, allow_small_or_imprecise_dtypes=True), [], ["idr"])
+    K(0.17, lambda q: q.iota(T.pi[:], [[0, 20]], 0, 1), [], ["pi"])
+    K(0.17, lambda q: q.iota(T.ci[:], [[16, 20]], 0, 0), [], ["ci"])
+    K(0.15, lambda q: q.iota(T.ui[:], [[16, 8]], 0, 0), [], ["ui"])
+    K(0.67, lambda q: q.iota(T.rs0[:], [[0, 20], [1, 16]], 0, 0, allow_small_or_imprecise_dtypes=True), [], ["rs0"])
+    V(0.3, lambda q: q.memset(T.one[:], 1.0), [], ["one"])
+    K(1.1, lambda q: q.affine_select(T.big[:], T.one[:], [[-1, 528]], A.is_equal, 0.0, 3, 4), ["one"], ["big"])
+    V(ROW, lambda q: q.tensor_scalar(T.dg[:], T.ji[:], 15, None, A.bitwise_and), ["ji"], ["dg"])
+    V(ROW, lambda q: q.tensor_scalar(T.t1[:], T.dg[:], 1.0, 320.0, A.is_equal, A.mult), ["dg"], ["t1"])
+    V(ROW, lambda q: q.tensor_scalar(T.t2[:], T.dg[:], 0.0, -16384.0, A.is_equal, A.mult), ["dg"], ["t2"])
+    V(2 * ROW, lambda q: q.tensor_tensor(T.wt[:], T.t1[:], T.t2[:], A.add), ["t1", "t2"], ["wt"])
+    V(ROW, lambda q: q.tensor_scalar(T.mask[:], T.dg[:], 0.0, None, A.is_equal), ["dg"], ["mask"])
+    V(ROW, lambda q: q.tensor_scalar(T.cap[:], T.mask[:], 2 * BIG, -BIG, A.mult, A.add), ["mask"], ["cap"])
+    V(ROW, lambda q: q.tensor_scalar(T.rs[:], T.rs0[:], 1.0, None, A.min), ["rs0"], ["rs"])
+    V(SMALL, lambda q: q.tensor_scalar(T.pa15[:], T.pi[:], 15, None, A.bitwise_and), ["pi"], ["pa15"])
+    V(SMALL, lambda q: q.tensor_scalar(L("f0"), T.pa15[:], 15.0, 320.0, A.is_equal, A.mult), ["pa15"], ["f0"])
+    V(SMALL, lambda q: q.tensor_scalar(L("col"), L("f0"), -160.0, None, A.add), ["f0"], ["col"])
+    V(SMALL, lambda q: q.tensor_tensor(L("cw"), T.pa15[:], T.ci[:], A.add), ["pa15", "ci"], ["cw"])
+    V(SMALL, lambda q: q.tensor_scalar(L("cwu"), L("cw"), 1.0 / C, None, A.mult), ["cw"], ["cwu"])
+    V(SMALL, lambda q: q.tensor_copy(T.uo[:], T.ui[:]), ["ui"], ["uo"])
+    for i in range(len(GROUPS)):
+        S(ROW, lambda q, i=i: copy(q, at("p%d" % i, 0), T.idr[:]), ["idr"], [("p%d" % i, 0, 1)])
+    for b in range(4):
+        V(0.16, lambda q, b=b: q.quantize_mx(T.eq[:, 128 * b:128 * b + 128], T.ep[:, 128 * b:128 * b + 128], T.big[:, 3 - b:515 - b]),
+          ["big"], [("eq", b, b + 1), ("ep", b, b + 1)])
+
+    V(0.16, lambda q: q.quantize_mx(T.uq[:], T.up[:], T.ut[:]), ["ut"], ["uq", "up"])
+    V(0.3, lambda q: q.tensor_copy(T.uqr[:].bitcast(dt.uint32), T.uq[:].bitcast(dt.uint32).indirect(T.uo[:])), ["uq", "uo"], ["uqr"])
+    V(0.3, lambda q: q.tensor_copy(T.upr[:], T.up[:].indirect(T.uo[:])), ["up", "uo"], ["upr"])
+    V(0.16, lambda q: q.quantize_mx(T.vq[:], T.vp[:], T.vt[:]), ["vt"], ["vq", "vp"])
+
+    V(SMALL, lambda q: q.tensor_copy(T.l0[:], T.nxi[:]), ["nxi"], ["l0"])
+    V(SMALL, lambda q: q.tensor_copy(L("fw"), T.nxi[:]), ["nxi"], ["fw"])
+    V(SMALL, lambda q: q.tensor_copy(T.mt16[:], T.mti[:]), ["mti"], ["mt16"])
+    V(SMALL, lambda q: q.tensor_copy(L("bd"), T.mti[:]), ["mti"], ["bd"])
+    V(SMALL, lambda q: q.tensor_tensor(L("be"), L("bd"), L("cw"), A.min), ["bd", "cw"], ["be"])
+    V(SMALL, lambda q: q.tensor_tensor(L("bf"), L("bd"), L("cw"), A.max), ["bd", "cw"], ["bf"])
+    V(SMALL, lambda q: q.tensor_copy(T.lo16[:], L("be")), ["be"], ["lo16"])
+    V(SMALL, lambda q: q.tensor_copy(T.hi16[:], L("bf")), ["bf"], ["hi16"])
+
+    def row(out, a, win, i, k):
+        S(GATHER, lambda q: copy(q, at(out, a), at(win, i).indirect(T["l%d" % k][:])), [(win, i, i + 1), "l%d" % k], [(out, a, a + 1)])
+
+    def look(dst, win, i, k, off):
+        S(GATHER, lambda q: copy(q, T[dst][:], T[win][:, C * i:C * k].indirect(T[off][:])), [(win, i, k), off], [dst])
+
+    def running(dst, src):
+        V(SCAN2, lambda q: q.tensor_tensor_scan(T[dst][:], T.rs[:], T[src][:], 0.0, A.mult, A.add), ["rs", src], [dst])
+
+    def weighted(dst, src, a=0):
+        V(SCAN2, lambda q: q.tensor_tensor_scan(T[dst][:], T.wt[:], at(src, a), 0.0, A.add, A.max), ["wt", (src, a, a + 1)], [dst])
+
+    def at_f(k):
+        return [("p%d" % i, 2 ** levels.index(k)) for i, levels in enumerate(GROUPS) if k in levels][0]
+
+    def powers():
+        row(*at_f(0), "idr", 0, 0)
+        for k in range(6):
+            l = "l%d" % (k + 1)
+            row(*at_f(k + 1), *at_f(k), k)
+            weighted("scn", *at_f(k + 1))
+            V(SMALL, lambda q, l=l: q.tensor_scalar(T[l][:], every16("scn"), col, None, A.add), ["scn", "col"], [l])
+        b, a = at_f(1)
+        S(ROW, lambda q: copy(q, at(LAST, 2), at(b, a)), [(b, a, a + 1)], [(LAST, 2, 3)])
+        for i, levels in enumerate(GROUPS):
+            for j, k in enumerate(levels):
+                for a2 in range(1, 2 ** j if k >= 0 else 0):
+                    row("p%d" % i, 2 ** j + a2, "p%d" % i, a2, k)
+
+    sent = [0]
+
+    def send(r, pairs, sem, land, latency):
+        dst, src = T.cores[(rank + r + 1) % n], T.cores[(rank - r - 1) % n]
+        rid, pid, _ = topo.addr(dst)
+        m = topo.mask(core, dst)
+        ids = []
+        for out, in_, name in pairs:
+            ids.append(task(P, "g", 0.1, lambda q, out=out, in_=in_: q.remote_dma(out, in_, T.sem[sem], T.sem.snd, pid, rid, m), [name], [], "send"))
+            sent[0] += len(topo.engines(core, dst))
+        return task(P, "net", latency, None, [], land, "land", sem, len(topo.engines(src, core)) * len(pairs), after=ids)
+
+    def compare(level, off, behind=()):
+        win = TABLES[level]
+        V(GATHER, lambda q: q.tensor_tensor(T.cb[:], T[win][:].indirect(T[off][:]), T.sm[:], A.is_le), [win, off, "sm"], ["cb"], behind)
+
+    def mm(out, b, wq, wp, a, xq, xp, unit):
+        E(0.35, lambda q: q.matmul_mx(T[out][:, BANK * b:BANK * b + C], T[wq][:, a:a + 128], T[wp][:, a:a + 128], T[xq][:], T[xp][:], True, True),
+          [(wq, unit, unit + 1), (wp, unit, unit + 1), xq, xp], [(out, b, b + 1)])
+
+    def bank(out, b):
+        return T[out][:, BANK * b:BANK * b + C]
+
+    powers()
+    for r in range(ROUNDS):
+        X, xq, xp, aq, ap = "x%d" % r, "xq%d" % r, "xp%d" % r, "aq%d" % r, "ap%d" % r
+        lp, lb, rp, rb = "lp%d" % r, "lb%d" % r, "rp%d" % r, "rb%d" % r
+        V(0.37, lambda q, xq=xq, xp=xp, X=X: q.quantize_mx(T[xq][:], T[xp][:], T[X][:]), [X], [xq, xp])
+        send(r, [(T[aq][:].bitcast(dt.uint8), T[xq][:].bitcast(dt.uint8), xq), (T[ap][:], T[xp][:], xp)], "ax%d" % r, [aq, ap], 6.0)
+        mm("pw", 0, "uqr", "upr", 0, xq, xp, 0)
+        mm("pw", 1, "uqr", "upr", 0, xq, xp, 0)
+        S(ROW, lambda q: copy(q, T.srow[:], bank("pw", 0)), [("pw", 0, 1)], ["srow"])
+        V(ROW, lambda q: q.tensor_tensor(T.sm[:], bank("pw", 1), T.cap[:], A.min), [("pw", 1, 2), "cap"], ["sm"])
+        V(GATHER, lambda q: q.tensor_copy(at("m0", 0), T.srow[:].indirect(T.l0[:])), ["srow", "l0"], [("m0", 0, 1)])
+        S(GATHER, lambda q: copy(q, at("ml", 0), T.srow[:].indirect(T.l0[:])), ["srow", "l0"], [("ml", 0, 1)])
+        for k in range(5):
+            twin, m0, m1 = ("d%d" % (k % 2) if k else "ml"), "m%d" % k, "m%d" % (k + 1)
+            V(GATHER, lambda q, k=k, twin=twin, m0=m0, m1=m1: q.tensor_tensor(at(m1, 0), at(m0, 0).indirect(T["l%d" % k][:]), at(twin, 0), A.max),
+              [(m0, 0, 1), (twin, 0, 1), "l%d" % k], [(m1, 0, 1)])
+            if k < 4:
+                d = "d%d" % ((k + 1) % 2)
+                S(ROW, lambda q, d=d, m1=m1: copy(q, at(d, 0), at(m1, 0)), [(m1, 0, 1)], [(d, 0, 1)])
+        for k, passed in PASSED.items():
+            for j, l in enumerate(passed):
+                for a in range(2 ** j):
+                    row(TABLES[k], 2 ** j + a, TABLES[k], a, l)
+        for b in range(4):
+            mm("pu", b, "eq", "ep", 128 * b, xq, xp, b)
+            (V if b < 2 else S)(ROW, lambda q, b=b: (q.tensor_copy if b < 2 else lambda o, i: copy(q, o, i))(at("fo", b), bank("pu", b)),
+                                [("pu", b, b + 1)], [("fo", b, b + 1)])
+        for b in range(4):
+            mm("pu", b, "eq", "ep", 128 * b, aq, ap, b)
+            S(ROW, lambda q, b=b: copy(q, at("fh", b), bank("pu", b), scale=0.5), [("pu", b, b + 1)], [("fh", b, b + 1)])
+        for i, levels in enumerate(GROUPS):
+            place, last = "cwu" if i == 0 else "pif", i == len(GROUPS) - 1
+            for j, k in enumerate(levels):
+                if i == 0 and j == 0:
+                    V(2 * ROW, lambda q: q.tensor_tensor(T.fb[:], at("m5", 0), T.sm[:], A.is_le), [("m5", 0, 1), "sm"], ["fb"])
+                    running("fs", "fb")
+                    V(GATHER, lambda q: q.tensor_tensor(T.cb[:], at("m5", 0).indirect(T.l5[:]), T.sm[:], A.is_le), [("m5", 0, 1), "l5", "sm"], ["cb"])
+                    running("cs", "cb")
+                    V(SMALL, lambda q: q.tensor_tensor(L("fv"), every16("cs"), every16("fs"), A.mult), ["cs", "fs"], ["fv"])
+                else:
+                    compare(k, off, behind)
+                    running("cs", "cb")
+                behind = []
+                if k < 0:
+                    break
+                f, off = "f%d" % (j % 2), "o%d" % (j % 2)
+                V(SMALL, lambda q, f=f, place=place, top=i + j == 0: q.tensor_tensor(L(f), L(place), L("fv") if top else every16("cs"), A.add),
+                  [place, "cs", "fv"] if i + j == 0 else [place, "cs"], [f])
+                V(SMALL, lambda q, f=f, off=off, j=j: q.tensor_scalar(T[off][:], L(f), float(C * 2 ** j), 0.25, A.mult, A.add), [f], [off])
+                if j + 1 < len(levels) and levels[j + 1] >= 0:
+                    place = "h%d" % (j % 2)
+                    behind = [V(SMALL, lambda q, f=f, place=place: q.tensor_scalar(L(place), L(f), 0.5, None, A.mult), [f], [place])]
+                if j + 1 < len(levels) and levels[j + 1] < 0:
+                    look("pr", LAST, 0, 2, off)
+                    look("fr", LAST, 1, 3, off)
+                    weighted("pws", "pr")
+                    V(SMALL, lambda q, lp=lp: q.tensor_scalar(T[lp][:], every16("pws"), col, None, A.add), ["pws", "col"], [lp])
+                    send(r, [(T[rp][:], T[lp][:], lp)], "arp%d" % r, [rp], 2.6)
+                    weighted("fsn", "fr")
+                    V(SMALL, lambda q: q.tensor_scalar(L("fv"), every16("fsn"), col, None, A.add), ["fsn", "col"], ["fv"])
+                    V(SMALL, lambda q: q.tensor_tensor(L("bd"), L("cw"), L("fv"), A.subtract), ["cw", "fv"], ["bd"])
+            if not last:
+                look("pb", "p%d" % i, 0, 2 ** len(levels), off)
+                weighted("psn", "pb")
+                V(SMALL, lambda q: q.tensor_scalar(L("pif"), every16("psn"), col, 1.0 / C, A.add, A.mult), ["psn", "col"], ["pif"])
+        V(SMALL, lambda q: q.tensor_tensor(L("be"), L("bd"), every16("cs"), A.mult), ["bd", "cs"], ["be"])
+        V(SMALL, lambda q: q.tensor_tensor(L("bf"), L("be"), L("fv"), A.add), ["be", "fv"], ["bf"])
+        V(SMALL, lambda q, lb=lb: q.tensor_copy(T[lb][:], L("bf")), ["bf"], [lb])
+        send(r, [(T[rb][:], T[lb][:], lb)], "arb%d" % r, [rb], 2.6)
+        S(GATHER, lambda q, lb=lb: copy(q, T.er[:], T.srow[:].indirect(T[lb][:])), ["srow", lb], ["er"])
+        S(GATHER, lambda q: copy(q, T.eh[:], T.er[:].indirect(T.hi16[:])), ["er", "hi16"], ["eh"])
+        V(GATHER, lambda q: q.tensor_tensor(T.sw[:], T.er[:].indirect(T.lo16[:]), T.eh[:], A.is_gt), ["er", "eh", "lo16"], ["sw"])
+        weighted("swn", "sw")
+        V(SMALL, lambda q: q.tensor_scalar(L("swc"), every16("swn"), col, -160.0, A.add, A.add), ["swn", "col"], ["swc"])
+        S(GATHER, lambda q: copy(q, T.fmr[:], at(*at_f(0)).indirect(T.mt16[:])), [at_f(0) + (at_f(0)[1] + 1,), "mt16"], ["fmr"])
+        weighted("fmn", "fmr")
+        V(SMALL, lambda q: q.tensor_scalar(L("fmv"), every16("fmn"), col, None, A.add), ["fmn", "col"], ["fmv"])
+        fw, fn = ("fw", "fn") if r % 2 == 0 else ("fn", "fw")
+        V(SMALL, lambda q, fw=fw: q.tensor_tensor(L("fd"), L("fmv"), L(fw), A.subtract), ["fmv", fw], ["fd"])
+        V(SMALL, lambda q: q.tensor_tensor(L("fe"), L("fd"), L("swc"), A.mult), ["fd", "swc"], ["fe"])
+        V(SMALL, lambda q, fw=fw, fn=fn: q.tensor_tensor(L(fn), L(fw), L("fe"), A.add), [fw, "fe"], [fn])
+        V(SMALL, lambda q, fn=fn: q.tensor_copy(T.l0[:], L(fn)), [fn], ["l0"])
+        if r < ROUNDS - 1:
+            powers()
+        else:
+            S(GATHER, lambda q: copy(q, T.er[:], T.idr[:].indirect(T.l0[:]), bias=160.0), ["idr", "l0"], ["er"])
+            task(P, "y", 0.07, lambda q: q.dma_start(T.nf[:], T.er[0:128:16, :]), ["er"], [], "dma", "st", 16)
+        for b in range(4):
+            S(GATHER, lambda q, b=b, rp=rp: copy(q, at("gp", b), at("fh", b).indirect(T[rp][:])), [("fh", b, b + 1), rp], [("gp", b, b + 1)])
+            V(GATHER, lambda q, b=b, rb=rb: q.tensor_tensor(T.z[:, b:4 * C:4], at("fh", b).indirect(T[rb][:]), at("gp", b), A.add),
+              [("fh", b, b + 1), rb, ("gp", b, b + 1)], [("z", b, b + 1)])
+        V(0.37, lambda q: q.quantize_mx(T.zq[:], T.zp[:], T.z[:]), ["z"], ["zq", "zp"])
+        Y = "x%d" % (r + 1)
+        for b in range(4):
+            mm("pw", b, "wq", "wp", 128 * b, "zq", "zp", b)
+            S(ROW, lambda q, b=b: copy(q, at("h", b), bank("pw", b), scale=0.03125), [("pw", b, b + 1)], [("h", b, b + 1)])
+            V(GATHER, lambda q, b=b, lb=lb, Y=Y: q.tensor_tensor(T[Y][:, b:4 * C:4], at("h", b).indirect(T[lb][:]), at("fo", b), A.add),
+              [("h", b, b + 1), lb, ("fo", b, b + 1)], [(Y, b, b + 1)])
+    xq, xp, X = "xq%d" % ROUNDS, "xp%d" % ROUNDS, "x%d" % ROUNDS
+    V(0.37, lambda q, xq=xq, xp=xp, X=X: q.quantize_mx(T[xq][:], T[xp][:], T[X][:]), [X], [xq, xp])
+    task(P, "y", 0.07, lambda q: q.dma_start(T.oc[:], T[xq][:].bitcast(dt.uint8)), [xq], [], "dma", "st", 16)
+    for k in range(4):
+        task(P, "y" if k % 2 else "s", 0.07, lambda q, k=k: q.dma_start(T.osc[4 * k:4 * k + 4, :], T[xp][32 * k:32 * k + 4, :]), [xp], [], "dma", "st", 16)
+    mm("pw", 0, "vq", "vp", 0, xq, xp, 0)
+    V(ROW, lambda q: q.tensor_copy(T.eh[:], bank("pw", 0)), [("pw", 0, 1)], ["eh"])
+    task(P, "y", 0.07, lambda q: q.dma_start(T.y[:], T.eh[:]), ["eh"], [], "dma", "st", 16)
+    return sent[0]
+
+
+def rank_program(g, core, T, topo):
+    if T.rank_of(core) is None:
+        return
+    P = new_plan()
+    sent = build(P, g, core, T, topo)
+    if "order" not in SHARED:
+        SHARED["order"] = schedule(P)
+    order, start, _ = SHARED["order"]
+    count = issue(P, order, start, g, T)
+    g.sync.wait_ge(T.sem.st, 16 * sum(1 for t in P["tasks"] if t["sem"] == "st"))
+    for s, k in sorted(count.items()):
+        g.sync.wait_ge(T.sem[s], k)
+    g.wait_ge(T.sem.snd, sent)

@@ -1,70 +1,75 @@
 import numpy as np
-from concourse.mybir import dt, AluOpType, ActivationFunctionType
+from concourse.mybir import dt, AluOpType, ActivationFunctionType, AxisListType
 A = AluOpType
 AF = ActivationFunctionType
 C = 320
 BANK = 512
 ROUNDS = 3
 BIG = 1e29
-GROUPS = [[6, 5], [4, 3], [2, 1], [0, -1]]
+KEY = 1024.0
+PAD = C + 32
+TW = C + PAD
+
+
+def sb(n, d):
+    return ("sbuf", [128, n], d)
+
 
 SCRATCH = {
-    "x0": ("sbuf", [128, 4 * C], "bfloat16"), "ut": ("sbuf", [128, 512], "bfloat16"), "vt": ("sbuf", [128, 512], "bfloat16"),
-    "nxi": ("sbuf", [128, 20], "int32"), "mti": ("sbuf", [128, 20], "int32"),
-    "wq": ("sbuf", [128, 512], "float8_e4m3fn_x4"), "wp": ("sbuf", [128, 512], "uint8"),
-    "uq": ("sbuf", [128, 128], "float8_e4m3fn_x4"), "up": ("sbuf", [128, 128], "uint8"),
-    "uqr": ("sbuf", [128, 128], "float8_e4m3fn_x4"), "upr": ("sbuf", [128, 128], "uint8"),
-    "vq": ("sbuf", [128, 128], "float8_e4m3fn_x4"), "vp": ("sbuf", [128, 128], "uint8"),
-    "eq": ("sbuf", [128, 512], "float8_e4m3fn_x4"), "ep": ("sbuf", [128, 512], "uint8"),
-    "one": ("sbuf", [128, 528], "bfloat16"), "big": ("sbuf", [128, 528], "bfloat16"),
-    "ji": ("sbuf", [128, C], "int32"), "dg": ("sbuf", [128, C], "int32"), "t1": ("sbuf", [128, C], "float32"), "t2": ("sbuf", [128, C], "float32"),
-    "rs0": ("sbuf", [128, C], "bfloat16"), "rs": ("sbuf", [128, C], "bfloat16"), "wt": ("sbuf", [128, C], "bfloat16"),
-    "mask": ("sbuf", [128, C], "bfloat16"), "cap": ("sbuf", [128, C], "float32"), "idr": ("sbuf", [128, C], "bfloat16"),
-    "pi": ("sbuf", [128, 20], "int32"), "pa15": ("sbuf", [128, 20], "int32"), "ci": ("sbuf", [128, 20], "int32"),
-    "ui": ("sbuf", [128, 8], "int32"), "uo": ("sbuf", [128, 8], "uint16"),
-    "mt16": ("sbuf", [128, 20], "uint16"), "lo16": ("sbuf", [128, 20], "uint16"), "hi16": ("sbuf", [128, 20], "uint16"),
-    "srow": ("sbuf", [128, C], "float32"), "sm": ("sbuf", [128, C], "float32"),
-    "pr": ("sbuf", [128, C], "bfloat16"), "pws": ("sbuf", [128, C], "float16"),
-    "d0": ("sbuf", [128, C], "float32"), "d1": ("sbuf", [128, C], "float32"),
-    "cb": ("sbuf", [128, C], "bfloat16"), "cs": ("sbuf", [128, C], "bfloat16"),
-    "pb": ("sbuf", [128, C], "bfloat16"), "psn": ("sbuf", [128, C], "float16"),
-    "fb": ("sbuf", [128, C], "bfloat16"), "fr": ("sbuf", [128, C], "bfloat16"), "fsn": ("sbuf", [128, C], "float16"),
-    "fs": ("sbuf", [128, C], "bfloat16"),
-    "o0": ("sbuf", [128, 20], "uint16"), "o1": ("sbuf", [128, 20], "uint16"), "o3": ("sbuf", [128, 20], "uint16"),
-    "er": ("sbuf", [128, C], "float32"), "eh": ("sbuf", [128, C], "float32"), "sw": ("sbuf", [128, C], "bfloat16"),
-    "scn": ("sbuf", [128, C], "float16"), "swn": ("sbuf", [128, C], "float16"), "fmn": ("sbuf", [128, C], "float16"), "fmr": ("sbuf", [128, C], "bfloat16"),
-    "fo": ("sbuf", [128, 4 * C], "bfloat16"), "fh": ("sbuf", [128, 4 * C], "bfloat16"), "gp": ("sbuf", [128, 4 * C], "bfloat16"),
-    "z": ("sbuf", [128, 4 * C], "bfloat16"), "zq": ("sbuf", [128, C], "float8_e4m3fn_x4"), "zp": ("sbuf", [128, C], "uint8"),
-    "h": ("sbuf", [128, 4 * C], "bfloat16"),
+    "x0": sb(4 * C, "bfloat16"), "ut": sb(512, "bfloat16"), "vt": sb(512, "bfloat16"),
+    "nxi": sb(20, "int32"), "mti": sb(20, "int32"),
+    "wq": sb(512, "float8_e4m3fn_x4"), "wp": sb(512, "uint8"),
+    "uq": sb(128, "float8_e4m3fn_x4"), "up": sb(128, "uint8"),
+    "uqr": sb(128, "float8_e4m3fn_x4"), "upr": sb(128, "uint8"),
+    "vq": sb(128, "float8_e4m3fn_x4"), "vp": sb(128, "uint8"),
+    "eq": sb(512, "float8_e4m3fn_x4"), "ep": sb(512, "uint8"),
+    "one": sb(528, "bfloat16"), "big": sb(528, "bfloat16"),
+    "ji": sb(C, "int32"), "dg": sb(C, "int32"), "t1": sb(C, "bfloat16"), "t2": sb(C, "bfloat16"),
+    "wt": sb(C, "bfloat16"), "idr": sb(C, "bfloat16"),
+    "ia": sb(C, "float32"), "ic": sb(C, "bfloat16"), "tid": sb(TW // 16, "bfloat16"),
+    "gs": sb(C, "bfloat16"), "f3": sb(C, "bfloat16"), "f4": sb(C, "bfloat16"), "f34": sb(C, "bfloat16"),
+    "pi": sb(32, "int32"), "pa": sb(32, "int32"), "ci": sb(32, "int32"), "cn": sb(32, "int32"), "bits": sb(12, "int32"),
+    "ui": sb(8, "int32"), "uo": sb(8, "uint16"), "pick": sb(6, "uint16"),
+    "cf": sb(64, "float32"),
+    "lo16": sb(20, "uint16"), "hi16": sb(20, "uint16"), "so": sb(20, "uint16"), "lq": sb(32, "uint16"), "ob": sb(32, "uint16"),
+    "sa": sb(C, "float32"), "sb": sb(C, "float32"), "s2": sb(C, "float32"),
+    "n1": sb(PAD, "bfloat16"), "n2": sb(PAD, "bfloat16"), "e1": sb(PAD, "float16"), "e2": sb(PAD, "float16"),
+    "tn1": sb(TW, "bfloat16"), "tn2": sb(TW, "bfloat16"), "te1": sb(TW, "float16"), "te2": sb(TW, "float16"),
+    "r1": sb(TW, "bfloat16"), "r2": sb(TW // 2, "bfloat16"),
+    "fw0": sb(2 * C, "bfloat16"), "fw1": sb(2 * C, "bfloat16"), "fa": sb(C, "bfloat16"), "fb": sb(C, "bfloat16"),
+    "br": sb(C, "bfloat16"), "bsn": sb(C, "float16"), "scn": sb(C, "float16"), "swn": sb(C, "float16"),
+    "er": sb(C, "float32"), "eh": sb(C, "float32"), "sw": sb(C, "bfloat16"),
+    "fo": sb(4 * C, "bfloat16"), "fh": sb(4 * C, "bfloat16"), "gp": sb(4 * C, "bfloat16"),
+    "z": sb(4 * C, "bfloat16"), "zq": sb(C, "float8_e4m3fn_x4"), "zp": sb(C, "uint8"),
+    "h": sb(4 * C, "bfloat16"),
     "pu": ("psum", [128, 2048], "float32"), "pw": ("psum", [128, 2048], "float32"),
 }
-LISTS = ["cw", "cwu", "col", "f0", "f1", "h0", "h1", "pif", "bd", "be", "bf", "swc", "fmv", "fw", "fd", "fe", "fn", "fv"]
-SCRATCH["sml"] = ("sbuf", [128, 20 * len(LISTS)], "float32")
-TABLES, PASSED = {}, {}
-for _i, _l in enumerate(GROUPS):
-    SCRATCH["p%d" % _i] = ("sbuf", [128, C * 2 ** len(_l)], "bfloat16")
-    for _j, _k in enumerate(_l):
-        TABLES[_k] = "m%d" % _k if _k >= 0 else "ml"
-        PASSED[_k] = _l[:_j] if _j else GROUPS[_i - 1] if _i else []
-        SCRATCH[TABLES[_k]] = ("sbuf", [128, C * 2 ** len(PASSED[_k])], "float32")
-LAST = "p%d" % (len(GROUPS) - 1)
+for _n in ("c", "f", "e"):
+    for _k in ("0", "1", "w"):
+        SCRATCH["m" + _n + _k] = sb(C, "float32")
+LISTS = ["cw", "c320", "bd", "be", "bf", "dm", "dc", "hl", "hm", "om", "sx", "sy"]
+SCRATCH["sml"] = sb(32 * len(LISTS), "float32")
+COLS = {"sc": 0, "kb": 12, "nb": 24, "bi": 36, "col": 48, "e15": 49, "a1": 50, "a2": 51, "b1": 52, "b2": 53, "od": 54, "ev": 55,
+        "k1": 56, "k2": 57, "z0": 58, "z1": 59, "f0": 60, "ko": 61}
 for _k in range(7):
-    SCRATCH["l%d" % _k] = ("sbuf", [128, 20], "uint16")
+    SCRATCH["l%d" % _k] = sb(20, "uint16")
 for _r in range(ROUNDS + 1):
     if _r:
-        SCRATCH["x%d" % _r] = ("sbuf", [128, 4 * C], "bfloat16")
-    SCRATCH["xq%d" % _r] = ("sbuf", [128, C], "float8_e4m3fn_x4")
-    SCRATCH["xp%d" % _r] = ("sbuf", [128, C], "uint8")
+        SCRATCH["x%d" % _r] = sb(4 * C, "bfloat16")
+    SCRATCH["xq%d" % _r] = sb(C, "float8_e4m3fn_x4")
+    SCRATCH["xp%d" % _r] = sb(C, "uint8")
 for _r in range(ROUNDS):
-    SCRATCH["aq%d" % _r] = ("sbuf", [128, C], "float8_e4m3fn_x4")
-    SCRATCH["ap%d" % _r] = ("sbuf", [128, C], "uint8")
-    for _n in ("lp", "lb", "rp", "rb"):
-        SCRATCH["%s%d" % (_n, _r)] = ("sbuf", [128, 20], "uint16")
+    SCRATCH["aq%d" % _r] = sb(C, "float8_e4m3fn_x4")
+    SCRATCH["ap%d" % _r] = sb(C, "uint8")
+    SCRATCH["lp%d" % _r] = sb(32, "uint16")
+    for _n in ("lb", "rp", "rb"):
+        SCRATCH["%s%d" % (_n, _r)] = sb(20, "uint16")
 SEMAPHORES = ["ev", "es", "et", "eg", "snd", "st"]
 SEMAPHORES += ["%s%d" % (_n, _r) for _n in ("ax", "arp", "arb") for _r in range(ROUNDS)]
 SEMAPHORES += ["ld_" + _n for _n in ("x", "u", "v", "nx", "mt", "wc", "ws")]
+SEMAPHORES += ["ld_%s%d" % (_n, _r) for _n in ("g0", "g1", "g2", "o") for _r in range(ROUNDS)]
 
-GATHER, SCAN2, SCAN4, ROW, SMALL = 0.58, 0.17, 0.33, 0.34, 0.08
+GATHER, HALF, ROW, SMALL = 0.58, 0.17, 0.34, 0.08
 HOP, SAME = 0.2, 0.1
 SHARED = {}
 
@@ -115,7 +120,7 @@ def task(P, eng, dur, fn, reads, writes, kind="op", sem=None, inc=1, after=(), b
 def schedule(P, tries=5000):
     ts = P["tasks"]
     n = len(ts)
-    lags = [[(d, HOP if ts[d]["eng"] != t["eng"] else SAME if t["deps"][d] else 0.0) for d in t["deps"]] for t in ts]
+    lags = [[(d, HOP if ts[d]["eng"] != t["eng"] else SAME) for d in t["deps"]] for t in ts]
     succ = [[] for _ in range(n)]
     for i in range(n):
         for d, _ in lags[i]:
@@ -193,7 +198,7 @@ def issue(P, order, start, g, T):
         q, have = queue[e], seen[e]
         need = {}
         for d, result in t["deps"].items():
-            if ts[d]["kind"] == "send" or (ts[d]["eng"] == e and not result and ts[d]["kind"] == "op"):
+            if ts[d]["kind"] in ("send", "dma"):
                 continue
             s, v = mark[d]
             need[s] = max(need.get(s, 0), v)
@@ -202,7 +207,7 @@ def issue(P, order, start, g, T):
                 q.wait_ge(T.sem[s], v)
                 have[s] = v
         for d, result in t["deps"].items():
-            if d in known and not (ts[d]["eng"] == e and not result):
+            if d in known:
                 for s, v in known[d].items():
                     have[s] = max(have.get(s, 0), v)
         k = dict(have)
@@ -221,14 +226,19 @@ def issue(P, order, start, g, T):
 def build(P, g, core, T, topo):
     rank = T.rank_of(core)
     n = len(T.cores)
-    lists = {name: T.sml[:, 20 * i:20 * i + 20] for i, name in enumerate(LISTS)}
-    col = T.sml[:, 20 * LISTS.index("col"):20 * LISTS.index("col") + 1]
 
-    def L(name):
-        return lists[name]
+    def L(name, w=20):
+        i = LISTS.index(name)
+        return T.sml[:, 32 * i:32 * i + w]
 
-    def V(dur, fn, reads, writes, behind=()):
-        return task(P, "v", dur, fn, reads, writes, behind=behind)
+    def cf(name, i=0, w=1):
+        return T.cf[:, COLS[name] + i:COLS[name] + i + w]
+
+    def cn(i, w=1):
+        return T.cn[:, i:i + w]
+
+    def V(dur, fn, reads, writes):
+        return task(P, "v", dur, fn, reads, writes)
 
     def S(dur, fn, reads, writes):
         return task(P, "s", dur, fn, reads, writes)
@@ -239,18 +249,37 @@ def build(P, g, core, T, topo):
     def K(dur, fn, reads, writes):
         return task(P, "g", dur, fn, reads, writes)
 
+    def ts(out, in_, s1, s2, op0, op1, reads, writes, dur=SMALL):
+        if op1 is None:
+            return V(dur, lambda q: q.tensor_scalar(out, in_, s1, None, op0), reads, writes)
+        return V(dur, lambda q: q.tensor_scalar(out, in_, s1, s2, op0, op1), reads, writes)
+
+    def tt(out, a, b, op, reads, writes, dur=SMALL):
+        return V(dur, lambda q: q.tensor_tensor(out, a, b, op), reads, writes)
+
+    def cp(out, in_, reads, writes, dur=SMALL):
+        return V(dur, lambda q: q.tensor_copy(out, in_), reads, writes)
+
+    def act(out, in_, reads, writes, dur=ROW, **kw):
+        f = AF.Identity if "bias" in kw and not isinstance(kw["bias"], float) else AF.Copy
+        return S(dur, lambda q: q.activation(out, in_, f, **kw), reads, writes)
+
     def every16(b):
         return T[b][:, 15:C:16]
 
-    def at(b, a):
+    def at(b, a=0):
         return T[b][:, C * a:C * a + C]
 
-    def copy(q, out, in_, **kw):
-        return q.activation(out, in_, AF.Copy, **kw)
+    def by(b, l, a=0):
+        return at(b, a).indirect(T[l][:, 0:20])
 
     def load(q, name, fn, writes):
         k = task(P, q, 0.07, fn, [], [], "dma", "ld_" + name, 16)
         task(P, "net", 2.0, None, [], writes, "land", "ld_" + name, 16, after=[k])
+
+    def move(name, out, in_, reads, writes):
+        k = task(P, "y", 0.07, lambda q: q.dma_start(out, in_), reads, writes, "dma", "ld_" + name, 16)
+        task(P, "net", 2.2, None, reads, writes, "land", "ld_" + name, 16, after=[k])
 
     load("y", "x", lambda q: q.dma_start(T.x0[:], T.x[:]), ["x0"])
     load("s", "nx", lambda q: q.dma_start(T.nxi[:], T.nx[:]), ["nxi"])
@@ -260,75 +289,138 @@ def build(P, g, core, T, topo):
     load("y", "ws", lambda q: q.dma_start(T.wp[:], T.ws[:]), ["wp"])
     load("y", "v", lambda q: q.dma_start(T.vt[:], T.v[:]), ["vt"])
 
-    K(0.67, lambda q: q.iota(T.ji[:], [[1, C]], 0, -1), [], ["ji"])
     K(0.67, lambda q: q.iota(T.idr[:], [[1, C]], -160, 0, allow_small_or_imprecise_dtypes=True), [], ["idr"])
-    K(0.17, lambda q: q.iota(T.pi[:], [[0, 20]], 0, 1), [], ["pi"])
-    K(0.17, lambda q: q.iota(T.ci[:], [[16, 20]], 0, 0), [], ["ci"])
+    K(0.67, lambda q: q.iota(T.ji[:], [[1, C]], 0, -1), [], ["ji"])
+    K(0.19, lambda q: q.iota(T.pi[:], [[0, 32]], 0, 1), [], ["pi"])
+    K(0.19, lambda q: q.iota(T.ci[:], [[16, 32]], 0, 0), [], ["ci"])
     K(0.15, lambda q: q.iota(T.ui[:], [[16, 8]], 0, 0), [], ["ui"])
-    K(0.67, lambda q: q.iota(T.rs0[:], [[0, 20], [1, 16]], 0, 0, allow_small_or_imprecise_dtypes=True), [], ["rs0"])
     V(0.3, lambda q: q.memset(T.one[:], 1.0), [], ["one"])
     K(1.1, lambda q: q.affine_select(T.big[:], T.one[:], [[-1, 528]], A.is_equal, 0.0, 3, 4), ["one"], ["big"])
-    V(ROW, lambda q: q.tensor_scalar(T.dg[:], T.ji[:], 15, None, A.bitwise_and), ["ji"], ["dg"])
-    V(ROW, lambda q: q.tensor_scalar(T.t1[:], T.dg[:], 1.0, 320.0, A.is_equal, A.mult), ["dg"], ["t1"])
-    V(ROW, lambda q: q.tensor_scalar(T.t2[:], T.dg[:], 0.0, -16384.0, A.is_equal, A.mult), ["dg"], ["t2"])
-    V(2 * ROW, lambda q: q.tensor_tensor(T.wt[:], T.t1[:], T.t2[:], A.add), ["t1", "t2"], ["wt"])
-    V(ROW, lambda q: q.tensor_scalar(T.mask[:], T.dg[:], 0.0, None, A.is_equal), ["dg"], ["mask"])
-    V(ROW, lambda q: q.tensor_scalar(T.cap[:], T.mask[:], 2 * BIG, -BIG, A.mult, A.add), ["mask"], ["cap"])
-    V(ROW, lambda q: q.tensor_scalar(T.rs[:], T.rs0[:], 1.0, None, A.min), ["rs0"], ["rs"])
-    V(SMALL, lambda q: q.tensor_scalar(T.pa15[:], T.pi[:], 15, None, A.bitwise_and), ["pi"], ["pa15"])
-    V(SMALL, lambda q: q.tensor_scalar(L("f0"), T.pa15[:], 15.0, 320.0, A.is_equal, A.mult), ["pa15"], ["f0"])
-    V(SMALL, lambda q: q.tensor_scalar(L("col"), L("f0"), -160.0, None, A.add), ["f0"], ["col"])
-    V(SMALL, lambda q: q.tensor_tensor(L("cw"), T.pa15[:], T.ci[:], A.add), ["pa15", "ci"], ["cw"])
-    V(SMALL, lambda q: q.tensor_scalar(L("cwu"), L("cw"), 1.0 / C, None, A.mult), ["cw"], ["cwu"])
-    V(SMALL, lambda q: q.tensor_copy(T.uo[:], T.ui[:]), ["ui"], ["uo"])
-    for i in range(len(GROUPS)):
-        S(ROW, lambda q, i=i: copy(q, at("p%d" % i, 0), T.idr[:]), ["idr"], [("p%d" % i, 0, 1)])
+    ts(T.dg[:], T.ji[:], 15, None, A.bitwise_and, None, ["ji"], ["dg"], ROW)
+    ts(T.t1[:], T.dg[:], 1.0, 320.0, A.is_equal, A.mult, ["dg"], ["t1"], ROW)
+    ts(T.t2[:], T.dg[:], 0.0, -16384.0, A.is_equal, A.mult, ["dg"], ["t2"], ROW)
+    tt(T.wt[:], T.t1[:], T.t2[:], A.add, ["t1", "t2"], ["wt"], 2 * ROW)
+    ts(T.pa[:], T.pi[:], 15, None, A.bitwise_and, None, ["pi"], ["pa"])
+    tt(L("cw", 32), T.pa[:], T.ci[:], A.add, ["pa", "ci"], ["cw"])
+    ts(L("c320", 32), L("cw", 32), 320.0, None, A.add, None, ["cw"], ["c320"])
+    cp(T.uo[:], T.ui[:], ["ui"], ["uo"])
+    row = T.pa[:, 0:1]
+    ts(cf("e15"), row, 15.0, None, A.is_equal, None, ["pa"], ["e15"])
+    ts(cf("col"), cf("e15"), 320.0, -160.0, A.mult, A.add, ["e15"], ["col"])
+    for b in ("fw0", "fw1"):
+        act(at(b, 1), T.idr[:], ["idr"], [(b, 1, 2)])
+    for b in ("n1", "n2", "e1", "e2"):
+        V(SMALL, lambda q, b=b: q.memset(T[b][:, 0:16], 0.0), [], [(b, 0, 1)])
+        V(SMALL, lambda q, b=b: q.memset(T[b][:, C + 16:PAD], 0.0), [], [(b, 2, 3)])
     for b in range(4):
         V(0.16, lambda q, b=b: q.quantize_mx(T.eq[:, 128 * b:128 * b + 128], T.ep[:, 128 * b:128 * b + 128], T.big[:, 3 - b:515 - b]),
           ["big"], [("eq", b, b + 1), ("ep", b, b + 1)])
 
+    ts(cn(0), row, -1.0, 15.0, A.mult, A.add, ["pa"], ["c0"])
+    ts(cn(1), cn(0), -1.0, 0.0, A.add, A.max, ["c0"], ["c1"])
+    ts(cn(2), row, 1, None, A.bitwise_and, None, ["pa"], ["c2"])
+    ts(cn(3), cn(0), 1, None, A.arith_shift_right, None, ["c0"], ["c3"])
+    cp(cf("od"), cn(2), ["c2"], ["od"])
+    ts(cn(4), cn(3), cf("od"), 0.0, A.subtract, A.max, ["c3", "od"], ["c4"])
+    for i, (src, k) in enumerate([(0, 0), (0, 1), (0, 2), (0, 3), (1, 2), (1, 3), (4, 0), (4, 1), (4, 2)]):
+        ts(T.bits[:, i:i + 1], cn(src), k, 1, A.arith_shift_right, A.bitwise_and, ["c%d" % src], [("bits", i, i + 1)])
+    cp(cf("sc", 0, 9), T.bits[:, 0:9], ["bits"], ["sc"])
+    ts(cf("ko"), cf("od"), KEY, None, A.mult, None, ["od"], ["ko"])
+    V(SMALL, lambda q: q.memset(cf("kb", 0, 4), 0.0), [], [("kb", 0, 1)])
+    ts(cf("kb", 4, 2), cf("sc", 4, 2), KEY, None, A.mult, None, ["sc"], [("kb", 1, 2)])
+    ts(cf("kb", 6, 3), cf("sc", 6, 3), cf("ko"), None, A.mult, None, ["sc", "ko"], [("kb", 2, 3)])
+    ts(cf("nb", 0, 9), cf("sc", 0, 9), BIG, -BIG, A.mult, A.add, ["sc"], ["nb"])
+    tt(cf("bi", 0, 9), cf("kb", 0, 9), cf("nb", 0, 9), A.add, ["kb", "nb"], ["bi"])
+    V(SMALL, lambda q: q.tensor_reduce(cf("k2"), cf("kb", 6, 3), AxisListType.X, A.add, negate=True), ["kb"], ["k2"])
+    tt(cf("a2"), cf("od"), cf("e15"), A.subtract, ["od", "e15"], ["a2"])
+    tt(cf("b2"), cf("e15"), cf("a2"), A.subtract, ["e15", "a2"], ["b2"])
+    act(T.ia[:], T.idr[:], ["idr", "a2"], ["ia"], scale=cf("a2"))
+    act(T.ic[:], T.idr[:], ["idr", "b2"], ["ic"], scale=cf("b2"))
+    ts(cf("z0"), row, 0.0, None, A.not_equal, None, ["pa"], ["z0"])
+    ts(cf("z1"), cf("z0"), BIG, -BIG, A.mult, A.add, ["z0"], ["z1"])
+    ts(cn(8, 2), L("cw", 2), 19.0, None, A.min, None, ["cw"], ["c8"])
+    ts(cn(10, 2), T.pi[:, 0:2], 4, 1, A.arith_shift_right, A.bitwise_and, ["pi"], ["c10"])
+    tt(cn(12, 2), cn(8, 2), cn(10, 2), A.add, ["c8", "c10"], ["c12"])
+    ts(cn(14, 2), cn(12, 2), 1, None, A.bitwise_and, None, ["c12"], ["c14"])
+    tt(cn(16, 2), cn(8, 2), cn(14, 2), A.add, ["c8", "c14"], ["c16"])
+    ts(cn(18, 2), cn(16, 2), 1, None, A.arith_shift_right, None, ["c16"], ["c18"])
+    ts(cn(20, 2), cn(14, 2), 10.0, None, A.mult, None, ["c14"], ["c20"])
+    tt(cn(22, 2), cn(18, 2), cn(20, 2), A.add, ["c18", "c20"], ["c22"])
+    ts(cn(24, 2), cn(22, 2), 2.0, None, A.mult, None, ["c22"], ["c24"])
+    tt(cn(26, 2), cn(24, 2), cn(10, 2), A.add, ["c24", "c10"], ["c26"])
+    for i, (a, b) in enumerate([(16.0, 0.0), (16.0, 15.0), (8.0, 7.0)]):
+        ts(T.pick[:, 2 * i:2 * i + 2], cn(26, 2), a, b, A.mult, A.add, ["c26"], [("pick", i, i + 1)])
+
+    def picked(b, i):
+        return T[b][:].indirect(T.pick[:, 2 * i:2 * i + 2])
+
     V(0.16, lambda q: q.quantize_mx(T.uq[:], T.up[:], T.ut[:]), ["ut"], ["uq", "up"])
-    V(0.3, lambda q: q.tensor_copy(T.uqr[:].bitcast(dt.uint32), T.uq[:].bitcast(dt.uint32).indirect(T.uo[:])), ["uq", "uo"], ["uqr"])
-    V(0.3, lambda q: q.tensor_copy(T.upr[:], T.up[:].indirect(T.uo[:])), ["up", "uo"], ["upr"])
+    cp(T.uqr[:].bitcast(dt.uint32), T.uq[:].bitcast(dt.uint32).indirect(T.uo[:]), ["uq", "uo"], ["uqr"], 0.3)
+    cp(T.upr[:], T.up[:].indirect(T.uo[:]), ["up", "uo"], ["upr"], 0.3)
     V(0.16, lambda q: q.quantize_mx(T.vq[:], T.vp[:], T.vt[:]), ["vt"], ["vq", "vp"])
 
-    V(SMALL, lambda q: q.tensor_copy(T.l0[:], T.nxi[:]), ["nxi"], ["l0"])
-    V(SMALL, lambda q: q.tensor_copy(L("fw"), T.nxi[:]), ["nxi"], ["fw"])
-    V(SMALL, lambda q: q.tensor_copy(T.mt16[:], T.mti[:]), ["mti"], ["mt16"])
-    V(SMALL, lambda q: q.tensor_copy(L("bd"), T.mti[:]), ["mti"], ["bd"])
-    V(SMALL, lambda q: q.tensor_tensor(L("be"), L("bd"), L("cw"), A.min), ["bd", "cw"], ["be"])
-    V(SMALL, lambda q: q.tensor_tensor(L("bf"), L("bd"), L("cw"), A.max), ["bd", "cw"], ["bf"])
-    V(SMALL, lambda q: q.tensor_copy(T.lo16[:], L("be")), ["be"], ["lo16"])
-    V(SMALL, lambda q: q.tensor_copy(T.hi16[:], L("bf")), ["bf"], ["hi16"])
+    cp(T.l0[:], T.nxi[:], ["nxi"], ["l0"])
+    cp(L("bd"), T.mti[:], ["mti"], ["bd"])
+    tt(L("be"), L("bd"), L("cw"), A.min, ["bd", "cw"], ["be"])
+    tt(L("bf"), L("bd"), L("cw"), A.max, ["bd", "cw"], ["bf"])
+    cp(T.lo16[:], L("be"), ["be"], ["lo16"])
+    cp(T.hi16[:], L("bf"), ["bf"], ["hi16"])
+    tt(L("dm"), L("bd"), L("cw"), A.subtract, ["bd", "cw"], ["dm"])
+    ts(cf("f0"), cf("col"), -160.0, None, A.add, None, ["col"], ["f0"])
+    ts(L("sx"), L("dm"), cf("f0"), None, A.mult, None, ["dm", "f0"], ["sx"])
+    tt(L("dc"), L("sx"), L("cw"), A.add, ["sx", "cw"], ["dc"])
 
-    def row(out, a, win, i, k):
-        S(GATHER, lambda q: copy(q, at(out, a), at(win, i).indirect(T["l%d" % k][:])), [(win, i, i + 1), "l%d" % k], [(out, a, a + 1)])
+    def weighted(dst, src):
+        V(HALF, lambda q: q.tensor_tensor_scan(T[dst][:], T.wt[:], at(src), 0.0, A.add, A.max), ["wt", (src, 0, 1)], [dst])
 
-    def look(dst, win, i, k, off):
-        S(GATHER, lambda q: copy(q, T[dst][:], T[win][:, C * i:C * k].indirect(T[off][:])), [(win, i, k), off], [dst])
+    def listed(l, src, tmp="scn"):
+        weighted(tmp, src)
+        ts(T[l][:], every16(tmp), cf("col"), None, A.add, None, [tmp, "col"], [l])
 
-    def running(dst, src):
-        V(SCAN2, lambda q: q.tensor_tensor_scan(T[dst][:], T.rs[:], T[src][:], 0.0, A.mult, A.add), ["rs", src], [dst])
-
-    def weighted(dst, src, a=0):
-        V(SCAN2, lambda q: q.tensor_tensor_scan(T[dst][:], T.wt[:], at(src, a), 0.0, A.add, A.max), ["wt", (src, a, a + 1)], [dst])
-
-    def at_f(k):
-        return [("p%d" % i, 2 ** levels.index(k)) for i, levels in enumerate(GROUPS) if k in levels][0]
-
-    def powers():
-        row(*at_f(0), "idr", 0, 0)
+    def powers(src):
         for k in range(6):
-            l = "l%d" % (k + 1)
-            row(*at_f(k + 1), *at_f(k), k)
-            weighted("scn", *at_f(k + 1))
-            V(SMALL, lambda q, l=l: q.tensor_scalar(T[l][:], every16("scn"), col, None, A.add), ["scn", "col"], [l])
-        b, a = at_f(1)
-        S(ROW, lambda q: copy(q, at(LAST, 2), at(b, a)), [(b, a, a + 1)], [(LAST, 2, 3)])
-        for i, levels in enumerate(GROUPS):
-            for j, k in enumerate(levels):
-                for a2 in range(1, 2 ** j if k >= 0 else 0):
-                    row("p%d" % i, 2 ** j + a2, "p%d" % i, a2, k)
+            dst = "f%d" % (k + 1) if k in (2, 3) else "fb" if k % 2 else "fa"
+            act(at(dst), by(src, "l%d" % k), [(src, 0, 1), "l%d" % k], [dst], GATHER)
+            listed("l%d" % (k + 1), dst)
+            src = dst
+
+    def steps(name, src, levels, first):
+        for i, k in enumerate(levels):
+            w, dst = "m%sw" % name, "m%s%d" % (name, i % 2)
+            if dst == src:
+                dst = "m%s%d" % (name, (i + 1) % 2)
+            if k >= first[0]:
+                c = first[1] + k - first[0]
+                act(at(w), at(src), [src, "sc", "bi"], [w], scale=cf("sc", c), bias=cf("bi", c))
+            elif i == 0:
+                w = "sb"
+            else:
+                act(at(w), at(src), [src], [w])
+            tt(at(dst), by(w, "l%d" % k), at(src), A.max, [w, src, "l%d" % k], [dst], GATHER)
+            src = dst
+        return src
+
+    def turn(dst, src):
+        V(HALF, lambda q: q.transpose(T[dst][:, 0:C], T[src][:, 16:C + 16]), [src], [(dst, 0, 1)])
+        V(HALF * 1.1, lambda q: q.transpose(T[dst][:, C:TW], T[src][:]), [src], [(dst, 1, 2)])
+
+    def mid(b):
+        return T[b][:, 16:C + 16]
+
+    cp(mid("n1"), T.idr[:], ["idr"], [("n1", 1, 2)], HALF)
+    turn("tn1", "n1")
+    cp(T.tid[:], T.tn1[:, 15:TW:16], ["tn1"], ["tid"])
+    act(T.gs[:], T.idr[:], ["idr"], ["gs"])
+
+    def places(r):
+        act(T.f34[:], by("f3", "l4"), ["f3", "l4"], ["f34"], GATHER)
+        for i, (src, a) in enumerate([("f3", 1), ("f4", 0), ("f34", 3)]):
+            move("g%d%d" % (i, r), T.gs[a:128:4, :], T[src][a:128:4, :], [src], [("gs", a, a + 1)])
+        e = steps("e", "gs", [5, 6], (5, 4))
+        act(T.mew[:], at(e), [e], ["mew"])
+        tt(mid("e1"), by("mew", "l3"), at(e), A.subtract, ["mew", e, "l3"], [("e1", 1, 2)], GATHER)
+        turn("te1", "e1")
+        cp(T.te1[:, 15:TW:16], T.tid[:], ["tid"], ["te1"])
 
     sent = [0]
 
@@ -342,10 +434,6 @@ def build(P, g, core, T, topo):
             sent[0] += len(topo.engines(core, dst))
         return task(P, "net", latency, None, [], land, "land", sem, len(topo.engines(src, core)) * len(pairs), after=ids)
 
-    def compare(level, off, behind=()):
-        win = TABLES[level]
-        V(GATHER, lambda q: q.tensor_tensor(T.cb[:], T[win][:].indirect(T[off][:]), T.sm[:], A.is_le), [win, off, "sm"], ["cb"], behind)
-
     def mm(out, b, wq, wp, a, xq, xp, unit):
         E(0.35, lambda q: q.matmul_mx(T[out][:, BANK * b:BANK * b + C], T[wq][:, a:a + 128], T[wp][:, a:a + 128], T[xq][:], T[xp][:], True, True),
           [(wq, unit, unit + 1), (wp, unit, unit + 1), xq, xp], [(out, b, b + 1)])
@@ -353,111 +441,78 @@ def build(P, g, core, T, topo):
     def bank(out, b):
         return T[out][:, BANK * b:BANK * b + C]
 
-    powers()
+    act(at("fw0"), by("idr", "l0"), ["idr", "l0"], [("fw0", 0, 1)], GATHER)
     for r in range(ROUNDS):
         X, xq, xp, aq, ap = "x%d" % r, "xq%d" % r, "xp%d" % r, "aq%d" % r, "ap%d" % r
         lp, lb, rp, rb = "lp%d" % r, "lb%d" % r, "rp%d" % r, "rb%d" % r
+        fw, fn = "fw%d" % (r % 2), "fw%d" % (1 - r % 2)
+        powers(fw)
+        places(r)
         V(0.37, lambda q, xq=xq, xp=xp, X=X: q.quantize_mx(T[xq][:], T[xp][:], T[X][:]), [X], [xq, xp])
         send(r, [(T[aq][:].bitcast(dt.uint8), T[xq][:].bitcast(dt.uint8), xq), (T[ap][:], T[xp][:], xp)], "ax%d" % r, [aq, ap], 6.0)
         mm("pw", 0, "uqr", "upr", 0, xq, xp, 0)
         mm("pw", 1, "uqr", "upr", 0, xq, xp, 0)
-        S(ROW, lambda q: copy(q, T.srow[:], bank("pw", 0)), [("pw", 0, 1)], ["srow"])
-        V(ROW, lambda q: q.tensor_tensor(T.sm[:], bank("pw", 1), T.cap[:], A.min), [("pw", 1, 2), "cap"], ["sm"])
-        V(GATHER, lambda q: q.tensor_copy(at("m0", 0), T.srow[:].indirect(T.l0[:])), ["srow", "l0"], [("m0", 0, 1)])
-        S(GATHER, lambda q: copy(q, at("ml", 0), T.srow[:].indirect(T.l0[:])), ["srow", "l0"], [("ml", 0, 1)])
-        for k in range(5):
-            twin, m0, m1 = ("d%d" % (k % 2) if k else "ml"), "m%d" % k, "m%d" % (k + 1)
-            V(GATHER, lambda q, k=k, twin=twin, m0=m0, m1=m1: q.tensor_tensor(at(m1, 0), at(m0, 0).indirect(T["l%d" % k][:]), at(twin, 0), A.max),
-              [(m0, 0, 1), (twin, 0, 1), "l%d" % k], [(m1, 0, 1)])
-            if k < 4:
-                d = "d%d" % ((k + 1) % 2)
-                S(ROW, lambda q, d=d, m1=m1: copy(q, at(d, 0), at(m1, 0)), [(m1, 0, 1)], [(d, 0, 1)])
-        for k, passed in PASSED.items():
-            for j, l in enumerate(passed):
-                for a in range(2 ** j):
-                    row(TABLES[k], 2 ** j + a, TABLES[k], a, l)
+        cp(T.sa[:], bank("pw", 0), [("pw", 0, 1)], ["sa"], ROW)
+        act(T.sb[:], bank("pw", 1), [("pw", 1, 2)], ["sb"])
+        act(T.s2[:], bank("pw", 1), [("pw", 1, 2), "z0", "z1"], ["s2"], scale=cf("z0"), bias=cf("z1"))
+        coarse = steps("c", "sa", range(7), (3, 0))
+        move("o%d" % r, T.sb[1:128:2, :], T.ia[1:128:2, :], ["ia"], ["sb"])
+        tt(at("mf1"), by("sb", "l0"), T.ic[:], A.add, ["sb", "ic", "l0"], ["mf1"], GATHER)
+        fine = steps("f", "mf1", range(3), (0, 6))
         for b in range(4):
             mm("pu", b, "eq", "ep", 128 * b, xq, xp, b)
-            (V if b < 2 else S)(ROW, lambda q, b=b: (q.tensor_copy if b < 2 else lambda o, i: copy(q, o, i))(at("fo", b), bank("pu", b)),
-                                [("pu", b, b + 1)], [("fo", b, b + 1)])
+            act(at("fo", b), bank("pu", b), [("pu", b, b + 1)], [("fo", b, b + 1)])
         for b in range(4):
             mm("pu", b, "eq", "ep", 128 * b, aq, ap, b)
-            S(ROW, lambda q, b=b: copy(q, at("fh", b), bank("pu", b), scale=0.5), [("pu", b, b + 1)], [("fh", b, b + 1)])
-        for i, levels in enumerate(GROUPS):
-            place, last = "cwu" if i == 0 else "pif", i == len(GROUPS) - 1
-            for j, k in enumerate(levels):
-                if i == 0 and j == 0:
-                    V(2 * ROW, lambda q: q.tensor_tensor(T.fb[:], at("m5", 0), T.sm[:], A.is_le), [("m5", 0, 1), "sm"], ["fb"])
-                    running("fs", "fb")
-                    V(GATHER, lambda q: q.tensor_tensor(T.cb[:], at("m5", 0).indirect(T.l5[:]), T.sm[:], A.is_le), [("m5", 0, 1), "l5", "sm"], ["cb"])
-                    running("cs", "cb")
-                    V(SMALL, lambda q: q.tensor_tensor(L("fv"), every16("cs"), every16("fs"), A.mult), ["cs", "fs"], ["fv"])
-                else:
-                    compare(k, off, behind)
-                    running("cs", "cb")
-                behind = []
-                if k < 0:
-                    break
-                f, off = "f%d" % (j % 2), "o%d" % (j % 2)
-                V(SMALL, lambda q, f=f, place=place, top=i + j == 0: q.tensor_tensor(L(f), L(place), L("fv") if top else every16("cs"), A.add),
-                  [place, "cs", "fv"] if i + j == 0 else [place, "cs"], [f])
-                V(SMALL, lambda q, f=f, off=off, j=j: q.tensor_scalar(T[off][:], L(f), float(C * 2 ** j), 0.25, A.mult, A.add), [f], [off])
-                if j + 1 < len(levels) and levels[j + 1] >= 0:
-                    place = "h%d" % (j % 2)
-                    behind = [V(SMALL, lambda q, f=f, place=place: q.tensor_scalar(L(place), L(f), 0.5, None, A.mult), [f], [place])]
-                if j + 1 < len(levels) and levels[j + 1] < 0:
-                    look("pr", LAST, 0, 2, off)
-                    look("fr", LAST, 1, 3, off)
-                    weighted("pws", "pr")
-                    V(SMALL, lambda q, lp=lp: q.tensor_scalar(T[lp][:], every16("pws"), col, None, A.add), ["pws", "col"], [lp])
-                    send(r, [(T[rp][:], T[lp][:], lp)], "arp%d" % r, [rp], 2.6)
-                    weighted("fsn", "fr")
-                    V(SMALL, lambda q: q.tensor_scalar(L("fv"), every16("fsn"), col, None, A.add), ["fsn", "col"], ["fv"])
-                    V(SMALL, lambda q: q.tensor_tensor(L("bd"), L("cw"), L("fv"), A.subtract), ["cw", "fv"], ["bd"])
-            if not last:
-                look("pb", "p%d" % i, 0, 2 ** len(levels), off)
-                weighted("psn", "pb")
-                V(SMALL, lambda q: q.tensor_scalar(L("pif"), every16("psn"), col, 1.0 / C, A.add, A.mult), ["psn", "col"], ["pif"])
-        V(SMALL, lambda q: q.tensor_tensor(L("be"), L("bd"), every16("cs"), A.mult), ["bd", "cs"], ["be"])
-        V(SMALL, lambda q: q.tensor_tensor(L("bf"), L("be"), L("fv"), A.add), ["be", "fv"], ["bf"])
-        V(SMALL, lambda q, lb=lb: q.tensor_copy(T[lb][:], L("bf")), ["bf"], [lb])
+            act(at("fh", b), bank("pu", b), [("pu", b, b + 1)], [("fh", b, b + 1)], scale=0.5)
+        tt(mid("n1"), by(coarse, "l0"), T.s2[:], A.is_le, [coarse, "l0", "s2"], [("n1", 1, 2)], GATHER)
+        turn("tn1", "n1")
+        V(2.1 * HALF, lambda q: q.tensor_tensor_scan(T.r1[:], T.tn1[:], T.te1[:], 0.0, A.mult, A.add), ["tn1", "te1"], ["r1"])
+        ts(T.lq[:], picked("r1", 1), 160.0, None, A.add, None, ["r1", "pick"], ["lq"], 0.1)
+        tt(mid("n2"), by(fine, "lq"), T.sa[:], A.is_le, [fine, "lq", "sa"], [("n2", 1, 2)], GATHER)
+        act(mid("e2"), by(fine, "lq"), [fine, "lq", "od", "k2"], [("e2", 1, 2)], GATHER, scale=cf("od"), bias=cf("k2"))
+        turn("tn2", "n2")
+        tt(L("hl", 32), picked("tn2", 0), L("c320", 32), A.mult, ["tn2", "pick", "c320"], ["hl"], 0.1)
+        V(SMALL, lambda q: q.memset(T.tn2[:, 0:TW:16], 0.0), [], ["tn2"])
+        ts(L("hm", 32), L("hl", 32), -160.0, None, A.add, None, ["hl"], ["hm"])
+        turn("te2", "e2")
+        V(1.05 * HALF, lambda q: q.tensor_tensor_scan(T.r2[:], T.tn2[:, 0:TW:2], T.te2[:, 1:TW:2], 0.0, A.mult, A.add), ["tn2", "te2"], ["r2"])
+        tt(L("om", 32), picked("r2", 2), L("hm", 32), A.max, ["r2", "pick", "hm"], ["om"], 0.1)
+        ts(T.ob[:], L("om", 32), 160.0, None, A.add, None, ["om"], ["ob"])
+        ts(T[lp][:], picked("r2", 2), 160.0, None, A.add, None, ["r2", "pick"], [lp], 0.1)
+        send(r, [(T[rp][:], T[lp][:, 0:20], lp)], "arp%d" % r, [rp], 2.6)
+        act(T.br[:], T[fw][:].indirect(T.ob[:, 0:20]), [fw, "ob"], ["br"], GATHER)
+        listed(lb, "br", "bsn")
         send(r, [(T[rb][:], T[lb][:], lb)], "arb%d" % r, [rb], 2.6)
-        S(GATHER, lambda q, lb=lb: copy(q, T.er[:], T.srow[:].indirect(T[lb][:])), ["srow", lb], ["er"])
-        S(GATHER, lambda q: copy(q, T.eh[:], T.er[:].indirect(T.hi16[:])), ["er", "hi16"], ["eh"])
-        V(GATHER, lambda q: q.tensor_tensor(T.sw[:], T.er[:].indirect(T.lo16[:]), T.eh[:], A.is_gt), ["er", "eh", "lo16"], ["sw"])
+        act(T.er[:], by("sa", lb), ["sa", lb], ["er"], GATHER)
+        act(T.eh[:], by("er", "hi16"), ["er", "hi16"], ["eh"], GATHER)
+        tt(T.sw[:], by("er", "lo16"), T.eh[:], A.is_gt, ["er", "eh", "lo16"], ["sw"], GATHER)
         weighted("swn", "sw")
-        V(SMALL, lambda q: q.tensor_scalar(L("swc"), every16("swn"), col, -160.0, A.add, A.add), ["swn", "col"], ["swc"])
-        S(GATHER, lambda q: copy(q, T.fmr[:], at(*at_f(0)).indirect(T.mt16[:])), [at_f(0) + (at_f(0)[1] + 1,), "mt16"], ["fmr"])
-        weighted("fmn", "fmr")
-        V(SMALL, lambda q: q.tensor_scalar(L("fmv"), every16("fmn"), col, None, A.add), ["fmn", "col"], ["fmv"])
-        fw, fn = ("fw", "fn") if r % 2 == 0 else ("fn", "fw")
-        V(SMALL, lambda q, fw=fw: q.tensor_tensor(L("fd"), L("fmv"), L(fw), A.subtract), ["fmv", fw], ["fd"])
-        V(SMALL, lambda q: q.tensor_tensor(L("fe"), L("fd"), L("swc"), A.mult), ["fd", "swc"], ["fe"])
-        V(SMALL, lambda q, fw=fw, fn=fn: q.tensor_tensor(L(fn), L(fw), L("fe"), A.add), [fw, "fe"], [fn])
-        V(SMALL, lambda q, fn=fn: q.tensor_copy(T.l0[:], L(fn)), [fn], ["l0"])
+        tt(L("sx"), every16("swn"), L("dm"), A.mult, ["swn", "dm"], ["sx"])
+        tt(L("sy"), L("sx"), L("dc"), A.add, ["sx", "dc"], ["sy"])
+        cp(T.so[:], L("sy"), ["sy"], ["so"])
         if r < ROUNDS - 1:
-            powers()
+            act(at(fn), by(fw, "so"), [(fw, 0, 1), "so"], [(fn, 0, 1)], GATHER)
+            listed("l0", fn)
         else:
-            S(GATHER, lambda q: copy(q, T.er[:], T.idr[:].indirect(T.l0[:]), bias=160.0), ["idr", "l0"], ["er"])
+            act(T.er[:], by(fw, "so"), [(fw, 0, 1), "so"], ["er"], GATHER, bias=160.0)
             task(P, "y", 0.07, lambda q: q.dma_start(T.nf[:], T.er[0:128:16, :]), ["er"], [], "dma", "st", 16)
         for b in range(4):
-            S(GATHER, lambda q, b=b, rp=rp: copy(q, at("gp", b), at("fh", b).indirect(T[rp][:])), [("fh", b, b + 1), rp], [("gp", b, b + 1)])
-            V(GATHER, lambda q, b=b, rb=rb: q.tensor_tensor(T.z[:, b:4 * C:4], at("fh", b).indirect(T[rb][:]), at("gp", b), A.add),
-              [("fh", b, b + 1), rb, ("gp", b, b + 1)], [("z", b, b + 1)])
+            act(at("gp", b), by("fh", rp, b), [("fh", b, b + 1), rp], [("gp", b, b + 1)], GATHER)
+            tt(T.z[:, b:4 * C:4], by("fh", rb, b), at("gp", b), A.add, [("fh", b, b + 1), rb, ("gp", b, b + 1)], [("z", b, b + 1)], GATHER)
         V(0.37, lambda q: q.quantize_mx(T.zq[:], T.zp[:], T.z[:]), ["z"], ["zq", "zp"])
         Y = "x%d" % (r + 1)
         for b in range(4):
             mm("pw", b, "wq", "wp", 128 * b, "zq", "zp", b)
-            S(ROW, lambda q, b=b: copy(q, at("h", b), bank("pw", b), scale=0.03125), [("pw", b, b + 1)], [("h", b, b + 1)])
-            V(GATHER, lambda q, b=b, lb=lb, Y=Y: q.tensor_tensor(T[Y][:, b:4 * C:4], at("h", b).indirect(T[lb][:]), at("fo", b), A.add),
-              [("h", b, b + 1), lb, ("fo", b, b + 1)], [(Y, b, b + 1)])
+            act(at("h", b), bank("pw", b), [("pw", b, b + 1)], [("h", b, b + 1)], scale=0.03125)
+            tt(T[Y][:, b:4 * C:4], by("h", lb, b), at("fo", b), A.add, [("h", b, b + 1), lb, ("fo", b, b + 1)], [(Y, b, b + 1)], GATHER)
     xq, xp, X = "xq%d" % ROUNDS, "xp%d" % ROUNDS, "x%d" % ROUNDS
-    V(0.37, lambda q, xq=xq, xp=xp, X=X: q.quantize_mx(T[xq][:], T[xp][:], T[X][:]), [X], [xq, xp])
+    V(0.37, lambda q: q.quantize_mx(T[xq][:], T[xp][:], T[X][:]), [X], [xq, xp])
     task(P, "y", 0.07, lambda q: q.dma_start(T.oc[:], T[xq][:].bitcast(dt.uint8)), [xq], [], "dma", "st", 16)
     for k in range(4):
         task(P, "y" if k % 2 else "s", 0.07, lambda q, k=k: q.dma_start(T.osc[4 * k:4 * k + 4, :], T[xp][32 * k:32 * k + 4, :]), [xp], [], "dma", "st", 16)
     mm("pw", 0, "vq", "vp", 0, xq, xp, 0)
-    V(ROW, lambda q: q.tensor_copy(T.eh[:], bank("pw", 0)), [("pw", 0, 1)], ["eh"])
+    cp(T.eh[:], bank("pw", 0), [("pw", 0, 1)], ["eh"], ROW)
     task(P, "y", 0.07, lambda q: q.dma_start(T.y[:], T.eh[:]), ["eh"], [], "dma", "st", 16)
     return sent[0]
 

@@ -1,3 +1,4 @@
+import math
 import numpy as np
 from concourse.mybir import dt, AluOpType, ActivationFunctionType, AxisListType
 A = AluOpType
@@ -24,15 +25,15 @@ SCRATCH = {
     "vq": sb(128, "float8_e4m3fn_x4"), "vp": sb(128, "uint8"),
     "eq": sb(512, "float8_e4m3fn_x4"), "ep": sb(512, "uint8"),
     "one": sb(528, "bfloat16"), "big": sb(528, "bfloat16"),
-    "ji": sb(C, "int32"), "dg": sb(C, "int32"), "t1": sb(C, "bfloat16"), "t2": sb(C, "bfloat16"),
+    "ji": sb(16, "int32"), "dg": sb(16, "int32"), "t1": sb(16, "bfloat16"), "t2": sb(16, "bfloat16"), "w16": sb(16, "bfloat16"),
     "wt": sb(C, "bfloat16"), "idr": sb(C, "bfloat16"),
-    "ia": sb(C, "float32"), "ic": sb(C, "bfloat16"), "tid": sb(TW // 16, "bfloat16"),
+    "ia": sb(C, "float32"), "ic": sb(C, "bfloat16"), "tid": sb(TW // 16, "bfloat16"), "ti": sb(TW // 16, "float32"), "s0": sb(C, "float32"),
     "gs": sb(C, "bfloat16"), "f3": sb(C, "bfloat16"), "f4": sb(C, "bfloat16"), "f34": sb(C, "bfloat16"),
     "pi": sb(32, "int32"), "pa": sb(32, "int32"), "ci": sb(32, "int32"), "cn": sb(32, "int32"), "bits": sb(12, "int32"),
-    "ui": sb(8, "int32"), "uo": sb(8, "uint16"), "pick": sb(6, "uint16"),
+    "uo": sb(8, "uint16"), "pick": sb(6, "uint16"),
     "cf": sb(64, "float32"),
     "lo16": sb(20, "uint16"), "hi16": sb(20, "uint16"), "so": sb(20, "uint16"), "lq": sb(32, "uint16"), "ob": sb(32, "uint16"),
-    "sa": sb(C, "float32"), "sb": sb(C, "float32"), "s2": sb(C, "float32"),
+    "sa": sb(2 * C, "float32"), "fs": sb(C, "float32"), "sb": sb(C, "float32"), "s2": sb(C, "float32"), "dt": sb(C, "float32"),
     "n1": sb(PAD, "bfloat16"), "n2": sb(PAD, "bfloat16"), "e1": sb(PAD, "float16"), "e2": sb(PAD, "float16"),
     "tn1": sb(TW, "bfloat16"), "tn2": sb(TW, "bfloat16"), "te1": sb(TW, "float16"), "te2": sb(TW, "float16"),
     "r1": sb(TW, "bfloat16"), "r2": sb(TW // 2, "bfloat16"),
@@ -67,11 +68,13 @@ for _r in range(ROUNDS):
 SEMAPHORES = ["ev", "es", "et", "eg", "snd", "st"]
 SEMAPHORES += ["%s%d" % (_n, _r) for _n in ("ax", "arp", "arb") for _r in range(ROUNDS)]
 SEMAPHORES += ["ld_" + _n for _n in ("x", "u", "v", "nx", "mt", "wc", "ws")]
-SEMAPHORES += ["ld_%s%d" % (_n, _r) for _n in ("g0", "g1", "g2", "o") for _r in range(ROUNDS)]
+SEMAPHORES += ["ld_%s%d" % (_n, _r) for _n in ("g0", "g1", "g2", "o", "n") for _r in range(ROUNDS)]
 
 GATHER, HALF, ROW, SMALL = 0.58, 0.17, 0.34, 0.08
 HOP, SAME = 0.2, 0.1
 SHARED = {}
+OPT = {"own": [], "brv": True, "erv": False, "ehv": False, "f0v": True, "fsv": True}
+SA = ("sa", 0, 1)
 
 
 def new_plan():
@@ -117,7 +120,7 @@ def task(P, eng, dur, fn, reads, writes, kind="op", sem=None, inc=1, after=(), b
     return n
 
 
-def schedule(P, tries=5000):
+def schedule(P, tries=25000):
     ts = P["tasks"]
     n = len(ts)
     lags = [[(d, HOP if ts[d]["eng"] != t["eng"] else SAME) for d in t["deps"]] for t in ts]
@@ -136,7 +139,7 @@ def schedule(P, tries=5000):
         slots = {}
         start, end = [0.0] * n, [0.0] * n
         while ready:
-            i = max(ready, key=lambda k: rank[k])
+            i = max(ready, key=lambda k: rank[k]) if len(ready) > 1 else ready[0]
             ready.remove(i)
             t = ts[i]
             at, dur = 0.0, t["dur"]
@@ -159,18 +162,22 @@ def schedule(P, tries=5000):
                 left[s] -= 1
                 if left[s] == 0:
                     ready.append(s)
-        return max(end), {e: [x[2] for x in line] for e, line in slots.items()}, start
-    best, rank = place(up), up
+        cost = 0.7 * max(end) + 0.6 * sum(end[i] for i in sends) / len(sends)
+        return cost, {e: [x[2] for x in line] for e, line in slots.items()}, start, max(end)
+    sends = [i for i in range(n) if ts[i]["kind"] == "send"]
+    best = now = place(up)
     rng = np.random.default_rng(7)
-    for _ in range(tries):
-        at, width = rng.random() * max(up), [2, 5, 10][rng.integers(3)]
-        part, step = [0.05, 0.15, 0.4][rng.integers(3)], [0.5, 1.5, 4.0][rng.integers(3)]
-        hit, by = rng.random(n) < part, rng.standard_normal(n) * step
-        trial = [float(rank[i] + by[i]) if hit[i] and abs(up[i] - at) < width else rank[i] for i in range(n)]
-        got = place(trial)
-        if got[0] <= best[0]:
-            best, rank = got, trial
-    return best[1], best[2], best[0]
+    for k in range(tries):
+        rank = -np.array(now[2])
+        at, width = -rng.random() * now[3], [1.5, 3.0, 6.0][rng.integers(3)]
+        part, step = [0.05, 0.15, 0.4][rng.integers(3)], [0.3, 1.0, 3.0][rng.integers(3)]
+        hit = (rng.random(n) < part) & (abs(rank - at) < width)
+        got = place((rank + hit * rng.standard_normal(n) * step).tolist())
+        if got[0] - now[0] <= -(0.005 + 0.03 * (1 - k / tries)) * math.log(1 - rng.random()):
+            now = got
+            if got[0] < best[0]:
+                best = got
+    return best[1], best[2], best[3]
 
 
 def issue(P, order, start, g, T):
@@ -246,8 +253,8 @@ def build(P, g, core, T, topo):
     def E(dur, fn, reads, writes):
         return task(P, "t", dur, fn, reads, writes)
 
-    def K(dur, fn, reads, writes):
-        return task(P, "g", dur, fn, reads, writes)
+    def K(dur, fn, reads, writes, after=()):
+        return task(P, "g", dur, fn, reads, writes, after=after)
 
     def ts(out, in_, s1, s2, op0, op1, reads, writes, dur=SMALL):
         if op1 is None:
@@ -273,42 +280,43 @@ def build(P, g, core, T, topo):
     def by(b, l, a=0):
         return at(b, a).indirect(T[l][:, 0:20])
 
-    def load(q, name, fn, writes):
-        k = task(P, q, 0.07, fn, [], [], "dma", "ld_" + name, 16)
-        task(P, "net", 2.0, None, [], writes, "land", "ld_" + name, 16, after=[k])
+    def load(q, name, fn, writes, latency, after=()):
+        k = task(P, q, 0.07, fn, [], [], "dma", "ld_" + name, 16, after=after)
+        return task(P, "net", latency, None, [], writes, "land", "ld_" + name, 16, after=[k])
 
     def move(name, out, in_, reads, writes):
         k = task(P, "y", 0.07, lambda q: q.dma_start(out, in_), reads, writes, "dma", "ld_" + name, 16)
         task(P, "net", 2.2, None, reads, writes, "land", "ld_" + name, 16, after=[k])
 
-    load("y", "x", lambda q: q.dma_start(T.x0[:], T.x[:]), ["x0"])
-    load("s", "nx", lambda q: q.dma_start(T.nxi[:], T.nx[:]), ["nxi"])
-    load("y", "u", lambda q: q.dma_start(T.ut[:], T.u[:]), ["ut"])
-    load("s", "mt", lambda q: q.dma_start(T.mti[:], T.mt[:]), ["mti"])
-    load("y", "wc", lambda q: q.dma_start(T.wq[:].bitcast(dt.uint8), T.wc[:]), ["wq"])
-    load("y", "ws", lambda q: q.dma_start(T.wp[:], T.ws[:]), ["wp"])
-    load("y", "v", lambda q: q.dma_start(T.vt[:], T.v[:]), ["vt"])
+    k = load("s", "nx", lambda q: q.dma_start(T.nxi[:], T.nx[:]), ["nxi"], 2.0)
+    k = load("s", "u", lambda q: q.dma_start(T.ut[:], T.u[:]), ["ut"], 2.4, [k - 1])
+    load("s", "mt", lambda q: q.dma_start(T.mti[:], T.mt[:]), ["mti"], 2.4, [k - 1])
+    k = load("y", "x", lambda q: q.dma_start(T.x0[:], T.x[:]), ["x0"], 3.0)
+    load("y", "wc", lambda q: q.dma_start(T.wq[:].bitcast(dt.uint8), T.wc[:]), ["wq"], 3.0, [k])
+    load("y", "ws", lambda q: q.dma_start(T.wp[:], T.ws[:]), ["wp"], 3.0, [k])
+    load("y", "v", lambda q: q.dma_start(T.vt[:], T.v[:]), ["vt"], 3.0, [k])
 
-    K(0.67, lambda q: q.iota(T.idr[:], [[1, C]], -160, 0, allow_small_or_imprecise_dtypes=True), [], ["idr"])
-    K(0.67, lambda q: q.iota(T.ji[:], [[1, C]], 0, -1), [], ["ji"])
-    K(0.19, lambda q: q.iota(T.pi[:], [[0, 32]], 0, 1), [], ["pi"])
-    K(0.19, lambda q: q.iota(T.ci[:], [[16, 32]], 0, 0), [], ["ci"])
-    K(0.15, lambda q: q.iota(T.ui[:], [[16, 8]], 0, 0), [], ["ui"])
+    k = K(0.19, lambda q: q.iota(T.pi[:], [[0, 32]], 0, 1), [], ["pi"])
+    k = K(0.16, lambda q: q.iota(T.ji[:], [[1, 16]], 0, -1), [], ["ji"], [k])
+    k = K(0.19, lambda q: q.iota(T.ci[:], [[16, 32]], 0, 0), [], ["ci"], [k])
+    K(0.67, lambda q: q.iota(T.idr[:], [[1, C]], -160, 0, allow_small_or_imprecise_dtypes=True), [], ["idr"], [k])
     V(0.3, lambda q: q.memset(T.one[:], 1.0), [], ["one"])
     K(1.1, lambda q: q.affine_select(T.big[:], T.one[:], [[-1, 528]], A.is_equal, 0.0, 3, 4), ["one"], ["big"])
-    ts(T.dg[:], T.ji[:], 15, None, A.bitwise_and, None, ["ji"], ["dg"], ROW)
-    ts(T.t1[:], T.dg[:], 1.0, 320.0, A.is_equal, A.mult, ["dg"], ["t1"], ROW)
-    ts(T.t2[:], T.dg[:], 0.0, -16384.0, A.is_equal, A.mult, ["dg"], ["t2"], ROW)
-    tt(T.wt[:], T.t1[:], T.t2[:], A.add, ["t1", "t2"], ["wt"], 2 * ROW)
     ts(T.pa[:], T.pi[:], 15, None, A.bitwise_and, None, ["pi"], ["pa"])
+    ts(T.dg[:], T.ji[:], 15, None, A.bitwise_and, None, ["ji"], ["dg"])
+    ts(T.t1[:], T.dg[:], 1.0, 320.0, A.is_equal, A.mult, ["dg"], ["t1"])
+    ts(T.t2[:], T.dg[:], 0.0, -16384.0, A.is_equal, A.mult, ["dg"], ["t2"])
+    tt(T.w16[:], T.t1[:], T.t2[:], A.add, ["t1", "t2"], ["w16"])
+    cp(T.so[:], T.pa[:, 0:20], ["pa"], ["so"])
+    act(T.wt[:], T.w16[:].indirect(T.so[:]), ["w16", "so"], ["wt"], GATHER)
     tt(L("cw", 32), T.pa[:], T.ci[:], A.add, ["pa", "ci"], ["cw"])
-    ts(L("c320", 32), L("cw", 32), 320.0, None, A.add, None, ["cw"], ["c320"])
-    cp(T.uo[:], T.ui[:], ["ui"], ["uo"])
+    act(L("c320", 32), L("cw", 32), ["cw"], ["c320"], SMALL, bias=-640.0)
+    cp(T.uo[:], T.ci[:, 0:8], ["ci"], ["uo"])
     row = T.pa[:, 0:1]
     ts(cf("e15"), row, 15.0, None, A.is_equal, None, ["pa"], ["e15"])
     ts(cf("col"), cf("e15"), 320.0, -160.0, A.mult, A.add, ["e15"], ["col"])
     for b in ("fw0", "fw1"):
-        act(at(b, 1), T.idr[:], ["idr"], [(b, 1, 2)])
+        act(at(b, 0), T.idr[:], ["idr"], [(b, 0, 1)])
     for b in ("n1", "n2", "e1", "e2"):
         V(SMALL, lambda q, b=b: q.memset(T[b][:, 0:16], 0.0), [], [(b, 0, 1)])
         V(SMALL, lambda q, b=b: q.memset(T[b][:, C + 16:PAD], 0.0), [], [(b, 2, 3)])
@@ -325,11 +333,11 @@ def build(P, g, core, T, topo):
     for i, (src, k) in enumerate([(0, 0), (0, 1), (0, 2), (0, 3), (1, 2), (1, 3), (4, 0), (4, 1), (4, 2)]):
         ts(T.bits[:, i:i + 1], cn(src), k, 1, A.arith_shift_right, A.bitwise_and, ["c%d" % src], [("bits", i, i + 1)])
     cp(cf("sc", 0, 9), T.bits[:, 0:9], ["bits"], ["sc"])
-    ts(cf("ko"), cf("od"), KEY, None, A.mult, None, ["od"], ["ko"])
-    V(SMALL, lambda q: q.memset(cf("kb", 0, 4), 0.0), [], [("kb", 0, 1)])
-    ts(cf("kb", 4, 2), cf("sc", 4, 2), KEY, None, A.mult, None, ["sc"], [("kb", 1, 2)])
-    ts(cf("kb", 6, 3), cf("sc", 6, 3), cf("ko"), None, A.mult, None, ["sc", "ko"], [("kb", 2, 3)])
-    ts(cf("nb", 0, 9), cf("sc", 0, 9), BIG, -BIG, A.mult, A.add, ["sc"], ["nb"])
+    act(cf("ko"), cf("od"), ["od"], ["ko"], SMALL, scale=KEY)
+    act(cf("kb", 0, 4), cf("sc", 0, 4), ["sc"], [("kb", 0, 1)], SMALL, scale=0.0)
+    act(cf("kb", 4, 2), cf("sc", 4, 2), ["sc"], [("kb", 1, 2)], SMALL, scale=KEY)
+    act(cf("kb", 6, 3), cf("sc", 6, 3), ["sc", "ko"], [("kb", 2, 3)], SMALL, scale=cf("ko"))
+    act(cf("nb", 0, 9), cf("sc", 0, 9), ["sc"], ["nb"], SMALL, scale=BIG, bias=-BIG)
     tt(cf("bi", 0, 9), cf("kb", 0, 9), cf("nb", 0, 9), A.add, ["kb", "nb"], ["bi"])
     V(SMALL, lambda q: q.tensor_reduce(cf("k2"), cf("kb", 6, 3), AxisListType.X, A.add, negate=True), ["kb"], ["k2"])
     tt(cf("a2"), cf("od"), cf("e15"), A.subtract, ["od", "e15"], ["a2"])
@@ -337,17 +345,13 @@ def build(P, g, core, T, topo):
     act(T.ia[:], T.idr[:], ["idr", "a2"], ["ia"], scale=cf("a2"))
     act(T.ic[:], T.idr[:], ["idr", "b2"], ["ic"], scale=cf("b2"))
     ts(cf("z0"), row, 0.0, None, A.not_equal, None, ["pa"], ["z0"])
-    ts(cf("z1"), cf("z0"), BIG, -BIG, A.mult, A.add, ["z0"], ["z1"])
+    act(cf("z1"), cf("z0"), ["z0"], ["z1"], SMALL, scale=BIG, bias=-BIG)
     ts(cn(8, 2), L("cw", 2), 19.0, None, A.min, None, ["cw"], ["c8"])
     ts(cn(10, 2), T.pi[:, 0:2], 4, 1, A.arith_shift_right, A.bitwise_and, ["pi"], ["c10"])
     tt(cn(12, 2), cn(8, 2), cn(10, 2), A.add, ["c8", "c10"], ["c12"])
     ts(cn(14, 2), cn(12, 2), 1, None, A.bitwise_and, None, ["c12"], ["c14"])
-    tt(cn(16, 2), cn(8, 2), cn(14, 2), A.add, ["c8", "c14"], ["c16"])
-    ts(cn(18, 2), cn(16, 2), 1, None, A.arith_shift_right, None, ["c16"], ["c18"])
-    ts(cn(20, 2), cn(14, 2), 10.0, None, A.mult, None, ["c14"], ["c20"])
-    tt(cn(22, 2), cn(18, 2), cn(20, 2), A.add, ["c18", "c20"], ["c22"])
-    ts(cn(24, 2), cn(22, 2), 2.0, None, A.mult, None, ["c22"], ["c24"])
-    tt(cn(26, 2), cn(24, 2), cn(10, 2), A.add, ["c24", "c10"], ["c26"])
+    ts(cn(20, 2), cn(14, 2), 21.0, None, A.mult, None, ["c14"], ["c20"])
+    tt(cn(26, 2), cn(8, 2), cn(20, 2), A.add, ["c8", "c20"], ["c26"])
     for i, (a, b) in enumerate([(16.0, 0.0), (16.0, 15.0), (8.0, 7.0)]):
         ts(T.pick[:, 2 * i:2 * i + 2], cn(26, 2), a, b, A.mult, A.add, ["c26"], [("pick", i, i + 1)])
 
@@ -356,7 +360,7 @@ def build(P, g, core, T, topo):
 
     V(0.16, lambda q: q.quantize_mx(T.uq[:], T.up[:], T.ut[:]), ["ut"], ["uq", "up"])
     cp(T.uqr[:].bitcast(dt.uint32), T.uq[:].bitcast(dt.uint32).indirect(T.uo[:]), ["uq", "uo"], ["uqr"], 0.3)
-    cp(T.upr[:], T.up[:].indirect(T.uo[:]), ["up", "uo"], ["upr"], 0.3)
+    act(T.upr[:], T.up[:].indirect(T.uo[:]), ["up", "uo"], ["upr"], 0.3)
     V(0.16, lambda q: q.quantize_mx(T.vq[:], T.vp[:], T.vt[:]), ["vt"], ["vq", "vp"])
 
     cp(T.l0[:], T.nxi[:], ["nxi"], ["l0"])
@@ -366,21 +370,22 @@ def build(P, g, core, T, topo):
     cp(T.lo16[:], L("be"), ["be"], ["lo16"])
     cp(T.hi16[:], L("bf"), ["bf"], ["hi16"])
     tt(L("dm"), L("bd"), L("cw"), A.subtract, ["bd", "cw"], ["dm"])
-    ts(cf("f0"), cf("col"), -160.0, None, A.add, None, ["col"], ["f0"])
-    ts(L("sx"), L("dm"), cf("f0"), None, A.mult, None, ["dm", "f0"], ["sx"])
+    act(cf("f0"), cf("col"), ["col"], ["f0"], SMALL, bias=-160.0)
+    act(L("sx"), L("dm"), ["dm", "f0"], ["sx"], SMALL, scale=cf("f0"))
     tt(L("dc"), L("sx"), L("cw"), A.add, ["sx", "cw"], ["dc"])
 
-    def weighted(dst, src):
-        V(HALF, lambda q: q.tensor_tensor_scan(T[dst][:], T.wt[:], at(src), 0.0, A.add, A.max), ["wt", (src, 0, 1)], [dst])
+    def weighted(dst, src, a=0):
+        V(HALF, lambda q: q.tensor_tensor_scan(T[dst][:], T.wt[:], at(src, a), 0.0, A.add, A.max), ["wt", (src, a, a + 1)], [dst])
 
-    def listed(l, src, tmp="scn"):
-        weighted(tmp, src)
+    def listed(l, src, tmp="scn", a=0):
+        weighted(tmp, src, a)
         ts(T[l][:], every16(tmp), cf("col"), None, A.add, None, [tmp, "col"], [l])
 
     def powers(src):
         for k in range(6):
             dst = "f%d" % (k + 1) if k in (2, 3) else "fb" if k % 2 else "fa"
-            act(at(dst), by(src, "l%d" % k), [(src, 0, 1), "l%d" % k], [dst], GATHER)
+            a = 0 if k else 1
+            act(at(dst), by(src, "l%d" % k, a), [(src, a, a + 1), "l%d" % k], [dst], GATHER)
             listed("l%d" % (k + 1), dst)
             src = dst
 
@@ -389,14 +394,20 @@ def build(P, g, core, T, topo):
             w, dst = "m%sw" % name, "m%s%d" % (name, i % 2)
             if dst == src:
                 dst = "m%s%d" % (name, (i + 1) % 2)
+            own = name + str(k) in OPT["own"]
             if k >= first[0]:
                 c = first[1] + k - first[0]
-                act(at(w), at(src), [src, "sc", "bi"], [w], scale=cf("sc", c), bias=cf("bi", c))
+                if own:
+                    ts(at(w), at(src), cf("sc", c), cf("bi", c), A.mult, A.add, [src, "sc", "bi"], [w], ROW)
+                else:
+                    act(at(w), at(src), [src, "sc", "bi"], [w], scale=cf("sc", c), bias=cf("bi", c))
             elif i == 0:
                 w = "sb"
+            elif own:
+                cp(at(w), at(src), [src], [w], ROW)
             else:
                 act(at(w), at(src), [src], [w])
-            tt(at(dst), by(w, "l%d" % k), at(src), A.max, [w, src, "l%d" % k], [dst], GATHER)
+            tt(at(dst), by(w, "l%d" % k), at(src), A.max, [w, SA if src == "sa" else src, "l%d" % k], [dst], GATHER)
             src = dst
         return src
 
@@ -407,13 +418,13 @@ def build(P, g, core, T, topo):
     def mid(b):
         return T[b][:, 16:C + 16]
 
-    cp(mid("n1"), T.idr[:], ["idr"], [("n1", 1, 2)], HALF)
-    turn("tn1", "n1")
-    cp(T.tid[:], T.tn1[:, 15:TW:16], ["tn1"], ["tid"])
+    K(0.2, lambda q: q.iota(T.ti[:], [[0, 2], [16, 21]], -160, 0, allow_small_or_imprecise_dtypes=True), [], ["ti"])
+    act(T.tid[:], T.ti[:], ["ti", "cw"], ["tid"], SMALL, bias=L("cw", 1))
+    act(cf("ev"), cf("od"), ["od"], ["ev"], SMALL, scale=-1.0, bias=1.0)
     act(T.gs[:], T.idr[:], ["idr"], ["gs"])
 
     def places(r):
-        act(T.f34[:], by("f3", "l4"), ["f3", "l4"], ["f34"], GATHER)
+        act(T.f34[:], by("f4", "l3"), ["f4", "l3"], ["f34"], GATHER)
         for i, (src, a) in enumerate([("f3", 1), ("f4", 0), ("f34", 3)]):
             move("g%d%d" % (i, r), T.gs[a:128:4, :], T[src][a:128:4, :], [src], [("gs", a, a + 1)])
         e = steps("e", "gs", [5, 6], (5, 4))
@@ -441,7 +452,7 @@ def build(P, g, core, T, topo):
     def bank(out, b):
         return T[out][:, BANK * b:BANK * b + C]
 
-    act(at("fw0"), by("idr", "l0"), ["idr", "l0"], [("fw0", 0, 1)], GATHER)
+    act(at("fw0", 1), by("idr", "l0"), ["idr", "l0"], [("fw0", 1, 2)], GATHER)
     for r in range(ROUNDS):
         X, xq, xp, aq, ap = "x%d" % r, "xq%d" % r, "xp%d" % r, "aq%d" % r, "ap%d" % r
         lp, lb, rp, rb = "lp%d" % r, "lb%d" % r, "rp%d" % r, "rb%d" % r
@@ -452,13 +463,19 @@ def build(P, g, core, T, topo):
         send(r, [(T[aq][:].bitcast(dt.uint8), T[xq][:].bitcast(dt.uint8), xq), (T[ap][:], T[xp][:], xp)], "ax%d" % r, [aq, ap], 6.0)
         mm("pw", 0, "uqr", "upr", 0, xq, xp, 0)
         mm("pw", 1, "uqr", "upr", 0, xq, xp, 0)
-        cp(T.sa[:], bank("pw", 0), [("pw", 0, 1)], ["sa"], ROW)
+        cp(at("sa"), bank("pw", 0), [("pw", 0, 1)], [SA], ROW)
         act(T.sb[:], bank("pw", 1), [("pw", 1, 2)], ["sb"])
         act(T.s2[:], bank("pw", 1), [("pw", 1, 2), "z0", "z1"], ["s2"], scale=cf("z0"), bias=cf("z1"))
         coarse = steps("c", "sa", range(7), (3, 0))
-        move("o%d" % r, T.sb[1:128:2, :], T.ia[1:128:2, :], ["ia"], ["sb"])
-        tt(at("mf1"), by("sb", "l0"), T.ic[:], A.add, ["sb", "ic", "l0"], ["mf1"], GATHER)
-        fine = steps("f", "mf1", range(3), (0, 6))
+        tt(T.dt[:], by("ia", "l0"), T.ic[:], A.add, ["ia", "ic", "l0"], ["dt"], GATHER)
+        act(at("sa", 1), by("sa", "l0"), [SA, "l0"], [("sa", 1, 2)], GATHER)
+        if OPT["fsv"]:
+            act(T.s0[:], bank("pw", 1), [("pw", 1, 2), "ev"], ["s0"], scale=cf("ev"))
+            tt(T.fs[:], by("s0", "l0"), T.dt[:], A.add, ["s0", "dt", "l0"], ["fs"], GATHER)
+        else:
+            move("o%d" % r, T.fs[1:128:2, :], T.dt[1:128:2, :], ["dt"], [("fs", 1, 2)])
+            move("n%d" % r, T.fs[0:128:2, :], T.sa[0:128:2, C:2 * C], [("sa", 1, 2)], [("fs", 0, 1)])
+        fine = steps("f", "fs", range(3), (0, 6))
         for b in range(4):
             mm("pu", b, "eq", "ep", 128 * b, xq, xp, b)
             act(at("fo", b), bank("pu", b), [("pu", b, b + 1)], [("fo", b, b + 1)])
@@ -469,33 +486,33 @@ def build(P, g, core, T, topo):
         turn("tn1", "n1")
         V(2.1 * HALF, lambda q: q.tensor_tensor_scan(T.r1[:], T.tn1[:], T.te1[:], 0.0, A.mult, A.add), ["tn1", "te1"], ["r1"])
         ts(T.lq[:], picked("r1", 1), 160.0, None, A.add, None, ["r1", "pick"], ["lq"], 0.1)
-        tt(mid("n2"), by(fine, "lq"), T.sa[:], A.is_le, [fine, "lq", "sa"], [("n2", 1, 2)], GATHER)
+        tt(mid("n2"), by(fine, "lq"), at("sa"), A.is_le, [fine, "lq", SA], [("n2", 1, 2)], GATHER)
         act(mid("e2"), by(fine, "lq"), [fine, "lq", "od", "k2"], [("e2", 1, 2)], GATHER, scale=cf("od"), bias=cf("k2"))
         turn("tn2", "n2")
         tt(L("hl", 32), picked("tn2", 0), L("c320", 32), A.mult, ["tn2", "pick", "c320"], ["hl"], 0.1)
         V(SMALL, lambda q: q.memset(T.tn2[:, 0:TW:16], 0.0), [], ["tn2"])
-        ts(L("hm", 32), L("hl", 32), -160.0, None, A.add, None, ["hl"], ["hm"])
+        ts(L("hm", 32), L("hl", 32), 160.0, None, A.add, None, ["hl"], ["hm"])
         turn("te2", "e2")
         V(1.05 * HALF, lambda q: q.tensor_tensor_scan(T.r2[:], T.tn2[:, 0:TW:2], T.te2[:, 1:TW:2], 0.0, A.mult, A.add), ["tn2", "te2"], ["r2"])
-        tt(L("om", 32), picked("r2", 2), L("hm", 32), A.max, ["r2", "pick", "hm"], ["om"], 0.1)
-        ts(T.ob[:], L("om", 32), 160.0, None, A.add, None, ["om"], ["ob"])
+        tt(L("om", 32), picked("r2", 2), L("hm", 32), A.min, ["r2", "pick", "hm"], ["om"], 0.1)
+        ts(T.ob[:], L("om", 32), 480.0, None, A.add, None, ["om"], ["ob"])
         ts(T[lp][:], picked("r2", 2), 160.0, None, A.add, None, ["r2", "pick"], [lp], 0.1)
         send(r, [(T[rp][:], T[lp][:, 0:20], lp)], "arp%d" % r, [rp], 2.6)
-        act(T.br[:], T[fw][:].indirect(T.ob[:, 0:20]), [fw, "ob"], ["br"], GATHER)
+        (cp if OPT["brv"] else act)(T.br[:], T[fw][:].indirect(T.ob[:, 0:20]), [fw, "ob"], ["br"], GATHER)
         listed(lb, "br", "bsn")
         send(r, [(T[rb][:], T[lb][:], lb)], "arb%d" % r, [rb], 2.6)
-        act(T.er[:], by("sa", lb), ["sa", lb], ["er"], GATHER)
-        act(T.eh[:], by("er", "hi16"), ["er", "hi16"], ["eh"], GATHER)
+        (cp if OPT["erv"] else act)(T.er[:], T.sa[:].indirect(T.ob[:, 0:20]), ["sa", "ob"], ["er"], GATHER)
+        (cp if OPT["ehv"] else act)(T.eh[:], by("er", "hi16"), ["er", "hi16"], ["eh"], GATHER)
         tt(T.sw[:], by("er", "lo16"), T.eh[:], A.is_gt, ["er", "eh", "lo16"], ["sw"], GATHER)
         weighted("swn", "sw")
         tt(L("sx"), every16("swn"), L("dm"), A.mult, ["swn", "dm"], ["sx"])
         tt(L("sy"), L("sx"), L("dc"), A.add, ["sx", "dc"], ["sy"])
         cp(T.so[:], L("sy"), ["sy"], ["so"])
         if r < ROUNDS - 1:
-            act(at(fn), by(fw, "so"), [(fw, 0, 1), "so"], [(fn, 0, 1)], GATHER)
-            listed("l0", fn)
+            (cp if OPT["f0v"] else act)(at(fn, 1), by(fw, "so", 1), [(fw, 1, 2), "so"], [(fn, 1, 2)], GATHER)
+            listed("l0", fn, "scn", 1)
         else:
-            act(T.er[:], by(fw, "so"), [(fw, 0, 1), "so"], ["er"], GATHER, bias=160.0)
+            act(T.er[:], by(fw, "so", 1), [(fw, 1, 2), "so"], ["er"], GATHER, bias=160.0)
             task(P, "y", 0.07, lambda q: q.dma_start(T.nf[:], T.er[0:128:16, :]), ["er"], [], "dma", "st", 16)
         for b in range(4):
             act(at("gp", b), by("fh", rp, b), [("fh", b, b + 1), rp], [("gp", b, b + 1)], GATHER)

@@ -8,8 +8,12 @@ BANK = 512
 ROUNDS = 3
 BIG = 1e29
 KEY = 1024.0
-PAD = C + 32
-TW = C + PAD
+NH = 1
+W = C // NH
+NB = W // 16
+KP = (NB + 15) // 16
+PW = W + 32
+TW = W + PW
 
 
 def sb(n, d):
@@ -27,20 +31,20 @@ SCRATCH = {
     "one": sb(528, "bfloat16"), "big": sb(528, "bfloat16"),
     "ji": sb(16, "int32"), "dg": sb(16, "int32"), "t1": sb(16, "bfloat16"), "t2": sb(16, "bfloat16"), "w16": sb(16, "bfloat16"),
     "wt": sb(C, "bfloat16"), "idr": sb(C, "bfloat16"),
-    "ia": sb(C, "float32"), "ic": sb(C, "bfloat16"), "tid": sb(TW // 16, "bfloat16"), "ti": sb(TW // 16, "float32"), "s0": sb(C, "float32"),
-    "gs": sb(C, "bfloat16"), "f3": sb(C, "bfloat16"), "f4": sb(C, "bfloat16"), "f34": sb(C, "bfloat16"),
+    "ia": sb(C, "bfloat16"), "ic": sb(C, "bfloat16"), "s0": sb(C, "float32"),
+    "gs": sb(C, "bfloat16"), "ft": sb(5 * C, "bfloat16"),
     "pi": sb(32, "int32"), "pa": sb(32, "int32"), "ci": sb(32, "int32"), "cn": sb(32, "int32"), "bits": sb(12, "int32"),
     "uo": sb(8, "uint16"), "pick": sb(6, "uint16"),
-    "cf": sb(64, "float32"),
-    "lo16": sb(20, "uint16"), "hi16": sb(20, "uint16"), "so": sb(20, "uint16"), "lq": sb(32, "uint16"), "ob": sb(32, "uint16"),
-    "sa": sb(2 * C, "float32"), "fs": sb(C, "float32"), "sb": sb(C, "float32"), "s2": sb(C, "float32"), "dt": sb(C, "float32"),
-    "n1": sb(PAD, "bfloat16"), "n2": sb(PAD, "bfloat16"), "e1": sb(PAD, "float16"), "e2": sb(PAD, "float16"),
-    "tn1": sb(TW, "bfloat16"), "tn2": sb(TW, "bfloat16"), "te1": sb(TW, "float16"), "te2": sb(TW, "float16"),
-    "r1": sb(TW, "bfloat16"), "r2": sb(TW // 2, "bfloat16"),
-    "fw0": sb(2 * C, "bfloat16"), "fw1": sb(2 * C, "bfloat16"), "fa": sb(C, "bfloat16"), "fb": sb(C, "bfloat16"),
+    "cf": sb(72, "float32"),
+    "fm": sb(C, "bfloat16"), "fmn": sb(C, "float16"), "mt16": sb(20, "uint16"), "lo16": sb(20, "uint16"), "hi16": sb(20, "uint16"), "so": sb(20, "uint16"), "lq": sb(32, "uint16"),
+    "sa": sb(2 * C, "float32"), "fs": sb(C, "float32"), "sb": sb(C, "float32"), "dt": sb(C, "float32"),
+    "n1": sb(NH * PW, "bfloat16"), "n2": sb(NH * PW, "bfloat16"), "e1": sb(C + 32, "float16"), "e2": sb(NH * PW, "float16"),
+    "tn1": sb(NH * TW, "bfloat16"), "tn2": sb(NH * TW, "bfloat16"), "te1": sb(NH * TW, "float16"), "te2": sb(NH * TW, "float16"),
+    "r1": sb(NH * TW, "bfloat16"), "r2": sb(NH * TW // 2, "bfloat16"),
+    "fw0": sb(2 * C, "bfloat16"), "fw1": sb(2 * C, "bfloat16"), "fa": sb(2 * C, "bfloat16"),
     "br": sb(C, "bfloat16"), "bsn": sb(C, "float16"), "scn": sb(C, "float16"), "swn": sb(C, "float16"),
     "er": sb(C, "float32"), "eh": sb(C, "float32"), "sw": sb(C, "bfloat16"),
-    "fo": sb(4 * C, "bfloat16"), "fh": sb(4 * C, "bfloat16"), "gp": sb(4 * C, "bfloat16"),
+    "fo": sb(4 * C, "bfloat16"), "fh": sb(8 * C, "bfloat16"), "gp": sb(4 * C, "bfloat16"),
     "z": sb(4 * C, "bfloat16"), "zq": sb(C, "float8_e4m3fn_x4"), "zp": sb(C, "uint8"),
     "h": sb(4 * C, "bfloat16"),
     "pu": ("psum", [128, 2048], "float32"), "pw": ("psum", [128, 2048], "float32"),
@@ -48,10 +52,10 @@ SCRATCH = {
 for _n in ("c", "f", "e"):
     for _k in ("0", "1", "w"):
         SCRATCH["m" + _n + _k] = sb(C, "float32")
-LISTS = ["cw", "c320", "bd", "be", "bf", "dm", "dc", "hl", "hm", "om", "sx", "sy"]
+LISTS = ["cw", "c320", "bd", "be", "bf", "dm", "dc", "hl", "hm", "om", "sx", "fl"]
 SCRATCH["sml"] = sb(32 * len(LISTS), "float32")
 COLS = {"sc": 0, "kb": 12, "nb": 24, "bi": 36, "col": 48, "e15": 49, "a1": 50, "a2": 51, "b1": 52, "b2": 53, "od": 54, "ev": 55,
-        "k1": 56, "k2": 57, "z0": 58, "z1": 59, "f0": 60, "ko": 61}
+        "k1": 56, "k2": 57, "z0": 58, "z1": 59, "f0": 60, "ko": 61, "pw": 64, "j0": 68, "j1": 69, "j2": 70, "nc": 71}
 for _k in range(7):
     SCRATCH["l%d" % _k] = sb(20, "uint16")
 for _r in range(ROUNDS + 1):
@@ -62,23 +66,26 @@ for _r in range(ROUNDS + 1):
 for _r in range(ROUNDS):
     SCRATCH["aq%d" % _r] = sb(C, "float8_e4m3fn_x4")
     SCRATCH["ap%d" % _r] = sb(C, "uint8")
-    SCRATCH["lp%d" % _r] = sb(32, "uint16")
-    for _n in ("lb", "rp", "rb"):
+    SCRATCH["lp%d" % _r] = sb(52, "uint16")
+    SCRATCH["rp%d" % _r] = sb(40, "uint16")
+    for _n in ("lb", "lf", "rb"):
         SCRATCH["%s%d" % (_n, _r)] = sb(20, "uint16")
 SEMAPHORES = ["ev", "es", "et", "eg", "snd", "st"]
 SEMAPHORES += ["%s%d" % (_n, _r) for _n in ("ax", "arp", "arb") for _r in range(ROUNDS)]
 SEMAPHORES += ["ld_" + _n for _n in ("x", "u", "v", "nx", "mt", "wc", "ws")]
-SEMAPHORES += ["ld_%s%d" % (_n, _r) for _n in ("g0", "g1", "g2", "o", "n") for _r in range(ROUNDS)]
+SEMAPHORES += ["ld_%s%d" % (_n, _r) for _n in ("g0", "g1", "g2", "g3", "g4", "g5", "g6", "a") for _r in range(ROUNDS)]
 
 GATHER, HALF, ROW, SMALL = 0.58, 0.17, 0.34, 0.08
-HOP, SAME = 0.2, 0.1
+GP = 0.06 + (GATHER - 0.06) / NH
+HOP, SAME = 0.22, 0.1
+COSTS = [(1.0, 1.0, 1.0, 0.2, 0.1), (0.9, 0.9, 0.8, 0.3, 0.15), (1.25, 1.0, 1.3, 0.2, 0.07), (0.8, 0.95, 1.1, 0.3, 0.06)]
 SHARED = {}
-OPT = {"own": [], "brv": True, "erv": False, "ehv": False, "f0v": True, "fsv": True}
+OPT = {"own": [], "brv": False, "erv": True, "ehv": True, "f0v": True, "halves": ["x"], "xps": [3], "sbd": False, "pv": [0], "ls": True, "net": 0.85, "hms": False, "cut": 192, "late": 4, "seed": 2, "sbv": True, "upv": False, "r0v": False, "hv": [], "f5": 1, "early": True, "gpv": [], "pace": {"h0": 2, "h1": 2, "h2": 2, "h3": 3, "sb0": 4}}
 SA = ("sa", 0, 1)
 
 
 def new_plan():
-    return {"tasks": [], "w": {}, "r": {}}
+    return {"tasks": [], "w": {}, "r": {}, "rounds": []}
 
 
 def overlap(a, b):
@@ -89,6 +96,8 @@ def task(P, eng, dur, fn, reads, writes, kind="op", sem=None, inc=1, after=(), b
     def reg(x):
         return (x, 0, 1 << 20) if isinstance(x, str) else x
     n = len(P["tasks"])
+    if eng == "net":
+        dur *= OPT["net"]
     deps = {}
     for a in after:
         deps[a] = True
@@ -116,11 +125,12 @@ def task(P, eng, dur, fn, reads, writes, kind="op", sem=None, inc=1, after=(), b
     deps.pop(n, None)
     for a in behind:
         deps.setdefault(a, False)
-    P["tasks"].append({"eng": eng, "dur": dur, "fn": fn, "deps": deps, "kind": kind, "sem": sem, "inc": inc})
+    P["tasks"].append({"eng": eng, "dur": dur, "fn": fn, "deps": deps, "kind": kind, "sem": sem, "inc": inc,
+                       "gather": eng in "vs" and min(abs(dur - 0.06 - (GATHER - 0.06) * w / C) for w in (128, 160, 192, C)) < 1e-6})
     return n
 
 
-def schedule(P, tries=25000):
+def schedule(P, tries=4000, moves=30000):
     ts = P["tasks"]
     n = len(ts)
     lags = [[(d, HOP if ts[d]["eng"] != t["eng"] else SAME) for d in t["deps"]] for t in ts]
@@ -166,7 +176,7 @@ def schedule(P, tries=25000):
         return cost, {e: [x[2] for x in line] for e, line in slots.items()}, start, max(end)
     sends = [i for i in range(n) if ts[i]["kind"] == "send"]
     best = now = place(up)
-    rng = np.random.default_rng(7)
+    rng = np.random.default_rng(OPT["seed"])
     for k in range(tries):
         rank = -np.array(now[2])
         at, width = -rng.random() * now[3], [1.5, 3.0, 6.0][rng.integers(3)]
@@ -177,7 +187,77 @@ def schedule(P, tries=25000):
             now = got
             if got[0] < best[0]:
                 best = got
-    return best[1], best[2], best[3]
+    order = refine(P, best[1], succ, moves, 0.04)[0]
+    return refine(P, order, succ, 2 * moves, 0.025)
+
+
+def refine(P, order, succ, moves, heat):
+    ts = P["tasks"]
+    n = len(ts)
+    durs = [[t["dur"] * (c if t["eng"] == "net" else a if t["gather"] else b) for t in ts] for a, b, c, _, _ in COSTS]
+    lags = [[[(d, hop if ts[d]["eng"] != t["eng"] else same) for d in t["deps"]] for t in ts] for _, _, _, hop, same in COSTS]
+    count = [len(t["deps"]) for t in ts]
+
+    def run(k):
+        left, nxt, prv = count[:], [-1] * n, [-1] * n
+        for line in order.values():
+            for a, b in zip(line, line[1:]):
+                nxt[a], prv[b] = b, a
+                left[b] += 1
+        todo = [i for i in range(n) if not left[i]]
+        for i in todo:
+            for s in succ[i] + [nxt[i]] * (nxt[i] >= 0):
+                left[s] -= 1
+                if not left[s]:
+                    todo.append(s)
+        if len(todo) < n:
+            return None
+        ends, arcs = [], []
+        for dur, lag in zip(durs, lags):
+            end = [0.0] * (n + 1)
+            for i in todo:
+                at = end[prv[i]]
+                for d, l in lag[i]:
+                    if end[d] + l > at:
+                        at = end[d] + l
+                end[i] = at + dur[i]
+            ends.append(end)
+        end, dur, lag = ends[k], durs[k], lags[k]
+        i = end.index(max(end))
+        while i >= 0:
+            at = end[i] - dur[i] - 1e-9
+            if prv[i] >= 0 and end[prv[i]] >= at:
+                arcs.append((prv[i], i))
+                i = prv[i]
+            else:
+                i = ([d for d, l in lag[i] if end[d] + l >= at] + [-1])[0]
+        return sum(max(e) for e in ends) / len(ends), arcs, [ends[0][i] - durs[0][i] for i in range(n)], max(ends[0])
+    rng = np.random.default_rng(8)
+    now = run(0)
+    best = (now, dict(order))
+    for it in range(moves):
+        r = rng.random(4)
+        if r[0] < 0.7:
+            a, b = now[1][int(r[1] * len(now[1]))]
+            e = ts[a]["eng"]
+            k, d = order[e].index(a), int(r[2] ** 2 * 5) if r[0] < 0.55 else int(r[2] * 60)
+            src, to = (k, k + 1 + d) if r[3] < 0.5 else (k + 1, k - d)
+        else:
+            e = "vs"[int(r[1] * 2)]
+            src, w = int(r[2] * len(order[e])), 4 if r[3] < 0.6 else 15 if r[3] < 0.85 else 60
+            to = src + int(rng.integers(-w, w + 1))
+        old = order[e]
+        line = old[:]
+        line.insert(max(to, 0), line.pop(src))
+        order[e] = line
+        got = run(it % len(COSTS))
+        if got is not None and got[0] - now[0] <= -(0.002 + heat * (1 - it / moves)) * math.log(1 - rng.random()):
+            now = got
+            if got[0] < best[0][0]:
+                best = (got, dict(order))
+        else:
+            order[e] = old
+    return best[1], best[0][2], best[0][0]
 
 
 def issue(P, order, start, g, T):
@@ -234,9 +314,9 @@ def build(P, g, core, T, topo):
     rank = T.rank_of(core)
     n = len(T.cores)
 
-    def L(name, w=20):
+    def L(name, w=20, a=0):
         i = LISTS.index(name)
-        return T.sml[:, 32 * i:32 * i + w]
+        return T.sml[:, 32 * i + a:32 * i + a + w]
 
     def cf(name, i=0, w=1):
         return T.cf[:, COLS[name] + i:COLS[name] + i + w]
@@ -284,8 +364,11 @@ def build(P, g, core, T, topo):
         k = task(P, q, 0.07, fn, [], [], "dma", "ld_" + name, 16, after=after)
         return task(P, "net", latency, None, [], writes, "land", "ld_" + name, 16, after=[k])
 
-    def move(name, out, in_, reads, writes):
-        k = task(P, "y", 0.07, lambda q: q.dma_start(out, in_), reads, writes, "dma", "ld_" + name, 16)
+    def move(name, out, in_, reads, writes, add=False):
+        if add:
+            k = task(P, "g", 1.0, lambda q: q.dma_start(out, in_, accum_op=A.add), reads, writes, "dma", "ld_" + name, 16)
+        else:
+            k = task(P, "y", 0.07, lambda q: q.dma_start(out, in_), reads, writes, "dma", "ld_" + name, 16)
         task(P, "net", 2.2, None, reads, writes, "land", "ld_" + name, 16, after=[k])
 
     k = load("s", "nx", lambda q: q.dma_start(T.nxi[:], T.nx[:]), ["nxi"], 2.0)
@@ -300,7 +383,7 @@ def build(P, g, core, T, topo):
     k = K(0.16, lambda q: q.iota(T.ji[:], [[1, 16]], 0, -1), [], ["ji"], [k])
     k = K(0.19, lambda q: q.iota(T.ci[:], [[16, 32]], 0, 0), [], ["ci"], [k])
     K(0.67, lambda q: q.iota(T.idr[:], [[1, C]], -160, 0, allow_small_or_imprecise_dtypes=True), [], ["idr"], [k])
-    V(0.3, lambda q: q.memset(T.one[:], 1.0), [], ["one"])
+    K(1.1, lambda q: q.iota(T.one[:], [[0, 528]], 1, 0, allow_small_or_imprecise_dtypes=True), ["idr"], ["one"])
     K(1.1, lambda q: q.affine_select(T.big[:], T.one[:], [[-1, 528]], A.is_equal, 0.0, 3, 4), ["one"], ["big"])
     ts(T.pa[:], T.pi[:], 15, None, A.bitwise_and, None, ["pi"], ["pa"])
     ts(T.dg[:], T.ji[:], 15, None, A.bitwise_and, None, ["ji"], ["dg"])
@@ -318,49 +401,58 @@ def build(P, g, core, T, topo):
     for b in ("fw0", "fw1"):
         act(at(b, 0), T.idr[:], ["idr"], [(b, 0, 1)])
     for b in ("n1", "n2", "e1", "e2"):
-        V(SMALL, lambda q, b=b: q.memset(T[b][:, 0:16], 0.0), [], [(b, 0, 1)])
-        V(SMALL, lambda q, b=b: q.memset(T[b][:, C + 16:PAD], 0.0), [], [(b, 2, 3)])
+        for a in sorted({0, C + 16} if b == "e1" else {PW * h + k for h in range(NH) for k in (0, W + 16)}):
+            act(T[b][:, a:a + 16], T.w16[:], ["w16"], [(b, 8 + a / 1024, 8 + (a + 1) / 1024)], SMALL, scale=0.0)
     for b in range(4):
         V(0.16, lambda q, b=b: q.quantize_mx(T.eq[:, 128 * b:128 * b + 128], T.ep[:, 128 * b:128 * b + 128], T.big[:, 3 - b:515 - b]),
           ["big"], [("eq", b, b + 1), ("ep", b, b + 1)])
 
-    ts(cn(0), row, -1.0, 15.0, A.mult, A.add, ["pa"], ["c0"])
-    ts(cn(1), cn(0), -1.0, 0.0, A.add, A.max, ["c0"], ["c1"])
+    for k in range(4):
+        V(SMALL, lambda q, k=k: q.memset(cf("pw", k), 2.0 ** (4 - k)), [], [("pow", k, k + 1)])
+    ts(cf("j0"), row, -1.0, 15.0, A.mult, A.add, ["pa"], ["j0"])
+    ts(cf("j1"), cf("j0"), -1.0, 0.0, A.add, A.max, ["j0"], ["j1"])
     ts(cn(2), row, 1, None, A.bitwise_and, None, ["pa"], ["c2"])
-    ts(cn(3), cn(0), 1, None, A.arith_shift_right, None, ["c0"], ["c3"])
     cp(cf("od"), cn(2), ["c2"], ["od"])
-    ts(cn(4), cn(3), cf("od"), 0.0, A.subtract, A.max, ["c3", "od"], ["c4"])
-    for i, (src, k) in enumerate([(0, 0), (0, 1), (0, 2), (0, 3), (1, 2), (1, 3), (4, 0), (4, 1), (4, 2)]):
-        ts(T.bits[:, i:i + 1], cn(src), k, 1, A.arith_shift_right, A.bitwise_and, ["c%d" % src], [("bits", i, i + 1)])
+    ts(cf("j2"), cf("j1"), cf("od"), 0.0, A.subtract, A.max, ["j1", "od"], ["j2"])
+    ts(cn(16, 4), cf("pw", 0, 4), cf("j0"), None, A.mult, None, ["pow", "j0"], [("nk", 0, 1)])
+    ts(cn(20, 2), cf("pw", 2, 2), cf("j1"), None, A.mult, None, ["pow", "j1"], [("nk", 1, 2)])
+    ts(cn(22, 3), cf("pw", 0, 3), cf("j2"), 0.5, A.mult, A.mult, ["pow", "j2"], [("nk", 2, 3)])
+    ts(T.bits[:, 0:9], cn(16, 9), 4, 1, A.arith_shift_right, A.bitwise_and, ["nk"], ["bits"])
     cp(cf("sc", 0, 9), T.bits[:, 0:9], ["bits"], ["sc"])
     act(cf("ko"), cf("od"), ["od"], ["ko"], SMALL, scale=KEY)
-    act(cf("kb", 0, 4), cf("sc", 0, 4), ["sc"], [("kb", 0, 1)], SMALL, scale=0.0)
+    act(cf("kb", 0, 3), cf("sc", 0, 3), ["sc"], [("kb", 0, 1)], SMALL, scale=0.0)
+    ts(cf("kb", 3), row, 0.0, BIG, A.is_equal, A.mult, ["pa"], [("kb", 3, 4)])
     act(cf("kb", 4, 2), cf("sc", 4, 2), ["sc"], [("kb", 1, 2)], SMALL, scale=KEY)
     act(cf("kb", 6, 3), cf("sc", 6, 3), ["sc", "ko"], [("kb", 2, 3)], SMALL, scale=cf("ko"))
     act(cf("nb", 0, 9), cf("sc", 0, 9), ["sc"], ["nb"], SMALL, scale=BIG, bias=-BIG)
     tt(cf("bi", 0, 9), cf("kb", 0, 9), cf("nb", 0, 9), A.add, ["kb", "nb"], ["bi"])
     V(SMALL, lambda q: q.tensor_reduce(cf("k2"), cf("kb", 6, 3), AxisListType.X, A.add, negate=True), ["kb"], ["k2"])
+    V(SMALL, lambda q: q.tensor_reduce(cf("k1"), cf("kb", 4, 2), AxisListType.X, A.add, negate=True), ["kb"], ["k1"])
     tt(cf("a2"), cf("od"), cf("e15"), A.subtract, ["od", "e15"], ["a2"])
     tt(cf("b2"), cf("e15"), cf("a2"), A.subtract, ["e15", "a2"], ["b2"])
-    act(T.ia[:], T.idr[:], ["idr", "a2"], ["ia"], scale=cf("a2"))
-    act(T.ic[:], T.idr[:], ["idr", "b2"], ["ic"], scale=cf("b2"))
-    ts(cf("z0"), row, 0.0, None, A.not_equal, None, ["pa"], ["z0"])
-    act(cf("z1"), cf("z0"), ["z0"], ["z1"], SMALL, scale=BIG, bias=-BIG)
-    ts(cn(8, 2), L("cw", 2), 19.0, None, A.min, None, ["cw"], ["c8"])
+    if OPT["sbd"]:
+        act(T.s0[:], T.idr[:], ["idr", "a2"], ["s0"], scale=cf("a2"))
+    else:
+        ts(T.ia[:], T.idr[:], cf("a2"), None, A.mult, None, ["idr", "a2"], ["ia"], HALF)
+    ts(T.ic[:], T.idr[:], cf("b2"), None, A.mult, None, ["idr", "b2"], ["ic"], HALF)
+    ts(cn(8, 2), L("cw", 2), NB - 1.0, None, A.min, None, ["cw"], ["c8"])
     ts(cn(10, 2), T.pi[:, 0:2], 4, 1, A.arith_shift_right, A.bitwise_and, ["pi"], ["c10"])
     tt(cn(12, 2), cn(8, 2), cn(10, 2), A.add, ["c8", "c10"], ["c12"])
     ts(cn(14, 2), cn(12, 2), 1, None, A.bitwise_and, None, ["c12"], ["c14"])
-    ts(cn(20, 2), cn(14, 2), 21.0, None, A.mult, None, ["c14"], ["c20"])
-    tt(cn(26, 2), cn(8, 2), cn(20, 2), A.add, ["c8", "c20"], ["c26"])
+    ts(cn(6, 2), cn(14, 2), NB + 1.0, None, A.mult, None, ["c14"], ["c6"])
+    tt(cn(26, 2), cn(8, 2), cn(6, 2), A.add, ["c8", "c6"], ["c26"])
     for i, (a, b) in enumerate([(16.0, 0.0), (16.0, 15.0), (8.0, 7.0)]):
         ts(T.pick[:, 2 * i:2 * i + 2], cn(26, 2), a, b, A.mult, A.add, ["c26"], [("pick", i, i + 1)])
 
-    def picked(b, i):
-        return T[b][:].indirect(T.pick[:, 2 * i:2 * i + 2])
+    def turned(b, h, k=1):
+        return T[b][:, TW // k * h:TW // k * (h + 1)]
+
+    def picked(b, i, h, k=1):
+        return turned(b, h, k).indirect(T.pick[:, 2 * i:2 * i + KP])
 
     V(0.16, lambda q: q.quantize_mx(T.uq[:], T.up[:], T.ut[:]), ["ut"], ["uq", "up"])
     cp(T.uqr[:].bitcast(dt.uint32), T.uq[:].bitcast(dt.uint32).indirect(T.uo[:]), ["uq", "uo"], ["uqr"], 0.3)
-    act(T.upr[:], T.up[:].indirect(T.uo[:]), ["up", "uo"], ["upr"], 0.3)
+    (cp if OPT["upv"] else act)(T.upr[:], T.up[:].indirect(T.uo[:]), ["up", "uo"], ["upr"], 0.3)
     V(0.16, lambda q: q.quantize_mx(T.vq[:], T.vp[:], T.vt[:]), ["vt"], ["vq", "vp"])
 
     cp(T.l0[:], T.nxi[:], ["nxi"], ["l0"])
@@ -369,27 +461,29 @@ def build(P, g, core, T, topo):
     tt(L("bf"), L("bd"), L("cw"), A.max, ["bd", "cw"], ["bf"])
     cp(T.lo16[:], L("be"), ["be"], ["lo16"])
     cp(T.hi16[:], L("bf"), ["bf"], ["hi16"])
-    tt(L("dm"), L("bd"), L("cw"), A.subtract, ["bd", "cw"], ["dm"])
+    cp(T.mt16[:], T.mti[:], ["mti"], ["mt16"])
+    cp(L("fl"), T.nxi[:], ["nxi"], ["fl"])
     act(cf("f0"), cf("col"), ["col"], ["f0"], SMALL, bias=-160.0)
-    act(L("sx"), L("dm"), ["dm", "f0"], ["sx"], SMALL, scale=cf("f0"))
-    tt(L("dc"), L("sx"), L("cw"), A.add, ["sx", "cw"], ["dc"])
+    act(cf("nc"), cf("col"), ["col"], ["nc"], SMALL, scale=-1.0)
 
     def weighted(dst, src, a=0):
         V(HALF, lambda q: q.tensor_tensor_scan(T[dst][:], T.wt[:], at(src, a), 0.0, A.add, A.max), ["wt", (src, a, a + 1)], [dst])
 
     def listed(l, src, tmp="scn", a=0):
         weighted(tmp, src, a)
-        ts(T[l][:], every16(tmp), cf("col"), None, A.add, None, [tmp, "col"], [l])
+        if OPT["ls"] and tmp == "scn":
+            act(T[l][:], every16(tmp), [tmp, "col"], [l], 0.1, bias=cf("col"))
+        else:
+            ts(T[l][:], every16(tmp), cf("col"), None, A.add, None, [tmp, "col"], [l])
 
-    def powers(src):
-        for k in range(6):
-            dst = "f%d" % (k + 1) if k in (2, 3) else "fb" if k % 2 else "fa"
-            a = 0 if k else 1
-            act(at(dst), by(src, "l%d" % k, a), [(src, a, a + 1), "l%d" % k], [dst], GATHER)
-            listed("l%d" % (k + 1), dst)
-            src = dst
+    def powers(src, later):
+        a = 1
+        for k, (dst, b) in enumerate([("fa", 0), ("fa", 1), ("ft", 1), ("ft", 2)]):
+            (cp if k in OPT["pv"] and later else act)(at(dst, b), by(src, "l%d" % k, a), [(src, a, a + 1), "l%d" % k], [(dst, b, b + 1), "F%d" % (k + 1)], GATHER)
+            listed("l%d" % (k + 1), dst, "scn", b)
+            src, a = dst, b
 
-    def steps(name, src, levels, first):
+    def steps(name, src, levels, first, end=None):
         for i, k in enumerate(levels):
             w, dst = "m%sw" % name, "m%s%d" % (name, i % 2)
             if dst == src:
@@ -397,7 +491,10 @@ def build(P, g, core, T, topo):
             own = name + str(k) in OPT["own"]
             if k >= first[0]:
                 c = first[1] + k - first[0]
-                if own:
+                if k == 6:
+                    k = 5
+                    act(at(w), by(src, "l5"), [src, "sc", "bi", "l5"], [w], GATHER, scale=cf("sc", c), bias=cf("bi", c))
+                elif own:
                     ts(at(w), at(src), cf("sc", c), cf("bi", c), A.mult, A.add, [src, "sc", "bi"], [w], ROW)
                 else:
                     act(at(w), at(src), [src, "sc", "bi"], [w], scale=cf("sc", c), bias=cf("bi", c))
@@ -407,31 +504,46 @@ def build(P, g, core, T, topo):
                 cp(at(w), at(src), [src], [w], ROW)
             else:
                 act(at(w), at(src), [src], [w])
-            tt(at(dst), by(w, "l%d" % k), at(src), A.max, [w, SA if src == "sa" else src, "l%d" % k], [dst], GATHER)
+            out, reg = end if end and i == len(levels) - 1 else (at(dst), dst)
+            tt(out, by(w, "l%d" % k), at(src), A.max, [w, SA if src == "sa" else src, "l%d" % k], [reg], GATHER)
             src = dst
         return src
 
-    def turn(dst, src):
-        V(HALF, lambda q: q.transpose(T[dst][:, 0:C], T[src][:, 16:C + 16]), [src], [(dst, 0, 1)])
-        V(HALF * 1.1, lambda q: q.transpose(T[dst][:, C:TW], T[src][:]), [src], [(dst, 1, 2)])
+    def turn(dst, src, h, a):
+        reads = [(src, 2 * h, 2 * h + 2), (src, 8, 9)]
+        V(HALF * W / C, lambda q: q.transpose(T[dst][:, TW * h:TW * h + W], T[src][:, a + 16:a + 16 + W]), reads, [(dst, 2 * h, 2 * h + 1)])
+        V(HALF * PW / C, lambda q: q.transpose(T[dst][:, TW * h + W:TW * h + TW], T[src][:, a:a + PW]), reads, [(dst, 2 * h + 1, 2 * h + 2)])
 
-    def mid(b):
-        return T[b][:, 16:C + 16]
+    def chain(out, n, e, h, k):
+        for i, (a, b) in enumerate([(TW * h, TW * h + W), (TW * h + W, TW * h + TW)]):
+            V(max(SMALL, HALF * (b - a) / C / k), lambda q, a=a, b=b: q.tensor_tensor_scan(
+                T[out][:, a // k:b // k], T[n][:, a:b:k], T[e][:, a + k - 1:b:k], 0.0, A.mult, A.add),
+              [(n, 2 * h + i, 2 * h + i + 1), (e, 2 * h + i, 2 * h + i + 1)], [(out, 2 * h + i, 2 * h + i + 1)])
 
-    K(0.2, lambda q: q.iota(T.ti[:], [[0, 2], [16, 21]], -160, 0, allow_small_or_imprecise_dtypes=True), [], ["ti"])
-    act(T.tid[:], T.ti[:], ["ti", "cw"], ["tid"], SMALL, bias=L("cw", 1))
+    def mid(b, h):
+        return T[b][:, PW * h + 16:PW * h + 16 + W]
+
     act(cf("ev"), cf("od"), ["od"], ["ev"], SMALL, scale=-1.0, bias=1.0)
-    act(T.gs[:], T.idr[:], ["idr"], ["gs"])
+    act(cf("a1"), cf("e15"), ["e15"], ["a1"], SMALL, scale=-1.0, bias=1.0)
+    act(cf("b1"), cf("e15"), ["e15"], ["b1"], SMALL, scale=-2.0, bias=1.0)
+    act(T.gs[:], T.idr[:], ["idr", "b1"], ["gs"], scale=cf("b1"))
 
     def places(r):
-        act(T.f34[:], by("f4", "l3"), ["f4", "l3"], ["f34"], GATHER)
-        for i, (src, a) in enumerate([("f3", 1), ("f4", 0), ("f34", 3)]):
-            move("g%d%d" % (i, r), T.gs[a:128:4, :], T[src][a:128:4, :], [src], [("gs", a, a + 1)])
-        e = steps("e", "gs", [5, 6], (5, 4))
-        act(T.mew[:], at(e), [e], ["mew"])
-        tt(mid("e1"), by("mew", "l3"), at(e), A.subtract, ["mew", e, "l3"], [("e1", 1, 2)], GATHER)
-        turn("te1", "e1")
-        cp(T.te1[:, 15:TW:16], T.tid[:], ["tid"], ["te1"])
+        act(at("ft", 4), by("ft", "l4", 2), [("ft", 2, 3), "l4"] + [("sb", 0, OPT["f5"])] * (r > 0 and OPT["f5"] > 0), [("ft", 4, 5)], GATHER)
+        listed("l5", "ft", "scn", 4)
+        act(at("ft", 3), by("ft", "l3", 2), [("ft", 2, 3), "l3"], [("ft", 3, 4)], GATHER)
+        for i, (b, a, step) in enumerate([(1, 1, 4), (2, 0, 4), (3, 3, 8), (3, 7, 16)]):
+            move("g%d%d" % (i, r), T.gs[a:128:step, :], T.ft[a:128:step, C * b:C * b + C], [("ft", b, b + 1)], [("gs", a, a + 1)])
+        if OPT["early"]:
+            act(T.mew[:], T.gs[:], ["gs", "a1", "k1"], ["mew"], scale=cf("a1"), bias=cf("k1"))
+            tt(at("me1"), by("mew", "l3"), T.gs[:], A.subtract, ["mew", "gs", "l3"], ["me1"], GATHER)
+            steps("e", "me1", [5, 6], (5, 4), (T.e1[:, 16:C + 16], ("e1", 0, 4)))
+        else:
+            e = steps("e", "gs", [5, 6], (5, 4))
+            act(T.mew[:], at(e), [e, "a1"], ["mew"], scale=cf("a1"))
+            tt(T.e1[:, 16:C + 16], by("mew", "l3"), at(e), A.subtract, ["mew", e, "l3"], [("e1", 0, 4)], GATHER)
+        for h in range(NH):
+            turn("te1", "e1", h, W * h)
 
     sent = [0]
 
@@ -445,92 +557,160 @@ def build(P, g, core, T, topo):
             sent[0] += len(topo.engines(core, dst))
         return task(P, "net", latency, None, [], land, "land", sem, len(topo.engines(src, core)) * len(pairs), after=ids)
 
-    def mm(out, b, wq, wp, a, xq, xp, unit):
-        E(0.35, lambda q: q.matmul_mx(T[out][:, BANK * b:BANK * b + C], T[wq][:, a:a + 128], T[wp][:, a:a + 128], T[xq][:], T[xp][:], True, True),
-          [(wq, unit, unit + 1), (wp, unit, unit + 1), xq, xp], [(out, b, b + 1)])
+    def bank(out, b, w=C):
+        return T[out][:, BANK * b:BANK * b + w]
 
-    def bank(out, b):
-        return T[out][:, BANK * b:BANK * b + C]
+    def behind(name, b, r):
+        k = OPT["pace"].get(name + str(b))
+        return ["F%d" % k] if k and r < ROUNDS - 1 else []
+
+    def parts(name):
+        return [(0, OPT["cut"]), (OPT["cut"], C)] if name in OPT["halves"] else [(0, C)]
+
+    def mm(out, b, wq, wp, a, xq, xp, unit, h=0, lo=0, hi=C):
+        whole = hi - lo == C
+        E(0.02 + 0.33 * (hi - lo) / C, lambda q: q.matmul_mx(bank(out, b, hi - lo), T[wq][:, a:a + 128], T[wp][:, a:a + 128],
+                                                             T[xq][:, lo:hi], T[xp][:, lo:hi], True, True),
+          [(wq, unit, unit + 1), (wp, unit, unit + 1), xq if whole else (xq, h, h + 1), xp if whole else (xp, h, h + 1)], [(out, b, b + 1)])
+
+    def quantize(xq, xp, X, h, lo, hi):
+        V(0.02 + 0.35 * (hi - lo) / C, lambda q: q.quantize_mx(T[xq][:, lo:hi], T[xp][:, lo:hi], T[X][:, 4 * lo:4 * hi]),
+          [(X, 4 * h, 4 * h + 4)], [(xq, h, h + 1), (xp, h, h + 1)])
+
+    def add_by(out, win, l, other, h, lo, hi, k=1, late=()):
+        for b in range(4):
+            more = list(late) if b >= OPT["late"] else []
+            if other == "fo" and b in OPT["xps"]:
+                act(T.gp[:, C * b + lo:C * b + hi], at(win, b).indirect(T[l][:, lo // 16:hi // 16]), [(win, b, b + 1), l],
+                    [("gp", b + lo / C, b + hi / C)], 0.06 + (GATHER - 0.06) * (hi - lo) / C)
+                tt(T[out][:, 4 * lo + b:4 * hi:4], T.pu[:, BANK * b + lo:BANK * b + hi], T.gp[:, C * b + lo:C * b + hi], A.add,
+                   [("pu", b, b + 1), ("gp", b + lo / C, b + hi / C)] + more, [(out, 4 * h + b, 4 * h + b + 1)], ROW * (hi - lo) / C + 0.01)
+                continue
+            tt(T[out][:, 4 * lo + b:4 * hi:4], T[win][:, k * C * b:k * C * (b + 1)].indirect(T[l][:, lo // 16:hi // 16]), T[other][:, C * b + lo:C * b + hi], A.add,
+               [(win, k * b, k * b + k), l, (other, b, b + 1)] + more, [(out, 4 * h + b, 4 * h + b + 1)], 0.06 + (GATHER - 0.06) * (hi - lo) / C)
+
+    def store(e, out, in_, reads):
+        k = task(P, e, 0.07, lambda q: q.dma_start(out, in_), reads, [], "dma", "st", 16)
+        task(P, "net", 2.0, None, [], [], "land", "st", 16, after=[k])
 
     act(at("fw0", 1), by("idr", "l0"), ["idr", "l0"], [("fw0", 1, 2)], GATHER)
     for r in range(ROUNDS):
         X, xq, xp, aq, ap = "x%d" % r, "xq%d" % r, "xp%d" % r, "aq%d" % r, "ap%d" % r
         lp, lb, rp, rb = "lp%d" % r, "lb%d" % r, "rp%d" % r, "rb%d" % r
         fw, fn = "fw%d" % (r % 2), "fw%d" % (1 - r % 2)
-        powers(fw)
-        places(r)
-        V(0.37, lambda q, xq=xq, xp=xp, X=X: q.quantize_mx(T[xq][:], T[xp][:], T[X][:]), [X], [xq, xp])
+        P["rounds"].append(len(P["tasks"]))
+        if r == 0:
+            powers(fw, False)
+        act(T["lf%d" % r][:], L("fl"), ["fl"], ["lf%d" % r], SMALL)
+        send(r, [(T[rb][:], T["lf%d" % r][:], "lf%d" % r)], "arb%d" % r, [rb], 2.6)
+        for h, (lo, hi) in enumerate(parts("x")):
+            if r == 0:
+                quantize(xq, xp, X, h, lo, hi)
+            w, last = ROW * (hi - lo) / C + 0.02, hi == C or r == 0 and OPT["r0v"]
+            mm("pw", 2 * h, "uqr", "upr", 0, xq, xp, 0, h, lo, hi)
+            (cp if last else act)(T.sa[:, lo:hi], bank("pw", 2 * h, hi - lo), [("pw", 2 * h, 2 * h + 1)], [("sa", lo / C, hi / C)], w)
+            k = 2 * h + 1 if last and not OPT["sbv"] else 2 * h
+            if k % 2:
+                mm("pw", k, "uqr", "upr", 0, xq, xp, 0, h, lo, hi)
+            (cp if last and OPT["sbv"] else act)(T.sb[:, lo:hi], bank("pw", k, hi - lo), [("pw", k, k + 1)] + behind("sb", h, 0 if r else ROUNDS), [("sb", h, h + 1)], w)
         send(r, [(T[aq][:].bitcast(dt.uint8), T[xq][:].bitcast(dt.uint8), xq), (T[ap][:], T[xp][:], xp)], "ax%d" % r, [aq, ap], 6.0)
-        mm("pw", 0, "uqr", "upr", 0, xq, xp, 0)
-        mm("pw", 1, "uqr", "upr", 0, xq, xp, 0)
-        cp(at("sa"), bank("pw", 0), [("pw", 0, 1)], [SA], ROW)
-        act(T.sb[:], bank("pw", 1), [("pw", 1, 2)], ["sb"])
-        act(T.s2[:], bank("pw", 1), [("pw", 1, 2), "z0", "z1"], ["s2"], scale=cf("z0"), bias=cf("z1"))
+        places(r)
         coarse = steps("c", "sa", range(7), (3, 0))
-        tt(T.dt[:], by("ia", "l0"), T.ic[:], A.add, ["ia", "ic", "l0"], ["dt"], GATHER)
         act(at("sa", 1), by("sa", "l0"), [SA, "l0"], [("sa", 1, 2)], GATHER)
-        if OPT["fsv"]:
-            act(T.s0[:], bank("pw", 1), [("pw", 1, 2), "ev"], ["s0"], scale=cf("ev"))
-            tt(T.fs[:], by("s0", "l0"), T.dt[:], A.add, ["s0", "dt", "l0"], ["fs"], GATHER)
+        if OPT["sbd"]:
+            move("a%d" % r, T.s0[0:128:2, :], T.sa[0:128:2, 0:C], [SA], ["s0"])
+            tt(T.fs[:], by("s0", "l0"), T.ic[:], A.add, ["s0", "ic", "l0"], ["fs"], GATHER)
         else:
-            move("o%d" % r, T.fs[1:128:2, :], T.dt[1:128:2, :], ["dt"], [("fs", 1, 2)])
-            move("n%d" % r, T.fs[0:128:2, :], T.sa[0:128:2, C:2 * C], [("sa", 1, 2)], [("fs", 0, 1)])
+            tt(T.dt[:], by("ia", "l0"), T.ic[:], A.add, ["ia", "ic", "l0"], ["dt"], GATHER)
+            act(T.s0[:], at("sb"), ["sb", "ev"], ["s0"], scale=cf("ev"))
+            tt(T.fs[:], by("s0", "l0"), T.dt[:], A.add, ["s0", "dt", "l0"], ["fs"], GATHER)
         fine = steps("f", "fs", range(3), (0, 6))
         for b in range(4):
-            mm("pu", b, "eq", "ep", 128 * b, xq, xp, b)
-            act(at("fo", b), bank("pu", b), [("pu", b, b + 1)], [("fo", b, b + 1)])
+            if b not in OPT["xps"]:
+                mm("pu", b, "eq", "ep", 128 * b, xq, xp, b)
+                act(at("fo", b), bank("pu", b), [("pu", b, b + 1)], [("fo", b, b + 1)])
         for b in range(4):
             mm("pu", b, "eq", "ep", 128 * b, aq, ap, b)
-            act(at("fh", b), bank("pu", b), [("pu", b, b + 1)], [("fh", b, b + 1)], scale=0.5)
-        tt(mid("n1"), by(coarse, "l0"), T.s2[:], A.is_le, [coarse, "l0", "s2"], [("n1", 1, 2)], GATHER)
-        turn("tn1", "n1")
-        V(2.1 * HALF, lambda q: q.tensor_tensor_scan(T.r1[:], T.tn1[:], T.te1[:], 0.0, A.mult, A.add), ["tn1", "te1"], ["r1"])
-        ts(T.lq[:], picked("r1", 1), 160.0, None, A.add, None, ["r1", "pick"], ["lq"], 0.1)
-        tt(mid("n2"), by(fine, "lq"), at("sa"), A.is_le, [fine, "lq", SA], [("n2", 1, 2)], GATHER)
-        act(mid("e2"), by(fine, "lq"), [fine, "lq", "od", "k2"], [("e2", 1, 2)], GATHER, scale=cf("od"), bias=cf("k2"))
-        turn("tn2", "n2")
-        tt(L("hl", 32), picked("tn2", 0), L("c320", 32), A.mult, ["tn2", "pick", "c320"], ["hl"], 0.1)
-        V(SMALL, lambda q: q.memset(T.tn2[:, 0:TW:16], 0.0), [], ["tn2"])
-        ts(L("hm", 32), L("hl", 32), 160.0, None, A.add, None, ["hl"], ["hm"])
-        turn("te2", "e2")
-        V(1.05 * HALF, lambda q: q.tensor_tensor_scan(T.r2[:], T.tn2[:, 0:TW:2], T.te2[:, 1:TW:2], 0.0, A.mult, A.add), ["tn2", "te2"], ["r2"])
-        tt(L("om", 32), picked("r2", 2), L("hm", 32), A.min, ["r2", "pick", "hm"], ["om"], 0.1)
-        ts(T.ob[:], L("om", 32), 480.0, None, A.add, None, ["om"], ["ob"])
-        ts(T[lp][:], picked("r2", 2), 160.0, None, A.add, None, ["r2", "pick"], [lp], 0.1)
-        send(r, [(T[rp][:], T[lp][:, 0:20], lp)], "arp%d" % r, [rp], 2.6)
-        (cp if OPT["brv"] else act)(T.br[:], T[fw][:].indirect(T.ob[:, 0:20]), [fw, "ob"], ["br"], GATHER)
-        listed(lb, "br", "bsn")
-        send(r, [(T[rb][:], T[lb][:], lb)], "arb%d" % r, [rb], 2.6)
-        (cp if OPT["erv"] else act)(T.er[:], T.sa[:].indirect(T.ob[:, 0:20]), ["sa", "ob"], ["er"], GATHER)
+            act(at("fh", 2 * b), bank("pu", b), [("pu", b, b + 1)], [("fh", 2 * b, 2 * b + 1)], scale=0.5)
+            act(at("fh", 2 * b + 1), by("fh", rb, 2 * b), [("fh", 2 * b, 2 * b + 1), rb], [("fh", 2 * b + 1, 2 * b + 2)], GATHER)
+            if b in OPT["xps"]:
+                mm("pu", b, "eq", "ep", 128 * b, xq, xp, b)
+        for h in range(NH):
+            def R(b):
+                return (b, 2 * h, 2 * h + 2)
+
+            def H(name):
+                return L(name, 16 * KP, 16 * h)
+            lo, hi, a, b, lq = W * h, W * h + W, NB * h, NB * h + NB, T.lq[:, 16 * h:16 * h + NB]
+            tt(mid("n1", h), at(coarse).indirect(T.l0[:, a:b]), T.sa[:, lo:hi], A.is_le, [coarse, "l0", SA], [R("n1")], GP)
+            turn("tn1", "n1", h, PW * h)
+            chain("r1", "tn1", "te1", h, 1)
+            ts(T.lq[:, 16 * h:16 * h + 16 * KP], picked("r1", 1, h), 160.0, None, A.add, None, [R("r1"), "pick"], [R("lq")], 0.1)
+            tt(mid("n2", h), at(fine).indirect(lq), T.sa[:, lo:hi], A.is_le, [fine, R("lq"), SA], [R("n2")], GP)
+            act(mid("e2", h), at(fine).indirect(lq), [fine, R("lq"), "od", "k2"], [R("e2")], GP, scale=cf("od"), bias=cf("k2"))
+            turn("tn2", "n2", h, PW * h)
+            tt(H("hl"), picked("tn2", 0, h), L("c320", 16 * KP, a), A.mult, [R("tn2"), "pick", "c320"], [R("hl")], 0.1)
+            V(SMALL, lambda q, h=h: q.memset(T.tn2[:, TW * h:TW * h + TW:16], 0.0), [], [R("tn2")])
+            if OPT["hms"]:
+                act(H("hm"), H("hl"), [R("hl")], [R("hm")], SMALL, bias=160.0)
+            else:
+                ts(H("hm"), H("hl"), 160.0, None, A.add, None, [R("hl")], [R("hm")])
+            turn("te2", "e2", h, PW * h)
+            chain("r2", "tn2", "te2", h, 2)
+            tt(H("om"), picked("r2", 2, h, 2), H("hm"), A.min, [R("r2"), "pick", R("hm")], [R("om")], 0.1)
+            ts(T[lp][:, a:b], L("om", NB, 16 * h), 480.0, None, A.add, None, [R("om")], [(lp, a, b)])
+            ts(T[lp][:, 20 + a:20 + a + 16 * KP], picked("r2", 2, h, 2), 160.0, None, A.add, None, [R("r2"), "pick"], [(lp, 20 + a, 20 + a + 16 * KP)], 0.1)
+            (cp if OPT["brv"] else act)(T.br[:, lo:hi], T[fw][:].indirect(T[lp][:, a:b]), [fw, (lp, a, b)], [R("br")], GP)
+            V(max(SMALL, HALF / NH), lambda q, lo=lo, hi=hi: q.tensor_tensor_scan(T.bsn[:, lo:hi], T.wt[:, 0:W], T.br[:, lo:hi], 0.0, A.add, A.max),
+              ["wt", R("br")], [R("bsn")])
+            act(T[lb][:, a:b], T.bsn[:, lo + 15:hi:16], [R("bsn"), "col"], [R(lb)], 0.1, bias=cf("col"))
+        send(r, [(T[rp][:], T[lp][:, 0:40], lp)], "arp%d" % r, [rp], 2.6)
+        (cp if OPT["erv"] else act)(T.er[:], T.sa[:].indirect(T[lp][:, 0:20]), ["sa", (lp, 0, 20)], ["er"], GATHER)
         (cp if OPT["ehv"] else act)(T.eh[:], by("er", "hi16"), ["er", "hi16"], ["eh"], GATHER)
         tt(T.sw[:], by("er", "lo16"), T.eh[:], A.is_gt, ["er", "eh", "lo16"], ["sw"], GATHER)
         weighted("swn", "sw")
+        act(T.fm[:], by(fw, "mt16", 1), [(fw, 1, 2), "mt16"], ["fm"], GATHER)
+        weighted("fmn", "fm")
+        act(L("be"), L("fl"), ["fl", "nc"], ["be"], SMALL, bias=cf("nc"))
+        tt(L("dm"), every16("fmn"), L("be"), A.subtract, ["fmn", "be"], ["dm"])
+        act(L("bf"), L("dm"), ["dm", "f0"], ["bf"], SMALL, scale=cf("f0"))
+        tt(L("dc"), L("bf"), L("fl"), A.add, ["bf", "fl"], ["dc"])
         tt(L("sx"), every16("swn"), L("dm"), A.mult, ["swn", "dm"], ["sx"])
-        tt(L("sy"), L("sx"), L("dc"), A.add, ["sx", "dc"], ["sy"])
-        cp(T.so[:], L("sy"), ["sy"], ["so"])
+        tt(T.l0[:], L("sx"), L("dc"), A.add, ["sx", "dc"], ["l0"])
         if r < ROUNDS - 1:
-            (cp if OPT["f0v"] else act)(at(fn, 1), by(fw, "so", 1), [(fw, 1, 2), "so"], [(fn, 1, 2)], GATHER)
-            listed("l0", fn, "scn", 1)
+            tt(L("fl"), L("sx"), L("dc"), A.add, ["sx", "dc"], ["fl"])
+        if r < ROUNDS - 1:
+            (cp if OPT["f0v"] else act)(at(fn, 1), by("idr", "l0"), ["idr", "l0"], [(fn, 1, 2)], GATHER)
+            powers(fn, True)
         else:
-            act(T.er[:], by(fw, "so", 1), [(fw, 1, 2), "so"], ["er"], GATHER, bias=160.0)
-            task(P, "y", 0.07, lambda q: q.dma_start(T.nf[:], T.er[0:128:16, :]), ["er"], [], "dma", "st", 16)
+            act(T.er[:], by("idr", "l0"), ["idr", "l0"], ["er"], GATHER, bias=160.0)
+            store("y", T.nf[:], T.er[0:128:16, :], ["er"])
         for b in range(4):
-            act(at("gp", b), by("fh", rp, b), [("fh", b, b + 1), rp], [("gp", b, b + 1)], GATHER)
-            tt(T.z[:, b:4 * C:4], by("fh", rb, b), at("gp", b), A.add, [("fh", b, b + 1), rb, ("gp", b, b + 1)], [("z", b, b + 1)], GATHER)
-        V(0.37, lambda q: q.quantize_mx(T.zq[:], T.zp[:], T.z[:]), ["z"], ["zq", "zp"])
-        Y = "x%d" % (r + 1)
-        for b in range(4):
-            mm("pw", b, "wq", "wp", 128 * b, "zq", "zp", b)
-            act(at("h", b), bank("pw", b), [("pw", b, b + 1)], [("h", b, b + 1)], scale=0.03125)
-            tt(T[Y][:, b:4 * C:4], by("h", lb, b), at("fo", b), A.add, [("h", b, b + 1), lb, ("fo", b, b + 1)], [(Y, b, b + 1)], GATHER)
+            (cp if b in OPT["gpv"] else act)(at("gp", b), at("fh", 2 * b).indirect(T[rp][:, 20:40]), [("fh", 2 * b, 2 * b + 1), rp] + behind("gp", b, r),
+                                             [("gp", b, b + 1)], GATHER)
+        for h, (lo, hi) in enumerate(parts("z%d" % r)):
+            add_by("z", "fh", rp, "gp", h, lo, hi, 2)
+            quantize("zq", "zp", "z", h, lo, hi)
+            ps = "pw"
+            for b in range(4):
+                mm(ps, b, "wq", "wp", 128 * b, "zq", "zp", b, h, lo, hi)
+                if b in OPT["hv"]:
+                    ts(T.h[:, C * b + lo:C * b + hi], bank(ps, b, hi - lo), 0.03125, None, A.mult, None, [(ps, b, b + 1)], [("h", b + lo / C, b + hi / C)], ROW * (hi - lo) / C)
+                    continue
+                act(T.h[:, C * b + lo:C * b + hi], bank(ps, b, hi - lo), [(ps, b, b + 1)] + behind("h", b, r), [("h", b + lo / C, b + hi / C)],
+                    ROW * (hi - lo) / C + 0.02, scale=0.03125)
+        for h, (lo, hi) in enumerate(parts("x")):
+            add_by("x%d" % (r + 1), "h", lb, "fo", h, lo, hi, 1, [("xq%d" % (r + 1), 0, 1)] * h)
+            quantize("xq%d" % (r + 1), "xp%d" % (r + 1), "x%d" % (r + 1), h, lo, hi)
+    P["rounds"].append(len(P["tasks"]))
     xq, xp, X = "xq%d" % ROUNDS, "xp%d" % ROUNDS, "x%d" % ROUNDS
-    V(0.37, lambda q: q.quantize_mx(T[xq][:], T[xp][:], T[X][:]), [X], [xq, xp])
-    task(P, "y", 0.07, lambda q: q.dma_start(T.oc[:], T[xq][:].bitcast(dt.uint8)), [xq], [], "dma", "st", 16)
+    for h, (lo, hi) in enumerate(parts("x")):
+        store("y", T.oc[:, 4 * lo:4 * hi], T[xq][:, lo:hi].bitcast(dt.uint8), [(xq, h, h + 1)])
+        mm("pw", h, "vq", "vp", 0, xq, xp, 0, h, lo, hi)
+        (cp if h or hi - lo == C else act)(T.eh[:, lo:hi], bank("pw", h, hi - lo), [("pw", h, h + 1)], [("eh", h, h + 1)], ROW * (hi - lo) / C)
+        store("y", T.y[:, lo:hi], T.eh[:, lo:hi], [("eh", h, h + 1)])
     for k in range(4):
-        task(P, "y" if k % 2 else "s", 0.07, lambda q, k=k: q.dma_start(T.osc[4 * k:4 * k + 4, :], T[xp][32 * k:32 * k + 4, :]), [xp], [], "dma", "st", 16)
-    mm("pw", 0, "vq", "vp", 0, xq, xp, 0)
-    cp(T.eh[:], bank("pw", 0), [("pw", 0, 1)], ["eh"], ROW)
-    task(P, "y", 0.07, lambda q: q.dma_start(T.y[:], T.eh[:]), ["eh"], [], "dma", "st", 16)
+        store("y" if k % 2 else "s", T.osc[4 * k:4 * k + 4, :], T[xp][32 * k:32 * k + 4, :], [xp])
     return sent[0]
 
 
@@ -543,7 +723,7 @@ def rank_program(g, core, T, topo):
         SHARED["order"] = schedule(P)
     order, start, _ = SHARED["order"]
     count = issue(P, order, start, g, T)
-    g.sync.wait_ge(T.sem.st, 16 * sum(1 for t in P["tasks"] if t["sem"] == "st"))
+    g.sync.wait_ge(T.sem.st, 16 * sum(1 for t in P["tasks"] if t["sem"] == "st" and t["kind"] == "dma"))
     for s, k in sorted(count.items()):
         g.sync.wait_ge(T.sem[s], k)
     g.wait_ge(T.sem.snd, sent)

@@ -8,12 +8,13 @@ BANK = 512
 ROUNDS = 3
 BIG = 1e29
 KEY = 1024.0
-NH = 1
-W = C // NH
-NB = W // 16
-KP = (NB + 15) // 16
-PW = W + 32
-TW = W + PW
+HIGH = 2.0 ** 75
+BASE = 512.0
+NB = C // 16
+B0 = 32
+PW = C + 32
+TW = C + PW
+YW = 256
 
 
 def sb(n, d):
@@ -30,34 +31,34 @@ SCRATCH = {
     "eq": sb(512, "float8_e4m3fn_x4"), "ep": sb(512, "uint8"),
     "one": sb(528, "bfloat16"), "big": sb(528, "bfloat16"),
     "ji": sb(16, "int32"), "dg": sb(16, "int32"), "t1": sb(16, "bfloat16"), "t2": sb(16, "bfloat16"), "w16": sb(16, "bfloat16"),
-    "wt": sb(C, "bfloat16"), "idr": sb(C, "bfloat16"),
-    "ia": sb(C, "bfloat16"), "ic": sb(C, "bfloat16"), "s0": sb(C, "float32"),
+    "wt": sb(C, "bfloat16"), "idr": sb(C, "bfloat16"), "nid": sb(C, "bfloat16"), "ic": sb(C, "float32"), "sg": sb(C, "bfloat16"),
     "gs": sb(C, "bfloat16"), "ft": sb(5 * C, "bfloat16"),
-    "pi": sb(32, "int32"), "pa": sb(32, "int32"), "ci": sb(32, "int32"), "cn": sb(32, "int32"), "bits": sb(12, "int32"),
-    "uo": sb(8, "uint16"), "pick": sb(6, "uint16"),
-    "cf": sb(72, "float32"),
-    "fm": sb(C, "bfloat16"), "fmn": sb(C, "float16"), "mt16": sb(20, "uint16"), "lo16": sb(20, "uint16"), "hi16": sb(20, "uint16"), "so": sb(20, "uint16"), "lq": sb(32, "uint16"),
-    "sa": sb(2 * C, "float32"), "fs": sb(C, "float32"), "sb": sb(C, "float32"), "dt": sb(C, "float32"),
-    "n1": sb(NH * PW, "bfloat16"), "n2": sb(NH * PW, "bfloat16"), "e1": sb(C + 32, "float16"), "e2": sb(NH * PW, "float16"),
-    "tn1": sb(NH * TW, "bfloat16"), "tn2": sb(NH * TW, "bfloat16"), "te1": sb(NH * TW, "float16"), "te2": sb(NH * TW, "float16"),
-    "r1": sb(NH * TW, "bfloat16"), "r2": sb(NH * TW // 2, "bfloat16"),
-    "fw0": sb(2 * C, "bfloat16"), "fw1": sb(2 * C, "bfloat16"), "fa": sb(2 * C, "bfloat16"),
-    "br": sb(C, "bfloat16"), "bsn": sb(C, "float16"), "scn": sb(C, "float16"), "swn": sb(C, "float16"),
+    "pi": sb(32, "int32"), "pa": sb(32, "int32"), "ci": sb(32, "int32"), "c32": sb(NB, "int32"), "sh": sb(10, "int32"), "bits": sb(10, "int32"),
+    "uo": sb(8, "uint16"), "pick": sb(4, "uint16"),
+    "cf": sb(64, "float32"),
+    "mt16": sb(NB, "uint16"), "so": sb(NB, "uint16"), "lq": sb(32, "uint16"), "sig": sb(NB, "uint16"),
+    "sa": sb(C, "float32"), "sb": sb(C, "float32"), "fs": sb(C, "float32"), "dt": sb(C, "float32"),
+    "n1": sb(PW, "bfloat16"), "e1": sb(PW, "float16"), "tn1": sb(TW, "bfloat16"), "te1": sb(TW, "float16"), "r1": sb(TW, "bfloat16"),
+    "n2": sb(C, "bfloat16"), "e2": sb(C, "float16"), "tn2": sb(C, "bfloat16"), "te2": sb(C, "float16"),
+    "rb": sb(C, "bfloat16"), "rp": sb(C, "bfloat16"), "yy": sb(2 * YW, "bfloat16"),
+    "f00": sb(C, "bfloat16"), "f01": sb(C, "bfloat16"), "fa": sb(2 * C, "bfloat16"), "fm": sb(C, "bfloat16"),
+    "scn": sb(C, "float16"), "swn": sb(C, "float16"), "fmn": sb(C, "float16"),
     "er": sb(C, "float32"), "eh": sb(C, "float32"), "sw": sb(C, "bfloat16"),
-    "fo": sb(4 * C, "bfloat16"), "fh": sb(8 * C, "bfloat16"), "gp": sb(4 * C, "bfloat16"),
+    "fo": sb(4 * C, "bfloat16"), "fh": sb(4 * C, "bfloat16"), "gp": sb(4 * C, "bfloat16"),
     "z": sb(4 * C, "bfloat16"), "zq": sb(C, "float8_e4m3fn_x4"), "zp": sb(C, "uint8"),
     "h": sb(4 * C, "bfloat16"),
     "pu": ("psum", [128, 2048], "float32"), "pw": ("psum", [128, 2048], "float32"),
 }
 for _n in ("c", "f", "e"):
-    for _k in ("0", "1", "w"):
+    for _k in ("0", "1", "w", "x"):
         SCRATCH["m" + _n + _k] = sb(C, "float32")
-LISTS = ["cw", "c320", "bd", "be", "bf", "dm", "dc", "hl", "hm", "om", "sx", "fl"]
+LISTS = ["cw", "ct", "pk", "dm", "dc", "fl", "be", "dn", "bf", "de", "sx", "ta", "ua", "tb", "yb"]
 SCRATCH["sml"] = sb(32 * len(LISTS), "float32")
-COLS = {"sc": 0, "kb": 12, "nb": 24, "bi": 36, "col": 48, "e15": 49, "a1": 50, "a2": 51, "b1": 52, "b2": 53, "od": 54, "ev": 55,
-        "k1": 56, "k2": 57, "z0": 58, "z1": 59, "f0": 60, "ko": 61, "pw": 64, "j0": 68, "j1": 69, "j2": 70, "nc": 71}
-for _k in range(7):
-    SCRATCH["l%d" % _k] = sb(20, "uint16")
+COLS = {"sc": 0, "bi": 12, "bt": 24, "nk": 34}
+for _n in ("e15", "pl", "col", "f0", "nc", "a1", "b1", "b2", "c2", "lo", "hi", "hj", "k1", "k2", "es", "e0", "par", "dd", "p21", "nl"):
+    COLS[_n] = 33 + len(COLS)
+for _k in range(6):
+    SCRATCH["l%d" % _k] = sb(NB, "uint16")
 for _r in range(ROUNDS + 1):
     if _r:
         SCRATCH["x%d" % _r] = sb(4 * C, "bfloat16")
@@ -66,198 +67,313 @@ for _r in range(ROUNDS + 1):
 for _r in range(ROUNDS):
     SCRATCH["aq%d" % _r] = sb(C, "float8_e4m3fn_x4")
     SCRATCH["ap%d" % _r] = sb(C, "uint8")
-    SCRATCH["lp%d" % _r] = sb(52, "uint16")
-    SCRATCH["rp%d" % _r] = sb(40, "uint16")
-    for _n in ("lb", "lf", "rb"):
-        SCRATCH["%s%d" % (_n, _r)] = sb(20, "uint16")
+    SCRATCH["lp%d" % _r] = sb(2 * B0, "uint16")
+    SCRATCH["al%d" % _r] = sb(B0 + NB, "uint16")
 SEMAPHORES = ["ev", "es", "et", "eg", "snd", "st"]
-SEMAPHORES += ["%s%d" % (_n, _r) for _n in ("ax", "arp", "arb") for _r in range(ROUNDS)]
-SEMAPHORES += ["ld_" + _n for _n in ("x", "u", "v", "nx", "mt", "wc", "ws")]
-SEMAPHORES += ["ld_%s%d" % (_n, _r) for _n in ("g0", "g1", "g2", "g3", "g4", "g5", "g6", "a") for _r in range(ROUNDS)]
+SEMAPHORES += ["%s%d" % (_n, _r) for _n in ("ax", "ap", "ab") for _r in range(ROUNDS)]
+SEMAPHORES += ["ld_" + _n for _n in ("x", "u", "v", "nx", "mt", "wc", "ws", "sg")]
+SEMAPHORES += ["ld_%s%d" % (_n, _r) for _n in ("g0", "g1", "g2", "g3", "a", "b") for _r in range(ROUNDS)]
 
 GATHER, HALF, ROW, SMALL = 0.58, 0.17, 0.34, 0.08
-GP = 0.06 + (GATHER - 0.06) / NH
-HOP, SAME = 0.22, 0.1
-COSTS = [(1.0, 1.0, 1.0, 0.2, 0.1), (0.9, 0.9, 0.8, 0.3, 0.15), (1.25, 1.0, 1.3, 0.2, 0.07), (0.8, 0.95, 1.1, 0.3, 0.06)]
+COSTS = [(0.65, 0.8, 0.85, 0.17, 0.15, 0.05), (1.0, 1.0, 1.0, 0.2, 0.17, 0.06), (0.7, 0.9, 0.77, 0.22, 0.12, 0.03)]
+SPAN = 120
 SHARED = {}
-OPT = {"own": [], "brv": False, "erv": True, "ehv": True, "f0v": True, "halves": ["x"], "xps": [3], "sbd": False, "pv": [0], "ls": True, "net": 0.85, "hms": False, "cut": 192, "late": 4, "seed": 2, "sbv": True, "upv": False, "r0v": False, "hv": [], "f5": 1, "early": True, "gpv": [], "pace": {"h0": 2, "h1": 2, "h2": 2, "h3": 3, "sb0": 4}}
-SA = ("sa", 0, 1)
+OPT = {"x": 192, "z": 160, "zg": [0], "zs": [0, 3], "xs": [3], "xps": [3], "xpl": [2, 3], "seed": 3}
 
 
 def new_plan():
-    return {"tasks": [], "w": {}, "r": {}, "rounds": []}
+    return {"tasks": [], "w": {}, "r": {}}
 
 
 def overlap(a, b):
     return a[0] < b[1] and b[0] < a[1]
 
 
-def task(P, eng, dur, fn, reads, writes, kind="op", sem=None, inc=1, after=(), behind=()):
+def gat(n=C):
+    return ("gather", 0.06 + (GATHER - 0.06) * n / C)
+
+
+def cost(t, e, w, c):
+    if e in "vs":
+        return c[5] + (0.06 + (w - 0.06) * c[0] if t["gather"] else max(0.07, w * c[1]) if w > 0.125 else 0.07)
+    return w * c[2] if e == "net" else w
+
+
+def task(P, eng, dur, fn, reads, writes, kind="op", sem=None, inc=1, after=(), alt=None):
     def reg(x):
         return (x, 0, 1 << 20) if isinstance(x, str) else x
     n = len(P["tasks"])
-    if eng == "net":
-        dur *= OPT["net"]
-    deps = {}
-    for a in after:
-        deps[a] = True
+    gather = isinstance(dur, tuple)
+    deps = set(after)
     rd, wr = [reg(x) for x in reads], [reg(x) for x in writes]
     for b, lo, hi in rd:
-        for (l, h, t) in P["w"].get(b, []):
-            if overlap((lo, hi), (l, h)):
-                deps[t] = True
+        deps.update(t for l, h, t in P["w"].get(b, []) if overlap((lo, hi), (l, h)))
         if b in ("pu", "pw"):
-            for (l, h, t) in P["r"].get(b, []):
-                if overlap((lo, hi), (l, h)) and P["tasks"][t]["eng"] != eng:
-                    deps.setdefault(t, False)
+            deps.update(t for l, h, t in P["r"].get(b, []) if overlap((lo, hi), (l, h)) and (P["tasks"][t]["eng"] != eng or alt or P["tasks"][t]["alt"]))
     for b, lo, hi in wr:
-        for (l, h, t) in P["w"].get(b, []):
-            if overlap((lo, hi), (l, h)):
-                deps[t] = True
-        for (l, h, t) in P["r"].get(b, []):
-            if overlap((lo, hi), (l, h)):
-                deps.setdefault(t, False)
+        deps.update(t for l, h, t in P["w"].get(b, []) + P["r"].get(b, []) if overlap((lo, hi), (l, h)))
     for b, lo, hi in wr:
         P["w"][b] = [e for e in P["w"].get(b, []) if not (lo <= e[0] and e[1] <= hi)] + [(lo, hi, n)]
         P["r"][b] = [e for e in P["r"].get(b, []) if not (lo <= e[0] and e[1] <= hi)]
     for b, lo, hi in rd:
         P["r"].setdefault(b, []).append((lo, hi, n))
-    deps.pop(n, None)
-    for a in behind:
-        deps.setdefault(a, False)
-    P["tasks"].append({"eng": eng, "dur": dur, "fn": fn, "deps": deps, "kind": kind, "sem": sem, "inc": inc,
-                       "gather": eng in "vs" and min(abs(dur - 0.06 - (GATHER - 0.06) * w / C) for w in (128, 160, 192, C)) < 1e-6})
+    P["tasks"].append({"eng": eng, "dur": dur[1] if gather else dur, "fn": fn, "deps": sorted(deps), "kind": kind, "sem": sem, "inc": inc,
+                       "gather": gather, "alt": alt})
     return n
 
 
-def schedule(P, tries=4000, moves=30000):
+def schedule(P, tries=1000, moves=45000, starts=8, last=100000, heat=0.015, sweeps=4):
     ts = P["tasks"]
     n = len(ts)
-    lags = [[(d, HOP if ts[d]["eng"] != t["eng"] else SAME) for d in t["deps"]] for t in ts]
-    succ = [[] for _ in range(n)]
+    ways = [[(e, cost(t, e, w, COSTS[0])) for e, w in [(t["eng"], t["dur"])] + ([t["alt"][:2]] if t["alt"] else [])] for t in ts]
+    hop, same = COSTS[0][3:5]
+    pre = [t["deps"] for t in ts]
+    post = [[] for _ in range(n)]
     for i in range(n):
-        for d, _ in lags[i]:
-            succ[d].append(i)
-    up = [t["dur"] for t in ts]
-    for i in range(n - 1, -1, -1):
-        for d, lag in lags[i]:
-            up[d] = max(up[d], ts[d]["dur"] + lag + up[i])
+        for d in pre[i]:
+            post[d].append(i)
 
-    def place(rank):
-        left = [len(x) for x in lags]
-        ready = [i for i in range(n) if left[i] == 0]
-        slots = {}
-        start, end = [0.0] * n, [0.0] * n
+    def place(rank, pre, post, lean):
+        left = [len(x) for x in pre]
+        ready = [i for i in range(n) if not left[i]]
+        lines = {e: [] for e in "vstgy"}
+        end, eng, dur = [0.0] * n, [""] * n, [0.0] * n
         while ready:
-            i = max(ready, key=lambda k: rank[k]) if len(ready) > 1 else ready[0]
+            i = ready[0]
+            for k in ready:
+                if rank[k] < rank[i]:
+                    i = k
             ready.remove(i)
-            t = ts[i]
-            at, dur = 0.0, t["dur"]
-            for d, lag in lags[i]:
-                at = max(at, end[d] + lag)
-            if t["eng"] != "net":
-                line = slots.setdefault(t["eng"], [])
-                k = len(line)
-                while k and line[k - 1][1] > at:
-                    k -= 1
-                while True:
-                    s = max(at, line[k - 1][1] if k else 0.0)
-                    if k == len(line) or s + dur <= line[k][0] + 1e-9:
-                        break
-                    k += 1
-                line.insert(k, (s, s + dur, i))
-                at = s
-            start[i], end[i] = at, at + dur
-            for s in succ[i]:
-                left[s] -= 1
-                if left[s] == 0:
-                    ready.append(s)
-        cost = 0.7 * max(end) + 0.6 * sum(end[i] for i in sends) / len(sends)
-        return cost, {e: [x[2] for x in line] for e, line in slots.items()}, start, max(end)
-    sends = [i for i in range(n) if ts[i]["kind"] == "send"]
-    best = now = place(up)
-    rng = np.random.default_rng(OPT["seed"])
-    for k in range(tries):
-        rank = -np.array(now[2])
-        at, width = -rng.random() * now[3], [1.5, 3.0, 6.0][rng.integers(3)]
-        part, step = [0.05, 0.15, 0.4][rng.integers(3)], [0.3, 1.0, 3.0][rng.integers(3)]
-        hit = (rng.random(n) < part) & (abs(rank - at) < width)
-        got = place((rank + hit * rng.standard_normal(n) * step).tolist())
-        if got[0] - now[0] <= -(0.005 + 0.03 * (1 - k / tries)) * math.log(1 - rng.random()):
-            now = got
-            if got[0] < best[0]:
-                best = got
-    order = refine(P, best[1], succ, moves, 0.04)[0]
-    return refine(P, order, succ, 2 * moves, 0.025)
-
-
-def refine(P, order, succ, moves, heat):
-    ts = P["tasks"]
-    n = len(ts)
-    durs = [[t["dur"] * (c if t["eng"] == "net" else a if t["gather"] else b) for t in ts] for a, b, c, _, _ in COSTS]
-    lags = [[[(d, hop if ts[d]["eng"] != t["eng"] else same) for d in t["deps"]] for t in ts] for _, _, _, hop, same in COSTS]
-    count = [len(t["deps"]) for t in ts]
-
-    def run(k):
-        left, nxt, prv = count[:], [-1] * n, [-1] * n
-        for line in order.values():
-            for a, b in zip(line, line[1:]):
-                nxt[a], prv[b] = b, a
-                left[b] += 1
-        todo = [i for i in range(n) if not left[i]]
-        for i in todo:
-            for s in succ[i] + [nxt[i]] * (nxt[i] >= 0):
+            best = None
+            for e, w in ways[i]:
+                at, k = 0.0, 0
+                for d in pre[i]:
+                    x = end[d] + (same if eng[d] == e else hop)
+                    if x > at:
+                        at = x
+                if e != "net":
+                    line = lines[e]
+                    k = len(line)
+                    while k and line[k - 1][1] > at:
+                        k -= 1
+                    while k < len(line) and at + w > line[k][0] + 1e-9:
+                        at = max(at, line[k][1])
+                        k += 1
+                x = at + w + (lean[i] if e == "v" else 0.0)
+                if best is None or x < best[0]:
+                    best = (x, e, w, at, k)
+            _, e, w, at, k = best
+            if e != "net":
+                lines[e].insert(k, (at, at + w))
+            end[i], eng[i], dur[i] = at + w, e, w
+            for s in post[i]:
                 left[s] -= 1
                 if not left[s]:
-                    todo.append(s)
-        if len(todo) < n:
-            return None
-        ends, arcs = [], []
-        for dur, lag in zip(durs, lags):
-            end = [0.0] * (n + 1)
-            for i in todo:
-                at = end[prv[i]]
-                for d, l in lag[i]:
-                    if end[d] + l > at:
-                        at = end[d] + l
-                end[i] = at + dur[i]
-            ends.append(end)
-        end, dur, lag = ends[k], durs[k], lags[k]
-        i = end.index(max(end))
-        while i >= 0:
-            at = end[i] - dur[i] - 1e-9
-            if prv[i] >= 0 and end[prv[i]] >= at:
-                arcs.append((prv[i], i))
+                    ready.append(s)
+        return max(end), end, eng, dur, lean
+    up = [w[0][1] for w in ways]
+    for i in range(n - 1, -1, -1):
+        for d in pre[i]:
+            up[d] = max(up[d], ways[d][0][1] + hop + up[i])
+    rng = np.random.default_rng(OPT["seed"])
+    pool = []
+    for _ in range(starts):
+        best = now = place([-x for x in up], pre, post, [0.5] * n)
+        for k in range(tries):
+            rank = -np.array(now[1])
+            at, width = -rng.random() * now[0], [2.0, 4.0, 8.0][rng.integers(3)]
+            part, step = [0.05, 0.15, 0.4][rng.integers(3)], [0.3, 1.0, 3.0][rng.integers(3)]
+            near = abs(rank - at) < width
+            hit = (rng.random(n) < part) & near
+            lean = np.where((rng.random(n) < 0.2) & near, rng.random(n) * 2.0 - 0.5, now[4]).tolist()
+            back = place((rank + hit * rng.standard_normal(n) * step).tolist(), post, pre, lean)
+            got = place([-x for x in back[1]], pre, post, lean)
+            if got[0] - now[0] <= -(0.005 + 0.05 * (1 - k / tries)) * math.log(1 - rng.random()):
+                now = got
+                if got[0] < best[0]:
+                    best = got
+        seq = sorted(range(n), key=lambda i: (best[1][i] - best[3][i], i))
+        pool.append(refine(P, seq, best[2], post, moves, heat, sweeps, rng))
+    best = min(pool)
+    for other in pool + pool:
+        for k in range(20, n, 12):
+            for a, b in ((best, other), (other, best)):
+                head = set(a[1][:k])
+                best = min(best, refine(P, a[1][:k] + [i for i in b[1] if i not in head],
+                                        [a[2][i] if i in head else b[2][i] for i in range(n)], post, 0, 0, 0, rng))
+    v, seq, eng, start = refine(P, best[1], best[2], post, last, heat / 2, sweeps, rng)
+    return {e: [i for i in seq if eng[i] == e] for e in "vstgy"}, start, v
+
+
+def refine(P, seq, eng, succ, moves, heat, sweeps, rng):
+    ts = P["tasks"]
+    n = len(ts)
+    ways = [{e: [cost(t, e, w, c) for c in COSTS] for e, w in [(t["eng"], t["dur"])] + ([t["alt"][:2]] if t["alt"] else [])} for t in ts]
+    deps = [t["deps"] for t in ts]
+    K = range(len(COSTS))
+    wait = [c[3:5] for c in COSTS]
+    end, tail = [[0.0] * (n + 1) for _ in K], [[0.0] * (n + 1) for _ in K]
+    prv = [n] * (n + 1)
+
+    def forward(seq, last):
+        last = dict(last)
+        for i in seq:
+            e = eng[i]
+            prv[i] = last.get(e, n)
+            if e != "net":
+                last[e] = i
+        for k in K:
+            en, w = end[k], wait[k]
+            for i in seq:
+                at, e = en[prv[i]], eng[i]
+                for d in deps[i]:
+                    x = en[d] + w[eng[d] == e]
+                    if x > at:
+                        at = x
+                en[i] = at + ways[i][e][k]
+        return last
+
+    def backward(seq, first):
+        for k in K:
+            ta, w, nxt = tail[k], wait[k], dict(first)
+            for i in reversed(seq):
+                e = eng[i]
+                at = ta[nxt.get(e, n)]
+                for s in succ[i]:
+                    x = ta[s] + w[eng[s] == e]
+                    if x > at:
+                        at = x
+                ta[i] = at + ways[i][e][k]
+                if e != "net":
+                    nxt[e] = i
+        return nxt
+
+    def through(some, last, first, pos, b):
+        out = []
+        for k in K:
+            en, ta, w, top, at = end[k], tail[k], wait[k], n, 0.0
+            for i in some:
+                x, e = 0.0, eng[i]
+                for s in succ[i]:
+                    if pos[s] >= b and ta[s] + w[eng[s] == e] > x:
+                        x = ta[s] + w[eng[s] == e]
+                if en[i] + x > at:
+                    top, at = i, en[i] + x
+            for e, i in last.items():
+                if en[i] + ta[first.get(e, n)] > at:
+                    top, at = i, en[i] + ta[first.get(e, n)]
+            out.append((at, top))
+        return out
+
+    def arcs(k, i, inside):
+        en, w, out = end[k], wait[k], []
+        while i in inside:
+            e = eng[i]
+            at = en[i] - ways[i][e][k] - 1e-9
+            if prv[i] < n and en[prv[i]] >= at:
+                if prv[i] in inside:
+                    out.append((prv[i], i))
                 i = prv[i]
             else:
-                i = ([d for d, l in lag[i] if end[d] + l >= at] + [-1])[0]
-        return sum(max(e) for e in ends) / len(ends), arcs, [ends[0][i] - durs[0][i] for i in range(n)], max(ends[0])
-    rng = np.random.default_rng(8)
-    now = run(0)
-    best = (now, dict(order))
-    for it in range(moves):
-        r = rng.random(4)
-        if r[0] < 0.7:
-            a, b = now[1][int(r[1] * len(now[1]))]
-            e = ts[a]["eng"]
-            k, d = order[e].index(a), int(r[2] ** 2 * 5) if r[0] < 0.55 else int(r[2] * 60)
-            src, to = (k, k + 1 + d) if r[3] < 0.5 else (k + 1, k - d)
-        else:
-            e = "vs"[int(r[1] * 2)]
-            src, w = int(r[2] * len(order[e])), 4 if r[3] < 0.6 else 15 if r[3] < 0.85 else 60
-            to = src + int(rng.integers(-w, w + 1))
-        old = order[e]
-        line = old[:]
-        line.insert(max(to, 0), line.pop(src))
-        order[e] = line
-        got = run(it % len(COSTS))
-        if got is not None and got[0] - now[0] <= -(0.002 + heat * (1 - it / moves)) * math.log(1 - rng.random()):
-            now = got
-            if got[0] < best[0][0]:
-                best = (got, dict(order))
-        else:
-            order[e] = old
-    return best[1], best[0][2], best[0][0]
+                i = ([d for d in deps[i] if en[d] + w[eng[d] == e] >= at] + [n])[0]
+        return out
+
+    def stretch(seq, lo, hi, moves, heat):
+        before, after = forward(seq[:lo], {}), backward(seq[hi:], {})
+        win, m = seq[lo:hi], hi - lo
+        inside, pos = set(win), [m] * n
+        for p, i in enumerate(win):
+            pos[i] = p
+        past = [x for x, _ in through(seq[:lo], {}, {}, [m if p >= hi else -1 for p in sorted(range(n), key=lambda p: seq[p])], m)]
+        free = [i for i in win if ts[i]["alt"]]
+        got = through(win, forward(win, before), after, pos, m)
+        now = sum(max(x, y) for (x, _), y in zip(got, past)) / len(end)
+        best, fresh = (now, win, eng[:]), m
+        for it, r in enumerate(rng.random((moves, 6)).tolist()):
+            if fresh:
+                crit = [x for k in K if got[k][0] >= past[k] for x in arcs(k, got[k][1], inside)]
+                lines = {e: [] for e in "vstgy"}
+                lasts, last = [], before
+                for p, i in enumerate(win):
+                    pos[i] = p
+                    lasts.append(last)
+                    if eng[i] != "net":
+                        lines[eng[i]].append(i)
+                        last = dict(last)
+                        last[eng[i]] = i
+                firsts, first = [after] * (m + 1), after
+                for p in range(m - 1, -1, -1):
+                    if eng[win[p]] != "net":
+                        first = dict(first)
+                        first[eng[win[p]]] = win[p]
+                    firsts[p] = first
+                backward(win[:fresh], firsts[fresh])
+                fresh = 0
+            flip = free[int(r[1] * len(free))] if r[0] < 0.1 and free else None
+            if flip is not None:
+                eng[flip] = "v" if eng[flip] == "s" else "s"
+                a = pos[flip]
+                b, span = a + 1, [flip]
+            else:
+                if r[0] < 0.7 and crit:
+                    a, b = crit[int(r[1] * len(crit))]
+                    line = lines[eng[a]]
+                    k, d = line.index(a), int(r[2] ** 2 * 5) if r[0] < 0.55 else int(r[2] * 30)
+                    i, j = (a, line[min(k + 1 + d, len(line) - 1)]) if r[3] < 0.5 else (b, line[max(k - d, 0)])
+                else:
+                    line = lines["vs"[int(r[1] * 2)]] or [n]
+                    k, w = int(r[2] * len(line)), 4 if r[3] < 0.6 else 12 if r[3] < 0.85 else 30
+                    i, j = line[k], line[min(max(k + int((r[4] * 2 - 1) * w), 0), len(line) - 1)]
+                    if i == j:
+                        continue
+                p, q, need = pos[i], pos[j], {i}
+                a, b = min(p, q), max(p, q) + 1
+                span = win[a:b]
+                if q < p:
+                    want = set(deps[i])
+                    for u in reversed(span[:-1]):
+                        if u in want:
+                            need.add(u)
+                            want.update(deps[u])
+                            want.add(prv[u])
+                else:
+                    for u in span[1:]:
+                        if (prv[u] in need and prv[u] != i) or any(d in need for d in deps[u]):
+                            need.add(u)
+                if j in need:
+                    continue
+                span = [u for u in span if (u in need) == (q < p)] + [u for u in span if (u in need) != (q < p)]
+            limit = now - (0.002 + heat * (1 - it / moves)) * math.log(1 - r[5])
+            kept = [(i, prv[i], [en[i] for en in end]) for i in span]
+            last = forward(span, lasts[a])
+            if sum(x for x, _ in through(span, last, firsts[b], pos, b)) <= limit * len(end):
+                new = win[:a] + span + win[b:]
+                kept += [(i, prv[i], [en[i] for en in end]) for i in win[b:]]
+                ways_out = through(new, forward(win[b:], last), after, pos, m)
+                v = sum(max(x, y) for (x, _), y in zip(ways_out, past)) / len(end)
+                if v <= limit:
+                    now, win, got, fresh = v, new, ways_out, b
+                    if it % 8 == 0:
+                        win, fresh = sorted(win, key=lambda i: end[0][i] - ways[i][eng[i]][0]), m
+                    if v < best[0] - 1e-9:
+                        best = (v, win, eng[:])
+                    continue
+            for i, p, x in kept:
+                prv[i] = p
+                for en, y in zip(end, x):
+                    en[i] = y
+            if flip is not None:
+                eng[flip] = "v" if eng[flip] == "s" else "s"
+        eng[:] = best[2]
+        seq = seq[:lo] + best[1] + seq[hi:]
+        forward(seq, {})
+        return sorted(seq, key=lambda i: end[0][i] - ways[i][eng[i]][0])
+    spots = [(lo, s) for s in range(sweeps) for lo in range(-(s * 23 % 40), n - SPAN // 2, SPAN // 2)]
+    for lo, s in spots:
+        seq = stretch(seq, max(lo, 0), min(lo + SPAN, n), moves // len(spots), heat * (1 - 0.5 * s / sweeps))
+    forward(seq, {})
+    start = [end[0][i] - ways[i][eng[i]][0] for i in range(n)]
+    return sum(max(e) for e in end) / len(end), sorted(seq, key=lambda i: start[i]), eng, start
 
 
 def issue(P, order, start, g, T):
@@ -271,42 +387,35 @@ def issue(P, order, start, g, T):
             if t["kind"] == "op":
                 count[counter[e]] = count.get(counter[e], 0) + 1
                 mark[i] = (counter[e], count[counter[e]])
-            else:
-                mark[i] = (t["sem"], t["inc"])
     for i, t in enumerate(ts):
         if t["kind"] == "land":
             mark[i] = (t["sem"], t["inc"])
     seen = {e: {} for e in queue}
     known = {}
-    pos = {i: k for line in order.values() for k, i in enumerate(line)}
-    for i in sorted(pos, key=lambda i: (start[i], pos[i])):
-        t = ts[i]
-        e = t["eng"]
-        q, have = queue[e], seen[e]
+    where = {i: e for e, line in order.items() for i in line}
+    for i in sorted(where, key=lambda i: start[i]):
+        t, e = ts[i], where[i]
+        q, have, fn = queue[e], seen[e], t["fn"] if e == t["eng"] else t["alt"][2]
         need = {}
-        for d, result in t["deps"].items():
-            if ts[d]["kind"] in ("send", "dma"):
-                continue
-            s, v = mark[d]
-            need[s] = max(need.get(s, 0), v)
+        for d in t["deps"]:
+            if d in mark:
+                s, v = mark[d]
+                need[s] = max(need.get(s, 0), v)
         for s, v in sorted(need.items()):
             if have.get(s, 0) < v:
                 q.wait_ge(T.sem[s], v)
                 have[s] = v
-        for d, result in t["deps"].items():
-            if d in known:
-                for s, v in known[d].items():
-                    have[s] = max(have.get(s, 0), v)
-        k = dict(have)
+        for d in t["deps"]:
+            for s, v in known.get(d, {}).items():
+                have[s] = max(have.get(s, 0), v)
         if t["kind"] == "op":
-            t["fn"](q).then_inc(T.sem[mark[i][0]], 1)
-            k[mark[i][0]] = max(k.get(mark[i][0], 0), mark[i][1])
+            fn(q).then_inc(T.sem[mark[i][0]], 1)
+            known[i] = dict(have)
+            known[i][mark[i][0]] = max(have.get(mark[i][0], 0), mark[i][1])
         elif t["kind"] == "dma":
-            t["fn"](q).then_inc(T.sem[t["sem"]], 16)
+            fn(q).then_inc(T.sem[t["sem"]], 16)
         else:
-            t["fn"](q)
-        if t["kind"] == "op":
-            known[i] = k
+            fn(q)
     return count
 
 
@@ -314,27 +423,18 @@ def build(P, g, core, T, topo):
     rank = T.rank_of(core)
     n = len(T.cores)
 
-    def L(name, w=20, a=0):
+    def L(name, w=NB):
         i = LISTS.index(name)
-        return T.sml[:, 32 * i + a:32 * i + a + w]
+        return T.sml[:, 32 * i:32 * i + w]
 
-    def cf(name, i=0, w=1):
-        return T.cf[:, COLS[name] + i:COLS[name] + i + w]
-
-    def cn(i, w=1):
-        return T.cn[:, i:i + w]
+    def cf(name, i=0, w=1, step=1):
+        return T.cf[:, COLS[name] + i:COLS[name] + i + w * step:step]
 
     def V(dur, fn, reads, writes):
         return task(P, "v", dur, fn, reads, writes)
 
-    def S(dur, fn, reads, writes):
-        return task(P, "s", dur, fn, reads, writes)
-
-    def E(dur, fn, reads, writes):
-        return task(P, "t", dur, fn, reads, writes)
-
-    def K(dur, fn, reads, writes, after=()):
-        return task(P, "g", dur, fn, reads, writes, after=after)
+    def K(dur, fn, reads, writes):
+        return task(P, "g", dur, fn, reads, writes)
 
     def ts(out, in_, s1, s2, op0, op1, reads, writes, dur=SMALL):
         if op1 is None:
@@ -347,21 +447,35 @@ def build(P, g, core, T, topo):
     def cp(out, in_, reads, writes, dur=SMALL):
         return V(dur, lambda q: q.tensor_copy(out, in_), reads, writes)
 
-    def act(out, in_, reads, writes, dur=ROW, **kw):
-        f = AF.Identity if "bias" in kw and not isinstance(kw["bias"], float) else AF.Copy
-        return S(dur, lambda q: q.activation(out, in_, f, **kw), reads, writes)
+    def act(out, in_, reads, writes, dur=ROW, scale=None, bias=None, short=False, only=False):
+        kw = {k: x for k, x in (("scale", scale), ("bias", bias)) if x is not None}
+        f = AF.Copy if bias is None or isinstance(bias, float) else AF.Identity
 
-    def every16(b):
-        return T[b][:, 15:C:16]
+        def on_v(q):
+            if scale is None and bias is None:
+                return q.tensor_copy(out, in_)
+            if bias is None:
+                return q.tensor_scalar(out, in_, scale, None, A.mult)
+            if scale is None:
+                return q.tensor_scalar(out, in_, bias, None, A.add)
+            return q.tensor_scalar(out, in_, scale, bias, A.mult, A.add)
+        w = dur[1] if isinstance(dur, tuple) else dur / 2 if short else dur
+        return task(P, "s", dur, lambda q: q.activation(out, in_, f, **kw), reads, writes, alt=None if only else ("v", w, on_v))
+
+    def every(b, k):
+        return T[b][:, k:C:16]
 
     def at(b, a=0):
         return T[b][:, C * a:C * a + C]
 
     def by(b, l, a=0):
-        return at(b, a).indirect(T[l][:, 0:20])
+        return at(b, a).indirect(T[l][:, 0:NB])
 
-    def load(q, name, fn, writes, latency, after=()):
-        k = task(P, q, 0.07, fn, [], [], "dma", "ld_" + name, 16, after=after)
+    def mid(b):
+        return T[b][:, 16:16 + C]
+
+    def load(q, name, out, in_, writes, latency, after=()):
+        k = task(P, q, 0.07, lambda q: q.dma_start(out, in_), [], [], "dma", "ld_" + name, 16, after=after)
         return task(P, "net", latency, None, [], writes, "land", "ld_" + name, 16, after=[k])
 
     def move(name, out, in_, reads, writes, add=False):
@@ -369,181 +483,142 @@ def build(P, g, core, T, topo):
             k = task(P, "g", 1.0, lambda q: q.dma_start(out, in_, accum_op=A.add), reads, writes, "dma", "ld_" + name, 16)
         else:
             k = task(P, "y", 0.07, lambda q: q.dma_start(out, in_), reads, writes, "dma", "ld_" + name, 16)
-        task(P, "net", 2.2, None, reads, writes, "land", "ld_" + name, 16, after=[k])
+        task(P, "net", 2.8 if add else 2.2, None, reads, writes, "land", "ld_" + name, 16, after=[k])
 
-    k = load("s", "nx", lambda q: q.dma_start(T.nxi[:], T.nx[:]), ["nxi"], 2.0)
-    k = load("s", "u", lambda q: q.dma_start(T.ut[:], T.u[:]), ["ut"], 2.4, [k - 1])
-    load("s", "mt", lambda q: q.dma_start(T.mti[:], T.mt[:]), ["mti"], 2.4, [k - 1])
-    k = load("y", "x", lambda q: q.dma_start(T.x0[:], T.x[:]), ["x0"], 3.0)
-    load("y", "wc", lambda q: q.dma_start(T.wq[:].bitcast(dt.uint8), T.wc[:]), ["wq"], 3.0, [k])
-    load("y", "ws", lambda q: q.dma_start(T.wp[:], T.ws[:]), ["wp"], 3.0, [k])
-    load("y", "v", lambda q: q.dma_start(T.vt[:], T.v[:]), ["vt"], 3.0, [k])
+    k = load("y", "nx", T.nxi[:], T.nx[:], ["nxi"], 2.0)
+    j = load("s", "u", T.ut[:], T.u[:], ["ut"], 2.4, [K(0.19, lambda q: q.iota(T.pi[:], [[0, 32]], 0, 1), [], ["pi"])])
+    load("s", "mt", T.mti[:], T.mt[:], ["mti"], 2.4, [j - 1])
+    k = load("y", "x", T.x0[:], T.x[:], ["x0"], 3.0, [k - 1])
+    load("y", "wc", T.wq[:].bitcast(dt.uint8), T.wc[:], ["wq"], 3.0, [k])
+    load("y", "ws", T.wp[:], T.ws[:], ["wp"], 3.0, [k])
+    load("y", "v", T.vt[:], T.v[:], ["vt"], 3.0, [k])
 
-    k = K(0.19, lambda q: q.iota(T.pi[:], [[0, 32]], 0, 1), [], ["pi"])
-    k = K(0.16, lambda q: q.iota(T.ji[:], [[1, 16]], 0, -1), [], ["ji"], [k])
-    k = K(0.19, lambda q: q.iota(T.ci[:], [[16, 32]], 0, 0), [], ["ci"], [k])
-    K(0.67, lambda q: q.iota(T.idr[:], [[1, C]], -160, 0, allow_small_or_imprecise_dtypes=True), [], ["idr"], [k])
-    K(1.1, lambda q: q.iota(T.one[:], [[0, 528]], 1, 0, allow_small_or_imprecise_dtypes=True), ["idr"], ["one"])
+    K(0.16, lambda q: q.iota(T.ji[:], [[1, 16]], 0, -1), [], ["ji"])
+    K(0.67, lambda q: q.iota(T.idr[:], [[1, C]], -160, 0, allow_small_or_imprecise_dtypes=True), [], ["idr"])
+    K(0.19, lambda q: q.iota(T.ci[:], [[16, 32]], 0, 0), [], ["ci"])
+    for k in range(5):
+        K(0.14, lambda q, k=k: q.iota(T.sh[:, 2 * k:2 * k + 2], [[-(16 >> k), 2]], 127 * (16 >> k), -(16 >> k)), [], [("sh", k, k + 1)])
+    K(0.17, lambda q: q.iota(T.c32[:], [[32, NB // 2], [0, 2]], -160, 0), [], ["c32"])
+    K(1.1, lambda q: q.iota(T.one[:], [[0, 528]], 1, 0, allow_small_or_imprecise_dtypes=True), [], ["one"])
     K(1.1, lambda q: q.affine_select(T.big[:], T.one[:], [[-1, 528]], A.is_equal, 0.0, 3, 4), ["one"], ["big"])
     ts(T.pa[:], T.pi[:], 15, None, A.bitwise_and, None, ["pi"], ["pa"])
     ts(T.dg[:], T.ji[:], 15, None, A.bitwise_and, None, ["ji"], ["dg"])
     ts(T.t1[:], T.dg[:], 1.0, 320.0, A.is_equal, A.mult, ["dg"], ["t1"])
     ts(T.t2[:], T.dg[:], 0.0, -16384.0, A.is_equal, A.mult, ["dg"], ["t2"])
     tt(T.w16[:], T.t1[:], T.t2[:], A.add, ["t1", "t2"], ["w16"])
-    cp(T.so[:], T.pa[:, 0:20], ["pa"], ["so"])
-    act(T.wt[:], T.w16[:].indirect(T.so[:]), ["w16", "so"], ["wt"], GATHER)
-    tt(L("cw", 32), T.pa[:], T.ci[:], A.add, ["pa", "ci"], ["cw"])
-    act(L("c320", 32), L("cw", 32), ["cw"], ["c320"], SMALL, bias=-640.0)
+    cp(T.so[:], T.pa[:, 0:NB], ["pa"], ["so"])
+    act(T.wt[:], T.w16[:].indirect(T.so[:]), ["w16", "so"], ["wt"], gat())
+    tt(L("cw"), T.pa[:, 0:NB], T.ci[:, 0:NB], A.add, ["pa", "ci"], ["cw"])
     cp(T.uo[:], T.ci[:, 0:8], ["ci"], ["uo"])
     row = T.pa[:, 0:1]
     ts(cf("e15"), row, 15.0, None, A.is_equal, None, ["pa"], ["e15"])
-    ts(cf("col"), cf("e15"), 320.0, -160.0, A.mult, A.add, ["e15"], ["col"])
-    for b in ("fw0", "fw1"):
-        act(at(b, 0), T.idr[:], ["idr"], [(b, 0, 1)])
-    for b in ("n1", "n2", "e1", "e2"):
-        for a in sorted({0, C + 16} if b == "e1" else {PW * h + k for h in range(NH) for k in (0, W + 16)}):
+    ts(cf("pl"), row, 8.0, None, A.is_lt, None, ["pa"], ["pl"])
+    for name, a, b in (("col", 320.0, -160.0), ("nc", -320.0, 160.0), ("f0", 320.0, -320.0), ("a1", -1.0, 1.0), ("b1", -2.0, 1.0)):
+        act(cf(name), cf("e15"), ["e15"], [name], SMALL, scale=a, bias=b)
+    for b in ("n1", "e1"):
+        for a in (0, C + 16):
             act(T[b][:, a:a + 16], T.w16[:], ["w16"], [(b, 8 + a / 1024, 8 + (a + 1) / 1024)], SMALL, scale=0.0)
+    V(0.25, lambda q: q.memset(T.yy[:], 0.0), [], ["yy"])
     for b in range(4):
         V(0.16, lambda q, b=b: q.quantize_mx(T.eq[:, 128 * b:128 * b + 128], T.ep[:, 128 * b:128 * b + 128], T.big[:, 3 - b:515 - b]),
           ["big"], [("eq", b, b + 1), ("ep", b, b + 1)])
 
-    for k in range(4):
-        V(SMALL, lambda q, k=k: q.memset(cf("pw", k), 2.0 ** (4 - k)), [], [("pow", k, k + 1)])
-    ts(cf("j0"), row, -1.0, 15.0, A.mult, A.add, ["pa"], ["j0"])
-    ts(cf("j1"), cf("j0"), -1.0, 0.0, A.add, A.max, ["j0"], ["j1"])
-    ts(cn(2), row, 1, None, A.bitwise_and, None, ["pa"], ["c2"])
-    cp(cf("od"), cn(2), ["c2"], ["od"])
-    ts(cf("j2"), cf("j1"), cf("od"), 0.0, A.subtract, A.max, ["j1", "od"], ["j2"])
-    ts(cn(16, 4), cf("pw", 0, 4), cf("j0"), None, A.mult, None, ["pow", "j0"], [("nk", 0, 1)])
-    ts(cn(20, 2), cf("pw", 2, 2), cf("j1"), None, A.mult, None, ["pow", "j1"], [("nk", 1, 2)])
-    ts(cn(22, 3), cf("pw", 0, 3), cf("j2"), 0.5, A.mult, A.mult, ["pow", "j2"], [("nk", 2, 3)])
-    ts(T.bits[:, 0:9], cn(16, 9), 4, 1, A.arith_shift_right, A.bitwise_and, ["nk"], ["bits"])
-    cp(cf("sc", 0, 9), T.bits[:, 0:9], ["bits"], ["sc"])
-    act(cf("ko"), cf("od"), ["od"], ["ko"], SMALL, scale=KEY)
-    act(cf("kb", 0, 3), cf("sc", 0, 3), ["sc"], [("kb", 0, 1)], SMALL, scale=0.0)
-    ts(cf("kb", 3), row, 0.0, BIG, A.is_equal, A.mult, ["pa"], [("kb", 3, 4)])
-    act(cf("kb", 4, 2), cf("sc", 4, 2), ["sc"], [("kb", 1, 2)], SMALL, scale=KEY)
-    act(cf("kb", 6, 3), cf("sc", 6, 3), ["sc", "ko"], [("kb", 2, 3)], SMALL, scale=cf("ko"))
-    act(cf("nb", 0, 9), cf("sc", 0, 9), ["sc"], ["nb"], SMALL, scale=BIG, bias=-BIG)
-    tt(cf("bi", 0, 9), cf("kb", 0, 9), cf("nb", 0, 9), A.add, ["kb", "nb"], ["bi"])
-    V(SMALL, lambda q: q.tensor_reduce(cf("k2"), cf("kb", 6, 3), AxisListType.X, A.add, negate=True), ["kb"], ["k2"])
-    V(SMALL, lambda q: q.tensor_reduce(cf("k1"), cf("kb", 4, 2), AxisListType.X, A.add, negate=True), ["kb"], ["k1"])
-    tt(cf("a2"), cf("od"), cf("e15"), A.subtract, ["od", "e15"], ["a2"])
-    tt(cf("b2"), cf("e15"), cf("a2"), A.subtract, ["e15", "a2"], ["b2"])
-    if OPT["sbd"]:
-        act(T.s0[:], T.idr[:], ["idr", "a2"], ["s0"], scale=cf("a2"))
-    else:
-        ts(T.ia[:], T.idr[:], cf("a2"), None, A.mult, None, ["idr", "a2"], ["ia"], HALF)
-    ts(T.ic[:], T.idr[:], cf("b2"), None, A.mult, None, ["idr", "b2"], ["ic"], HALF)
-    ts(cn(8, 2), L("cw", 2), NB - 1.0, None, A.min, None, ["cw"], ["c8"])
-    ts(cn(10, 2), T.pi[:, 0:2], 4, 1, A.arith_shift_right, A.bitwise_and, ["pi"], ["c10"])
-    tt(cn(12, 2), cn(8, 2), cn(10, 2), A.add, ["c8", "c10"], ["c12"])
-    ts(cn(14, 2), cn(12, 2), 1, None, A.bitwise_and, None, ["c12"], ["c14"])
-    ts(cn(6, 2), cn(14, 2), NB + 1.0, None, A.mult, None, ["c14"], ["c6"])
-    tt(cn(26, 2), cn(8, 2), cn(6, 2), A.add, ["c8", "c6"], ["c26"])
-    for i, (a, b) in enumerate([(16.0, 0.0), (16.0, 15.0), (8.0, 7.0)]):
-        ts(T.pick[:, 2 * i:2 * i + 2], cn(26, 2), a, b, A.mult, A.add, ["c26"], [("pick", i, i + 1)])
-
-    def turned(b, h, k=1):
-        return T[b][:, TW // k * h:TW // k * (h + 1)]
-
-    def picked(b, i, h, k=1):
-        return turned(b, h, k).indirect(T.pick[:, 2 * i:2 * i + KP])
+    ts(T.bits[:], T.sh[:], 4, 1, A.arith_shift_right, A.bitwise_and, ["sh"], ["bits"])
+    cp(cf("bt", 0, 10), T.bits[:], ["bits"], ["bt"])
+    act(cf("sc", 0, 4, 3), cf("bt", 0, 4, 2), ["bt"], [("sc", 0, 1)], SMALL)
+    act(cf("sc", 1, 4, 3), cf("bt", 1, 4, 2), ["bt", "a1"], [("sc", 1, 2)], SMALL, scale=cf("a1"))
+    tt(cf("nk", 0, 3), cf("bt", 0, 3, 2), cf("bt", 1, 3, 2), A.subtract, ["bt"], ["nk"])
+    act(cf("nk", 0, 3), cf("nk", 0, 3), ["nk", "pl"], ["nk"], SMALL, scale=cf("pl"))
+    tt(cf("sc", 2, 3, 3), cf("nk", 0, 3), cf("bt", 1, 3, 2), A.add, ["bt", "nk"], [("sc", 2, 3)])
+    act(cf("bi", 0, 3, 3), cf("bt", 0, 3, 2), ["bt"], [("bi", 0, 0.5)], SMALL, scale=BIG, bias=-BIG)
+    ts(cf("e0"), row, 0.0, -BIG, A.not_equal, A.mult, ["pa"], ["e0"])
+    act(cf("bi", 9), cf("bt", 6), ["bt", "e0"], [("bi", 0.5, 1)], SMALL, scale=BIG, bias=cf("e0"))
+    act(cf("bi", 7, 2, 3), cf("sc", 7, 2, 3), [("sc", 1, 2)], [("bi", 1, 2)], SMALL, scale=5 * KEY, bias=-4 * KEY)
+    act(cf("k1"), cf("sc", 7), [("sc", 1, 2)], ["k1"], SMALL, scale=-KEY)
+    act(cf("k1"), cf("sc", 10), [("sc", 1, 2), "k1"], ["k1"], SMALL, scale=-KEY, bias=cf("k1"))
+    act(cf("lo"), cf("pl"), ["pl"], ["lo"], SMALL, scale=BIG, bias=-BIG)
+    act(cf("hi"), cf("pl"), ["pl"], ["hi"], SMALL, scale=-BIG, bias=BIG)
+    act(cf("hj"), cf("pl"), ["pl", "hi"], ["hj"], SMALL, scale=KEY * HIGH, bias=cf("hi"))
+    act(cf("bi", 2, 3, 3), cf("sc", 2, 3, 3), [("sc", 2, 3), "hj", "lo"], [("bi", 2, 3)], SMALL, scale=cf("hj"), bias=cf("lo"))
+    V(SMALL, lambda q: q.tensor_reduce(cf("nl"), cf("sc", 2, 3, 3), AxisListType.X, A.add), [("sc", 2, 3)], ["nl"])
+    act(cf("nl"), cf("nl"), ["nl"], ["nl"], SMALL, scale=-KEY, bias=-BASE)
+    act(cf("k2"), cf("nl"), ["nl", "pl"], ["k2"], SMALL, scale=cf("pl"))
+    act(cf("es"), cf("pl"), ["pl"], ["es"], SMALL, scale=1.0 / HIGH)
+    ts(cf("b2"), row, 7.0, -HIGH, A.is_lt, A.mult, ["pa"], ["b2"])
+    act(cf("c2"), cf("pl"), ["pl", "lo"], ["c2"], SMALL, scale=BASE * HIGH, bias=cf("lo"))
+    for b in ("dt", "ic"):
+        act(T[b][:], T.idr[:], ["idr", "b2", "c2"], [b], scale=cf("b2"), bias=cf("c2"))
+    act(T.gs[:], T.idr[:], ["idr", "b1"], ["gs"], scale=cf("b1"), short=True)
+    tt(cf("par"), cf("bt", 8), cf("bt", 0), A.not_equal, ["bt"], ["par"])
+    act(cf("p21"), cf("par"), ["par"], ["p21"], SMALL, scale=16.0 * (NB + 1), bias=15.0)
+    ts(L("pk", 2), L("cw", 2), NB - 1.0, 16.0, A.min, A.mult, ["cw"], ["pk"])
+    ts(T.pick[:, 0:2], L("pk", 2), cf("p21"), None, A.add, None, ["pk", "p21"], [("pick", 0, 1)])
+    act(cf("dd"), cf("bt", 8), ["bt"], ["dd"], SMALL, scale=30.0, bias=-95.0)
+    act(cf("dd"), cf("dd"), ["dd", "par"], ["dd"], SMALL, scale=cf("par"), bias=96.0)
+    ts(T.pick[:, 2:4], L("cw", 2), NB - 1.0, cf("dd"), A.min, A.add, ["cw", "dd"], [("pick", 1, 2)])
+    ts(T.pi[:, 0:NB], T.pi[:, 0:NB], 31, None, A.bitwise_and, None, ["pi"], ["pi"])
+    tt(L("ct"), T.pi[:, 0:NB], T.c32[:], A.add, ["pi", "c32"], ["ct"])
 
     V(0.16, lambda q: q.quantize_mx(T.uq[:], T.up[:], T.ut[:]), ["ut"], ["uq", "up"])
-    cp(T.uqr[:].bitcast(dt.uint32), T.uq[:].bitcast(dt.uint32).indirect(T.uo[:]), ["uq", "uo"], ["uqr"], 0.3)
-    (cp if OPT["upv"] else act)(T.upr[:], T.up[:].indirect(T.uo[:]), ["up", "uo"], ["upr"], 0.3)
+    cp(T.uqr[:].bitcast(dt.uint32), T.uq[:].bitcast(dt.uint32).indirect(T.uo[:]), ["uq", "uo"], ["uqr"], gat(128))
+    act(T.upr[:], T.up[:].indirect(T.uo[:]), ["up", "uo"], ["upr"], gat(128))
     V(0.16, lambda q: q.quantize_mx(T.vq[:], T.vp[:], T.vt[:]), ["vt"], ["vq", "vp"])
 
     cp(T.l0[:], T.nxi[:], ["nxi"], ["l0"])
-    cp(L("bd"), T.mti[:], ["mti"], ["bd"])
-    tt(L("be"), L("bd"), L("cw"), A.min, ["bd", "cw"], ["be"])
-    tt(L("bf"), L("bd"), L("cw"), A.max, ["bd", "cw"], ["bf"])
-    cp(T.lo16[:], L("be"), ["be"], ["lo16"])
-    cp(T.hi16[:], L("bf"), ["bf"], ["hi16"])
     cp(T.mt16[:], T.mti[:], ["mti"], ["mt16"])
-    cp(L("fl"), T.nxi[:], ["nxi"], ["fl"])
-    act(cf("f0"), cf("col"), ["col"], ["f0"], SMALL, bias=-160.0)
-    act(cf("nc"), cf("col"), ["col"], ["nc"], SMALL, scale=-1.0)
+    tt(L("dm"), T.mti[:], L("cw"), A.subtract, ["mti", "cw"], ["dm"])
+    act(L("bf"), L("dm"), ["dm", "f0"], ["bf"], SMALL, scale=cf("f0"))
+    tt(L("dc"), L("bf"), L("cw"), A.add, ["bf", "cw"], ["dc"])
+    act(T.nid[:], T.idr[:], ["idr"], ["nid"], scale=-1.0, short=True)
+    act(T.sw[:], by("idr", "mt16"), ["mt16", "idr"], ["sw"], gat())
+    move("sg", T.sw[:], T.nid[:], ["nid"], ["sw"], True)
+    task(P, "s", ROW, lambda q: q.activation(T.sg[:], T.sw[:], AF.Sign), ["sw"], ["sg"])
 
     def weighted(dst, src, a=0):
         V(HALF, lambda q: q.tensor_tensor_scan(T[dst][:], T.wt[:], at(src, a), 0.0, A.add, A.max), ["wt", (src, a, a + 1)], [dst])
 
-    def listed(l, src, tmp="scn", a=0):
-        weighted(tmp, src, a)
-        if OPT["ls"] and tmp == "scn":
-            act(T[l][:], every16(tmp), [tmp, "col"], [l], 0.1, bias=cf("col"))
-        else:
-            ts(T[l][:], every16(tmp), cf("col"), None, A.add, None, [tmp, "col"], [l])
-
-    def powers(src, later):
-        a = 1
-        for k, (dst, b) in enumerate([("fa", 0), ("fa", 1), ("ft", 1), ("ft", 2)]):
-            (cp if k in OPT["pv"] and later else act)(at(dst, b), by(src, "l%d" % k, a), [(src, a, a + 1), "l%d" % k], [(dst, b, b + 1), "F%d" % (k + 1)], GATHER)
-            listed("l%d" % (k + 1), dst, "scn", b)
+    def powers(f0):
+        act(T[f0][:], by("idr", "l0"), ["idr", "l0"], [f0], gat(), scale=HIGH)
+        src, a = f0, 0
+        for k, (dst, b) in enumerate([("fa", 0), ("fa", 1), ("ft", 1), ("ft", 2), ("ft", 4)]):
+            act(at(dst, b), by(src, "l%d" % k, a), [(src, a, a + 1), "l%d" % k], [(dst, b, b + 1)], gat(), scale=None if k else 1.0 / HIGH)
+            weighted("scn", dst, b)
+            act(T["l%d" % (k + 1)][:], every("scn", 15), ["scn", "col"], ["l%d" % (k + 1)], 0.1, bias=cf("col"))
             src, a = dst, b
 
-    def steps(name, src, levels, first, end=None):
+    def steps(name, t, src, levels, first, end=None):
         for i, k in enumerate(levels):
-            w, dst = "m%sw" % name, "m%s%d" % (name, i % 2)
-            if dst == src:
-                dst = "m%s%d" % (name, (i + 1) % 2)
-            own = name + str(k) in OPT["own"]
-            if k >= first[0]:
-                c = first[1] + k - first[0]
-                if k == 6:
-                    k = 5
-                    act(at(w), by(src, "l5"), [src, "sc", "bi", "l5"], [w], GATHER, scale=cf("sc", c), bias=cf("bi", c))
-                elif own:
-                    ts(at(w), at(src), cf("sc", c), cf("bi", c), A.mult, A.add, [src, "sc", "bi"], [w], ROW)
-                else:
-                    act(at(w), at(src), [src, "sc", "bi"], [w], scale=cf("sc", c), bias=cf("bi", c))
-            elif i == 0:
-                w = "sb"
-            elif own:
-                cp(at(w), at(src), [src], [w], ROW)
+            w, dst = "m%s%s" % (name, "wx"[i % 2]), "m%s%d" % (name, i % 2)
+            c = 3 * (first[1] + k - first[0]) + t
+            mask = {"scale": cf("sc", c), "bias": cf("bi", c)} if k >= first[0] else {}
+            reads = [src] + [("sc", t, t + 1), ("bi", t, t + 1)] * bool(mask)
+            if k == 6:
+                k = 5
+                act(at(w), by(src, "l5"), reads + ["l5"], [w], gat(), **mask)
+            elif k or mask:
+                act(at(w), at(src), reads, [w], **mask)
             else:
-                act(at(w), at(src), [src], [w])
+                w = "sb"
             out, reg = end if end and i == len(levels) - 1 else (at(dst), dst)
-            tt(out, by(w, "l%d" % k), at(src), A.max, [w, SA if src == "sa" else src, "l%d" % k], [reg], GATHER)
+            tt(out, by(w, "l%d" % k), at(src), A.max, [w, src, "l%d" % k], [reg], gat())
             src = dst
         return src
 
-    def turn(dst, src, h, a):
-        reads = [(src, 2 * h, 2 * h + 2), (src, 8, 9)]
-        V(HALF * W / C, lambda q: q.transpose(T[dst][:, TW * h:TW * h + W], T[src][:, a + 16:a + 16 + W]), reads, [(dst, 2 * h, 2 * h + 1)])
-        V(HALF * PW / C, lambda q: q.transpose(T[dst][:, TW * h + W:TW * h + TW], T[src][:, a:a + PW]), reads, [(dst, 2 * h + 1, 2 * h + 2)])
+    def turn(dst, src):
+        V(HALF, lambda q: q.transpose(T[dst][:, 0:C], mid(src)), [(src, 0, 4)], [(dst, 0, 1)])
+        V(HALF * PW / C, lambda q: q.transpose(T[dst][:, C:TW], T[src][:]), [src], [(dst, 1, 2)])
 
-    def chain(out, n, e, h, k):
-        for i, (a, b) in enumerate([(TW * h, TW * h + W), (TW * h + W, TW * h + TW)]):
-            V(max(SMALL, HALF * (b - a) / C / k), lambda q, a=a, b=b: q.tensor_tensor_scan(
-                T[out][:, a // k:b // k], T[n][:, a:b:k], T[e][:, a + k - 1:b:k], 0.0, A.mult, A.add),
-              [(n, 2 * h + i, 2 * h + i + 1), (e, 2 * h + i, 2 * h + i + 1)], [(out, 2 * h + i, 2 * h + i + 1)])
-
-    def mid(b, h):
-        return T[b][:, PW * h + 16:PW * h + 16 + W]
-
-    act(cf("ev"), cf("od"), ["od"], ["ev"], SMALL, scale=-1.0, bias=1.0)
-    act(cf("a1"), cf("e15"), ["e15"], ["a1"], SMALL, scale=-1.0, bias=1.0)
-    act(cf("b1"), cf("e15"), ["e15"], ["b1"], SMALL, scale=-2.0, bias=1.0)
-    act(T.gs[:], T.idr[:], ["idr", "b1"], ["gs"], scale=cf("b1"))
+    def chain(out, n, e, reads, writes, w=C):
+        V(HALF * w / C, lambda q: q.tensor_tensor_scan(out, n, e, 0.0, A.mult, A.add), reads, writes)
 
     def places(r):
-        act(at("ft", 4), by("ft", "l4", 2), [("ft", 2, 3), "l4"] + [("sb", 0, OPT["f5"])] * (r > 0 and OPT["f5"] > 0), [("ft", 4, 5)], GATHER)
-        listed("l5", "ft", "scn", 4)
-        act(at("ft", 3), by("ft", "l3", 2), [("ft", 2, 3), "l3"], [("ft", 3, 4)], GATHER)
+        act(at("ft", 3), by("ft", "l3", 2), [("ft", 2, 3), "l3"], [("ft", 3, 4)], gat())
         for i, (b, a, step) in enumerate([(1, 1, 4), (2, 0, 4), (3, 3, 8), (3, 7, 16)]):
             move("g%d%d" % (i, r), T.gs[a:128:step, :], T.ft[a:128:step, C * b:C * b + C], [("ft", b, b + 1)], [("gs", a, a + 1)])
-        if OPT["early"]:
-            act(T.mew[:], T.gs[:], ["gs", "a1", "k1"], ["mew"], scale=cf("a1"), bias=cf("k1"))
-            tt(at("me1"), by("mew", "l3"), T.gs[:], A.subtract, ["mew", "gs", "l3"], ["me1"], GATHER)
-            steps("e", "me1", [5, 6], (5, 4), (T.e1[:, 16:C + 16], ("e1", 0, 4)))
-        else:
-            e = steps("e", "gs", [5, 6], (5, 4))
-            act(T.mew[:], at(e), [e, "a1"], ["mew"], scale=cf("a1"))
-            tt(T.e1[:, 16:C + 16], by("mew", "l3"), at(e), A.subtract, ["mew", e, "l3"], [("e1", 0, 4)], GATHER)
-        for h in range(NH):
-            turn("te1", "e1", h, W * h)
+        act(T.mex[:], T.gs[:], ["gs", "a1", "k1"], ["mex"], scale=cf("a1"), bias=cf("k1"))
+        tt(T.me1[:], by("mex", "l3"), T.gs[:], A.subtract, ["mex", "gs", "l3"], ["me1"], gat())
+        steps("e", 1, "me1", [5, 6], (5, 2), (mid("e1"), ("e1", 0, 4)))
+        turn("te1", "e1")
 
     sent = [0]
 
@@ -557,157 +632,143 @@ def build(P, g, core, T, topo):
             sent[0] += len(topo.engines(core, dst))
         return task(P, "net", latency, None, [], land, "land", sem, len(topo.engines(src, core)) * len(pairs), after=ids)
 
+    def home(r, k, a, b, op, reads):
+        y, lp, al, o = YW * k, "lp%d" % r, "al%d" % r, B0 * k
+        tt(T.yy[:, y + 96:y + 96 + NB], a, b, op, reads, [("yy", y + 96, y + 128)])
+        V(SMALL, lambda q: q.transpose(T.yy[:, y + 176:y + 208], T.yy[:, y + 96:y + 128]), [("yy", y + 96, y + 128)], [("yy", y + 176, y + 208)])
+        V(SMALL, lambda q: q.transpose(T.yy[:, y:y + 64], T.yy[:, y + 160:y + 224]), [("yy", y + 160, y + 224)], [("yy", y, y + 64)])
+        ts(T[lp][:, o:o + 32], T.yy[:, y:y + 128].indirect(T.pick[:, 2:4]), 160.0, None, A.add, None, [("yy", y, y + 128), ("pick", 1, 2)],
+           [(lp, o, o + 32)], 0.12)
+        send(r, [(T[al][:, o:o + NB], T[lp][:, o:o + NB], (lp, o, o + NB))], "a%s%d" % ("pb"[k], r), [(al, o, o + NB)], 2.6)
+
     def bank(out, b, w=C):
         return T[out][:, BANK * b:BANK * b + w]
 
-    def behind(name, b, r):
-        k = OPT["pace"].get(name + str(b))
-        return ["F%d" % k] if k and r < ROUNDS - 1 else []
-
     def parts(name):
-        return [(0, OPT["cut"]), (OPT["cut"], C)] if name in OPT["halves"] else [(0, C)]
+        return enumerate([(0, OPT[name]), (OPT[name], C)])
 
     def mm(out, b, wq, wp, a, xq, xp, unit, h=0, lo=0, hi=C):
         whole = hi - lo == C
-        E(0.02 + 0.33 * (hi - lo) / C, lambda q: q.matmul_mx(bank(out, b, hi - lo), T[wq][:, a:a + 128], T[wp][:, a:a + 128],
-                                                             T[xq][:, lo:hi], T[xp][:, lo:hi], True, True),
-          [(wq, unit, unit + 1), (wp, unit, unit + 1), xq if whole else (xq, h, h + 1), xp if whole else (xp, h, h + 1)], [(out, b, b + 1)])
+        task(P, "t", 0.02 + 0.33 * (hi - lo) / C,
+             lambda q: q.matmul_mx(bank(out, b, hi - lo), T[wq][:, a:a + 128], T[wp][:, a:a + 128], T[xq][:, lo:hi], T[xp][:, lo:hi], True, True),
+             [(wq, unit, unit + 1), (wp, unit, unit + 1), xq if whole else (xq, h, h + 1), xp if whole else (xp, h, h + 1)], [(out, b, b + 1)])
 
     def quantize(xq, xp, X, h, lo, hi):
         V(0.02 + 0.35 * (hi - lo) / C, lambda q: q.quantize_mx(T[xq][:, lo:hi], T[xp][:, lo:hi], T[X][:, 4 * lo:4 * hi]),
           [(X, 4 * h, 4 * h + 4)], [(xq, h, h + 1), (xp, h, h + 1)])
 
-    def add_by(out, win, l, other, h, lo, hi, k=1, late=()):
+    def look(win, l, a, b, lo, hi):
+        act(T.gp[:, C * b + lo:C * b + hi], at(win, b).indirect(T[l][:, a + lo // 16:a + hi // 16]),
+            [(win, b, b + 1), (l, a + lo // 16, a + hi // 16)], [("gp", b + lo / C, b + hi / C)], gat(hi - lo))
+
+    def add_by(out, win, l, other, h, lo, end, cut, xps=()):
         for b in range(4):
-            more = list(late) if b >= OPT["late"] else []
-            if other == "fo" and b in OPT["xps"]:
-                act(T.gp[:, C * b + lo:C * b + hi], at(win, b).indirect(T[l][:, lo // 16:hi // 16]), [(win, b, b + 1), l],
-                    [("gp", b + lo / C, b + hi / C)], 0.06 + (GATHER - 0.06) * (hi - lo) / C)
+            hi, written = end, [(out, 4 * h + b, 4 * h + b + 1)]
+            if b not in cut:
+                if h:
+                    continue
+                hi, written = C, written + [(out, 4 + b, 5 + b)]
+            if b in xps:
                 tt(T[out][:, 4 * lo + b:4 * hi:4], T.pu[:, BANK * b + lo:BANK * b + hi], T.gp[:, C * b + lo:C * b + hi], A.add,
-                   [("pu", b, b + 1), ("gp", b + lo / C, b + hi / C)] + more, [(out, 4 * h + b, 4 * h + b + 1)], ROW * (hi - lo) / C + 0.01)
+                   [("pu", b, b + 1), ("gp", b + lo / C, b + hi / C)], written, ROW * (hi - lo) / C + 0.01)
                 continue
-            tt(T[out][:, 4 * lo + b:4 * hi:4], T[win][:, k * C * b:k * C * (b + 1)].indirect(T[l][:, lo // 16:hi // 16]), T[other][:, C * b + lo:C * b + hi], A.add,
-               [(win, k * b, k * b + k), l, (other, b, b + 1)] + more, [(out, 4 * h + b, 4 * h + b + 1)], 0.06 + (GATHER - 0.06) * (hi - lo) / C)
+            tt(T[out][:, 4 * lo + b:4 * hi:4], at(win, b).indirect(T[l][:, B0 + lo // 16:B0 + hi // 16]), T[other][:, C * b + lo:C * b + hi], A.add,
+               [(win, b, b + 1), (l, B0 + lo // 16, B0 + hi // 16), (other, b + lo / C, b + hi / C)], written, gat(hi - lo))
 
     def store(e, out, in_, reads):
         k = task(P, e, 0.07, lambda q: q.dma_start(out, in_), reads, [], "dma", "st", 16)
         task(P, "net", 2.0, None, [], [], "land", "st", 16, after=[k])
 
-    act(at("fw0", 1), by("idr", "l0"), ["idr", "l0"], [("fw0", 1, 2)], GATHER)
+    powers("f00")
+    for h, (lo, hi) in parts("x"):
+        quantize("xq0", "xp0", "x0", h, lo, hi)
     for r in range(ROUNDS):
-        X, xq, xp, aq, ap = "x%d" % r, "xq%d" % r, "xp%d" % r, "aq%d" % r, "ap%d" % r
-        lp, lb, rp, rb = "lp%d" % r, "lb%d" % r, "rp%d" % r, "rb%d" % r
-        fw, fn = "fw%d" % (r % 2), "fw%d" % (1 - r % 2)
-        P["rounds"].append(len(P["tasks"]))
-        if r == 0:
-            powers(fw, False)
-        act(T["lf%d" % r][:], L("fl"), ["fl"], ["lf%d" % r], SMALL)
-        send(r, [(T[rb][:], T["lf%d" % r][:], "lf%d" % r)], "arb%d" % r, [rb], 2.6)
-        for h, (lo, hi) in enumerate(parts("x")):
-            if r == 0:
-                quantize(xq, xp, X, h, lo, hi)
-            w, last = ROW * (hi - lo) / C + 0.02, hi == C or r == 0 and OPT["r0v"]
+        xq, xp, aq, ap = "xq%d" % r, "xp%d" % r, "aq%d" % r, "ap%d" % r
+        lp, al, f0 = "lp%d" % r, "al%d" % r, "f0%d" % (r % 2)
+        xps = OPT["xps"] if r < ROUNDS - 1 else OPT["xpl"]
+        for h, (lo, hi) in parts("x"):
             mm("pw", 2 * h, "uqr", "upr", 0, xq, xp, 0, h, lo, hi)
-            (cp if last else act)(T.sa[:, lo:hi], bank("pw", 2 * h, hi - lo), [("pw", 2 * h, 2 * h + 1)], [("sa", lo / C, hi / C)], w)
-            k = 2 * h + 1 if last and not OPT["sbv"] else 2 * h
-            if k % 2:
-                mm("pw", k, "uqr", "upr", 0, xq, xp, 0, h, lo, hi)
-            (cp if last and OPT["sbv"] else act)(T.sb[:, lo:hi], bank("pw", k, hi - lo), [("pw", k, k + 1)] + behind("sb", h, 0 if r else ROUNDS), [("sb", h, h + 1)], w)
+            for b in ("sa", "sb"):
+                a = (T[b][:, lo:hi], bank("pw", 2 * h, hi - lo), [("pw", 2 * h, 2 * h + 1)], [(b, h, h + 1)], ROW * (hi - lo) / C + 0.02)
+                if h:
+                    cp(*a)
+                else:
+                    act(*a, only=True)
         send(r, [(T[aq][:].bitcast(dt.uint8), T[xq][:].bitcast(dt.uint8), xq), (T[ap][:], T[xp][:], xp)], "ax%d" % r, [aq, ap], 6.0)
         places(r)
-        coarse = steps("c", "sa", range(7), (3, 0))
-        act(at("sa", 1), by("sa", "l0"), [SA, "l0"], [("sa", 1, 2)], GATHER)
-        if OPT["sbd"]:
-            move("a%d" % r, T.s0[0:128:2, :], T.sa[0:128:2, 0:C], [SA], ["s0"])
-            tt(T.fs[:], by("s0", "l0"), T.ic[:], A.add, ["s0", "ic", "l0"], ["fs"], GATHER)
-        else:
-            tt(T.dt[:], by("ia", "l0"), T.ic[:], A.add, ["ia", "ic", "l0"], ["dt"], GATHER)
-            act(T.s0[:], at("sb"), ["sb", "ev"], ["s0"], scale=cf("ev"))
-            tt(T.fs[:], by("s0", "l0"), T.dt[:], A.add, ["s0", "dt", "l0"], ["fs"], GATHER)
-        fine = steps("f", "fs", range(3), (0, 6))
+        coarse = steps("c", 0, "sa", range(7), (3, 0))
+        if r:
+            move("b%d" % r, T.dt[:], T.ic[:], ["ic"], ["dt"])
+        move("a%d" % r, T.dt[:], T[f0][:], [f0], ["dt"], True)
+        tt(T.fs[:], by("sa", "l0"), T.dt[:], A.max, ["sa", "dt", "l0"], ["fs"], gat())
+        fine = steps("f", 2, "fs", range(3), (0, 0))
         for b in range(4):
-            if b not in OPT["xps"]:
+            if b not in xps:
                 mm("pu", b, "eq", "ep", 128 * b, xq, xp, b)
                 act(at("fo", b), bank("pu", b), [("pu", b, b + 1)], [("fo", b, b + 1)])
         for b in range(4):
             mm("pu", b, "eq", "ep", 128 * b, aq, ap, b)
-            act(at("fh", 2 * b), bank("pu", b), [("pu", b, b + 1)], [("fh", 2 * b, 2 * b + 1)], scale=0.5)
-            act(at("fh", 2 * b + 1), by("fh", rb, 2 * b), [("fh", 2 * b, 2 * b + 1), rb], [("fh", 2 * b + 1, 2 * b + 2)], GATHER)
-            if b in OPT["xps"]:
+            act(at("fh", b), bank("pu", b), [("pu", b, b + 1)], [("fh", b, b + 1)], scale=0.5)
+            if b in xps:
                 mm("pu", b, "eq", "ep", 128 * b, xq, xp, b)
-        for h in range(NH):
-            def R(b):
-                return (b, 2 * h, 2 * h + 2)
-
-            def H(name):
-                return L(name, 16 * KP, 16 * h)
-            lo, hi, a, b, lq = W * h, W * h + W, NB * h, NB * h + NB, T.lq[:, 16 * h:16 * h + NB]
-            tt(mid("n1", h), at(coarse).indirect(T.l0[:, a:b]), T.sa[:, lo:hi], A.is_le, [coarse, "l0", SA], [R("n1")], GP)
-            turn("tn1", "n1", h, PW * h)
-            chain("r1", "tn1", "te1", h, 1)
-            ts(T.lq[:, 16 * h:16 * h + 16 * KP], picked("r1", 1, h), 160.0, None, A.add, None, [R("r1"), "pick"], [R("lq")], 0.1)
-            tt(mid("n2", h), at(fine).indirect(lq), T.sa[:, lo:hi], A.is_le, [fine, R("lq"), SA], [R("n2")], GP)
-            act(mid("e2", h), at(fine).indirect(lq), [fine, R("lq"), "od", "k2"], [R("e2")], GP, scale=cf("od"), bias=cf("k2"))
-            turn("tn2", "n2", h, PW * h)
-            tt(H("hl"), picked("tn2", 0, h), L("c320", 16 * KP, a), A.mult, [R("tn2"), "pick", "c320"], [R("hl")], 0.1)
-            V(SMALL, lambda q, h=h: q.memset(T.tn2[:, TW * h:TW * h + TW:16], 0.0), [], [R("tn2")])
-            if OPT["hms"]:
-                act(H("hm"), H("hl"), [R("hl")], [R("hm")], SMALL, bias=160.0)
-            else:
-                ts(H("hm"), H("hl"), 160.0, None, A.add, None, [R("hl")], [R("hm")])
-            turn("te2", "e2", h, PW * h)
-            chain("r2", "tn2", "te2", h, 2)
-            tt(H("om"), picked("r2", 2, h, 2), H("hm"), A.min, [R("r2"), "pick", R("hm")], [R("om")], 0.1)
-            ts(T[lp][:, a:b], L("om", NB, 16 * h), 480.0, None, A.add, None, [R("om")], [(lp, a, b)])
-            ts(T[lp][:, 20 + a:20 + a + 16 * KP], picked("r2", 2, h, 2), 160.0, None, A.add, None, [R("r2"), "pick"], [(lp, 20 + a, 20 + a + 16 * KP)], 0.1)
-            (cp if OPT["brv"] else act)(T.br[:, lo:hi], T[fw][:].indirect(T[lp][:, a:b]), [fw, (lp, a, b)], [R("br")], GP)
-            V(max(SMALL, HALF / NH), lambda q, lo=lo, hi=hi: q.tensor_tensor_scan(T.bsn[:, lo:hi], T.wt[:, 0:W], T.br[:, lo:hi], 0.0, A.add, A.max),
-              ["wt", R("br")], [R("bsn")])
-            act(T[lb][:, a:b], T.bsn[:, lo + 15:hi:16], [R("bsn"), "col"], [R(lb)], 0.1, bias=cf("col"))
-        send(r, [(T[rp][:], T[lp][:, 0:40], lp)], "arp%d" % r, [rp], 2.6)
-        (cp if OPT["erv"] else act)(T.er[:], T.sa[:].indirect(T[lp][:, 0:20]), ["sa", (lp, 0, 20)], ["er"], GATHER)
-        (cp if OPT["ehv"] else act)(T.eh[:], by("er", "hi16"), ["er", "hi16"], ["eh"], GATHER)
-        tt(T.sw[:], by("er", "lo16"), T.eh[:], A.is_gt, ["er", "eh", "lo16"], ["sw"], GATHER)
+        tt(mid("n1"), by(coarse, "l0"), T.sa[:], A.is_le, [coarse, "l0", "sa"], [("n1", 0, 4)], gat())
+        turn("tn1", "n1")
+        for h, (a, b) in enumerate([(0, C), (C, TW)]):
+            chain(T.r1[:, a:b], T.tn1[:, a:b], T.te1[:, a:b], [("tn1", h, h + 1), ("te1", h, h + 1)], [("r1", h, h + 1)], b - a)
+        ts(T.lq[:], T.r1[:].indirect(T.pick[:, 0:2]), 160.0, None, A.add, None, ["r1", ("pick", 0, 1)], ["lq"], 0.1)
+        tt(T.n2[:], by(fine, "lq"), T.sa[:], A.is_le, [fine, "lq", "sa"], ["n2"], gat())
+        act(T.e2[:], by(fine, "lq"), [fine, "lq", "es", "k2"], ["e2"], gat(), scale=cf("es"), bias=cf("k2"))
+        for x in ("n2", "e2"):
+            V(HALF, lambda q, x=x: q.transpose(T["t" + x][:], T[x][:]), [x], ["t" + x])
+        for x, j in (("rp", 1), ("rb", 0)):
+            chain(T[x][:, 0:C - 7], T.tn2[:, 7:C], T.te2[:, j:C - 7 + j], ["tn2", "te2"], [x])
+        tt(L("ta"), every("tn2", 14), every("r1", 15), A.mult, ["tn2", ("r1", 0, 1)], ["ta"])
+        tt(L("ua"), every("r1", 15), L("ta"), A.subtract, [("r1", 0, 1), "ta"], ["ua"])
+        home(r, 0, every("rp", 7), L("ua"), A.add, ["rp", "ua"])
+        tt(L("tb"), every("tn2", 15), L("ct"), A.mult, ["tn2", "ct"], ["tb"])
+        tt(L("yb"), every("rb", 8), L("tb"), A.subtract, ["rb", "tb"], ["yb"])
+        home(r, 1, every("rb", 7), L("yb"), A.subtract, ["rb", "yb"])
+        tt(T.er[:], T.sa[:].indirect(T[lp][:, B0:B0 + NB]), T.sg[:], A.mult, ["sa", "sg", (lp, B0, B0 + NB)], ["er"], gat())
+        act(T.eh[:], T.er[:], ["er"], ["eh"], scale=-1.0)
+        tt(T.sw[:], by("er", "mt16"), T.eh[:], A.is_gt, ["er", "eh", "mt16"], ["sw"], gat())
         weighted("swn", "sw")
-        act(T.fm[:], by(fw, "mt16", 1), [(fw, 1, 2), "mt16"], ["fm"], GATHER)
-        weighted("fmn", "fm")
-        act(L("be"), L("fl"), ["fl", "nc"], ["be"], SMALL, bias=cf("nc"))
-        tt(L("dm"), every16("fmn"), L("be"), A.subtract, ["fmn", "be"], ["dm"])
-        act(L("bf"), L("dm"), ["dm", "f0"], ["bf"], SMALL, scale=cf("f0"))
-        tt(L("dc"), L("bf"), L("fl"), A.add, ["bf", "fl"], ["dc"])
-        tt(L("sx"), every16("swn"), L("dm"), A.mult, ["swn", "dm"], ["sx"])
-        tt(T.l0[:], L("sx"), L("dc"), A.add, ["sx", "dc"], ["l0"])
         if r < ROUNDS - 1:
-            tt(L("fl"), L("sx"), L("dc"), A.add, ["sx", "dc"], ["fl"])
-        if r < ROUNDS - 1:
-            (cp if OPT["f0v"] else act)(at(fn, 1), by("idr", "l0"), ["idr", "l0"], [(fn, 1, 2)], GATHER)
-            powers(fn, True)
+            act(T.fm[:], by(f0, "mt16"), [f0, "mt16"], ["fm"], gat(), scale=1.0 / HIGH)
+            weighted("fmn", "fm")
+            cp(L("fl"), T.l0[:], ["l0"], ["fl"])
+            act(L("be"), L("fl"), ["fl", "nc"], ["be"], SMALL, bias=cf("nc"))
+            tt(L("dn"), every("fmn", 15), L("be"), A.subtract, ["fmn", "be"], ["dn"])
+            act(L("bf"), L("dn"), ["dn", "f0"], ["bf"], SMALL, scale=cf("f0"))
+            tt(L("de"), L("bf"), L("fl"), A.add, ["bf", "fl"], ["de"])
+            tt(L("sx"), every("swn", 15), L("dn"), A.mult, ["swn", "dn"], ["sx"])
+            tt(T.l0[:], L("sx"), L("de"), A.add, ["sx", "de"], ["l0"])
+            powers("f0%d" % (1 - r % 2))
         else:
-            act(T.er[:], by("idr", "l0"), ["idr", "l0"], ["er"], GATHER, bias=160.0)
+            tt(L("sx"), every("swn", 15), L("dm"), A.mult, ["swn", "dm"], ["sx"])
+            tt(T.sig[:], L("sx"), L("dc"), A.add, ["sx", "dc"], ["sig"])
+            act(T.er[:], by(f0, "sig"), [f0, "sig"], ["er"], gat(), scale=1.0 / HIGH, bias=160.0)
             store("y", T.nf[:], T.er[0:128:16, :], ["er"])
         for b in range(4):
-            (cp if b in OPT["gpv"] else act)(at("gp", b), at("fh", 2 * b).indirect(T[rp][:, 20:40]), [("fh", 2 * b, 2 * b + 1), rp] + behind("gp", b, r),
-                                             [("gp", b, b + 1)], GATHER)
-        for h, (lo, hi) in enumerate(parts("z%d" % r)):
-            add_by("z", "fh", rp, "gp", h, lo, hi, 2)
+            for h, (lo, hi) in parts("z") if b in OPT["zg"] else [(0, (0, C))]:
+                look("fh", al, 0, b, lo, hi)
+        for h, (lo, hi) in parts("z"):
+            add_by("z", "fh", al, "gp", h, lo, hi, OPT["zs"])
             quantize("zq", "zp", "z", h, lo, hi)
-            ps = "pw"
             for b in range(4):
+                ps = "pu" if h and b not in xps else "pw"
                 mm(ps, b, "wq", "wp", 128 * b, "zq", "zp", b, h, lo, hi)
-                if b in OPT["hv"]:
-                    ts(T.h[:, C * b + lo:C * b + hi], bank(ps, b, hi - lo), 0.03125, None, A.mult, None, [(ps, b, b + 1)], [("h", b + lo / C, b + hi / C)], ROW * (hi - lo) / C)
-                    continue
-                act(T.h[:, C * b + lo:C * b + hi], bank(ps, b, hi - lo), [(ps, b, b + 1)] + behind("h", b, r), [("h", b + lo / C, b + hi / C)],
+                act(T.h[:, C * b + lo:C * b + hi], bank(ps, b, hi - lo), [(ps, b, b + 1)], [("h", b + lo / C, b + hi / C)],
                     ROW * (hi - lo) / C + 0.02, scale=0.03125)
-        for h, (lo, hi) in enumerate(parts("x")):
-            add_by("x%d" % (r + 1), "h", lb, "fo", h, lo, hi, 1, [("xq%d" % (r + 1), 0, 1)] * h)
+        for b in xps:
+            look("h", lp, B0, b, 0, C)
+        for h, (lo, hi) in parts("x"):
+            add_by("x%d" % (r + 1), "h", lp, "fo", h, lo, hi, OPT["xs"], xps)
             quantize("xq%d" % (r + 1), "xp%d" % (r + 1), "x%d" % (r + 1), h, lo, hi)
-    P["rounds"].append(len(P["tasks"]))
-    xq, xp, X = "xq%d" % ROUNDS, "xp%d" % ROUNDS, "x%d" % ROUNDS
-    for h, (lo, hi) in enumerate(parts("x")):
+    xq, xp = "xq%d" % ROUNDS, "xp%d" % ROUNDS
+    for h, (lo, hi) in parts("x"):
         store("y", T.oc[:, 4 * lo:4 * hi], T[xq][:, lo:hi].bitcast(dt.uint8), [(xq, h, h + 1)])
         mm("pw", h, "vq", "vp", 0, xq, xp, 0, h, lo, hi)
-        (cp if h or hi - lo == C else act)(T.eh[:, lo:hi], bank("pw", h, hi - lo), [("pw", h, h + 1)], [("eh", h, h + 1)], ROW * (hi - lo) / C)
+        act(T.eh[:, lo:hi], bank("pw", h, hi - lo), [("pw", h, h + 1)], [("eh", h, h + 1)], ROW * (hi - lo) / C)
         store("y", T.y[:, lo:hi], T.eh[:, lo:hi], [("eh", h, h + 1)])
     for k in range(4):
         store("y" if k % 2 else "s", T.osc[4 * k:4 * k + 4, :], T[xp][32 * k:32 * k + 4, :], [xp])

@@ -7,6 +7,8 @@ C = 320
 BANK = 512
 ROUNDS = 3
 BIG = 1e29
+OWN = 64
+ZC = C - OWN
 KEY = 1024.0
 HIGH = 2.0 ** 75
 BASE = 512.0
@@ -30,35 +32,39 @@ SCRATCH = {
     "vq": sb(128, "float8_e4m3fn_x4"), "vp": sb(128, "uint8"),
     "eq": sb(512, "float8_e4m3fn_x4"), "ep": sb(512, "uint8"),
     "one": sb(528, "bfloat16"), "big": sb(528, "bfloat16"),
-    "ji": sb(16, "int32"), "dg": sb(16, "int32"), "t1": sb(16, "bfloat16"), "t2": sb(16, "bfloat16"), "w16": sb(16, "bfloat16"),
-    "wt": sb(C, "bfloat16"), "idr": sb(C, "bfloat16"), "nid": sb(C, "bfloat16"), "ic": sb(C, "float32"), "sg": sb(C, "bfloat16"),
+    "ji": sb(16, "int32"), "t1": sb(32, "bfloat16"), "w16": sb(16, "bfloat16"),
+    "wt": sb(C, "bfloat16"), "idr": sb(C, "bfloat16"), "ic": sb(C, "float32"), "sg": sb(C, "bfloat16"),
     "gs": sb(C, "bfloat16"), "ft": sb(5 * C, "bfloat16"),
-    "pi": sb(32, "int32"), "pa": sb(32, "int32"), "ci": sb(32, "int32"), "c32": sb(NB, "int32"), "sh": sb(10, "int32"), "bits": sb(10, "int32"),
-    "uo": sb(8, "uint16"), "pick": sb(4, "uint16"),
+    "cq": sb(48, "float32"), "idk": sb(C, "float32"), "le": sb(64, "uint16"),
+    "pw0": sb(C, "float32"), "pw1": sb(C, "float32"), "pw2": sb(C, "float32"),
+    "pi": sb(48, "int32"), "pa": sb(32, "int32"), "ci": sb(32, "int32"), "sh": sb(10, "int32"), "bits": sb(10, "int32"),
+    "uo": sb(8, "uint16"), "pick": sb(6, "uint16"),
     "cf": sb(64, "float32"),
-    "mt16": sb(NB, "uint16"), "so": sb(NB, "uint16"), "lq": sb(32, "uint16"), "sig": sb(NB, "uint16"),
-    "sa": sb(C, "float32"), "sb": sb(C, "float32"), "fs": sb(C, "float32"), "dt": sb(C, "float32"),
+    "wd": sb(2 * C, "float32"), "d1": sb(C, "float32"),
+    "hq": sb(ROUNDS * C, "float8_e4m3fn_x4"), "hp": sb(ROUNDS * C, "uint8"),
+    "sa": sb(2 * C, "float32"), "sb": sb(C, "float32"), "fs": sb(C, "float32"), "dt": sb(C, "float32"),
     "n1": sb(PW, "bfloat16"), "e1": sb(PW, "float16"), "tn1": sb(TW, "bfloat16"), "te1": sb(TW, "float16"), "r1": sb(TW, "bfloat16"),
     "n2": sb(C, "bfloat16"), "e2": sb(C, "float16"), "tn2": sb(C, "bfloat16"), "te2": sb(C, "float16"),
-    "rb": sb(C, "bfloat16"), "rp": sb(C, "bfloat16"), "yy": sb(2 * YW, "bfloat16"),
+    "rb": sb(C, "float16"), "rp": sb(640, "bfloat16"), "yy": sb(224, "float32"),
     "f00": sb(C, "bfloat16"), "f01": sb(C, "bfloat16"), "fa": sb(2 * C, "bfloat16"), "fm": sb(C, "bfloat16"),
     "scn": sb(C, "float16"), "swn": sb(C, "float16"), "fmn": sb(C, "float16"),
     "er": sb(C, "float32"), "eh": sb(C, "float32"), "sw": sb(C, "bfloat16"),
     "fo": sb(4 * C, "bfloat16"), "fh": sb(4 * C, "bfloat16"), "gp": sb(4 * C, "bfloat16"),
-    "z": sb(4 * C, "bfloat16"), "zq": sb(C, "float8_e4m3fn_x4"), "zp": sb(C, "uint8"),
+    "z": sb(4 * ZC, "bfloat16"), "go": sb(8 * OWN, "bfloat16"), "zo": sb(512, "bfloat16"),
+    "oq": sb(128 * ROUNDS, "float8_e4m3fn_x4"), "op": sb(128 * ROUNDS, "uint8"),
     "h": sb(4 * C, "bfloat16"),
     "pu": ("psum", [128, 2048], "float32"), "pw": ("psum", [128, 2048], "float32"),
 }
 for _n in ("c", "f", "e"):
     for _k in ("0", "1", "w", "x"):
         SCRATCH["m" + _n + _k] = sb(C, "float32")
-LISTS = ["cw", "ct", "pk", "dm", "dc", "fl", "be", "dn", "bf", "de", "sx", "ta", "ua", "tb", "yb"]
+LISTS = ["cw", "pk", "dm", "dc", "fl", "be", "dn", "bf", "de", "sx", "ta", "ua", "c0", "c1", "cm", "cn"]
 SCRATCH["sml"] = sb(32 * len(LISTS), "float32")
-COLS = {"sc": 0, "bi": 12, "bt": 24, "nk": 34}
-for _n in ("e15", "pl", "col", "f0", "nc", "a1", "b1", "b2", "c2", "lo", "hi", "hj", "k1", "k2", "es", "e0", "par", "dd", "p21", "nl"):
+COLS = {"sc": 0, "bi": 12, "bt": 24}
+for _n in ("e15", "col", "f0", "nc", "a1", "b1", "k1", "e0", "par", "dd", "p21", "kv", "ka", "na", "nv", "kr", "m1", "d0", "e8", "up_"):
     COLS[_n] = 33 + len(COLS)
-for _k in range(6):
-    SCRATCH["l%d" % _k] = sb(NB, "uint16")
+OFFSETS = ["l0", "l1", "l2", "l3", "l4", "l5", "mt16", "so", "lq", "sig", "dl0", "dl3"]
+SCRATCH["lu"] = sb(32 * len(OFFSETS), "uint16")
 for _r in range(ROUNDS + 1):
     if _r:
         SCRATCH["x%d" % _r] = sb(4 * C, "bfloat16")
@@ -67,18 +73,21 @@ for _r in range(ROUNDS + 1):
 for _r in range(ROUNDS):
     SCRATCH["aq%d" % _r] = sb(C, "float8_e4m3fn_x4")
     SCRATCH["ap%d" % _r] = sb(C, "uint8")
+    SCRATCH["zq%d" % _r] = sb(C, "float8_e4m3fn_x4")
+    SCRATCH["zp%d" % _r] = sb(C, "uint8")
     SCRATCH["lp%d" % _r] = sb(2 * B0, "uint16")
     SCRATCH["al%d" % _r] = sb(B0 + NB, "uint16")
 SEMAPHORES = ["ev", "es", "et", "eg", "snd", "st"]
-SEMAPHORES += ["%s%d" % (_n, _r) for _n in ("ax", "ap", "ab") for _r in range(ROUNDS)]
+SEMAPHORES += ["%s%d" % (_n, _r) for _n in ("ax", "ap", "ab", "az", "hx") for _r in range(ROUNDS)]
 SEMAPHORES += ["ld_" + _n for _n in ("x", "u", "v", "nx", "mt", "wc", "ws", "sg")]
-SEMAPHORES += ["ld_%s%d" % (_n, _r) for _n in ("g0", "g1", "g2", "g3", "a", "b") for _r in range(ROUNDS)]
+SEMAPHORES += ["ld_%s%d" % (_n, _r) for _n in ("g0", "g1", "g2", "g3", "a", "b", "s", "t", "u", "v", "w") for _r in range(ROUNDS)]
 
 GATHER, HALF, ROW, SMALL = 0.58, 0.17, 0.34, 0.08
-COSTS = [(0.65, 0.8, 0.85, 0.17, 0.15, 0.05), (1.0, 1.0, 1.0, 0.2, 0.17, 0.06), (0.7, 0.9, 0.77, 0.22, 0.12, 0.03)]
+COSTS = [(0.65, 0.8, 0.85, 0.17, 0.15, 0.05), (1.0, 1.0, 1.0, 0.2, 0.17, 0.06), (0.75, 0.85, 0.85, 0.17, 0.19, 0.02)]
 SPAN = 120
 SHARED = {}
-OPT = {"x": 192, "z": 160, "zg": [0], "zs": [0, 3], "xs": [3], "xps": [3], "xpl": [2, 3], "seed": 3}
+OPT = {"x": 192, "z": 128, "zg": [0], "zs": [0, 3], "xs": [3], "xps": [3], "xpl": [2, 3], "seed": 4,
+       "pl": "vnn", "ex": "nn", "fn": "Qpp", "tw": 0, "relay": 1, "one": 0, "ap": "nnn", "hs": [0, 1, 2, 3], "cut": [], "ll": 2.6, "zl": 2.9, "ta": 0.5}
 
 
 def new_plan():
@@ -122,7 +131,7 @@ def task(P, eng, dur, fn, reads, writes, kind="op", sem=None, inc=1, after=(), a
     return n
 
 
-def schedule(P, tries=1000, moves=45000, starts=8, last=100000, heat=0.015, sweeps=4):
+def schedule(P, tries=500, moves=35000, starts=7, last=120000, heat=0.04, sweeps=4):
     ts = P["tasks"]
     n = len(ts)
     ways = [[(e, cost(t, e, w, COSTS[0])) for e, w in [(t["eng"], t["dur"])] + ([t["alt"][:2]] if t["alt"] else [])] for t in ts]
@@ -436,6 +445,9 @@ def build(P, g, core, T, topo):
     def K(dur, fn, reads, writes):
         return task(P, "g", dur, fn, reads, writes)
 
+    def whole(dur, out, pattern, base, step, writes):
+        return K(dur, lambda q: q.iota(out, pattern, base, step, allow_small_or_imprecise_dtypes=True), [], writes)
+
     def ts(out, in_, s1, s2, op0, op1, reads, writes, dur=SMALL):
         if op1 is None:
             return V(dur, lambda q: q.tensor_scalar(out, in_, s1, None, op0), reads, writes)
@@ -468,8 +480,12 @@ def build(P, g, core, T, topo):
     def at(b, a=0):
         return T[b][:, C * a:C * a + C]
 
+    def U(name, w=NB):
+        i = OFFSETS.index(name)
+        return T.lu[:, 32 * i:32 * i + w]
+
     def by(b, l, a=0):
-        return at(b, a).indirect(T[l][:, 0:NB])
+        return at(b, a).indirect(U(l))
 
     def mid(b):
         return T[b][:, 16:16 + C]
@@ -480,13 +496,21 @@ def build(P, g, core, T, topo):
 
     def move(name, out, in_, reads, writes, add=False):
         if add:
-            k = task(P, "g", 1.0, lambda q: q.dma_start(out, in_, accum_op=A.add), reads, writes, "dma", "ld_" + name, 16)
+            k = task(P, "g", 2.0 if name == "a0" else 1.0, lambda q: q.dma_start(out, in_, accum_op=A.add), reads, writes, "dma", "ld_" + name, 16)
         else:
             k = task(P, "y", 0.07, lambda q: q.dma_start(out, in_), reads, writes, "dma", "ld_" + name, 16)
         task(P, "net", 2.8 if add else 2.2, None, reads, writes, "land", "ld_" + name, 16, after=[k])
 
+    def lay(name, rows):
+        def region(b, a, step):
+            return [(b, 16 + x, 17 + x) for x in range(a, 16, step)] + [(b, 0, 2)] * (b == "sa")
+        ks = [task(P, "y", 0.07, lambda q, d=d, b=b, a=a, step=step: q.dma_start(T[d][a:128:step, 0:C], T[b][a:128:step, 0:C]), region(b, a, step),
+                   region(d, a, step), "dma", "ld_" + name, 16) for d, b, a, step in rows]
+        task(P, "net", 2.2, None, [x for _, b, a, step in rows for x in region(b, a, step)], [x for d, _, a, step in rows for x in region(d, a, step)],
+             "land", "ld_" + name, 16 * len(rows), after=ks)
+
     k = load("y", "nx", T.nxi[:], T.nx[:], ["nxi"], 2.0)
-    j = load("s", "u", T.ut[:], T.u[:], ["ut"], 2.4, [K(0.19, lambda q: q.iota(T.pi[:], [[0, 32]], 0, 1), [], ["pi"])])
+    j = load("s", "u", T.ut[:], T.u[:], ["ut"], 2.4, [K(0.19, lambda q: q.iota(T.pa[:], [[0, 32]], 0, 1), [], ["pa"])])
     load("s", "mt", T.mti[:], T.mt[:], ["mti"], 2.4, [j - 1])
     k = load("y", "x", T.x0[:], T.x[:], ["x0"], 3.0, [k - 1])
     load("y", "wc", T.wq[:].bitcast(dt.uint8), T.wc[:], ["wq"], 3.0, [k])
@@ -498,107 +522,147 @@ def build(P, g, core, T, topo):
     K(0.19, lambda q: q.iota(T.ci[:], [[16, 32]], 0, 0), [], ["ci"])
     for k in range(5):
         K(0.14, lambda q, k=k: q.iota(T.sh[:, 2 * k:2 * k + 2], [[-(16 >> k), 2]], 127 * (16 >> k), -(16 >> k)), [], [("sh", k, k + 1)])
-    K(0.17, lambda q: q.iota(T.c32[:], [[32, NB // 2], [0, 2]], -160, 0), [], ["c32"])
+    for h, (a, b) in enumerate([(0, NB), (NB, 48)]):
+        whole(0.17, T.cq[:, a:b], [[32, (b - a) // 2], [0, 2]], -160 - 16 * h, 0, [("cq", h, h + 1)])
+    K(0.21, lambda q: q.iota(T.pi[:], [[0, 48]], 0, 1), [], ["pi"])
+    ts(T.pi[:], T.pi[:], 31, None, A.bitwise_and, None, ["pi"], ["pi"])
+    tt(T.cq[:], T.pi[:], T.cq[:], A.add, ["pi", "cq"], ["cq"])
+    for b in ("dt", "ic")[OPT["fn"][0] not in "pq":]:
+        whole(0.67, T[b][:], [[-1, C]], 160, 0, [b])
+    whole(0.4, T.yy[:, 64:224], [[0, 160]], 0, 0, ["yy"])
+    whole(0.7, T.rp[:, 304:640], [[0, 336]], 0, 0, ["rp"])
+    whole(0.56, T.zo[:, 4 * OWN:512], [[0, 512 - 4 * OWN]], 0, 0, [("zo", 1, 2)])
+    for a in (0, C + 16) * (not OPT["one"]):
+        whole(0.16, T.n1[:, a:a + 16], [[0, 16]], 0, 0, [("n1", 8 + a / 1024, 8 + (a + 1) / 1024)])
     K(1.1, lambda q: q.iota(T.one[:], [[0, 528]], 1, 0, allow_small_or_imprecise_dtypes=True), [], ["one"])
     K(1.1, lambda q: q.affine_select(T.big[:], T.one[:], [[-1, 528]], A.is_equal, 0.0, 3, 4), ["one"], ["big"])
-    ts(T.pa[:], T.pi[:], 15, None, A.bitwise_and, None, ["pi"], ["pa"])
-    ts(T.dg[:], T.ji[:], 15, None, A.bitwise_and, None, ["ji"], ["dg"])
-    ts(T.t1[:], T.dg[:], 1.0, 320.0, A.is_equal, A.mult, ["dg"], ["t1"])
-    ts(T.t2[:], T.dg[:], 0.0, -16384.0, A.is_equal, A.mult, ["dg"], ["t2"])
-    tt(T.w16[:], T.t1[:], T.t2[:], A.add, ["t1", "t2"], ["w16"])
-    cp(T.so[:], T.pa[:, 0:NB], ["pa"], ["so"])
-    act(T.wt[:], T.w16[:].indirect(T.so[:]), ["w16", "so"], ["wt"], gat())
-    tt(L("cw"), T.pa[:, 0:NB], T.ci[:, 0:NB], A.add, ["pa", "ci"], ["cw"])
+    ts(T.pa[:], T.pa[:], 15, None, A.bitwise_and, None, ["pa"], ["pa"])
+    ts(T.ji[:], T.ji[:], 15, None, A.bitwise_and, None, ["ji"], ["ji"])
+    ts(T.t1[:, 0:16], T.ji[:], 1.0, 320.0, A.is_equal, A.mult, ["ji"], [("t1", 0, 1)])
+    ts(T.t1[:, 16:32], T.ji[:], 0.0, -16384.0, A.is_equal, A.mult, ["ji"], [("t1", 1, 2)])
+    tt(T.w16[:], T.t1[:, 0:16], T.t1[:, 16:32], A.add, ["t1"], ["w16"])
+    cp(U("so"), T.pa[:, 0:NB], ["pa"], ["so"])
+    act(T.wt[:], T.w16[:].indirect(U("so")), ["w16", "so"], ["wt"], gat())
+    tt(L("cw", 32), T.pa[:], T.ci[:], A.add, ["pa", "ci"], ["cw"])
     cp(T.uo[:], T.ci[:, 0:8], ["ci"], ["uo"])
     row = T.pa[:, 0:1]
     ts(cf("e15"), row, 15.0, None, A.is_equal, None, ["pa"], ["e15"])
-    ts(cf("pl"), row, 8.0, None, A.is_lt, None, ["pa"], ["pl"])
-    for name, a, b in (("col", 320.0, -160.0), ("nc", -320.0, 160.0), ("f0", 320.0, -320.0), ("a1", -1.0, 1.0), ("b1", -2.0, 1.0)):
-        act(cf(name), cf("e15"), ["e15"], [name], SMALL, scale=a, bias=b)
-    for b in ("n1", "e1"):
-        for a in (0, C + 16):
-            act(T[b][:, a:a + 16], T.w16[:], ["w16"], [(b, 8 + a / 1024, 8 + (a + 1) / 1024)], SMALL, scale=0.0)
-    V(0.25, lambda q: q.memset(T.yy[:], 0.0), [], ["yy"])
+    for name, a, b in (("col", 320.0, -160.0), ("nc", -320.0, 160.0), ("f0", 320.0, -320.0), ("a1", -1.0, 1.0)):
+        if name != "nc" or "n" in OPT["ex"]:
+            act(cf(name), cf("e15"), ["e15"], [name], SMALL, scale=a, bias=b)
+    for a in (0, C + 16) * (not OPT["one"]):
+        act(T.e1[:, a:a + 16], T.w16[:], ["w16"], [("e1", 8 + a / 1024, 8 + (a + 1) / 1024)], SMALL, scale=0.0)
     for b in range(4):
         V(0.16, lambda q, b=b: q.quantize_mx(T.eq[:, 128 * b:128 * b + 128], T.ep[:, 128 * b:128 * b + 128], T.big[:, 3 - b:515 - b]),
           ["big"], [("eq", b, b + 1), ("ep", b, b + 1)])
 
     ts(T.bits[:], T.sh[:], 4, 1, A.arith_shift_right, A.bitwise_and, ["sh"], ["bits"])
     cp(cf("bt", 0, 10), T.bits[:], ["bits"], ["bt"])
-    act(cf("sc", 0, 4, 3), cf("bt", 0, 4, 2), ["bt"], [("sc", 0, 1)], SMALL)
     act(cf("sc", 1, 4, 3), cf("bt", 1, 4, 2), ["bt", "a1"], [("sc", 1, 2)], SMALL, scale=cf("a1"))
-    tt(cf("nk", 0, 3), cf("bt", 0, 3, 2), cf("bt", 1, 3, 2), A.subtract, ["bt"], ["nk"])
-    act(cf("nk", 0, 3), cf("nk", 0, 3), ["nk", "pl"], ["nk"], SMALL, scale=cf("pl"))
-    tt(cf("sc", 2, 3, 3), cf("nk", 0, 3), cf("bt", 1, 3, 2), A.add, ["bt", "nk"], [("sc", 2, 3)])
     act(cf("bi", 0, 3, 3), cf("bt", 0, 3, 2), ["bt"], [("bi", 0, 0.5)], SMALL, scale=BIG, bias=-BIG)
     ts(cf("e0"), row, 0.0, -BIG, A.not_equal, A.mult, ["pa"], ["e0"])
     act(cf("bi", 9), cf("bt", 6), ["bt", "e0"], [("bi", 0.5, 1)], SMALL, scale=BIG, bias=cf("e0"))
-    act(cf("bi", 7, 2, 3), cf("sc", 7, 2, 3), [("sc", 1, 2)], [("bi", 1, 2)], SMALL, scale=5 * KEY, bias=-4 * KEY)
-    act(cf("k1"), cf("sc", 7), [("sc", 1, 2)], ["k1"], SMALL, scale=-KEY)
-    act(cf("k1"), cf("sc", 10), [("sc", 1, 2), "k1"], ["k1"], SMALL, scale=-KEY, bias=cf("k1"))
-    act(cf("lo"), cf("pl"), ["pl"], ["lo"], SMALL, scale=BIG, bias=-BIG)
-    act(cf("hi"), cf("pl"), ["pl"], ["hi"], SMALL, scale=-BIG, bias=BIG)
-    act(cf("hj"), cf("pl"), ["pl", "hi"], ["hj"], SMALL, scale=KEY * HIGH, bias=cf("hi"))
-    act(cf("bi", 2, 3, 3), cf("sc", 2, 3, 3), [("sc", 2, 3), "hj", "lo"], [("bi", 2, 3)], SMALL, scale=cf("hj"), bias=cf("lo"))
-    V(SMALL, lambda q: q.tensor_reduce(cf("nl"), cf("sc", 2, 3, 3), AxisListType.X, A.add), [("sc", 2, 3)], ["nl"])
-    act(cf("nl"), cf("nl"), ["nl"], ["nl"], SMALL, scale=-KEY, bias=-BASE)
-    act(cf("k2"), cf("nl"), ["nl", "pl"], ["k2"], SMALL, scale=cf("pl"))
-    act(cf("es"), cf("pl"), ["pl"], ["es"], SMALL, scale=1.0 / HIGH)
-    ts(cf("b2"), row, 7.0, -HIGH, A.is_lt, A.mult, ["pa"], ["b2"])
-    act(cf("c2"), cf("pl"), ["pl", "lo"], ["c2"], SMALL, scale=BASE * HIGH, bias=cf("lo"))
-    for b in ("dt", "ic"):
-        act(T[b][:], T.idr[:], ["idr", "b2", "c2"], [b], scale=cf("b2"), bias=cf("c2"))
-    act(T.gs[:], T.idr[:], ["idr", "b1"], ["gs"], scale=cf("b1"), short=True)
+    act(cf("bi", 1, 4, 3), cf("sc", 1, 4, 3), [("sc", 1, 2)], [("bi", 1, 2)], SMALL, scale=9 * KEY, bias=-8 * KEY)
+    if "v" in OPT["pl"]:
+        V(SMALL, lambda q: q.tensor_reduce(cf("kv"), cf("sc", 1, 4, 3), AxisListType.X, A.add), [("sc", 1, 2)], ["kv"])
+        act(cf("kv"), cf("kv"), ["kv"], ["kv"], SMALL, scale=KEY)
+        act(T.idk[:], T.idr[:], ["idr", "kv"], ["idk"], bias=cf("kv"))
+    if set("nm") & set(OPT["pl"]):
+        act(cf("k1"), cf("sc", 7), [("sc", 1, 2)], ["k1"], SMALL, scale=-KEY)
+        if "m" in OPT["pl"]:
+            act(cf("k1"), cf("sc", 4), [("sc", 1, 2), "k1"], ["k1"], SMALL, scale=-KEY, bias=cf("k1"))
+        act(cf("k1"), cf("sc", 10), [("sc", 1, 2), "k1"], ["k1"], SMALL, scale=-KEY, bias=cf("k1"))
+        act(cf("b1"), cf("e15"), ["e15"], ["b1"], SMALL, scale=-2.0, bias=1.0)
+        act(T.gs[:], T.idr[:], ["idr", "b1"], ["gs"], scale=cf("b1"), short=True)
+    if "w" in OPT["pl"]:
+        V(SMALL, lambda q: q.tensor_reduce(cf("nv"), cf("sc", 1, 4, 3), AxisListType.X, A.add), [("sc", 1, 2)], ["nv"])
+        act(cf("nv"), cf("nv"), ["nv"], ["nv"], SMALL, scale=-KEY)
+    if set("wbrs") & set(OPT["pl"] + OPT["fn"]):
+        whole(1.2, T.wd[:], [[1, 2 * C]], -C, 0, ["wd"])
+        act(L("cm"), L("cw"), ["cw"], ["cm"], SMALL, bias=-float(C))
+        if set("wb") & set(OPT["pl"]) or "s" in OPT["ex"]:
+            ts(L("cn"), L("cm"), cf("col"), None, A.subtract, None, ["cm", "col"], ["cn"])
+    if "a" in OPT["pl"]:
+        act(cf("ka"), cf("sc", 10), [("sc", 1, 2)], ["ka"], SMALL, scale=KEY)
+        act(T.ida[:], T.idr[:], ["idr", "ka"], ["ida"], bias=cf("ka"))
+    if "b" in OPT["pl"]:
+        act(cf("na"), cf("sc", 10), [("sc", 1, 2)], ["na"], SMALL, scale=-KEY)
+    if set("ab") & set(OPT["pl"]):
+        act(cf("kr"), cf("e15"), ["e15"], ["kr"], SMALL, scale=8 * KEY, bias=-8 * KEY)
+        act(T.gr[:], T.idr[:], ["idr", "e15", "kr"], ["gr"], scale=cf("e15"), bias=cf("kr"))
+        K(0.67, lambda q: q.iota(T.gw[:], [[0, C]], -8 * int(KEY), 0, allow_small_or_imprecise_dtypes=True), [], ["gw"])
+    pl = cf("bt", 6)
+    act(cf("up_"), pl, ["bt"], ["up_"], SMALL, scale=BIG)
+    act(T.fs[:], T.idr[:], ["idr", "up_"], ["fs"], bias=cf("up_"))
     tt(cf("par"), cf("bt", 8), cf("bt", 0), A.not_equal, ["bt"], ["par"])
-    act(cf("p21"), cf("par"), ["par"], ["p21"], SMALL, scale=16.0 * (NB + 1), bias=15.0)
+    if not OPT["one"]:
+        act(cf("p21"), cf("par"), ["par"], ["p21"], SMALL, scale=16.0 * (NB + 1), bias=15.0)
     ts(L("pk", 2), L("cw", 2), NB - 1.0, 16.0, A.min, A.mult, ["cw"], ["pk"])
-    ts(T.pick[:, 0:2], L("pk", 2), cf("p21"), None, A.add, None, ["pk", "p21"], [("pick", 0, 1)])
+    if not OPT["one"]:
+        ts(T.pick[:, 0:2], L("pk", 2), cf("p21"), None, A.add, None, ["pk", "p21"], [("pick", 0, 1)])
     act(cf("dd"), cf("bt", 8), ["bt"], ["dd"], SMALL, scale=30.0, bias=-95.0)
     act(cf("dd"), cf("dd"), ["dd", "par"], ["dd"], SMALL, scale=cf("par"), bias=96.0)
     ts(T.pick[:, 2:4], L("cw", 2), NB - 1.0, cf("dd"), A.min, A.add, ["cw", "dd"], [("pick", 1, 2)])
-    ts(T.pi[:, 0:NB], T.pi[:, 0:NB], 31, None, A.bitwise_and, None, ["pi"], ["pi"])
-    tt(L("ct"), T.pi[:, 0:NB], T.c32[:], A.add, ["pi", "c32"], ["ct"])
+    act(cf("m1"), cf("par"), ["par"], ["m1"], SMALL, scale=-15.0 / 16, bias=1.0)
+    act(cf("d0"), cf("bt", 8), ["bt"], ["d0"], SMALL, scale=30.0, bias=506.0)
+    act(cf("d0"), cf("d0"), ["d0", "par"], ["d0"], SMALL, scale=cf("par"), bias=7.0)
+    act(T.pick[:, 4:6], L("pk", 2), ["pk", "m1", "d0"], [("pick", 2, 3)], SMALL, scale=cf("m1"), bias=cf("d0"))
+    if OPT["one"]:
+        act(cf("p21"), cf("bt", 8), ["bt"], ["p21"], SMALL, scale=30.0, bias=498.0)
+        act(cf("p21"), cf("p21"), ["p21", "par"], ["p21"], SMALL, scale=cf("par"), bias=15.0)
+        act(T.pick[:, 0:2], L("pk", 2), ["pk", "m1", "p21"], [("pick", 0, 1)], SMALL, scale=cf("m1"), bias=cf("p21"))
+        whole(0.7, T.r1[:, C:640], [[0, C]], 0, 0, ["r1"])
+    ts(cf("e8"), row, 8.0, -1.0, A.is_equal, A.mult, ["pa"], ["e8"])
+    act(cf("e8"), pl, ["bt", "e8"], ["e8"], SMALL, bias=cf("e8"))
 
     V(0.16, lambda q: q.quantize_mx(T.uq[:], T.up[:], T.ut[:]), ["ut"], ["uq", "up"])
     cp(T.uqr[:].bitcast(dt.uint32), T.uq[:].bitcast(dt.uint32).indirect(T.uo[:]), ["uq", "uo"], ["uqr"], gat(128))
     act(T.upr[:], T.up[:].indirect(T.uo[:]), ["up", "uo"], ["upr"], gat(128))
     V(0.16, lambda q: q.quantize_mx(T.vq[:], T.vp[:], T.vt[:]), ["vt"], ["vq", "vp"])
 
-    cp(T.l0[:], T.nxi[:], ["nxi"], ["l0"])
-    cp(T.mt16[:], T.mti[:], ["mti"], ["mt16"])
+    cp(U("l0"), T.nxi[:], ["nxi"], ["l0"])
+    cp(U("mt16"), T.mti[:], ["mti"], ["mt16"])
     tt(L("dm"), T.mti[:], L("cw"), A.subtract, ["mti", "cw"], ["dm"])
     act(L("bf"), L("dm"), ["dm", "f0"], ["bf"], SMALL, scale=cf("f0"))
     tt(L("dc"), L("bf"), L("cw"), A.add, ["bf", "cw"], ["dc"])
-    act(T.nid[:], T.idr[:], ["idr"], ["nid"], scale=-1.0, short=True)
-    act(T.sw[:], by("idr", "mt16"), ["mt16", "idr"], ["sw"], gat())
-    move("sg", T.sw[:], T.nid[:], ["nid"], ["sw"], True)
-    task(P, "s", ROW, lambda q: q.activation(T.sg[:], T.sw[:], AF.Sign), ["sw"], ["sg"])
+    if OPT["tw"]:
+        for i, op in enumerate((A.is_lt, A.is_gt)):
+            ts(L("c%d" % i), L("dm"), 0.0, float(C), op, A.mult, ["dm"], ["c%d" % i])
+    else:
+        act(T.sw[:], by("idr", "mt16"), ["mt16", "idr"], ["sw"], gat())
+        move("sg", T.sw[:], T.ic[:], ["ic"], ["sw"], True)
+        task(P, "s", ROW, lambda q: q.activation(T.sg[:], T.sw[:], AF.Sign), ["sw"], ["sg"])
 
     def weighted(dst, src, a=0):
         V(HALF, lambda q: q.tensor_tensor_scan(T[dst][:], T.wt[:], at(src, a), 0.0, A.add, A.max), ["wt", (src, a, a + 1)], [dst])
 
-    def powers(f0):
-        act(T[f0][:], by("idr", "l0"), ["idr", "l0"], [f0], gat(), scale=HIGH)
+    def powers(r, first=True):
+        f0 = "f0%d" % (r % 2)
+        if first:
+            act(T[f0][:], by("idr", "l0"), ["idr", "l0"], [f0], gat())
         src, a = f0, 0
         for k, (dst, b) in enumerate([("fa", 0), ("fa", 1), ("ft", 1), ("ft", 2), ("ft", 4)]):
-            act(at(dst, b), by(src, "l%d" % k, a), [(src, a, a + 1), "l%d" % k], [(dst, b, b + 1)], gat(), scale=None if k else 1.0 / HIGH)
+            act(at(dst, b), by(src, "l%d" % k, a), [(src, a, a + 1), "l%d" % k], [(dst, b, b + 1)], gat())
             weighted("scn", dst, b)
-            act(T["l%d" % (k + 1)][:], every("scn", 15), ["scn", "col"], ["l%d" % (k + 1)], 0.1, bias=cf("col"))
+            act(U("l%d" % (k + 1)), every("scn", 15), ["scn", "col"], ["l%d" % (k + 1)], 0.1, bias=cf("col"))
+            if k == 2 and OPT["pl"][r] in "wb":
+                tt(U("dl3"), every("scn", 15), L("cn"), A.subtract, ["scn", "cn"], ["dl3"])
             src, a = dst, b
 
     def steps(name, t, src, levels, first, end=None):
         for i, k in enumerate(levels):
             w, dst = "m%s%s" % (name, "wx"[i % 2]), "m%s%d" % (name, i % 2)
             c = 3 * (first[1] + k - first[0]) + t
-            mask = {"scale": cf("sc", c), "bias": cf("bi", c)} if k >= first[0] else {}
-            reads = [src] + [("sc", t, t + 1), ("bi", t, t + 1)] * bool(mask)
+            mask = {"scale": cf("sc", c) if t else cf("bt", 2 * c // 3), "bias": cf("bi", c)} if k >= first[0] else {}
+            reads = [src] + [("sc", t, t + 1) if t else "bt", ("bi", t, t + 1)] * bool(mask)
             if k == 6:
                 k = 5
                 act(at(w), by(src, "l5"), reads + ["l5"], [w], gat(), **mask)
-            elif k or mask:
-                act(at(w), at(src), reads, [w], **mask)
+            elif name + str(k) in OPT["cut"]:
+                for h, (lo, hi) in enumerate([(0, C // 2), (C // 2, C)]):
+                    act(T[w][:, lo:hi], T[src][:, lo:hi], reads, [(w, h, h + 1)], ROW / 2 + 0.02, **mask)
             else:
-                w = "sb"
+                act(at(w), at(src), reads, [w], **mask)
             out, reg = end if end and i == len(levels) - 1 else (at(dst), dst)
             tt(out, by(w, "l%d" % k), at(src), A.max, [w, src, "l%d" % k], [reg], gat())
             src = dst
@@ -606,12 +670,54 @@ def build(P, g, core, T, topo):
 
     def turn(dst, src):
         V(HALF, lambda q: q.transpose(T[dst][:, 0:C], mid(src)), [(src, 0, 4)], [(dst, 0, 1)])
-        V(HALF * PW / C, lambda q: q.transpose(T[dst][:, C:TW], T[src][:]), [src], [(dst, 1, 2)])
+        if not OPT["one"]:
+            V(HALF * PW / C, lambda q: q.transpose(T[dst][:, C:TW], T[src][:]), [src], [(dst, 1, 2)])
 
     def chain(out, n, e, reads, writes, w=C):
         V(HALF * w / C, lambda q: q.tensor_tensor_scan(out, n, e, 0.0, A.mult, A.add), reads, writes)
 
+    def less(dst, l, key=None):
+        act(T[dst][:], T.wd[:].indirect(U("d" + l)), ["wd", "d" + l] + [key] * bool(key), [dst], gat(), bias=cf(key) if key else None)
+
     def places(r):
+        if OPT["pl"][r] == "w":
+            less("me1", "l3", "nv")
+            steps("e", 1, "me1", [3, 4, 5, 6], (3, 0), (mid("e1"), ("e1", 0, 4)))
+            turn("te1", "e1")
+            act(T.te1[:, 15:TW:16], T.cq[:, 0:TW // 16], ["cq", "te1"], ["te1"], SMALL)
+            return
+        places2(r)
+
+    def places2(r):
+        if OPT["pl"][r] == "v":
+            tt(T.me1[:], by("fa", "l2", 1), T.idk[:], A.subtract, [("fa", 1, 2), "l2", "idk"], ["me1"], gat())
+            steps("e", 1, "me1", [3, 4, 5, 6], (3, 0), (mid("e1"), ("e1", 0, 4)))
+            turn("te1", "e1")
+            w = C if OPT["one"] else TW
+            act(T.te1[:, 15:w:16], T.cq[:, 0:w // 16], ["cq", "te1"], ["te1"], SMALL)
+            return
+        if OPT["pl"][r] in "ab":
+            if OPT["pl"][r] == "a":
+                tt(T.me1[:], by("fa", "l2", 1), T.ida[:], A.subtract, [("fa", 1, 2), "l2", "ida"], ["me1"], gat())
+            else:
+                less("me1", "l3", "na")
+            for b, src, l in (("d1", "me1", "l3"), ("d2", "me1", "l4"), ("d3", "d1", "l4")):
+                act(T[b][:], by(src, l), [src, l], [b], gat())
+            lay("g0%d" % r, [("gr", "me1", 6, 8), ("gw", "me1", 2, 8), ("gr", "d1", 5, 8), ("gw", "d1", 1, 8)])
+            lay("g1%d" % r, [("gr", "d2", 4, 8), ("gw", "d2", 0, 8), ("gr", "d3", 3, 8), ("gw", "d3", 7, 16)])
+            tt(T.me0[:], by("gw", "l5"), T.gr[:], A.max, ["gw", "gr", "l5"], ["me0"], gat())
+            act(T.mex[:], by("me0", "l5"), ["me0", "l5", ("sc", 1, 2), ("bi", 1, 2)], ["mex"], gat(), scale=cf("sc", 10), bias=cf("bi", 10))
+            tt(mid("e1"), by("mex", "l5"), T.me0[:], A.max, ["mex", "me0", "l5"], [("e1", 0, 4)], gat())
+            turn("te1", "e1")
+            return
+        if OPT["pl"][r] == "m":
+            for i, (a, step) in enumerate([(1, 4), (3, 8), (7, 16)]):
+                move("g%d%d" % (i, r), T.gs[a:128:step, :], T.ft[a:128:step, C:2 * C], [("ft", 1, 2)], [("gs", a, a + 1)])
+            act(T.mex[:], T.gs[:], ["gs", "a1", "k1"], ["mex"], scale=cf("a1"), bias=cf("k1"))
+            tt(T.d1[:], by("mex", "l3"), T.gs[:], A.subtract, ["mex", "gs", "l3"], ["d1"], gat())
+            steps("e", 1, "d1", [4, 5, 6], (4, 1), (mid("e1"), ("e1", 0, 4)))
+            turn("te1", "e1")
+            return
         act(at("ft", 3), by("ft", "l3", 2), [("ft", 2, 3), "l3"], [("ft", 3, 4)], gat())
         for i, (b, a, step) in enumerate([(1, 1, 4), (2, 0, 4), (3, 3, 8), (3, 7, 16)]):
             move("g%d%d" % (i, r), T.gs[a:128:step, :], T.ft[a:128:step, C * b:C * b + C], [("ft", b, b + 1)], [("gs", a, a + 1)])
@@ -622,36 +728,52 @@ def build(P, g, core, T, topo):
 
     sent = [0]
 
-    def send(r, pairs, sem, land, latency):
+    def send(r, pairs, sem, land, latency, relay=False):
         dst, src = T.cores[(rank + r + 1) % n], T.cores[(rank - r - 1) % n]
+        there = sem
+        if relay:
+            dst, src, there = neighbour(core, T, topo), neighbour(src, T, topo), "hx%d" % r
         rid, pid, _ = topo.addr(dst)
         m = topo.mask(core, dst)
         ids = []
         for out, in_, name in pairs:
-            ids.append(task(P, "g", 0.1, lambda q, out=out, in_=in_: q.remote_dma(out, in_, T.sem[sem], T.sem.snd, pid, rid, m), [name], [], "send"))
+            ids.append(task(P, "g", 0.1, lambda q, out=out, in_=in_: q.remote_dma(out, in_, T.sem[there], T.sem.snd, pid, rid, m), [name], [], "send"))
             sent[0] += len(topo.engines(core, dst))
         return task(P, "net", latency, None, [], land, "land", sem, len(topo.engines(src, core)) * len(pairs), after=ids)
 
-    def home(r, k, a, b, op, reads):
-        y, lp, al, o = YW * k, "lp%d" % r, "al%d" % r, B0 * k
-        tt(T.yy[:, y + 96:y + 96 + NB], a, b, op, reads, [("yy", y + 96, y + 128)])
-        V(SMALL, lambda q: q.transpose(T.yy[:, y + 176:y + 208], T.yy[:, y + 96:y + 128]), [("yy", y + 96, y + 128)], [("yy", y + 176, y + 208)])
-        V(SMALL, lambda q: q.transpose(T.yy[:, y:y + 64], T.yy[:, y + 160:y + 224]), [("yy", y + 160, y + 224)], [("yy", y, y + 64)])
-        ts(T[lp][:, o:o + 32], T.yy[:, y:y + 128].indirect(T.pick[:, 2:4]), 160.0, None, A.add, None, [("yy", y, y + 128), ("pick", 1, 2)],
-           [(lp, o, o + 32)], 0.12)
-        send(r, [(T[al][:, o:o + NB], T[lp][:, o:o + NB], (lp, o, o + NB))], "a%s%d" % ("pb"[k], r), [(al, o, o + NB)], 2.6)
+    def home(r, k):
+        lp, al, o = "lp%d" % r, "al%d" % r, B0 * k
+        if k:
+            tt(T.yy[:, 96:96 + NB], every("rb", 7), every("rb", 8), A.subtract, ["rb"], [("yy", 96, 128)])
+            V(SMALL, lambda q: q.transpose(T.yy[:, 176:208], T.yy[:, 96:128]), [("yy", 96, 128)], [("yy", 176, 208)])
+            V(SMALL, lambda q: q.transpose(T.yy[:, 0:64], T.yy[:, 160:224]), [("yy", 160, 224)], [("yy", 0, 64)])
+            tt(T[lp][:, o:o + 32], T.yy[:, 0:128].indirect(T.pick[:, 2:4]), L("ua", 32), A.add, [("yy", 0, 128), ("pick", 1, 2), "ua"], [(lp, o, o + 32)], 0.12)
+        else:
+            V(SMALL, lambda q: q.transpose(T.rp[:, 592:624], T.rp[:, 7:512:16]), [("rp", 0, 512)], [("rp", 592, 624)])
+            V(SMALL, lambda q: q.transpose(T.rp[:, 512:576], T.rp[:, 576:640]), [("rp", 576, 640)], [("rp", 512, 576)])
+            act(T[lp][:, o:o + 32], T.rp[:, 0:576].indirect(T.pick[:, 4:6]), [("rp", 0, 576), ("pick", 2, 3)], [(lp, o, o + 32)], 0.12, bias=160.0)
+        send(r, [(T[al][:, o:o + ZC // 16], T[lp][:, o:o + ZC // 16], (lp, o, o + NB))], "a%s%d" % ("pb"[k], r), [(al, o, o + NB)], OPT["ll"])
+        for t in range(4):
+            act(T.go[:, 4 * OWN * k + t:4 * OWN * (k + 1):4], at("fo", t).indirect(T[lp][:, o + ZC // 16:o + NB]), [("fo", t, t + 1), (lp, o, o + NB)],
+                [("go", 4 * k + t, 4 * k + t + 1)], gat(OWN), scale=0.5)
+        if k:
+            a, zq, zp = 128 * r, "zq%d" % r, "zp%d" % r
+            tt(T.zo[:, 0:4 * OWN], T.go[:, 0:4 * OWN], T.go[:, 4 * OWN:8 * OWN], A.add, ["go"], [("zo", 0, 1)], OPT["ta"])
+            V(0.16, lambda q: q.quantize_mx(T.oq[:, a:a + 128], T["op"][:, a:a + 128], T.zo[:]), ["zo"], [("oq", r, r + 1), ("op", r, r + 1)])
+            send(r, [(T[zq][:, ZC:C].bitcast(dt.uint8), T.oq[:, a:a + OWN].bitcast(dt.uint8), ("oq", r, r + 1)),
+                     (T[zp][:, ZC:C], T["op"][:, a:a + OWN], ("op", r, r + 1))], "az%d" % r, [(zq, 2, 3), (zp, 2, 3)], OPT["zl"])
 
     def bank(out, b, w=C):
         return T[out][:, BANK * b:BANK * b + w]
 
     def parts(name):
-        return enumerate([(0, OPT[name]), (OPT[name], C)])
+        return enumerate([(0, OPT[name]), (OPT[name], ZC if name == "z" else C)])
 
     def mm(out, b, wq, wp, a, xq, xp, unit, h=0, lo=0, hi=C):
         whole = hi - lo == C
         task(P, "t", 0.02 + 0.33 * (hi - lo) / C,
              lambda q: q.matmul_mx(bank(out, b, hi - lo), T[wq][:, a:a + 128], T[wp][:, a:a + 128], T[xq][:, lo:hi], T[xp][:, lo:hi], True, True),
-             [(wq, unit, unit + 1), (wp, unit, unit + 1), xq if whole else (xq, h, h + 1), xp if whole else (xp, h, h + 1)], [(out, b, b + 1)])
+             [(wq, unit, unit + 1), (wp, unit, unit + 1), xq if whole else (xq, h, 2 * h + 1), xp if whole else (xp, h, 2 * h + 1)], [(out, b, b + 1)])
 
     def quantize(xq, xp, X, h, lo, hi):
         V(0.02 + 0.35 * (hi - lo) / C, lambda q: q.quantize_mx(T[xq][:, lo:hi], T[xp][:, lo:hi], T[X][:, 4 * lo:4 * hi]),
@@ -661,13 +783,13 @@ def build(P, g, core, T, topo):
         act(T.gp[:, C * b + lo:C * b + hi], at(win, b).indirect(T[l][:, a + lo // 16:a + hi // 16]),
             [(win, b, b + 1), (l, a + lo // 16, a + hi // 16)], [("gp", b + lo / C, b + hi / C)], gat(hi - lo))
 
-    def add_by(out, win, l, other, h, lo, end, cut, xps=()):
+    def add_by(out, win, l, other, h, lo, end, cut, xps=(), full=C):
         for b in range(4):
             hi, written = end, [(out, 4 * h + b, 4 * h + b + 1)]
             if b not in cut:
                 if h:
                     continue
-                hi, written = C, written + [(out, 4 + b, 5 + b)]
+                hi, written = full, written + [(out, 4 + b, 5 + b)]
             if b in xps:
                 tt(T[out][:, 4 * lo + b:4 * hi:4], T.pu[:, BANK * b + lo:BANK * b + hi], T.gp[:, C * b + lo:C * b + hi], A.add,
                    [("pu", b, b + 1), ("gp", b + lo / C, b + hi / C)], written, ROW * (hi - lo) / C + 0.01)
@@ -679,7 +801,9 @@ def build(P, g, core, T, topo):
         k = task(P, e, 0.07, lambda q: q.dma_start(out, in_), reads, [], "dma", "st", 16)
         task(P, "net", 2.0, None, [], [], "land", "st", 16, after=[k])
 
-    powers("f00")
+    if OPT["fn"][0] in "rs":
+        tt(U("dl0"), T.nxi[:], L("cm"), A.subtract, ["nxi", "cm"], ["dl0"])
+    powers(0)
     for h, (lo, hi) in parts("x"):
         quantize("xq0", "xp0", "x0", h, lo, hi)
     for r in range(ROUNDS):
@@ -687,76 +811,134 @@ def build(P, g, core, T, topo):
         lp, al, f0 = "lp%d" % r, "al%d" % r, "f0%d" % (r % 2)
         xps = OPT["xps"] if r < ROUNDS - 1 else OPT["xpl"]
         for h, (lo, hi) in parts("x"):
-            mm("pw", 2 * h, "uqr", "upr", 0, xq, xp, 0, h, lo, hi)
-            for b in ("sa", "sb"):
-                a = (T[b][:, lo:hi], bank("pw", 2 * h, hi - lo), [("pw", 2 * h, 2 * h + 1)], [(b, h, h + 1)], ROW * (hi - lo) / C + 0.02)
-                if h:
-                    cp(*a)
-                else:
-                    act(*a, only=True)
-        send(r, [(T[aq][:].bitcast(dt.uint8), T[xq][:].bitcast(dt.uint8), xq), (T[ap][:], T[xp][:], xp)], "ax%d" % r, [aq, ap], 6.0)
+            for i, b in enumerate(("sa", "sb")):
+                k = 2 * h + i
+                mm("pw", k, "uqr", "upr", 0, xq, xp, 0, h, lo, hi)
+                act(T[b][:, lo:hi], bank("pw", k, hi - lo), [("pw", k, k + 1)], [(b, h, h + 1)], ROW * (hi - lo) / C + 0.02)
+        if OPT["relay"]:
+            send(r, [(at("hq", r).bitcast(dt.uint8), T[xq][:].bitcast(dt.uint8), xq), (at("hp", r), T[xp][:], xp)], "ax%d" % r, [aq, ap], 8.5, True)
+        else:
+            send(r, [(T[aq][:].bitcast(dt.uint8), T[xq][:].bitcast(dt.uint8), xq), (T[ap][:], T[xp][:], xp)], "ax%d" % r, [aq, ap], 6.0)
         places(r)
-        coarse = steps("c", 0, "sa", range(7), (3, 0))
-        if r:
-            move("b%d" % r, T.dt[:], T.ic[:], ["ic"], ["dt"])
-        move("a%d" % r, T.dt[:], T[f0][:], [f0], ["dt"], True)
-        tt(T.fs[:], by("sa", "l0"), T.dt[:], A.max, ["sa", "dt", "l0"], ["fs"], gat())
-        fine = steps("f", 2, "fs", range(3), (0, 0))
+        s = ("sa", 0, 2)
+        fn = OPT["fn"][r]
+        tt(T.er[:], by("sb", "l0"), at("sa"), A.max, ["sb", s, "l0"], ["er"], gat())
+        tt(T.eh[:], by("er", "l0"), at("sa"), A.max, ["er", s, "l0"], ["eh"], gat())
+        act(T.mfw[:], by("er", "l1"), ["er", "l1"], ["mfw"], gat())
+        tt(T.mfx[:], by("eh", "l2"), T.mfw[:], A.max, ["eh", "mfw", "l2"], ["mfx"], gat())
+        tt(T.mf1[:], by("mfx", "l0"), T.eh[:], A.max, ["mfx", "eh", "l0"], ["mf1"], gat())
+        coarse = steps("c", 0, "mf1", range(3, 7), (3, 0))
+        if fn in "PQ":
+            tt(T.dt[:], by("idr", "l0"), T.ic[:], A.add, ["idr", "l0", "ic"], ["dt"], gat())
+        elif fn in "rs":
+            less("dt", "l0")
+        else:
+            if r:
+                move("b%d" % r, T.dt[:], T.ic[:], ["ic"], ["dt"])
+            move("a%d" % r, T.dt[:], T[f0][:], [f0], ["dt"], True)
+        act(T.pw0[:], by("dt", "l0"), ["dt", "l0"], ["pw0"], gat())
+        if fn in "pPr":
+            lay("t%d" % r, [("pw0", "dt", 1, 2)])
+            act(T.pw1[:], by("pw0", "l2"), ["pw0", "l2"], ["pw1"], gat())
+            rows = [("pw1", "pw0", a, 16) for a in range(4, 8)]
+        else:
+            act(T.pw1[:], by("pw0", "l2"), ["pw0", "l2"], ["pw1"], gat())
+            act(T.pw2[:], by("dt", "l2"), ["dt", "l2"], ["pw2"], gat())
+            rows = [("pw1", b, a, 16) for b, a in (("pw2", 1), ("pw2", 3), ("pw0", 4), ("dt", 5), ("pw0", 6), ("dt", 7))]
+        apart = OPT["ap"][r] == "a"
+        lay("u%d" % r, rows + [("pw1", "eh", 10, 16), ("pw1", "mfw", 9, 16)] * (not apart))
+        act(T.pw2[:], by("pw1", "l1"), ["pw1", "l1"], ["pw2"], gat())
+        lay("s%d" % r, [("fs", b, a, 16) for b, a in (("sa", 14), ("er", 13), ("eh", 12), ("mfw", 11), ("mfx", 8), ("mf1", 15))])
+        if apart:
+            act(T.sb[:], by("er", "l2"), ["er", "l2"], ["sb"], gat())
+            act(T.mf0[:], by("eh", "l1"), ["eh", "l1"], ["mf0"], gat())
+            lay("w%d" % r, [("fs", "sb", 9, 16), ("fs", "mf0", 10, 16)])
+        else:
+            lay("w%d" % r, [("fs", "pw2", 9, 16), ("fs", "pw2", 10, 16)])
+        lay("v%d" % r, [("pw2", "pw1", a, 16) for a in (2, 3, 6, 7)] + [("pw2", "ic", 8, 16)])
+        act(T.mf0[:], by("fs", "l0"), ["fs", "l0"], ["mf0"], gat())
         for b in range(4):
-            if b not in xps:
-                mm("pu", b, "eq", "ep", 128 * b, xq, xp, b)
-                act(at("fo", b), bank("pu", b), [("pu", b, b + 1)], [("fo", b, b + 1)])
+            mm("pu", b, "eq", "ep", 128 * b, xq, xp, b)
+            act(at("fo", b), bank("pu", b), [("pu", b, b + 1)], [("fo", b, b + 1)])
         for b in range(4):
             mm("pu", b, "eq", "ep", 128 * b, aq, ap, b)
             act(at("fh", b), bank("pu", b), [("pu", b, b + 1)], [("fh", b, b + 1)], scale=0.5)
             if b in xps:
                 mm("pu", b, "eq", "ep", 128 * b, xq, xp, b)
-        tt(mid("n1"), by(coarse, "l0"), T.sa[:], A.is_le, [coarse, "l0", "sa"], [("n1", 0, 4)], gat())
+        tt(mid("n1"), by(coarse, "l0"), at("sa"), A.is_le, [coarse, "l0", s], [("n1", 0, 4)], gat())
         turn("tn1", "n1")
-        for h, (a, b) in enumerate([(0, C), (C, TW)]):
+        for h, (a, b) in enumerate([(0, C), (C, TW)][:2 - OPT["one"]]):
             chain(T.r1[:, a:b], T.tn1[:, a:b], T.te1[:, a:b], [("tn1", h, h + 1), ("te1", h, h + 1)], [("r1", h, h + 1)], b - a)
-        ts(T.lq[:], T.r1[:].indirect(T.pick[:, 0:2]), 160.0, None, A.add, None, ["r1", ("pick", 0, 1)], ["lq"], 0.1)
-        tt(T.n2[:], by(fine, "lq"), T.sa[:], A.is_le, [fine, "lq", "sa"], ["n2"], gat())
-        act(T.e2[:], by(fine, "lq"), [fine, "lq", "es", "k2"], ["e2"], gat(), scale=cf("es"), bias=cf("k2"))
+        if OPT["one"]:
+            V(SMALL, lambda q: q.transpose(T.r1[:, 592:624], T.r1[:, 15:512:16]), [("r1", 0, 2)], [("r1", 3, 4)])
+            V(SMALL, lambda q: q.transpose(T.r1[:, 512:576], T.r1[:, 576:640]), [("r1", 3, 4)], [("r1", 2, 3)])
+        got = T.r1[:, 0:576 if OPT["one"] else TW].indirect(T.pick[:, 0:2])
+        act(U("lq", 32), got, [("r1", 0, 3), ("pick", 0, 1)], ["lq"], 0.1, bias=160.0)
+        tt(T.n2[:], by("mf0", "lq"), at("sa"), A.is_le, ["mf0", "lq", s], ["n2"], gat())
+        act(T.e2[:], by("pw2", "lq"), ["pw2", "lq", "e8"], ["e2"], gat(), scale=cf("e8"))
         for x in ("n2", "e2"):
             V(HALF, lambda q, x=x: q.transpose(T["t" + x][:], T[x][:]), [x], ["t" + x])
-        for x, j in (("rp", 1), ("rb", 0)):
-            chain(T[x][:, 0:C - 7], T.tn2[:, 7:C], T.te2[:, j:C - 7 + j], ["tn2", "te2"], [x])
-        tt(L("ta"), every("tn2", 14), every("r1", 15), A.mult, ["tn2", ("r1", 0, 1)], ["ta"])
-        tt(L("ua"), every("r1", 15), L("ta"), A.subtract, [("r1", 0, 1), "ta"], ["ua"])
-        home(r, 0, every("rp", 7), L("ua"), A.add, ["rp", "ua"])
-        tt(L("tb"), every("tn2", 15), L("ct"), A.mult, ["tn2", "ct"], ["tb"])
-        tt(L("yb"), every("rb", 8), L("tb"), A.subtract, ["rb", "tb"], ["yb"])
-        home(r, 1, every("rb", 7), L("yb"), A.subtract, ["rb", "yb"])
-        tt(T.er[:], T.sa[:].indirect(T[lp][:, B0:B0 + NB]), T.sg[:], A.mult, ["sa", "sg", (lp, B0, B0 + NB)], ["er"], gat())
-        act(T.eh[:], T.er[:], ["er"], ["eh"], scale=-1.0)
+        chain(T.rp[:, 0:C - 7], T.tn2[:, 7:C], T.te2[:, 1:C - 6], ["tn2", "te2"], [("rp", 0, C)])
+        home(r, 0)
+        tt(L("ua", 32), got, L("cw", 32), A.add, [("r1", 0, 3), ("pick", 0, 1), "cw"], ["ua"], 0.1)
+        tt(L("ta"), every("r1", 15), T.cq[:, 0:NB], A.subtract, ["cq", ("r1", 0, 1)], ["ta"])
+        tt(every("te2", 7), every("te2", 7), L("ta"), A.add, ["te2", "ta"], ["te2"])
+        chain(T.rb[:, 0:C - 7], T.tn2[:, 7:C], T.te2[:, 0:C - 7], ["tn2", "te2"], ["rb"])
+        home(r, 1)
+        if OPT["tw"]:
+            act(at("sa", 1), at("sa"), [s], [("sa", 2, 3)], scale=-1.0)
+            for i, b in enumerate(("er", "eh")):
+                tt(T.le[:, 32 * i:32 * i + NB], T[lp][:, B0:B0 + NB], L("c%d" % i), A.add, [(lp, B0, B0 + NB), "c%d" % i], [("le", i, i + 1)])
+                act(T[b][:], T.sa[:].indirect(T.le[:, 32 * i:32 * i + NB]), ["sa", ("le", i, i + 1)], [b], gat())
+        else:
+            tt(T.er[:], at("sa").indirect(T[lp][:, B0:B0 + NB]), T.sg[:], A.mult, [s, "sg", (lp, B0, B0 + NB)], ["er"], gat())
+            act(T.eh[:], T.er[:], ["er"], ["eh"], scale=-1.0)
         tt(T.sw[:], by("er", "mt16"), T.eh[:], A.is_gt, ["er", "eh", "mt16"], ["sw"], gat())
         weighted("swn", "sw")
-        if r < ROUNDS - 1:
-            act(T.fm[:], by(f0, "mt16"), [f0, "mt16"], ["fm"], gat(), scale=1.0 / HIGH)
+        if r < ROUNDS - 1 and OPT["ex"][r] == "s":
+            f1 = "f0%d" % (1 - r % 2)
+            tt(L("sx"), every("swn", 15), L("dm"), A.mult, ["swn", "dm"], ["sx"])
+            tt(U("sig"), L("sx"), L("dc"), A.add, ["sx", "dc"], ["sig"])
+            act(T[f1][:], by(f0, "sig"), [f0, "sig"], [f1], gat())
+            weighted("fmn", f1)
+            act(U("l0"), every("fmn", 15), ["fmn", "col"], ["l0"], 0.1, bias=cf("col"))
+            if OPT["fn"][r + 1] in "rs":
+                tt(U("dl0"), every("fmn", 15), L("cn"), A.subtract, ["fmn", "cn"], ["dl0"])
+            powers(r + 1, False)
+        elif r < ROUNDS - 1:
+            act(T.fm[:], by(f0, "mt16"), [f0, "mt16"], ["fm"], gat())
             weighted("fmn", "fm")
-            cp(L("fl"), T.l0[:], ["l0"], ["fl"])
+            cp(L("fl"), U("l0"), ["l0"], ["fl"])
             act(L("be"), L("fl"), ["fl", "nc"], ["be"], SMALL, bias=cf("nc"))
             tt(L("dn"), every("fmn", 15), L("be"), A.subtract, ["fmn", "be"], ["dn"])
             act(L("bf"), L("dn"), ["dn", "f0"], ["bf"], SMALL, scale=cf("f0"))
             tt(L("de"), L("bf"), L("fl"), A.add, ["bf", "fl"], ["de"])
             tt(L("sx"), every("swn", 15), L("dn"), A.mult, ["swn", "dn"], ["sx"])
-            tt(T.l0[:], L("sx"), L("de"), A.add, ["sx", "de"], ["l0"])
-            powers("f0%d" % (1 - r % 2))
+            tt(U("l0"), L("sx"), L("de"), A.add, ["sx", "de"], ["l0"])
+            if OPT["fn"][r + 1] in "rs":
+                tt(L("be"), L("de"), L("cm"), A.subtract, ["de", "cm"], ["be"])
+                tt(U("dl0"), L("sx"), L("be"), A.add, ["sx", "be"], ["dl0"])
+            powers(r + 1)
         else:
             tt(L("sx"), every("swn", 15), L("dm"), A.mult, ["swn", "dm"], ["sx"])
-            tt(T.sig[:], L("sx"), L("dc"), A.add, ["sx", "dc"], ["sig"])
-            act(T.er[:], by(f0, "sig"), [f0, "sig"], ["er"], gat(), scale=1.0 / HIGH, bias=160.0)
+            tt(U("sig"), L("sx"), L("dc"), A.add, ["sx", "dc"], ["sig"])
+            act(T.er[:], by(f0, "sig"), [f0, "sig"], ["er"], gat(), bias=160.0)
             store("y", T.nf[:], T.er[0:128:16, :], ["er"])
         for b in range(4):
-            for h, (lo, hi) in parts("z") if b in OPT["zg"] else [(0, (0, C))]:
+            for h, (lo, hi) in parts("z") if b in OPT["zg"] else [(0, (0, ZC))]:
                 look("fh", al, 0, b, lo, hi)
         for h, (lo, hi) in parts("z"):
-            add_by("z", "fh", al, "gp", h, lo, hi, OPT["zs"])
-            quantize("zq", "zp", "z", h, lo, hi)
+            add_by("z", "fh", al, "gp", h, lo, hi, OPT["zs"], (), ZC)
+            quantize("zq%d" % r, "zp%d" % r, "z", h, lo, hi)
+            hi = C if h else hi
             for b in range(4):
                 ps = "pu" if h and b not in xps else "pw"
-                mm(ps, b, "wq", "wp", 128 * b, "zq", "zp", b, h, lo, hi)
+                if b not in OPT["hs"]:
+                    if h:
+                        mm("pw", b, "wq", "wp", 128 * b, "zq%d" % r, "zp%d" % r, b)
+                        act(at("h", b), bank("pw", b), [("pw", b, b + 1)], [("h", b, b + 1)], scale=0.03125)
+                    continue
+                mm(ps, b, "wq", "wp", 128 * b, "zq%d" % r, "zp%d" % r, b, h, lo, hi)
                 act(T.h[:, C * b + lo:C * b + hi], bank(ps, b, hi - lo), [(ps, b, b + 1)], [("h", b + lo / C, b + hi / C)],
                     ROW * (hi - lo) / C + 0.02, scale=0.03125)
         for b in xps:
@@ -775,8 +957,28 @@ def build(P, g, core, T, topo):
     return sent[0]
 
 
+def neighbour(core, T, topo):
+    return [c for c in topo.cores_of(core) if T.rank_of(c) is None and topo.die(c) == topo.die(core)
+            and all(topo.may_write(c, d) for d in T.cores if d != core)][0]
+
+
+def hand_on(g, core, rank, T, topo):
+    sent = 0
+    for r in range(ROUNDS):
+        dst = T.cores[(rank + r + 1) % len(T.cores)]
+        rid, pid, _ = topo.addr(dst)
+        g.wait_ge(T.sem["hx%d" % r], 2 * len(topo.engines(T.cores[rank], core)))
+        for out, in_ in ((T["aq%d" % r][:].bitcast(dt.uint8), T.hq[:, C * r:C * r + C].bitcast(dt.uint8)), (T["ap%d" % r][:], T.hp[:, C * r:C * r + C])):
+            g.remote_dma(out, in_, T.sem["ax%d" % r], T.sem.snd, pid, rid, topo.mask(core, dst))
+            sent += len(topo.engines(core, dst))
+    g.wait_ge(T.sem.snd, sent)
+
+
 def rank_program(g, core, T, topo):
     if T.rank_of(core) is None:
+        for rank, c in enumerate(T.cores):
+            if OPT["relay"] and neighbour(c, T, topo) == core:
+                hand_on(g, core, rank, T, topo)
         return
     P = new_plan()
     sent = build(P, g, core, T, topo)

import math
import numpy as np
from concourse.mybir import dt, AluOpType, ActivationFunctionType, AxisListType
A = AluOpType
AF = ActivationFunctionType
C = 320
BANK = 512
ROUNDS = 3
BIG = 1e29
OWN = 64
ZC = C - OWN
KEY = 1024.0
HIGH = 2.0 ** 75
BASE = 512.0
NB = C // 16
B0 = 32
PW = C + 32
TW = C + PW
YW = 256


def sb(n, d):
    return ("sbuf", [128, n], d)


SCRATCH = {
    "x0": sb(4 * C, "bfloat16"), "ut": sb(512, "bfloat16"), "vt": sb(512, "bfloat16"),
    "nxi": sb(20, "int32"), "mti": sb(20, "int32"),
    "wq": sb(512, "float8_e4m3fn_x4"), "wp": sb(512, "uint8"),
    "uq": sb(128, "float8_e4m3fn_x4"), "up": sb(128, "uint8"),
    "uqr": sb(128, "float8_e4m3fn_x4"), "upr": sb(128, "uint8"),
    "vq": sb(128, "float8_e4m3fn_x4"), "vp": sb(128, "uint8"),
    "eq": sb(512, "float8_e4m3fn_x4"), "ep": sb(512, "uint8"),
    "one": sb(528, "bfloat16"), "big": sb(528, "bfloat16"),
    "ji": sb(16, "int32"), "t1": sb(32, "bfloat16"), "w16": sb(16, "bfloat16"),
    "wt": sb(C, "bfloat16"), "idr": sb(C, "bfloat16"), "ic": sb(C, "float32"), "sg": sb(C, "bfloat16"),
    "gs": sb(C, "bfloat16"), "ft": sb(5 * C, "bfloat16"),
    "cq": sb(48, "float32"), "idk": sb(C, "float32"), "le": sb(64, "uint16"),
    "pw0": sb(C, "float32"), "pw1": sb(C, "float32"), "pw2": sb(C, "float32"),
    "pi": sb(48, "int32"), "pa": sb(32, "int32"), "ci": sb(32, "int32"), "sh": sb(10, "int32"), "bits": sb(10, "int32"),
    "uo": sb(8, "uint16"), "pick": sb(6, "uint16"),
    "cf": sb(64, "float32"),
    "wd": sb(2 * C, "float32"), "d1": sb(C, "float32"),
    "hq": sb(ROUNDS * C, "float8_e4m3fn_x4"), "hp": sb(ROUNDS * C, "uint8"),
    "sa": sb(2 * C, "float32"), "sb": sb(C, "float32"), "fs": sb(C, "float32"), "dt": sb(C, "float32"),
    "n1": sb(PW, "bfloat16"), "e1": sb(PW, "float16"), "tn1": sb(TW, "bfloat16"), "te1": sb(TW, "float16"), "r1": sb(TW, "bfloat16"),
    "n2": sb(C, "bfloat16"), "e2": sb(C, "float16"), "tn2": sb(C, "bfloat16"), "te2": sb(C, "float16"),
    "rb": sb(C, "float16"), "rp": sb(640, "bfloat16"), "yy": sb(224, "float32"),
    "f00": sb(C, "bfloat16"), "f01": sb(C, "bfloat16"), "fa": sb(2 * C, "bfloat16"), "fm": sb(C, "bfloat16"),
    "scn": sb(C, "float16"), "swn": sb(C, "float16"), "fmn": sb(C, "float16"),
    "er": sb(C, "float32"), "eh": sb(C, "float32"), "sw": sb(C, "bfloat16"),
    "fo": sb(4 * C, "bfloat16"), "fh": sb(4 * C, "bfloat16"), "gp": sb(4 * C, "bfloat16"),
    "z": sb(4 * ZC, "bfloat16"), "go": sb(8 * OWN, "bfloat16"), "zo": sb(512, "bfloat16"),
    "oq": sb(128 * ROUNDS, "float8_e4m3fn_x4"), "op": sb(128 * ROUNDS, "uint8"),
    "h": sb(4 * C, "bfloat16"),
    "pu": ("psum", [128, 2048], "float32"), "pw": ("psum", [128, 2048], "float32"),
}
for _n in ("c", "f", "e"):
    for _k in ("0", "1", "w", "x"):
        SCRATCH["m" + _n + _k] = sb(C, "float32")
LISTS = ["cw", "pk", "dm", "dc", "fl", "be", "dn", "bf", "de", "sx", "ta", "ua", "c0", "c1", "cm", "cn"]
SCRATCH["sml"] = sb(32 * len(LISTS), "float32")
COLS = {"sc": 0, "bi": 12, "bt": 24}
for _n in ("e15", "col", "f0", "nc", "a1", "b1", "k1", "e0", "par", "dd", "p21", "kv", "ka", "na", "nv", "kr", "m1", "d0", "e8", "up_"):
    COLS[_n] = 33 + len(COLS)
OFFSETS = ["l0", "l1", "l2", "l3", "l4", "l5", "mt16", "so", "lq", "sig", "dl0", "dl3"]
SCRATCH["lu"] = sb(32 * len(OFFSETS), "uint16")
for _r in range(ROUNDS + 1):
    if _r:
        SCRATCH["x%d" % _r] = sb(4 * C, "bfloat16")
    SCRATCH["xq%d" % _r] = sb(C, "float8_e4m3fn_x4")
    SCRATCH["xp%d" % _r] = sb(C, "uint8")
for _r in range(ROUNDS):
    SCRATCH["aq%d" % _r] = sb(C, "float8_e4m3fn_x4")
    SCRATCH["ap%d" % _r] = sb(C, "uint8")
    SCRATCH["zq%d" % _r] = sb(C, "float8_e4m3fn_x4")
    SCRATCH["zp%d" % _r] = sb(C, "uint8")
    SCRATCH["lp%d" % _r] = sb(2 * B0, "uint16")
    SCRATCH["al%d" % _r] = sb(B0 + NB, "uint16")
SEMAPHORES = ["ev", "es", "et", "eg", "snd", "st"]
SEMAPHORES += ["%s%d" % (_n, _r) for _n in ("ax", "ap", "ab", "az", "hx") for _r in range(ROUNDS)]
SEMAPHORES += ["ld_" + _n for _n in ("x", "u", "v", "nx", "mt", "wc", "ws", "sg")]
SEMAPHORES += ["ld_%s%d" % (_n, _r) for _n in ("g0", "g1", "g2", "g3", "a", "b", "s", "t", "u", "v", "w") for _r in range(ROUNDS)]

GATHER, HALF, ROW, SMALL = 0.58, 0.17, 0.34, 0.08
COSTS = [(0.65, 0.8, 0.85, 0.17, 0.15, 0.05), (1.0, 1.0, 1.0, 0.2, 0.17, 0.06), (0.75, 0.85, 0.85, 0.17, 0.19, 0.02)]
SPAN = 120
SHARED = {}
OPT = {"x": 192, "z": 128, "zg": [0], "zs": [0, 3], "xs": [3], "xps": [3], "xpl": [2, 3], "seed": 4,
       "pl": "vnn", "ex": "nn", "fn": "Qpp", "tw": 0, "relay": 1, "one": 0, "ap": "nnn", "hs": [0, 1, 2, 3], "cut": [], "ll": 2.6, "zl": 2.9, "ta": 0.5}


def new_plan():
    return {"tasks": [], "w": {}, "r": {}}


def overlap(a, b):
    return a[0] < b[1] and b[0] < a[1]


def gat(n=C):
    return ("gather", 0.06 + (GATHER - 0.06) * n / C)


def cost(t, e, w, c):
    if e in "vs":
        return c[5] + (0.06 + (w - 0.06) * c[0] if t["gather"] else max(0.07, w * c[1]) if w > 0.125 else 0.07)
    return w * c[2] if e == "net" else w


def task(P, eng, dur, fn, reads, writes, kind="op", sem=None, inc=1, after=(), alt=None):
    def reg(x):
        return (x, 0, 1 << 20) if isinstance(x, str) else x
    n = len(P["tasks"])
    gather = isinstance(dur, tuple)
    deps = set(after)
    rd, wr = [reg(x) for x in reads], [reg(x) for x in writes]
    for b, lo, hi in rd:
        deps.update(t for l, h, t in P["w"].get(b, []) if overlap((lo, hi), (l, h)))
        if b in ("pu", "pw"):
            deps.update(t for l, h, t in P["r"].get(b, []) if overlap((lo, hi), (l, h)) and (P["tasks"][t]["eng"] != eng or alt or P["tasks"][t]["alt"]))
    for b, lo, hi in wr:
        deps.update(t for l, h, t in P["w"].get(b, []) + P["r"].get(b, []) if overlap((lo, hi), (l, h)))
    for b, lo, hi in wr:
        P["w"][b] = [e for e in P["w"].get(b, []) if not (lo <= e[0] and e[1] <= hi)] + [(lo, hi, n)]
        P["r"][b] = [e for e in P["r"].get(b, []) if not (lo <= e[0] and e[1] <= hi)]
    for b, lo, hi in rd:
        P["r"].setdefault(b, []).append((lo, hi, n))
    P["tasks"].append({"eng": eng, "dur": dur[1] if gather else dur, "fn": fn, "deps": sorted(deps), "kind": kind, "sem": sem, "inc": inc,
                       "gather": gather, "alt": alt})
    return n


def schedule(P, tries=500, moves=35000, starts=7, last=120000, heat=0.04, sweeps=4):
    ts = P["tasks"]
    n = len(ts)
    ways = [[(e, cost(t, e, w, COSTS[0])) for e, w in [(t["eng"], t["dur"])] + ([t["alt"][:2]] if t["alt"] else [])] for t in ts]
    hop, same = COSTS[0][3:5]
    pre = [t["deps"] for t in ts]
    post = [[] for _ in range(n)]
    for i in range(n):
        for d in pre[i]:
            post[d].append(i)

    def place(rank, pre, post, lean):
        left = [len(x) for x in pre]
        ready = [i for i in range(n) if not left[i]]
        lines = {e: [] for e in "vstgy"}
        end, eng, dur = [0.0] * n, [""] * n, [0.0] * n
        while ready:
            i = ready[0]
            for k in ready:
                if rank[k] < rank[i]:
                    i = k
            ready.remove(i)
            best = None
            for e, w in ways[i]:
                at, k = 0.0, 0
                for d in pre[i]:
                    x = end[d] + (same if eng[d] == e else hop)
                    if x > at:
                        at = x
                if e != "net":
                    line = lines[e]
                    k = len(line)
                    while k and line[k - 1][1] > at:
                        k -= 1
                    while k < len(line) and at + w > line[k][0] + 1e-9:
                        at = max(at, line[k][1])
                        k += 1
                x = at + w + (lean[i] if e == "v" else 0.0)
                if best is None or x < best[0]:
                    best = (x, e, w, at, k)
            _, e, w, at, k = best
            if e != "net":
                lines[e].insert(k, (at, at + w))
            end[i], eng[i], dur[i] = at + w, e, w
            for s in post[i]:
                left[s] -= 1
                if not left[s]:
                    ready.append(s)
        return max(end), end, eng, dur, lean
    up = [w[0][1] for w in ways]
    for i in range(n - 1, -1, -1):
        for d in pre[i]:
            up[d] = max(up[d], ways[d][0][1] + hop + up[i])
    rng = np.random.default_rng(OPT["seed"])
    pool = []
    for _ in range(starts):
        best = now = place([-x for x in up], pre, post, [0.5] * n)
        for k in range(tries):
            rank = -np.array(now[1])
            at, width = -rng.random() * now[0], [2.0, 4.0, 8.0][rng.integers(3)]
            part, step = [0.05, 0.15, 0.4][rng.integers(3)], [0.3, 1.0, 3.0][rng.integers(3)]
            near = abs(rank - at) < width
            hit = (rng.random(n) < part) & near
            lean = np.where((rng.random(n) < 0.2) & near, rng.random(n) * 2.0 - 0.5, now[4]).tolist()
            back = place((rank + hit * rng.standard_normal(n) * step).tolist(), post, pre, lean)
            got = place([-x for x in back[1]], pre, post, lean)
            if got[0] - now[0] <= -(0.005 + 0.05 * (1 - k / tries)) * math.log(1 - rng.random()):
                now = got
                if got[0] < best[0]:
                    best = got
        seq = sorted(range(n), key=lambda i: (best[1][i] - best[3][i], i))
        pool.append(refine(P, seq, best[2], post, moves, heat, sweeps, rng))
    best = min(pool)
    for other in pool + pool:
        for k in range(20, n, 12):
            for a, b in ((best, other), (other, best)):
                head = set(a[1][:k])
                best = min(best, refine(P, a[1][:k] + [i for i in b[1] if i not in head],
                                        [a[2][i] if i in head else b[2][i] for i in range(n)], post, 0, 0, 0, rng))
    v, seq, eng, start = refine(P, best[1], best[2], post, last, heat / 2, sweeps, rng)
    return {e: [i for i in seq if eng[i] == e] for e in "vstgy"}, start, v


def refine(P, seq, eng, succ, moves, heat, sweeps, rng):
    ts = P["tasks"]
    n = len(ts)
    ways = [{e: [cost(t, e, w, c) for c in COSTS] for e, w in [(t["eng"], t["dur"])] + ([t["alt"][:2]] if t["alt"] else [])} for t in ts]
    deps = [t["deps"] for t in ts]
    K = range(len(COSTS))
    wait = [c[3:5] for c in COSTS]
    end, tail = [[0.0] * (n + 1) for _ in K], [[0.0] * (n + 1) for _ in K]
    prv = [n] * (n + 1)

    def forward(seq, last):
        last = dict(last)
        for i in seq:
            e = eng[i]
            prv[i] = last.get(e, n)
            if e != "net":
                last[e] = i
        for k in K:
            en, w = end[k], wait[k]
            for i in seq:
                at, e = en[prv[i]], eng[i]
                for d in deps[i]:
                    x = en[d] + w[eng[d] == e]
                    if x > at:
                        at = x
                en[i] = at + ways[i][e][k]
        return last

    def backward(seq, first):
        for k in K:
            ta, w, nxt = tail[k], wait[k], dict(first)
            for i in reversed(seq):
                e = eng[i]
                at = ta[nxt.get(e, n)]
                for s in succ[i]:
                    x = ta[s] + w[eng[s] == e]
                    if x > at:
                        at = x
                ta[i] = at + ways[i][e][k]
                if e != "net":
                    nxt[e] = i
        return nxt

    def through(some, last, first, pos, b):
        out = []
        for k in K:
            en, ta, w, top, at = end[k], tail[k], wait[k], n, 0.0
            for i in some:
                x, e = 0.0, eng[i]
                for s in succ[i]:
                    if pos[s] >= b and ta[s] + w[eng[s] == e] > x:
                        x = ta[s] + w[eng[s] == e]
                if en[i] + x > at:
                    top, at = i, en[i] + x
            for e, i in last.items():
                if en[i] + ta[first.get(e, n)] > at:
                    top, at = i, en[i] + ta[first.get(e, n)]
            out.append((at, top))
        return out

    def arcs(k, i, inside):
        en, w, out = end[k], wait[k], []
        while i in inside:
            e = eng[i]
            at = en[i] - ways[i][e][k] - 1e-9
            if prv[i] < n and en[prv[i]] >= at:
                if prv[i] in inside:
                    out.append((prv[i], i))
                i = prv[i]
            else:
                i = ([d for d in deps[i] if en[d] + w[eng[d] == e] >= at] + [n])[0]
        return out

    def stretch(seq, lo, hi, moves, heat):
        before, after = forward(seq[:lo], {}), backward(seq[hi:], {})
        win, m = seq[lo:hi], hi - lo
        inside, pos = set(win), [m] * n
        for p, i in enumerate(win):
            pos[i] = p
        past = [x for x, _ in through(seq[:lo], {}, {}, [m if p >= hi else -1 for p in sorted(range(n), key=lambda p: seq[p])], m)]
        free = [i for i in win if ts[i]["alt"]]
        got = through(win, forward(win, before), after, pos, m)
        now = sum(max(x, y) for (x, _), y in zip(got, past)) / len(end)
        best, fresh = (now, win, eng[:]), m
        for it, r in enumerate(rng.random((moves, 6)).tolist()):
            if fresh:
                crit = [x for k in K if got[k][0] >= past[k] for x in arcs(k, got[k][1], inside)]
                lines = {e: [] for e in "vstgy"}
                lasts, last = [], before
                for p, i in enumerate(win):
                    pos[i] = p
                    lasts.append(last)
                    if eng[i] != "net":
                        lines[eng[i]].append(i)
                        last = dict(last)
                        last[eng[i]] = i
                firsts, first = [after] * (m + 1), after
                for p in range(m - 1, -1, -1):
                    if eng[win[p]] != "net":
                        first = dict(first)
                        first[eng[win[p]]] = win[p]
                    firsts[p] = first
                backward(win[:fresh], firsts[fresh])
                fresh = 0
            flip = free[int(r[1] * len(free))] if r[0] < 0.1 and free else None
            if flip is not None:
                eng[flip] = "v" if eng[flip] == "s" else "s"
                a = pos[flip]
                b, span = a + 1, [flip]
            else:
                if r[0] < 0.7 and crit:
                    a, b = crit[int(r[1] * len(crit))]
                    line = lines[eng[a]]
                    k, d = line.index(a), int(r[2] ** 2 * 5) if r[0] < 0.55 else int(r[2] * 30)
                    i, j = (a, line[min(k + 1 + d, len(line) - 1)]) if r[3] < 0.5 else (b, line[max(k - d, 0)])
                else:
                    line = lines["vs"[int(r[1] * 2)]] or [n]
                    k, w = int(r[2] * len(line)), 4 if r[3] < 0.6 else 12 if r[3] < 0.85 else 30
                    i, j = line[k], line[min(max(k + int((r[4] * 2 - 1) * w), 0), len(line) - 1)]
                    if i == j:
                        continue
                p, q, need = pos[i], pos[j], {i}
                a, b = min(p, q), max(p, q) + 1
                span = win[a:b]
                if q < p:
                    want = set(deps[i])
                    for u in reversed(span[:-1]):
                        if u in want:
                            need.add(u)
                            want.update(deps[u])
                            want.add(prv[u])
                else:
                    for u in span[1:]:
                        if (prv[u] in need and prv[u] != i) or any(d in need for d in deps[u]):
                            need.add(u)
                if j in need:
                    continue
                span = [u for u in span if (u in need) == (q < p)] + [u for u in span if (u in need) != (q < p)]
            limit = now - (0.002 + heat * (1 - it / moves)) * math.log(1 - r[5])
            kept = [(i, prv[i], [en[i] for en in end]) for i in span]
            last = forward(span, lasts[a])
            if sum(x for x, _ in through(span, last, firsts[b], pos, b)) <= limit * len(end):
                new = win[:a] + span + win[b:]
                kept += [(i, prv[i], [en[i] for en in end]) for i in win[b:]]
                ways_out = through(new, forward(win[b:], last), after, pos, m)
                v = sum(max(x, y) for (x, _), y in zip(ways_out, past)) / len(end)
                if v <= limit:
                    now, win, got, fresh = v, new, ways_out, b
                    if it % 8 == 0:
                        win, fresh = sorted(win, key=lambda i: end[0][i] - ways[i][eng[i]][0]), m
                    if v < best[0] - 1e-9:
                        best = (v, win, eng[:])
                    continue
            for i, p, x in kept:
                prv[i] = p
                for en, y in zip(end, x):
                    en[i] = y
            if flip is not None:
                eng[flip] = "v" if eng[flip] == "s" else "s"
        eng[:] = best[2]
        seq = seq[:lo] + best[1] + seq[hi:]
        forward(seq, {})
        return sorted(seq, key=lambda i: end[0][i] - ways[i][eng[i]][0])
    spots = [(lo, s) for s in range(sweeps) for lo in range(-(s * 23 % 40), n - SPAN // 2, SPAN // 2)]
    for lo, s in spots:
        seq = stretch(seq, max(lo, 0), min(lo + SPAN, n), moves // len(spots), heat * (1 - 0.5 * s / sweeps))
    forward(seq, {})
    start = [end[0][i] - ways[i][eng[i]][0] for i in range(n)]
    return sum(max(e) for e in end) / len(end), sorted(seq, key=lambda i: start[i]), eng, start


def issue(P, order, start, g, T):
    ts = P["tasks"]
    queue = {"v": g.vector, "s": g.scalar, "t": g.tensor, "g": g, "y": g.sync}
    counter = {"v": "ev", "s": "es", "t": "et", "g": "eg"}
    mark, count = {}, {}
    for e, line in order.items():
        for i in line:
            t = ts[i]
            if t["kind"] == "op":
                count[counter[e]] = count.get(counter[e], 0) + 1
                mark[i] = (counter[e], count[counter[e]])
    for i, t in enumerate(ts):
        if t["kind"] == "land":
            mark[i] = (t["sem"], t["inc"])
    seen = {e: {} for e in queue}
    known = {}
    where = {i: e for e, line in order.items() for i in line}
    for i in sorted(where, key=lambda i: start[i]):
        t, e = ts[i], where[i]
        q, have, fn = queue[e], seen[e], t["fn"] if e == t["eng"] else t["alt"][2]
        need = {}
        for d in t["deps"]:
            if d in mark:
                s, v = mark[d]
                need[s] = max(need.get(s, 0), v)
        for s, v in sorted(need.items()):
            if have.get(s, 0) < v:
                q.wait_ge(T.sem[s], v)
                have[s] = v
        for d in t["deps"]:
            for s, v in known.get(d, {}).items():
                have[s] = max(have.get(s, 0), v)
        if t["kind"] == "op":
            fn(q).then_inc(T.sem[mark[i][0]], 1)
            known[i] = dict(have)
            known[i][mark[i][0]] = max(have.get(mark[i][0], 0), mark[i][1])
        elif t["kind"] == "dma":
            fn(q).then_inc(T.sem[t["sem"]], 16)
        else:
            fn(q)
    return count


def build(P, g, core, T, topo):
    rank = T.rank_of(core)
    n = len(T.cores)

    def L(name, w=NB):
        i = LISTS.index(name)
        return T.sml[:, 32 * i:32 * i + w]

    def cf(name, i=0, w=1, step=1):
        return T.cf[:, COLS[name] + i:COLS[name] + i + w * step:step]

    def V(dur, fn, reads, writes):
        return task(P, "v", dur, fn, reads, writes)

    def K(dur, fn, reads, writes):
        return task(P, "g", dur, fn, reads, writes)

    def whole(dur, out, pattern, base, step, writes):
        return K(dur, lambda q: q.iota(out, pattern, base, step, allow_small_or_imprecise_dtypes=True), [], writes)

    def ts(out, in_, s1, s2, op0, op1, reads, writes, dur=SMALL):
        if op1 is None:
            return V(dur, lambda q: q.tensor_scalar(out, in_, s1, None, op0), reads, writes)
        return V(dur, lambda q: q.tensor_scalar(out, in_, s1, s2, op0, op1), reads, writes)

    def tt(out, a, b, op, reads, writes, dur=SMALL):
        return V(dur, lambda q: q.tensor_tensor(out, a, b, op), reads, writes)

    def cp(out, in_, reads, writes, dur=SMALL):
        return V(dur, lambda q: q.tensor_copy(out, in_), reads, writes)

    def act(out, in_, reads, writes, dur=ROW, scale=None, bias=None, short=False, only=False):
        kw = {k: x for k, x in (("scale", scale), ("bias", bias)) if x is not None}
        f = AF.Copy if bias is None or isinstance(bias, float) else AF.Identity

        def on_v(q):
            if scale is None and bias is None:
                return q.tensor_copy(out, in_)
            if bias is None:
                return q.tensor_scalar(out, in_, scale, None, A.mult)
            if scale is None:
                return q.tensor_scalar(out, in_, bias, None, A.add)
            return q.tensor_scalar(out, in_, scale, bias, A.mult, A.add)
        w = dur[1] if isinstance(dur, tuple) else dur / 2 if short else dur
        return task(P, "s", dur, lambda q: q.activation(out, in_, f, **kw), reads, writes, alt=None if only else ("v", w, on_v))

    def every(b, k):
        return T[b][:, k:C:16]

    def at(b, a=0):
        return T[b][:, C * a:C * a + C]

    def U(name, w=NB):
        i = OFFSETS.index(name)
        return T.lu[:, 32 * i:32 * i + w]

    def by(b, l, a=0):
        return at(b, a).indirect(U(l))

    def mid(b):
        return T[b][:, 16:16 + C]

    def load(q, name, out, in_, writes, latency, after=()):
        k = task(P, q, 0.07, lambda q: q.dma_start(out, in_), [], [], "dma", "ld_" + name, 16, after=after)
        return task(P, "net", latency, None, [], writes, "land", "ld_" + name, 16, after=[k])

    def move(name, out, in_, reads, writes, add=False):
        if add:
            k = task(P, "g", 2.0 if name == "a0" else 1.0, lambda q: q.dma_start(out, in_, accum_op=A.add), reads, writes, "dma", "ld_" + name, 16)
        else:
            k = task(P, "y", 0.07, lambda q: q.dma_start(out, in_), reads, writes, "dma", "ld_" + name, 16)
        task(P, "net", 2.8 if add else 2.2, None, reads, writes, "land", "ld_" + name, 16, after=[k])

    def lay(name, rows):
        def region(b, a, step):
            return [(b, 16 + x, 17 + x) for x in range(a, 16, step)] + [(b, 0, 2)] * (b == "sa")
        ks = [task(P, "y", 0.07, lambda q, d=d, b=b, a=a, step=step: q.dma_start(T[d][a:128:step, 0:C], T[b][a:128:step, 0:C]), region(b, a, step),
                   region(d, a, step), "dma", "ld_" + name, 16) for d, b, a, step in rows]
        task(P, "net", 2.2, None, [x for _, b, a, step in rows for x in region(b, a, step)], [x for d, _, a, step in rows for x in region(d, a, step)],
             "land", "ld_" + name, 16 * len(rows), after=ks)

    k = load("y", "nx", T.nxi[:], T.nx[:], ["nxi"], 2.0)
    j = load("s", "u", T.ut[:], T.u[:], ["ut"], 2.4, [K(0.19, lambda q: q.iota(T.pa[:], [[0, 32]], 0, 1), [], ["pa"])])
    load("s", "mt", T.mti[:], T.mt[:], ["mti"], 2.4, [j - 1])
    k = load("y", "x", T.x0[:], T.x[:], ["x0"], 3.0, [k - 1])
    load("y", "wc", T.wq[:].bitcast(dt.uint8), T.wc[:], ["wq"], 3.0, [k])
    load("y", "ws", T.wp[:], T.ws[:], ["wp"], 3.0, [k])
    load("y", "v", T.vt[:], T.v[:], ["vt"], 3.0, [k])

    K(0.16, lambda q: q.iota(T.ji[:], [[1, 16]], 0, -1), [], ["ji"])
    K(0.67, lambda q: q.iota(T.idr[:], [[1, C]], -160, 0, allow_small_or_imprecise_dtypes=True), [], ["idr"])
    K(0.19, lambda q: q.iota(T.ci[:], [[16, 32]], 0, 0), [], ["ci"])
    for k in range(5):
        K(0.14, lambda q, k=k: q.iota(T.sh[:, 2 * k:2 * k + 2], [[-(16 >> k), 2]], 127 * (16 >> k), -(16 >> k)), [], [("sh", k, k + 1)])
    for h, (a, b) in enumerate([(0, NB), (NB, 48)]):
        whole(0.17, T.cq[:, a:b], [[32, (b - a) // 2], [0, 2]], -160 - 16 * h, 0, [("cq", h, h + 1)])
    K(0.21, lambda q: q.iota(T.pi[:], [[0, 48]], 0, 1), [], ["pi"])
    ts(T.pi[:], T.pi[:], 31, None, A.bitwise_and, None, ["pi"], ["pi"])
    tt(T.cq[:], T.pi[:], T.cq[:], A.add, ["pi", "cq"], ["cq"])
    for b in ("dt", "ic")[OPT["fn"][0] not in "pq":]:
        whole(0.67, T[b][:], [[-1, C]], 160, 0, [b])
    whole(0.4, T.yy[:, 64:224], [[0, 160]], 0, 0, ["yy"])
    whole(0.7, T.rp[:, 304:640], [[0, 336]], 0, 0, ["rp"])
    whole(0.56, T.zo[:, 4 * OWN:512], [[0, 512 - 4 * OWN]], 0, 0, [("zo", 1, 2)])
    for a in (0, C + 16) * (not OPT["one"]):
        whole(0.16, T.n1[:, a:a + 16], [[0, 16]], 0, 0, [("n1", 8 + a / 1024, 8 + (a + 1) / 1024)])
    K(1.1, lambda q: q.iota(T.one[:], [[0, 528]], 1, 0, allow_small_or_imprecise_dtypes=True), [], ["one"])
    K(1.1, lambda q: q.affine_select(T.big[:], T.one[:], [[-1, 528]], A.is_equal, 0.0, 3, 4), ["one"], ["big"])
    ts(T.pa[:], T.pa[:], 15, None, A.bitwise_and, None, ["pa"], ["pa"])
    ts(T.ji[:], T.ji[:], 15, None, A.bitwise_and, None, ["ji"], ["ji"])
    ts(T.t1[:, 0:16], T.ji[:], 1.0, 320.0, A.is_equal, A.mult, ["ji"], [("t1", 0, 1)])
    ts(T.t1[:, 16:32], T.ji[:], 0.0, -16384.0, A.is_equal, A.mult, ["ji"], [("t1", 1, 2)])
    tt(T.w16[:], T.t1[:, 0:16], T.t1[:, 16:32], A.add, ["t1"], ["w16"])
    cp(U("so"), T.pa[:, 0:NB], ["pa"], ["so"])
    act(T.wt[:], T.w16[:].indirect(U("so")), ["w16", "so"], ["wt"], gat())
    tt(L("cw", 32), T.pa[:], T.ci[:], A.add, ["pa", "ci"], ["cw"])
    cp(T.uo[:], T.ci[:, 0:8], ["ci"], ["uo"])
    row = T.pa[:, 0:1]
    ts(cf("e15"), row, 15.0, None, A.is_equal, None, ["pa"], ["e15"])
    for name, a, b in (("col", 320.0, -160.0), ("nc", -320.0, 160.0), ("f0", 320.0, -320.0), ("a1", -1.0, 1.0)):
        if name != "nc" or "n" in OPT["ex"]:
            act(cf(name), cf("e15"), ["e15"], [name], SMALL, scale=a, bias=b)
    for a in (0, C + 16) * (not OPT["one"]):
        act(T.e1[:, a:a + 16], T.w16[:], ["w16"], [("e1", 8 + a / 1024, 8 + (a + 1) / 1024)], SMALL, scale=0.0)
    for b in range(4):
        V(0.16, lambda q, b=b: q.quantize_mx(T.eq[:, 128 * b:128 * b + 128], T.ep[:, 128 * b:128 * b + 128], T.big[:, 3 - b:515 - b]),
          ["big"], [("eq", b, b + 1), ("ep", b, b + 1)])

    ts(T.bits[:], T.sh[:], 4, 1, A.arith_shift_right, A.bitwise_and, ["sh"], ["bits"])
    cp(cf("bt", 0, 10), T.bits[:], ["bits"], ["bt"])
    act(cf("sc", 1, 4, 3), cf("bt", 1, 4, 2), ["bt", "a1"], [("sc", 1, 2)], SMALL, scale=cf("a1"))
    act(cf("bi", 0, 3, 3), cf("bt", 0, 3, 2), ["bt"], [("bi", 0, 0.5)], SMALL, scale=BIG, bias=-BIG)
    ts(cf("e0"), row, 0.0, -BIG, A.not_equal, A.mult, ["pa"], ["e0"])
    act(cf("bi", 9), cf("bt", 6), ["bt", "e0"], [("bi", 0.5, 1)], SMALL, scale=BIG, bias=cf("e0"))
    act(cf("bi", 1, 4, 3), cf("sc", 1, 4, 3), [("sc", 1, 2)], [("bi", 1, 2)], SMALL, scale=9 * KEY, bias=-8 * KEY)
    if "v" in OPT["pl"]:
        V(SMALL, lambda q: q.tensor_reduce(cf("kv"), cf("sc", 1, 4, 3), AxisListType.X, A.add), [("sc", 1, 2)], ["kv"])
        act(cf("kv"), cf("kv"), ["kv"], ["kv"], SMALL, scale=KEY)
        act(T.idk[:], T.idr[:], ["idr", "kv"], ["idk"], bias=cf("kv"))
    if set("nm") & set(OPT["pl"]):
        act(cf("k1"), cf("sc", 7), [("sc", 1, 2)], ["k1"], SMALL, scale=-KEY)
        if "m" in OPT["pl"]:
            act(cf("k1"), cf("sc", 4), [("sc", 1, 2), "k1"], ["k1"], SMALL, scale=-KEY, bias=cf("k1"))
        act(cf("k1"), cf("sc", 10), [("sc", 1, 2), "k1"], ["k1"], SMALL, scale=-KEY, bias=cf("k1"))
        act(cf("b1"), cf("e15"), ["e15"], ["b1"], SMALL, scale=-2.0, bias=1.0)
        act(T.gs[:], T.idr[:], ["idr", "b1"], ["gs"], scale=cf("b1"), short=True)
    if "w" in OPT["pl"]:
        V(SMALL, lambda q: q.tensor_reduce(cf("nv"), cf("sc", 1, 4, 3), AxisListType.X, A.add), [("sc", 1, 2)], ["nv"])
        act(cf("nv"), cf("nv"), ["nv"], ["nv"], SMALL, scale=-KEY)
    if set("wbrs") & set(OPT["pl"] + OPT["fn"]):
        whole(1.2, T.wd[:], [[1, 2 * C]], -C, 0, ["wd"])
        act(L("cm"), L("cw"), ["cw"], ["cm"], SMALL, bias=-float(C))
        if set("wb") & set(OPT["pl"]) or "s" in OPT["ex"]:
            ts(L("cn"), L("cm"), cf("col"), None, A.subtract, None, ["cm", "col"], ["cn"])
    if "a" in OPT["pl"]:
        act(cf("ka"), cf("sc", 10), [("sc", 1, 2)], ["ka"], SMALL, scale=KEY)
        act(T.ida[:], T.idr[:], ["idr", "ka"], ["ida"], bias=cf("ka"))
    if "b" in OPT["pl"]:
        act(cf("na"), cf("sc", 10), [("sc", 1, 2)], ["na"], SMALL, scale=-KEY)
    if set("ab") & set(OPT["pl"]):
        act(cf("kr"), cf("e15"), ["e15"], ["kr"], SMALL, scale=8 * KEY, bias=-8 * KEY)
        act(T.gr[:], T.idr[:], ["idr", "e15", "kr"], ["gr"], scale=cf("e15"), bias=cf("kr"))
        K(0.67, lambda q: q.iota(T.gw[:], [[0, C]], -8 * int(KEY), 0, allow_small_or_imprecise_dtypes=True), [], ["gw"])
    pl = cf("bt", 6)
    act(cf("up_"), pl, ["bt"], ["up_"], SMALL, scale=BIG)
    act(T.fs[:], T.idr[:], ["idr", "up_"], ["fs"], bias=cf("up_"))
    tt(cf("par"), cf("bt", 8), cf("bt", 0), A.not_equal, ["bt"], ["par"])
    if not OPT["one"]:
        act(cf("p21"), cf("par"), ["par"], ["p21"], SMALL, scale=16.0 * (NB + 1), bias=15.0)
    ts(L("pk", 2), L("cw", 2), NB - 1.0, 16.0, A.min, A.mult, ["cw"], ["pk"])
    if not OPT["one"]:
        ts(T.pick[:, 0:2], L("pk", 2), cf("p21"), None, A.add, None, ["pk", "p21"], [("pick", 0, 1)])
    act(cf("dd"), cf("bt", 8), ["bt"], ["dd"], SMALL, scale=30.0, bias=-95.0)
    act(cf("dd"), cf("dd"), ["dd", "par"], ["dd"], SMALL, scale=cf("par"), bias=96.0)
    ts(T.pick[:, 2:4], L("cw", 2), NB - 1.0, cf("dd"), A.min, A.add, ["cw", "dd"], [("pick", 1, 2)])
    act(cf("m1"), cf("par"), ["par"], ["m1"], SMALL, scale=-15.0 / 16, bias=1.0)
    act(cf("d0"), cf("bt", 8), ["bt"], ["d0"], SMALL, scale=30.0, bias=506.0)
    act(cf("d0"), cf("d0"), ["d0", "par"], ["d0"], SMALL, scale=cf("par"), bias=7.0)
    act(T.pick[:, 4:6], L("pk", 2), ["pk", "m1", "d0"], [("pick", 2, 3)], SMALL, scale=cf("m1"), bias=cf("d0"))
    if OPT["one"]:
        act(cf("p21"), cf("bt", 8), ["bt"], ["p21"], SMALL, scale=30.0, bias=498.0)
        act(cf("p21"), cf("p21"), ["p21", "par"], ["p21"], SMALL, scale=cf("par"), bias=15.0)
        act(T.pick[:, 0:2], L("pk", 2), ["pk", "m1", "p21"], [("pick", 0, 1)], SMALL, scale=cf("m1"), bias=cf("p21"))
        whole(0.7, T.r1[:, C:640], [[0, C]], 0, 0, ["r1"])
    ts(cf("e8"), row, 8.0, -1.0, A.is_equal, A.mult, ["pa"], ["e8"])
    act(cf("e8"), pl, ["bt", "e8"], ["e8"], SMALL, bias=cf("e8"))

    V(0.16, lambda q: q.quantize_mx(T.uq[:], T.up[:], T.ut[:]), ["ut"], ["uq", "up"])
    cp(T.uqr[:].bitcast(dt.uint32), T.uq[:].bitcast(dt.uint32).indirect(T.uo[:]), ["uq", "uo"], ["uqr"], gat(128))
    act(T.upr[:], T.up[:].indirect(T.uo[:]), ["up", "uo"], ["upr"], gat(128))
    V(0.16, lambda q: q.quantize_mx(T.vq[:], T.vp[:], T.vt[:]), ["vt"], ["vq", "vp"])

    cp(U("l0"), T.nxi[:], ["nxi"], ["l0"])
    cp(U("mt16"), T.mti[:], ["mti"], ["mt16"])
    tt(L("dm"), T.mti[:], L("cw"), A.subtract, ["mti", "cw"], ["dm"])
    act(L("bf"), L("dm"), ["dm", "f0"], ["bf"], SMALL, scale=cf("f0"))
    tt(L("dc"), L("bf"), L("cw"), A.add, ["bf", "cw"], ["dc"])
    if OPT["tw"]:
        for i, op in enumerate((A.is_lt, A.is_gt)):
            ts(L("c%d" % i), L("dm"), 0.0, float(C), op, A.mult, ["dm"], ["c%d" % i])
    else:
        act(T.sw[:], by("idr", "mt16"), ["mt16", "idr"], ["sw"], gat())
        move("sg", T.sw[:], T.ic[:], ["ic"], ["sw"], True)
        task(P, "s", ROW, lambda q: q.activation(T.sg[:], T.sw[:], AF.Sign), ["sw"], ["sg"])

    def weighted(dst, src, a=0):
        V(HALF, lambda q: q.tensor_tensor_scan(T[dst][:], T.wt[:], at(src, a), 0.0, A.add, A.max), ["wt", (src, a, a + 1)], [dst])

    def powers(r, first=True):
        f0 = "f0%d" % (r % 2)
        if first:
            act(T[f0][:], by("idr", "l0"), ["idr", "l0"], [f0], gat())
        src, a = f0, 0
        for k, (dst, b) in enumerate([("fa", 0), ("fa", 1), ("ft", 1), ("ft", 2), ("ft", 4)]):
            act(at(dst, b), by(src, "l%d" % k, a), [(src, a, a + 1), "l%d" % k], [(dst, b, b + 1)], gat())
            weighted("scn", dst, b)
            act(U("l%d" % (k + 1)), every("scn", 15), ["scn", "col"], ["l%d" % (k + 1)], 0.1, bias=cf("col"))
            if k == 2 and OPT["pl"][r] in "wb":
                tt(U("dl3"), every("scn", 15), L("cn"), A.subtract, ["scn", "cn"], ["dl3"])
            src, a = dst, b

    def steps(name, t, src, levels, first, end=None):
        for i, k in enumerate(levels):
            w, dst = "m%s%s" % (name, "wx"[i % 2]), "m%s%d" % (name, i % 2)
            c = 3 * (first[1] + k - first[0]) + t
            mask = {"scale": cf("sc", c) if t else cf("bt", 2 * c // 3), "bias": cf("bi", c)} if k >= first[0] else {}
            reads = [src] + [("sc", t, t + 1) if t else "bt", ("bi", t, t + 1)] * bool(mask)
            if k == 6:
                k = 5
                act(at(w), by(src, "l5"), reads + ["l5"], [w], gat(), **mask)
            elif name + str(k) in OPT["cut"]:
                for h, (lo, hi) in enumerate([(0, C // 2), (C // 2, C)]):
                    act(T[w][:, lo:hi], T[src][:, lo:hi], reads, [(w, h, h + 1)], ROW / 2 + 0.02, **mask)
            else:
                act(at(w), at(src), reads, [w], **mask)
            out, reg = end if end and i == len(levels) - 1 else (at(dst), dst)
            tt(out, by(w, "l%d" % k), at(src), A.max, [w, src, "l%d" % k], [reg], gat())
            src = dst
        return src

    def turn(dst, src):
        V(HALF, lambda q: q.transpose(T[dst][:, 0:C], mid(src)), [(src, 0, 4)], [(dst, 0, 1)])
        if not OPT["one"]:
            V(HALF * PW / C, lambda q: q.transpose(T[dst][:, C:TW], T[src][:]), [src], [(dst, 1, 2)])

    def chain(out, n, e, reads, writes, w=C):
        V(HALF * w / C, lambda q: q.tensor_tensor_scan(out, n, e, 0.0, A.mult, A.add), reads, writes)

    def less(dst, l, key=None):
        act(T[dst][:], T.wd[:].indirect(U("d" + l)), ["wd", "d" + l] + [key] * bool(key), [dst], gat(), bias=cf(key) if key else None)

    def places(r):
        if OPT["pl"][r] == "w":
            less("me1", "l3", "nv")
            steps("e", 1, "me1", [3, 4, 5, 6], (3, 0), (mid("e1"), ("e1", 0, 4)))
            turn("te1", "e1")
            act(T.te1[:, 15:TW:16], T.cq[:, 0:TW // 16], ["cq", "te1"], ["te1"], SMALL)
            return
        places2(r)

    def places2(r):
        if OPT["pl"][r] == "v":
            tt(T.me1[:], by("fa", "l2", 1), T.idk[:], A.subtract, [("fa", 1, 2), "l2", "idk"], ["me1"], gat())
            steps("e", 1, "me1", [3, 4, 5, 6], (3, 0), (mid("e1"), ("e1", 0, 4)))
            turn("te1", "e1")
            w = C if OPT["one"] else TW
            act(T.te1[:, 15:w:16], T.cq[:, 0:w // 16], ["cq", "te1"], ["te1"], SMALL)
            return
        if OPT["pl"][r] in "ab":
            if OPT["pl"][r] == "a":
                tt(T.me1[:], by("fa", "l2", 1), T.ida[:], A.subtract, [("fa", 1, 2), "l2", "ida"], ["me1"], gat())
            else:
                less("me1", "l3", "na")
            for b, src, l in (("d1", "me1", "l3"), ("d2", "me1", "l4"), ("d3", "d1", "l4")):
                act(T[b][:], by(src, l), [src, l], [b], gat())
            lay("g0%d" % r, [("gr", "me1", 6, 8), ("gw", "me1", 2, 8), ("gr", "d1", 5, 8), ("gw", "d1", 1, 8)])
            lay("g1%d" % r, [("gr", "d2", 4, 8), ("gw", "d2", 0, 8), ("gr", "d3", 3, 8), ("gw", "d3", 7, 16)])
            tt(T.me0[:], by("gw", "l5"), T.gr[:], A.max, ["gw", "gr", "l5"], ["me0"], gat())
            act(T.mex[:], by("me0", "l5"), ["me0", "l5", ("sc", 1, 2), ("bi", 1, 2)], ["mex"], gat(), scale=cf("sc", 10), bias=cf("bi", 10))
            tt(mid("e1"), by("mex", "l5"), T.me0[:], A.max, ["mex", "me0", "l5"], [("e1", 0, 4)], gat())
            turn("te1", "e1")
            return
        if OPT["pl"][r] == "m":
            for i, (a, step) in enumerate([(1, 4), (3, 8), (7, 16)]):
                move("g%d%d" % (i, r), T.gs[a:128:step, :], T.ft[a:128:step, C:2 * C], [("ft", 1, 2)], [("gs", a, a + 1)])
            act(T.mex[:], T.gs[:], ["gs", "a1", "k1"], ["mex"], scale=cf("a1"), bias=cf("k1"))
            tt(T.d1[:], by("mex", "l3"), T.gs[:], A.subtract, ["mex", "gs", "l3"], ["d1"], gat())
            steps("e", 1, "d1", [4, 5, 6], (4, 1), (mid("e1"), ("e1", 0, 4)))
            turn("te1", "e1")
            return
        act(at("ft", 3), by("ft", "l3", 2), [("ft", 2, 3), "l3"], [("ft", 3, 4)], gat())
        for i, (b, a, step) in enumerate([(1, 1, 4), (2, 0, 4), (3, 3, 8), (3, 7, 16)]):
            move("g%d%d" % (i, r), T.gs[a:128:step, :], T.ft[a:128:step, C * b:C * b + C], [("ft", b, b + 1)], [("gs", a, a + 1)])
        act(T.mex[:], T.gs[:], ["gs", "a1", "k1"], ["mex"], scale=cf("a1"), bias=cf("k1"))
        tt(T.me1[:], by("mex", "l3"), T.gs[:], A.subtract, ["mex", "gs", "l3"], ["me1"], gat())
        steps("e", 1, "me1", [5, 6], (5, 2), (mid("e1"), ("e1", 0, 4)))
        turn("te1", "e1")

    sent = [0]

    def send(r, pairs, sem, land, latency, relay=False):
        dst, src = T.cores[(rank + r + 1) % n], T.cores[(rank - r - 1) % n]
        there = sem
        if relay:
            dst, src, there = neighbour(core, T, topo), neighbour(src, T, topo), "hx%d" % r
        rid, pid, _ = topo.addr(dst)
        m = topo.mask(core, dst)
        ids = []
        for out, in_, name in pairs:
            ids.append(task(P, "g", 0.1, lambda q, out=out, in_=in_: q.remote_dma(out, in_, T.sem[there], T.sem.snd, pid, rid, m), [name], [], "send"))
            sent[0] += len(topo.engines(core, dst))
        return task(P, "net", latency, None, [], land, "land", sem, len(topo.engines(src, core)) * len(pairs), after=ids)

    def home(r, k):
        lp, al, o = "lp%d" % r, "al%d" % r, B0 * k
        if k:
            tt(T.yy[:, 96:96 + NB], every("rb", 7), every("rb", 8), A.subtract, ["rb"], [("yy", 96, 128)])
            V(SMALL, lambda q: q.transpose(T.yy[:, 176:208], T.yy[:, 96:128]), [("yy", 96, 128)], [("yy", 176, 208)])
            V(SMALL, lambda q: q.transpose(T.yy[:, 0:64], T.yy[:, 160:224]), [("yy", 160, 224)], [("yy", 0, 64)])
            tt(T[lp][:, o:o + 32], T.yy[:, 0:128].indirect(T.pick[:, 2:4]), L("ua", 32), A.add, [("yy", 0, 128), ("pick", 1, 2), "ua"], [(lp, o, o + 32)], 0.12)
        else:
            V(SMALL, lambda q: q.transpose(T.rp[:, 592:624], T.rp[:, 7:512:16]), [("rp", 0, 512)], [("rp", 592, 624)])
            V(SMALL, lambda q: q.transpose(T.rp[:, 512:576], T.rp[:, 576:640]), [("rp", 576, 640)], [("rp", 512, 576)])
            act(T[lp][:, o:o + 32], T.rp[:, 0:576].indirect(T.pick[:, 4:6]), [("rp", 0, 576), ("pick", 2, 3)], [(lp, o, o + 32)], 0.12, bias=160.0)
        send(r, [(T[al][:, o:o + ZC // 16], T[lp][:, o:o + ZC // 16], (lp, o, o + NB))], "a%s%d" % ("pb"[k], r), [(al, o, o + NB)], OPT["ll"])
        for t in range(4):
            act(T.go[:, 4 * OWN * k + t:4 * OWN * (k + 1):4], at("fo", t).indirect(T[lp][:, o + ZC // 16:o + NB]), [("fo", t, t + 1), (lp, o, o + NB)],
                [("go", 4 * k + t, 4 * k + t + 1)], gat(OWN), scale=0.5)
        if k:
            a, zq, zp = 128 * r, "zq%d" % r, "zp%d" % r
            tt(T.zo[:, 0:4 * OWN], T.go[:, 0:4 * OWN], T.go[:, 4 * OWN:8 * OWN], A.add, ["go"], [("zo", 0, 1)], OPT["ta"])
            V(0.16, lambda q: q.quantize_mx(T.oq[:, a:a + 128], T["op"][:, a:a + 128], T.zo[:]), ["zo"], [("oq", r, r + 1), ("op", r, r + 1)])
            send(r, [(T[zq][:, ZC:C].bitcast(dt.uint8), T.oq[:, a:a + OWN].bitcast(dt.uint8), ("oq", r, r + 1)),
                     (T[zp][:, ZC:C], T["op"][:, a:a + OWN], ("op", r, r + 1))], "az%d" % r, [(zq, 2, 3), (zp, 2, 3)], OPT["zl"])

    def bank(out, b, w=C):
        return T[out][:, BANK * b:BANK * b + w]

    def parts(name):
        return enumerate([(0, OPT[name]), (OPT[name], ZC if name == "z" else C)])

    def mm(out, b, wq, wp, a, xq, xp, unit, h=0, lo=0, hi=C):
        whole = hi - lo == C
        task(P, "t", 0.02 + 0.33 * (hi - lo) / C,
             lambda q: q.matmul_mx(bank(out, b, hi - lo), T[wq][:, a:a + 128], T[wp][:, a:a + 128], T[xq][:, lo:hi], T[xp][:, lo:hi], True, True),
             [(wq, unit, unit + 1), (wp, unit, unit + 1), xq if whole else (xq, h, 2 * h + 1), xp if whole else (xp, h, 2 * h + 1)], [(out, b, b + 1)])

    def quantize(xq, xp, X, h, lo, hi):
        V(0.02 + 0.35 * (hi - lo) / C, lambda q: q.quantize_mx(T[xq][:, lo:hi], T[xp][:, lo:hi], T[X][:, 4 * lo:4 * hi]),
          [(X, 4 * h, 4 * h + 4)], [(xq, h, h + 1), (xp, h, h + 1)])

    def look(win, l, a, b, lo, hi):
        act(T.gp[:, C * b + lo:C * b + hi], at(win, b).indirect(T[l][:, a + lo // 16:a + hi // 16]),
            [(win, b, b + 1), (l, a + lo // 16, a + hi // 16)], [("gp", b + lo / C, b + hi / C)], gat(hi - lo))

    def add_by(out, win, l, other, h, lo, end, cut, xps=(), full=C):
        for b in range(4):
            hi, written = end, [(out, 4 * h + b, 4 * h + b + 1)]
            if b not in cut:
                if h:
                    continue
                hi, written = full, written + [(out, 4 + b, 5 + b)]
            if b in xps:
                tt(T[out][:, 4 * lo + b:4 * hi:4], T.pu[:, BANK * b + lo:BANK * b + hi], T.gp[:, C * b + lo:C * b + hi], A.add,
                   [("pu", b, b + 1), ("gp", b + lo / C, b + hi / C)], written, ROW * (hi - lo) / C + 0.01)
                continue
            tt(T[out][:, 4 * lo + b:4 * hi:4], at(win, b).indirect(T[l][:, B0 + lo // 16:B0 + hi // 16]), T[other][:, C * b + lo:C * b + hi], A.add,
               [(win, b, b + 1), (l, B0 + lo // 16, B0 + hi // 16), (other, b + lo / C, b + hi / C)], written, gat(hi - lo))

    def store(e, out, in_, reads):
        k = task(P, e, 0.07, lambda q: q.dma_start(out, in_), reads, [], "dma", "st", 16)
        task(P, "net", 2.0, None, [], [], "land", "st", 16, after=[k])

    if OPT["fn"][0] in "rs":
        tt(U("dl0"), T.nxi[:], L("cm"), A.subtract, ["nxi", "cm"], ["dl0"])
    powers(0)
    for h, (lo, hi) in parts("x"):
        quantize("xq0", "xp0", "x0", h, lo, hi)
    for r in range(ROUNDS):
        xq, xp, aq, ap = "xq%d" % r, "xp%d" % r, "aq%d" % r, "ap%d" % r
        lp, al, f0 = "lp%d" % r, "al%d" % r, "f0%d" % (r % 2)
        xps = OPT["xps"] if r < ROUNDS - 1 else OPT["xpl"]
        for h, (lo, hi) in parts("x"):
            for i, b in enumerate(("sa", "sb")):
                k = 2 * h + i
                mm("pw", k, "uqr", "upr", 0, xq, xp, 0, h, lo, hi)
                act(T[b][:, lo:hi], bank("pw", k, hi - lo), [("pw", k, k + 1)], [(b, h, h + 1)], ROW * (hi - lo) / C + 0.02)
        if OPT["relay"]:
            send(r, [(at("hq", r).bitcast(dt.uint8), T[xq][:].bitcast(dt.uint8), xq), (at("hp", r), T[xp][:], xp)], "ax%d" % r, [aq, ap], 8.5, True)
        else:
            send(r, [(T[aq][:].bitcast(dt.uint8), T[xq][:].bitcast(dt.uint8), xq), (T[ap][:], T[xp][:], xp)], "ax%d" % r, [aq, ap], 6.0)
        places(r)
        s = ("sa", 0, 2)
        fn = OPT["fn"][r]
        tt(T.er[:], by("sb", "l0"), at("sa"), A.max, ["sb", s, "l0"], ["er"], gat())
        tt(T.eh[:], by("er", "l0"), at("sa"), A.max, ["er", s, "l0"], ["eh"], gat())
        act(T.mfw[:], by("er", "l1"), ["er", "l1"], ["mfw"], gat())
        tt(T.mfx[:], by("eh", "l2"), T.mfw[:], A.max, ["eh", "mfw", "l2"], ["mfx"], gat())
        tt(T.mf1[:], by("mfx", "l0"), T.eh[:], A.max, ["mfx", "eh", "l0"], ["mf1"], gat())
        coarse = steps("c", 0, "mf1", range(3, 7), (3, 0))
        if fn in "PQ":
            tt(T.dt[:], by("idr", "l0"), T.ic[:], A.add, ["idr", "l0", "ic"], ["dt"], gat())
        elif fn in "rs":
            less("dt", "l0")
        else:
            if r:
                move("b%d" % r, T.dt[:], T.ic[:], ["ic"], ["dt"])
            move("a%d" % r, T.dt[:], T[f0][:], [f0], ["dt"], True)
        act(T.pw0[:], by("dt", "l0"), ["dt", "l0"], ["pw0"], gat())
        if fn in "pPr":
            lay("t%d" % r, [("pw0", "dt", 1, 2)])
            act(T.pw1[:], by("pw0", "l2"), ["pw0", "l2"], ["pw1"], gat())
            rows = [("pw1", "pw0", a, 16) for a in range(4, 8)]
        else:
            act(T.pw1[:], by("pw0", "l2"), ["pw0", "l2"], ["pw1"], gat())
            act(T.pw2[:], by("dt", "l2"), ["dt", "l2"], ["pw2"], gat())
            rows = [("pw1", b, a, 16) for b, a in (("pw2", 1), ("pw2", 3), ("pw0", 4), ("dt", 5), ("pw0", 6), ("dt", 7))]
        apart = OPT["ap"][r] == "a"
        lay("u%d" % r, rows + [("pw1", "eh", 10, 16), ("pw1", "mfw", 9, 16)] * (not apart))
        act(T.pw2[:], by("pw1", "l1"), ["pw1", "l1"], ["pw2"], gat())
        lay("s%d" % r, [("fs", b, a, 16) for b, a in (("sa", 14), ("er", 13), ("eh", 12), ("mfw", 11), ("mfx", 8), ("mf1", 15))])
        if apart:
            act(T.sb[:], by("er", "l2"), ["er", "l2"], ["sb"], gat())
            act(T.mf0[:], by("eh", "l1"), ["eh", "l1"], ["mf0"], gat())
            lay("w%d" % r, [("fs", "sb", 9, 16), ("fs", "mf0", 10, 16)])
        else:
            lay("w%d" % r, [("fs", "pw2", 9, 16), ("fs", "pw2", 10, 16)])
        lay("v%d" % r, [("pw2", "pw1", a, 16) for a in (2, 3, 6, 7)] + [("pw2", "ic", 8, 16)])
        act(T.mf0[:], by("fs", "l0"), ["fs", "l0"], ["mf0"], gat())
        for b in range(4):
            mm("pu", b, "eq", "ep", 128 * b, xq, xp, b)
            act(at("fo", b), bank("pu", b), [("pu", b, b + 1)], [("fo", b, b + 1)])
        for b in range(4):
            mm("pu", b, "eq", "ep", 128 * b, aq, ap, b)
            act(at("fh", b), bank("pu", b), [("pu", b, b + 1)], [("fh", b, b + 1)], scale=0.5)
            if b in xps:
                mm("pu", b, "eq", "ep", 128 * b, xq, xp, b)
        tt(mid("n1"), by(coarse, "l0"), at("sa"), A.is_le, [coarse, "l0", s], [("n1", 0, 4)], gat())
        turn("tn1", "n1")
        for h, (a, b) in enumerate([(0, C), (C, TW)][:2 - OPT["one"]]):
            chain(T.r1[:, a:b], T.tn1[:, a:b], T.te1[:, a:b], [("tn1", h, h + 1), ("te1", h, h + 1)], [("r1", h, h + 1)], b - a)
        if OPT["one"]:
            V(SMALL, lambda q: q.transpose(T.r1[:, 592:624], T.r1[:, 15:512:16]), [("r1", 0, 2)], [("r1", 3, 4)])
            V(SMALL, lambda q: q.transpose(T.r1[:, 512:576], T.r1[:, 576:640]), [("r1", 3, 4)], [("r1", 2, 3)])
        got = T.r1[:, 0:576 if OPT["one"] else TW].indirect(T.pick[:, 0:2])
        act(U("lq", 32), got, [("r1", 0, 3), ("pick", 0, 1)], ["lq"], 0.1, bias=160.0)
        tt(T.n2[:], by("mf0", "lq"), at("sa"), A.is_le, ["mf0", "lq", s], ["n2"], gat())
        act(T.e2[:], by("pw2", "lq"), ["pw2", "lq", "e8"], ["e2"], gat(), scale=cf("e8"))
        for x in ("n2", "e2"):
            V(HALF, lambda q, x=x: q.transpose(T["t" + x][:], T[x][:]), [x], ["t" + x])
        chain(T.rp[:, 0:C - 7], T.tn2[:, 7:C], T.te2[:, 1:C - 6], ["tn2", "te2"], [("rp", 0, C)])
        home(r, 0)
        tt(L("ua", 32), got, L("cw", 32), A.add, [("r1", 0, 3), ("pick", 0, 1), "cw"], ["ua"], 0.1)
        tt(L("ta"), every("r1", 15), T.cq[:, 0:NB], A.subtract, ["cq", ("r1", 0, 1)], ["ta"])
        tt(every("te2", 7), every("te2", 7), L("ta"), A.add, ["te2", "ta"], ["te2"])
        chain(T.rb[:, 0:C - 7], T.tn2[:, 7:C], T.te2[:, 0:C - 7], ["tn2", "te2"], ["rb"])
        home(r, 1)
        if OPT["tw"]:
            act(at("sa", 1), at("sa"), [s], [("sa", 2, 3)], scale=-1.0)
            for i, b in enumerate(("er", "eh")):
                tt(T.le[:, 32 * i:32 * i + NB], T[lp][:, B0:B0 + NB], L("c%d" % i), A.add, [(lp, B0, B0 + NB), "c%d" % i], [("le", i, i + 1)])
                act(T[b][:], T.sa[:].indirect(T.le[:, 32 * i:32 * i + NB]), ["sa", ("le", i, i + 1)], [b], gat())
        else:
            tt(T.er[:], at("sa").indirect(T[lp][:, B0:B0 + NB]), T.sg[:], A.mult, [s, "sg", (lp, B0, B0 + NB)], ["er"], gat())
            act(T.eh[:], T.er[:], ["er"], ["eh"], scale=-1.0)
        tt(T.sw[:], by("er", "mt16"), T.eh[:], A.is_gt, ["er", "eh", "mt16"], ["sw"], gat())
        weighted("swn", "sw")
        if r < ROUNDS - 1 and OPT["ex"][r] == "s":
            f1 = "f0%d" % (1 - r % 2)
            tt(L("sx"), every("swn", 15), L("dm"), A.mult, ["swn", "dm"], ["sx"])
            tt(U("sig"), L("sx"), L("dc"), A.add, ["sx", "dc"], ["sig"])
            act(T[f1][:], by(f0, "sig"), [f0, "sig"], [f1], gat())
            weighted("fmn", f1)
            act(U("l0"), every("fmn", 15), ["fmn", "col"], ["l0"], 0.1, bias=cf("col"))
            if OPT["fn"][r + 1] in "rs":
                tt(U("dl0"), every("fmn", 15), L("cn"), A.subtract, ["fmn", "cn"], ["dl0"])
            powers(r + 1, False)
        elif r < ROUNDS - 1:
            act(T.fm[:], by(f0, "mt16"), [f0, "mt16"], ["fm"], gat())
            weighted("fmn", "fm")
            cp(L("fl"), U("l0"), ["l0"], ["fl"])
            act(L("be"), L("fl"), ["fl", "nc"], ["be"], SMALL, bias=cf("nc"))
            tt(L("dn"), every("fmn", 15), L("be"), A.subtract, ["fmn", "be"], ["dn"])
            act(L("bf"), L("dn"), ["dn", "f0"], ["bf"], SMALL, scale=cf("f0"))
            tt(L("de"), L("bf"), L("fl"), A.add, ["bf", "fl"], ["de"])
            tt(L("sx"), every("swn", 15), L("dn"), A.mult, ["swn", "dn"], ["sx"])
            tt(U("l0"), L("sx"), L("de"), A.add, ["sx", "de"], ["l0"])
            if OPT["fn"][r + 1] in "rs":
                tt(L("be"), L("de"), L("cm"), A.subtract, ["de", "cm"], ["be"])
                tt(U("dl0"), L("sx"), L("be"), A.add, ["sx", "be"], ["dl0"])
            powers(r + 1)
        else:
            tt(L("sx"), every("swn", 15), L("dm"), A.mult, ["swn", "dm"], ["sx"])
            tt(U("sig"), L("sx"), L("dc"), A.add, ["sx", "dc"], ["sig"])
            act(T.er[:], by(f0, "sig"), [f0, "sig"], ["er"], gat(), bias=160.0)
            store("y", T.nf[:], T.er[0:128:16, :], ["er"])
        for b in range(4):
            for h, (lo, hi) in parts("z") if b in OPT["zg"] else [(0, (0, ZC))]:
                look("fh", al, 0, b, lo, hi)
        for h, (lo, hi) in parts("z"):
            add_by("z", "fh", al, "gp", h, lo, hi, OPT["zs"], (), ZC)
            quantize("zq%d" % r, "zp%d" % r, "z", h, lo, hi)
            hi = C if h else hi
            for b in range(4):
                ps = "pu" if h and b not in xps else "pw"
                if b not in OPT["hs"]:
                    if h:
                        mm("pw", b, "wq", "wp", 128 * b, "zq%d" % r, "zp%d" % r, b)
                        act(at("h", b), bank("pw", b), [("pw", b, b + 1)], [("h", b, b + 1)], scale=0.03125)
                    continue
                mm(ps, b, "wq", "wp", 128 * b, "zq%d" % r, "zp%d" % r, b, h, lo, hi)
                act(T.h[:, C * b + lo:C * b + hi], bank(ps, b, hi - lo), [(ps, b, b + 1)], [("h", b + lo / C, b + hi / C)],
                    ROW * (hi - lo) / C + 0.02, scale=0.03125)
        for b in xps:
            look("h", lp, B0, b, 0, C)
        for h, (lo, hi) in parts("x"):
            add_by("x%d" % (r + 1), "h", lp, "fo", h, lo, hi, OPT["xs"], xps)
            quantize("xq%d" % (r + 1), "xp%d" % (r + 1), "x%d" % (r + 1), h, lo, hi)
    xq, xp = "xq%d" % ROUNDS, "xp%d" % ROUNDS
    for h, (lo, hi) in parts("x"):
        store("y", T.oc[:, 4 * lo:4 * hi], T[xq][:, lo:hi].bitcast(dt.uint8), [(xq, h, h + 1)])
        mm("pw", h, "vq", "vp", 0, xq, xp, 0, h, lo, hi)
        act(T.eh[:, lo:hi], bank("pw", h, hi - lo), [("pw", h, h + 1)], [("eh", h, h + 1)], ROW * (hi - lo) / C)
        store("y", T.y[:, lo:hi], T.eh[:, lo:hi], [("eh", h, h + 1)])
    for k in range(4):
        store("y" if k % 2 else "s", T.osc[4 * k:4 * k + 4, :], T[xp][32 * k:32 * k + 4, :], [xp])
    return sent[0]


def neighbour(core, T, topo):
    return [c for c in topo.cores_of(core) if T.rank_of(c) is None and topo.die(c) == topo.die(core)
            and all(topo.may_write(c, d) for d in T.cores if d != core)][0]


def hand_on(g, core, rank, T, topo):
    sent = 0
    for r in range(ROUNDS):
        dst = T.cores[(rank + r + 1) % len(T.cores)]
        rid, pid, _ = topo.addr(dst)
        g.wait_ge(T.sem["hx%d" % r], 2 * len(topo.engines(T.cores[rank], core)))
        for out, in_ in ((T["aq%d" % r][:].bitcast(dt.uint8), T.hq[:, C * r:C * r + C].bitcast(dt.uint8)), (T["ap%d" % r][:], T.hp[:, C * r:C * r + C])):
            g.remote_dma(out, in_, T.sem["ax%d" % r], T.sem.snd, pid, rid, topo.mask(core, dst))
            sent += len(topo.engines(core, dst))
    g.wait_ge(T.sem.snd, sent)


def rank_program(g, core, T, topo):
    if T.rank_of(core) is None:
        for rank, c in enumerate(T.cores):
            if OPT["relay"] and neighbour(c, T, topo) == core:
                hand_on(g, core, rank, T, topo)
        return
    P = new_plan()
    sent = build(P, g, core, T, topo)
    if "order" not in SHARED:
        SHARED["order"] = schedule(P)
    order, start, _ = SHARED["order"]
    count = issue(P, order, start, g, T)
    g.sync.wait_ge(T.sem.st, 16 * sum(1 for t in P["tasks"] if t["sem"] == "st" and t["kind"] == "dma"))
    for s, k in sorted(count.items()):
        g.sync.wait_ge(T.sem[s], k)
    g.wait_ge(T.sem.snd, sent)
